import numpy as np
import ml_dtypes


def mxq(x, axis, fmt="e4m3"):
    dtype, down = {"e4m3": (ml_dtypes.float8_e4m3fn, 7), "e5m2": (ml_dtypes.float8_e5m2, 14)}[fmt]
    v = np.moveaxis(np.asarray(x, np.float32).astype(ml_dtypes.bfloat16).astype(np.float64), axis, -1)
    blocks = v.reshape(v.shape[:-1] + (-1, 32))
    amax = np.abs(blocks).max(-1, keepdims=True)
    byte = np.maximum(np.where(amax > 0, np.frexp(amax)[1] - 1 + 127, 0) - down, 1)
    scale = np.exp2(byte - 127.0)
    codes = (blocks / scale).astype(np.float32).astype(dtype).astype(np.float64)
    return np.moveaxis((codes * scale).reshape(v.shape), -1, axis)


WIDE = False


def mx_kscale(k):
    if not WIDE:
        return np.ones(k)
    levels = np.array([10, -10, 5, -5, 0])
    if k % 512:
        return np.exp2(np.random.permutation(np.resize(levels, k // 32))).repeat(32)
    a = np.empty((k // 512, 16))
    for p in range(k // 512):
        a[p, :8] = np.random.permutation(np.resize(levels, 8))
        for g in range(8):
            far = levels[np.abs(levels - a[p, g]) >= 10]
            a[p, g + 8] = far[np.random.randint(len(far))]
    return np.exp2(a.ravel()).repeat(32)


BF16 = ml_dtypes.bfloat16


def bf(x):
    return np.asarray(x, np.float32).astype(BF16)


def f64(x):
    return np.asarray(x).astype(np.float64)

E4M3FN = np.array([(-1.0 if i & 128 else 1.0) * ((1.0 + (i & 7) / 8.0) * 2.0 ** (((i >> 3) & 15) - 7) if i & 120 else (i & 7) * 2.0 ** -9) for i in range(256)])


def e4m3fn_bytes(y):
    return np.clip(np.asarray(y, np.float64), -448.0, 448.0).astype(np.float32).astype(ml_dtypes.float8_e4m3fn).view(np.uint8)


def e4m3fn_values(b):
    return E4M3FN[b]


T, K, N, R, G = 1024, 2048, 1536, 512, 128
FP8_MAX = 448.0


def setup_inputs():
    s, t = mx_kscale(K), mx_kscale(R)
    x = np.random.standard_normal((T, K)) * s
    w = np.random.standard_normal((N, K)) / np.sqrt(K) / s
    x_scale = (np.abs(x).reshape(T, K // G, G).max(axis=2) / FP8_MAX).astype(np.float32)
    w_scale = (np.abs(w).reshape(N // G, G, K // G, G).max(axis=(1, 3)) / FP8_MAX).astype(np.float32)
    x_bytes = e4m3fn_bytes(x / np.repeat(f64(x_scale), G, axis=1))
    w_bytes = e4m3fn_bytes(w / np.repeat(np.repeat(f64(w_scale), G, axis=0), G, axis=1))
    return {"x_bytes": x_bytes, "x_scale": x_scale,
            "w_bytes": w_bytes, "w_scale": w_scale,
            "a": bf(np.random.standard_normal((K, R)) / np.sqrt(K) / s[:, None] * t),
            "lam": bf(1 + 0.1 * np.random.standard_normal(R)),
            "b": bf(np.random.standard_normal((R, N)) / np.sqrt(R) / t[:, None]),
            "c": bf(np.random.uniform(0.5, 1.5, T))}


def reference(x_bytes, x_scale, w_bytes, w_scale, a, lam, b, c):
    x = e4m3fn_values(x_bytes) * np.repeat(f64(x_scale), G, axis=1)
    w = e4m3fn_values(w_bytes) * np.repeat(np.repeat(f64(w_scale), G, axis=0), G, axis=1)
    xq = mxq(x, 1, "e4m3")
    base = xq @ mxq(w, 1, "e4m3").T
    h = (xq @ mxq(f64(a), 0, "e4m3")) * f64(lam)
    d = mxq(h, 1, "e4m3") @ mxq(f64(b), 0, "e4m3")
    return base + f64(c)[:, None] * d

@@ -1,0 +1,321 @@
+from contextlib import ExitStack
+
+import concourse.mybir as mybir
+from concourse.masks import make_identity
+
+T, K, N, R, G = 1024, 2048, 1536, 512, 128
+P = 128
+FLOPS = 2 * T * K * N + 2 * T * K * R + 2 * T * R * N
+
+F32 = mybir.dt.float32
+BF16 = mybir.dt.bfloat16
+U32 = mybir.dt.uint32
+U8 = mybir.dt.uint8
+FP8 = mybir.dt.float8_e4m3fn
+FP8X4 = mybir.dt.float8_e4m3fn_x4
+MULT = mybir.AluOpType.mult
+ADD = mybir.AluOpType.add
+COPY = mybir.ActivationFunctionType.Copy
+
+XT = T // P
+PASSES = K // 512
+CHUNKS = ((0, 512), (512, 512), (1024, 256), (1280, 256))
+ORDER = (("x", 0), ("x", 1), ("x", 2), ("x", 3), ("x", 4), ("x", 5), ("x", 6), ("x", 7), ("w", 0), ("w", 1), ("w", 2), ("w", 3))
+SBLOCKS = frozenset(((0, 3), (1, 3), (2, 3), (3, 3), (4, 3), (5, 3), (6, 3), (7, 3), (8, 3), (9, 3), (10, 3), (11, 3), (12, 3), (13, 3), (14, 3), (15, 3), (16, 3), (17, 3), (18, 3), (19, 3),))
+AIL = "SVSV"
+BIL = "SSS"
+
+
+def tile_fp8_base_lora_d2_kernel(tc, x_bytes, x_scale, w_bytes, w_scale, a, lam, b, c, out):
+    nc = tc.nc
+    with ExitStack() as ctx:
+        const = ctx.enter_context(tc.tile_pool(name="const", bufs=1))
+        codes = ctx.enter_context(tc.tile_pool(name="codes", bufs=1))
+        xload = ctx.enter_context(tc.tile_pool(name="xload", bufs=8))
+        wload = ctx.enter_context(tc.tile_pool(name="wload", bufs=12))
+        rload = ctx.enter_context(tc.tile_pool(name="rload", bufs=5))
+        widep = ctx.enter_context(tc.tile_pool(name="widep", bufs=3))
+        groupp = ctx.enter_context(tc.tile_pool(name="groupp", bufs=3))
+        hpool = ctx.enter_context(tc.tile_pool(name="hpool", bufs=3))
+        ypool = ctx.enter_context(tc.tile_pool(name="ypool", bufs=1))
+        ps_t = ctx.enter_context(tc.psum_pool(name="ps_t", bufs=4))
+        ps_h = ctx.enter_context(tc.psum_pool(name="ps_h", bufs=2))
+        ps_b = ctx.enter_context(tc.psum_pool(name="ps_b", bufs=2))
+
+        xs = const.tile([P, XT * 16], F32, name="xs")
+        nc.sync.dma_start(out=xs[:], in_=x_scale.rearrange("(p m) j -> p (m j)", m=XT))
+        x_view = x_bytes.rearrange("(p m) k -> p m k", m=XT)
+        a_view = a.rearrange("(g p j) r -> g p j r", p=P, j=4)
+        b_view = b.rearrange("(p j) n -> p j n", j=4)
+        w_view = w_bytes.rearrange("(r p) k -> r p k", p=P)
+        xb, araw, braw, wb = {}, {}, {}, {}
+
+        def load_x(m):
+            t = xload.tile([P, K], U8, name="x_b", align_bytes=64)
+            nc.sync.dma_start(out=t[:], in_=x_view[:, m, :])
+            xb[m] = t
+
+        def load_a(g):
+            t = rload.tile([P, 4, 512], BF16, name="ab_raw", align_bytes=64)
+            nc.sync.dma_start(out=t[:], in_=a_view[g])
+            araw[g] = t
+
+        def load_b(i):
+            t = rload.tile([P, 4, 512], BF16, name="ab_raw", align_bytes=64)
+            nc.sync.dma_start(out=t[:], in_=b_view[:, :, 512 * i : 512 * (i + 1)])
+            braw[i] = t
+
+        def load_w(r):
+            t = wload.tile([P, K], U8, name="w_b", align_bytes=64)
+            nc.sync.dma_start(out=t[:], in_=w_view[r])
+            wb[r] = t
+
+        ident = const.tile([P, P], F32, name="ident")
+        make_identity(nc, ident[:])
+
+        lam_b = const.tile([P, 4], BF16, name="lam_b")
+        c_b = const.tile([P, XT], BF16, name="c_b")
+        ws = const.tile([P, 192], F32, name="ws")
+        for what in "x0 a0 a1 lam c x1 a2 a3 x2 x3 ws x4 x5 w0 w1 w2 w3 x6 x7 b0 b1 b2 w4 w5 w6 w7 w8 w9 w10 w11".split(" "):
+            if what == "lam":
+                nc.sync.dma_start(out=lam_b[:], in_=lam.rearrange("(p t) -> p t", t=4))
+            elif what == "c":
+                nc.sync.dma_start(out=c_b[:], in_=c.rearrange("(p m) -> p m", m=XT))
+            elif what == "ws":
+                nc.sync.dma_start(out=ws[:], in_=w_scale.rearrange("i j -> (i j)").partition_broadcast(P))
+            elif what[0] == "x":
+                load_x(int(what[1:]))
+            elif what[0] == "a":
+                load_a(int(what[1:]))
+            elif what[0] == "b":
+                load_b(int(what[1:]))
+            else:
+                load_w(int(what[1:]))
+
+        lam_f = const.tile([P, 4], F32, name="lam_f")
+        nc.scalar.activation(out=lam_f[:], in_=lam_b[:], func=COPY)
+        c_f = const.tile([P, XT], F32, name="c_f")
+        nc.scalar.activation(out=c_f[:], in_=c_b[:], func=COPY)
+
+        units = []
+        x_unit, w_unit = {}, {}
+        for kind, idx in ORDER:
+            if kind == "x":
+                x_unit[idx] = len(units)
+                units.append([("x", idx, g) for g in range(PASSES)])
+            else:
+                n0, rows = CHUNKS[idx]
+                w_unit[idx] = len(units)
+                blocks = [("w", n0 // P + r, g) for g in range(PASSES) for r in range(rows // P)]
+                units.extend([blocks[i : i + 4] for i in range(0, len(blocks), 4)])
+        SLOTS = len(units)
+        wide = {}
+        grouped = {}
+        ucodes = {}
+        uscales = {}
+
+        def widen(s):
+            wide[s] = widep.tile([P, 4, 2, P, 2], BF16, name="wide", align_bytes=64)
+            for i, (kind, row, g) in enumerate(units[s]):
+                src = xb[row] if kind == "x" else wb[row]
+                sc = xs if kind == "x" else ws
+                if (s, i) in SBLOCKS:
+                    flat = wide[s][:, i, :, :, :].rearrange("p u w e -> p (u w e)")
+                    for q in range(4):
+                        k0 = 512 * g + P * q
+                        j = 16 * row + 4 * g + q
+                        nc.scalar.activation(
+                            out=flat[:, P * q : P * (q + 1)], in_=src[:, k0 : k0 + P].bitcast(FP8), func=COPY, scale=sc[:, j : j + 1]
+                        )
+                    continue
+                for q in range(4):
+                    k0 = 512 * g + P * q
+                    j = 16 * row + 4 * g + q
+                    nc.vector.tensor_scalar(
+                        out=wide[s][:, i, :, 32 * q : 32 * (q + 1), :].rearrange("p u w e -> p w u e"),
+                        in0=src[:, k0 : k0 + P].bitcast(FP8).rearrange("p (w u e) -> p w u e", u=2, e=2),
+                        scalar1=sc[:, j : j + 1],
+                        scalar2=None,
+                        op0=MULT,
+                    )
+
+        def turn(s):
+            grouped[s] = groupp.tile([P, 4, P, 4], BF16, name="grouped", align_bytes=64)
+            for h in range(2):
+                xt = ps_t.tile([P, 4, P], F32, name="xt")
+                for i in range(2):
+                    for u in range(2):
+                        if (s, 2 * h + i) in SBLOCKS:
+                            words = wide[s][:, 2 * h + i, :, :, :].rearrange("p u w e -> p (u w e)").bitcast(F32)[:, u :: 2]
+                        else:
+                            words = wide[s][:, 2 * h + i, u, :, :].rearrange("p w e -> p (w e)").bitcast(F32)
+                        nc.tensor.transpose(xt[:, 2 * i + u, :], words, ident[:])
+                nc.scalar.copy(
+                    out=grouped[s][:, 2 * h : 2 * h + 2, :, :].rearrange("p i w t -> p (i w t)").bitcast(F32).rearrange("p (i w u) -> p i w u", i=2, u=2),
+                    in_=xt[:].rearrange("p (i u) w -> p i w u", u=2),
+                )
+
+        def quant(s):
+            ucodes[s] = codes.tile([P, 512], U32, name="codes%d" % s, align_bytes=64)
+            uscales[s] = codes.tile([P, 512], U8, name="scales%d" % s, align_bytes=64)
+            nc.vector.quantize_mx(
+                out=ucodes[s][:].bitcast(FP8X4), scales=uscales[s][:], in_=grouped[s][:].rearrange("p i w t -> p (i w t)")
+            )
+
+        a_int, a_codes, a_scales = {}, {}, {}
+        b_int, b_codes, b_scales = {}, {}, {}
+
+        def inter_a(g, eng):
+            a_int[g] = groupp.tile([P, 4, P, 4], BF16, name="ab_int", align_bytes=64)
+            (nc.scalar.copy if eng == "S" else nc.vector.tensor_copy)(
+                out=a_int[g][:], in_=araw[g][:].rearrange("p j (m t) -> p t m j", t=4)
+            )
+
+        def quant_a(g):
+            a_codes[g] = codes.tile([P, 512], U32, name="acodes%d" % g, align_bytes=64)
+            a_scales[g] = codes.tile([P, 512], U8, name="ascales%d" % g, align_bytes=64)
+            nc.vector.quantize_mx(
+                out=a_codes[g][:].bitcast(FP8X4), scales=a_scales[g][:], in_=a_int[g][:].rearrange("p t m j -> p (t m j)")
+            )
+
+        def inter_b(i, eng):
+            b_int[i] = groupp.tile([P, 4, P, 4], BF16, name="ab_int", align_bytes=64)
+            (nc.scalar.copy if eng == "S" else nc.vector.tensor_copy)(
+                out=b_int[i][:].rearrange("p t m j -> p (t m) j"), in_=braw[i][:].rearrange("p j n -> p n j")
+            )
+
+        def quant_b(i):
+            b_codes[i] = codes.tile([P, 512], U32, name="bcodes%d" % i, align_bytes=64)
+            b_scales[i] = codes.tile([P, 512], U8, name="bscales%d" % i, align_bytes=64)
+            nc.vector.quantize_mx(
+                out=b_codes[i][:].bitcast(FP8X4), scales=b_scales[i][:], in_=b_int[i][:].rearrange("p t m j -> p (t m j)")
+            )
+
+        hps, hg, h_codes, h_scales = {}, {}, {}, {}
+
+        def down(m):
+            hps[m] = ps_h.tile([P, 4, P], F32, name="hd")
+            for t in range(4):
+                for g in range(PASSES):
+                    nc.tensor.matmul_mx(
+                        out=hps[m][:, t, :],
+                        lhsT=a_codes[g][:, P * t : P * (t + 1)].bitcast(FP8X4),
+                        lhsT_scale=a_scales[g][:, P * t : P * (t + 1)],
+                        rhs=ucodes[x_unit[m]][:, P * g : P * (g + 1)].bitcast(FP8X4),
+                        rhs_scale=uscales[x_unit[m]][:, P * g : P * (g + 1)],
+                        start=(g == 0),
+                        stop=(g == PASSES - 1),
+                    )
+
+        def scale_h(m):
+            hg[m] = hpool.tile([P, P, 4], BF16, name="h_grouped", align_bytes=64)
+            nc.vector.tensor_tensor(
+                out=hg[m][:],
+                in0=hps[m][:].rearrange("p t w -> p w t"),
+                in1=lam_f[:].unsqueeze(1).to_broadcast([P, P, 4]),
+                op=MULT,
+            )
+
+        def quant_h(m):
+            h_codes[m] = codes.tile([P, P], U32, name="hcodes%d" % m, align_bytes=64)
+            h_scales[m] = codes.tile([P, P], U8, name="hscales%d" % m, align_bytes=64)
+            nc.vector.quantize_mx(
+                out=h_codes[m][:].bitcast(FP8X4), scales=h_scales[m][:], in_=hg[m][:].rearrange("p w t -> p (w t)")
+            )
+
+        y = {}
+        dps = {}
+
+        def up(m, i):
+            ps = ps_h.tile([P, 512], F32, name="hd")
+            nc.tensor.matmul_mx(
+                out=ps[:],
+                lhsT=h_codes[m][:].bitcast(FP8X4),
+                lhsT_scale=h_scales[m][:],
+                rhs=b_codes[i][:].bitcast(FP8X4),
+                rhs_scale=b_scales[i][:],
+                start=True,
+                stop=True,
+            )
+            y[m, i] = ypool.tile([P, 512], F32, name="y%d_%d" % (m, i), align_bytes=64)
+            nc.scalar.activation(out=y[m, i][:], in_=ps[:], func=COPY, scale=c_f[:, m : m + 1])
+
+        out_view = out.rearrange("(p m) n -> p m n", m=XT)
+        bps = {}
+
+        def base(m, ci):
+            n0, rows = CHUNKS[ci]
+            first = w_unit[ci]
+            ps = ps_b.tile([P, 512], F32, name="base")
+            bps[m, ci] = ps
+            for g in range(PASSES):
+                blk = g * (rows // P)
+                s, c0 = first + blk // 4, P * (blk % 4)
+                nc.tensor.matmul_mx(
+                    out=ps[:, :rows],
+                    lhsT=ucodes[x_unit[m]][:, P * g : P * (g + 1)].bitcast(FP8X4),
+                    lhsT_scale=uscales[x_unit[m]][:, P * g : P * (g + 1)],
+                    rhs=ucodes[s][:, c0 : c0 + rows].bitcast(FP8X4),
+                    rhs_scale=uscales[s][:, c0 : c0 + rows],
+                    start=(g == 0),
+                    stop=(g == PASSES - 1),
+                )
+
+        def finish(m, ci):
+            n0, rows = CHUNKS[ci]
+            yt = y[m, n0 // 512][:, n0 % 512 : n0 % 512 + rows]
+            nc.vector.tensor_tensor(out=yt, in0=bps[m, ci][:, :rows], in1=yt, op=ADD)
+            nc.sync.dma_start(out=out_view[:, m, n0 : n0 + rows], in_=yt)
+
+        jobs = {}
+
+        def at(s, fn, *args):
+            jobs.setdefault(s, []).append((fn, args))
+
+        for g in range(4):
+            at(g, inter_a, g, AIL[g])
+            at(g + 1, quant_a, g)
+        for i in range(3):
+            at(6 + i, inter_b, i, BIL[i])
+            at(6 + 2 + i, quant_b, i)
+        ready_h = {}
+        for m in range(XT):
+            s = max(x_unit[m] + 3, 5 + (m + 1) // 2)
+            at(s, down, m)
+            at(s + 1, scale_h, m)
+            at(s + 2, quant_h, m)
+            ready_h[m] = s + 2
+        ready_u = {}
+        load = {}
+        todo = []
+        for ci in range(len(CHUNKS)):
+            w_ready = w_unit[ci] + CHUNKS[ci][1] // P - 1 + 3
+            for m in range(XT):
+                todo.append((max(w_ready, x_unit[m] + 3), ci, m))
+        todo = sorted(todo)
+        for s, ci, m in todo:
+            i = CHUNKS[ci][0] // 512
+            s = max(s, ready_h[m] + 2, 6 + 4 + i + 1)
+            cost = CHUNKS[ci][1] // 256
+            while load.get(s, 0) + cost > 6:
+                s += 1
+            load[s] = load.get(s, 0) + cost
+            if (m, i) not in ready_u:
+                ready_u[m, i] = s
+                at(s - 1, up, m, i)
+            at(s, base, m, ci)
+            at(s, finish, m, ci)
+        last = max(jobs)
+        for s in range(last + 1):
+            if s < SLOTS:
+                widen(s)
+            if 0 <= s - 2 < SLOTS:
+                quant(s - 2)
+            if 0 <= s - 1 < SLOTS:
+                turn(s - 1)
+            for fn, args in jobs.get(s, []):
+                if fn == up:
+                    fn(*args)
+            for fn, args in jobs.get(s, []):
+                if fn != up:
+                    fn(*args)

@@ -19,11 +19,17 @@ COPY = mybir.ActivationFunctionType.Copy
 
 XT = T // P
 PASSES = K // 512
-CHUNKS = ((0, 512), (512, 512), (1024, 256), (1280, 256))
-ORDER = (("x", 0), ("x", 1), ("x", 2), ("x", 3), ("x", 4), ("x", 5), ("x", 6), ("x", 7), ("w", 0), ("w", 1), ("w", 2), ("w", 3))
-SBLOCKS = frozenset(((0, 3), (1, 3), (2, 3), (3, 3), (4, 3), (5, 3), (6, 3), (7, 3), (8, 3), (9, 3), (10, 3), (11, 3), (12, 3), (13, 3), (14, 3), (15, 3), (16, 3), (17, 3), (18, 3), (19, 3),))
-AIL = "SVSV"
-BIL = "SSS"
+WIDTH = 256
+CHUNKS = N // WIDTH
+ORDER = "x0 x1 x2 x3 x4 x5 x6 x7 w0 w1 w2 w3 w4 w5"
+LOADS = "xs x0 a0 a1 x1 a2 lam a3 x2 x3 x4 ws x5 c x6 x7 w0 b0 w1 b1 w2 b2 w3 b3 w4 b4 w5 b5"
+SX = (2, 2, 2, 2, 2, 2, 2, 2)
+SW = (1, 0, 0, 0, 0, 0)
+A_ENG = "VSVV"
+A_STEP = (0, 0, 1, 1)
+DOWN = (2, 2, 3, 4, 5, 6, 7, 8)
+TB, HB, BB = 4, 2, 2
+WIDE, GROUP, YB = 5, 3, 4
 
 
 def tile_fp8_base_lora_d2_kernel(tc, x_bytes, x_scale, w_bytes, w_scale, a, lam, b, c, out):
@@ -31,106 +37,94 @@ def tile_fp8_base_lora_d2_kernel(tc, x_bytes, x_scale, w_bytes, w_scale, a, lam,
     with ExitStack() as ctx:
         const = ctx.enter_context(tc.tile_pool(name="const", bufs=1))
         codes = ctx.enter_context(tc.tile_pool(name="codes", bufs=1))
-        xload = ctx.enter_context(tc.tile_pool(name="xload", bufs=8))
-        wload = ctx.enter_context(tc.tile_pool(name="wload", bufs=12))
-        rload = ctx.enter_context(tc.tile_pool(name="rload", bufs=5))
-        widep = ctx.enter_context(tc.tile_pool(name="widep", bufs=3))
-        groupp = ctx.enter_context(tc.tile_pool(name="groupp", bufs=3))
-        hpool = ctx.enter_context(tc.tile_pool(name="hpool", bufs=3))
-        ypool = ctx.enter_context(tc.tile_pool(name="ypool", bufs=1))
-        ps_t = ctx.enter_context(tc.psum_pool(name="ps_t", bufs=4))
-        ps_h = ctx.enter_context(tc.psum_pool(name="ps_h", bufs=2))
-        ps_b = ctx.enter_context(tc.psum_pool(name="ps_b", bufs=2))
+        loads = ctx.enter_context(tc.tile_pool(name="loads", bufs=1))
+        widep = ctx.enter_context(tc.tile_pool(name="widep", bufs=WIDE))
+        groupp = ctx.enter_context(tc.tile_pool(name="groupp", bufs=GROUP))
+        hpool = ctx.enter_context(tc.tile_pool(name="hpool", bufs=2))
+        ypool = ctx.enter_context(tc.tile_pool(name="ypool", bufs=YB))
+        ps_t = ctx.enter_context(tc.psum_pool(name="ps_t", bufs=TB))
+        ps_h = ctx.enter_context(tc.psum_pool(name="ps_h", bufs=HB))
+        ps_b = ctx.enter_context(tc.psum_pool(name="ps_b", bufs=BB))
+        ctx.enter_context(tc.manual_schedule())
 
-        xs = const.tile([P, XT * 16], F32, name="xs")
-        nc.sync.dma_start(out=xs[:], in_=x_scale.rearrange("(p m) j -> p (m j)", m=XT))
         x_view = x_bytes.rearrange("(p m) k -> p m k", m=XT)
         a_view = a.rearrange("(g p j) r -> g p j r", p=P, j=4)
         b_view = b.rearrange("(p j) n -> p j n", j=4)
-        w_view = w_bytes.rearrange("(r p) k -> r p k", p=P)
+        w_view = w_bytes.rearrange("(r p) k -> p r k", p=P)
         xb, araw, braw, wb = {}, {}, {}, {}
-
-        def load_x(m):
-            t = xload.tile([P, K], U8, name="x_b", align_bytes=64)
-            nc.sync.dma_start(out=t[:], in_=x_view[:, m, :])
-            xb[m] = t
-
-        def load_a(g):
-            t = rload.tile([P, 4, 512], BF16, name="ab_raw", align_bytes=64)
-            nc.sync.dma_start(out=t[:], in_=a_view[g])
-            araw[g] = t
-
-        def load_b(i):
-            t = rload.tile([P, 4, 512], BF16, name="ab_raw", align_bytes=64)
-            nc.sync.dma_start(out=t[:], in_=b_view[:, :, 512 * i : 512 * (i + 1)])
-            braw[i] = t
-
-        def load_w(r):
-            t = wload.tile([P, K], U8, name="w_b", align_bytes=64)
-            nc.sync.dma_start(out=t[:], in_=w_view[r])
-            wb[r] = t
 
         ident = const.tile([P, P], F32, name="ident")
         make_identity(nc, ident[:])
 
+        xs = const.tile([P, XT * 16], F32, name="xs")
         lam_b = const.tile([P, 4], BF16, name="lam_b")
         c_b = const.tile([P, XT], BF16, name="c_b")
         ws = const.tile([P, 192], F32, name="ws")
-        for what in "x0 a0 a1 lam c x1 a2 a3 x2 x3 ws x4 x5 w0 w1 w2 w3 x6 x7 b0 b1 b2 w4 w5 w6 w7 w8 w9 w10 w11".split(" "):
-            if what == "lam":
+        for what in LOADS.split(" "):
+            if what == "xs":
+                nc.sync.dma_start(out=xs[:], in_=x_scale.rearrange("(p m) j -> p (m j)", m=XT))
+            elif what == "lam":
                 nc.sync.dma_start(out=lam_b[:], in_=lam.rearrange("(p t) -> p t", t=4))
             elif what == "c":
                 nc.sync.dma_start(out=c_b[:], in_=c.rearrange("(p m) -> p m", m=XT))
             elif what == "ws":
                 nc.sync.dma_start(out=ws[:], in_=w_scale.rearrange("i j -> (i j)").partition_broadcast(P))
             elif what[0] == "x":
-                load_x(int(what[1:]))
+                m = int(what[1:])
+                xb[m] = loads.tile([P, K], U8, name="x_b%d" % m, align_bytes=64)
+                nc.sync.dma_start(out=xb[m][:], in_=x_view[:, m, :])
             elif what[0] == "a":
-                load_a(int(what[1:]))
+                g = int(what[1:])
+                araw[g] = loads.tile([P, 4, 512], BF16, name="a_raw%d" % g, align_bytes=64)
+                nc.sync.dma_start(out=araw[g][:], in_=a_view[g])
             elif what[0] == "b":
-                load_b(int(what[1:]))
+                ci = int(what[1:])
+                braw[ci] = loads.tile([P, 4, WIDTH], BF16, name="b_raw%d" % ci, align_bytes=64)
+                nc.sync.dma_start(out=braw[ci][:], in_=b_view[:, :, WIDTH * ci : WIDTH * (ci + 1)])
             else:
-                load_w(int(what[1:]))
+                ci = int(what[1:])
+                for r in range(2 * ci, 2 * ci + 2):
+                    wb[r] = loads.tile([P, K], U8, name="w_b%d" % r, align_bytes=64)
+                    nc.sync.dma_start(out=wb[r][:], in_=w_view[:, r, :])
 
         lam_f = const.tile([P, 4], F32, name="lam_f")
-        nc.scalar.activation(out=lam_f[:], in_=lam_b[:], func=COPY)
         c_f = const.tile([P, XT], F32, name="c_f")
-        nc.scalar.activation(out=c_f[:], in_=c_b[:], func=COPY)
 
-        units = []
-        x_unit, w_unit = {}, {}
-        for kind, idx in ORDER:
-            if kind == "x":
+        units, on_scalar, stages = [], [], []
+        x_unit, w_unit, x_stage, w_stage = {}, {}, {}, {}
+        for what in ORDER.split(" "):
+            idx = int(what[1:])
+            if what[0] == "x":
                 x_unit[idx] = len(units)
+                x_stage[idx] = len(stages)
+                stages.append([len(units)])
                 units.append([("x", idx, g) for g in range(PASSES)])
+                on_scalar.append(SX[idx])
             else:
-                n0, rows = CHUNKS[idx]
                 w_unit[idx] = len(units)
-                blocks = [("w", n0 // P + r, g) for g in range(PASSES) for r in range(rows // P)]
-                units.extend([blocks[i : i + 4] for i in range(0, len(blocks), 4)])
-        SLOTS = len(units)
-        wide = {}
-        grouped = {}
-        ucodes = {}
-        uscales = {}
+                w_stage[idx] = len(stages)
+                stages.append([len(units), len(units) + 1])
+                blocks = [("w", 2 * idx + r, g) for g in range(PASSES) for r in range(2)]
+                for i in range(0, len(blocks), 4):
+                    units.append(blocks[i : i + 4])
+                    on_scalar.append(SW[idx])
+        wide, grouped, ucodes, uscales = {}, {}, {}, {}
 
-        def widen(s):
-            wide[s] = widep.tile([P, 4, 2, P, 2], BF16, name="wide", align_bytes=64)
-            for i, (kind, row, g) in enumerate(units[s]):
-                src = xb[row] if kind == "x" else wb[row]
-                sc = xs if kind == "x" else ws
-                if (s, i) in SBLOCKS:
+        def widen(s, i):
+            if s not in wide:
+                wide[s] = widep.tile([P, 4, 2, P, 2], BF16, name="wide", align_bytes=64)
+            kind, row, g = units[s][i]
+            src = xb[row] if kind == "x" else wb[row]
+            sc = xs if kind == "x" else ws
+            for q in range(4):
+                k0 = 512 * g + P * q
+                j = 16 * row + 4 * g + q
+                if i >= 4 - on_scalar[s]:
                     flat = wide[s][:, i, :, :, :].rearrange("p u w e -> p (u w e)")
-                    for q in range(4):
-                        k0 = 512 * g + P * q
-                        j = 16 * row + 4 * g + q
-                        nc.scalar.activation(
-                            out=flat[:, P * q : P * (q + 1)], in_=src[:, k0 : k0 + P].bitcast(FP8), func=COPY, scale=sc[:, j : j + 1]
-                        )
-                    continue
-                for q in range(4):
-                    k0 = 512 * g + P * q
-                    j = 16 * row + 4 * g + q
+                    nc.scalar.activation(
+                        out=flat[:, P * q : P * (q + 1)], in_=src[:, k0 : k0 + P].bitcast(FP8), func=COPY, scale=sc[:, j : j + 1]
+                    )
+                else:
                     nc.vector.tensor_scalar(
                         out=wide[s][:, i, :, 32 * q : 32 * (q + 1), :].rearrange("p u w e -> p w u e"),
                         in0=src[:, k0 : k0 + P].bitcast(FP8).rearrange("p (w u e) -> p w u e", u=2, e=2),
@@ -139,21 +133,21 @@ def tile_fp8_base_lora_d2_kernel(tc, x_bytes, x_scale, w_bytes, w_scale, a, lam,
                         op0=MULT,
                     )
 
-        def turn(s):
-            grouped[s] = groupp.tile([P, 4, P, 4], BF16, name="grouped", align_bytes=64)
-            for h in range(2):
-                xt = ps_t.tile([P, 4, P], F32, name="xt")
-                for i in range(2):
-                    for u in range(2):
-                        if (s, 2 * h + i) in SBLOCKS:
-                            words = wide[s][:, 2 * h + i, :, :, :].rearrange("p u w e -> p (u w e)").bitcast(F32)[:, u :: 2]
-                        else:
-                            words = wide[s][:, 2 * h + i, u, :, :].rearrange("p w e -> p (w e)").bitcast(F32)
-                        nc.tensor.transpose(xt[:, 2 * i + u, :], words, ident[:])
-                nc.scalar.copy(
-                    out=grouped[s][:, 2 * h : 2 * h + 2, :, :].rearrange("p i w t -> p (i w t)").bitcast(F32).rearrange("p (i w u) -> p i w u", i=2, u=2),
-                    in_=xt[:].rearrange("p (i u) w -> p i w u", u=2),
-                )
+        def turn(s, h):
+            if h == 0:
+                grouped[s] = groupp.tile([P, 4, P, 4], BF16, name="grouped", align_bytes=64)
+            xt = ps_t.tile([P, 4, P], F32, name="xt")
+            for i in range(2):
+                for u in range(2):
+                    if 2 * h + i >= 4 - on_scalar[s]:
+                        words = wide[s][:, 2 * h + i, :, :, :].rearrange("p u w e -> p (u w e)").bitcast(F32)[:, u :: 2]
+                    else:
+                        words = wide[s][:, 2 * h + i, u, :, :].rearrange("p w e -> p (w e)").bitcast(F32)
+                    nc.tensor.transpose(xt[:, 2 * i + u, :], words, ident[:])
+            nc.scalar.copy(
+                out=grouped[s][:, 2 * h : 2 * h + 2, :, :].rearrange("p i w t -> p (i w t)").bitcast(F32).rearrange("p (i w u) -> p i w u", i=2, u=2),
+                in_=xt[:].rearrange("p (i u) w -> p i w u", u=2),
+            )
 
         def quant(s):
             ucodes[s] = codes.tile([P, 512], U32, name="codes%d" % s, align_bytes=64)
@@ -165,9 +159,9 @@ def tile_fp8_base_lora_d2_kernel(tc, x_bytes, x_scale, w_bytes, w_scale, a, lam,
         a_int, a_codes, a_scales = {}, {}, {}
         b_int, b_codes, b_scales = {}, {}, {}
 
-        def inter_a(g, eng):
+        def inter_a(g):
             a_int[g] = groupp.tile([P, 4, P, 4], BF16, name="ab_int", align_bytes=64)
-            (nc.scalar.copy if eng == "S" else nc.vector.tensor_copy)(
+            (nc.scalar.copy if A_ENG[g] == "S" else nc.vector.tensor_copy)(
                 out=a_int[g][:], in_=araw[g][:].rearrange("p j (m t) -> p t m j", t=4)
             )
 
@@ -178,17 +172,15 @@ def tile_fp8_base_lora_d2_kernel(tc, x_bytes, x_scale, w_bytes, w_scale, a, lam,
                 out=a_codes[g][:].bitcast(FP8X4), scales=a_scales[g][:], in_=a_int[g][:].rearrange("p t m j -> p (t m j)")
             )
 
-        def inter_b(i, eng):
-            b_int[i] = groupp.tile([P, 4, P, 4], BF16, name="ab_int", align_bytes=64)
-            (nc.scalar.copy if eng == "S" else nc.vector.tensor_copy)(
-                out=b_int[i][:].rearrange("p t m j -> p (t m) j"), in_=braw[i][:].rearrange("p j n -> p n j")
-            )
+        def inter_b(ci):
+            b_int[ci] = groupp.tile([P, WIDTH, 4], BF16, name="ab_int", align_bytes=64)
+            nc.scalar.copy(out=b_int[ci][:], in_=braw[ci][:].rearrange("p j n -> p n j"))
 
-        def quant_b(i):
-            b_codes[i] = codes.tile([P, 512], U32, name="bcodes%d" % i, align_bytes=64)
-            b_scales[i] = codes.tile([P, 512], U8, name="bscales%d" % i, align_bytes=64)
+        def quant_b(ci):
+            b_codes[ci] = codes.tile([P, WIDTH], U32, name="bcodes%d" % ci, align_bytes=64)
+            b_scales[ci] = codes.tile([P, WIDTH], U8, name="bscales%d" % ci, align_bytes=64)
             nc.vector.quantize_mx(
-                out=b_codes[i][:].bitcast(FP8X4), scales=b_scales[i][:], in_=b_int[i][:].rearrange("p t m j -> p (t m j)")
+                out=b_codes[ci][:].bitcast(FP8X4), scales=b_scales[ci][:], in_=b_int[ci][:].rearrange("p n j -> p (n j)")
             )
 
         hps, hg, h_codes, h_scales = {}, {}, {}, {}
@@ -223,99 +215,126 @@ def tile_fp8_base_lora_d2_kernel(tc, x_bytes, x_scale, w_bytes, w_scale, a, lam,
                 out=h_codes[m][:].bitcast(FP8X4), scales=h_scales[m][:], in_=hg[m][:].rearrange("p w t -> p (w t)")
             )
 
-        y = {}
-        dps = {}
-
-        def up(m, i):
-            ps = ps_h.tile([P, 512], F32, name="hd")
-            nc.tensor.matmul_mx(
-                out=ps[:],
-                lhsT=h_codes[m][:].bitcast(FP8X4),
-                lhsT_scale=h_scales[m][:],
-                rhs=b_codes[i][:].bitcast(FP8X4),
-                rhs_scale=b_scales[i][:],
-                start=True,
-                stop=True,
-            )
-            y[m, i] = ypool.tile([P, 512], F32, name="y%d_%d" % (m, i), align_bytes=64)
-            nc.scalar.activation(out=y[m, i][:], in_=ps[:], func=COPY, scale=c_f[:, m : m + 1])
-
+        y, bps = {}, {}
         out_view = out.rearrange("(p m) n -> p m n", m=XT)
-        bps = {}
 
-        def base(m, ci):
-            n0, rows = CHUNKS[ci]
-            first = w_unit[ci]
-            ps = ps_b.tile([P, 512], F32, name="base")
-            bps[m, ci] = ps
-            for g in range(PASSES):
-                blk = g * (rows // P)
-                s, c0 = first + blk // 4, P * (blk % 4)
+        def up(j, ci):
+            ps = ps_h.tile([P, 2, WIDTH], F32, name="hd")
+            y[j, ci] = ypool.tile([P, 2, WIDTH], F32, name="y", align_bytes=64)
+            for i in range(2):
                 nc.tensor.matmul_mx(
-                    out=ps[:, :rows],
-                    lhsT=ucodes[x_unit[m]][:, P * g : P * (g + 1)].bitcast(FP8X4),
-                    lhsT_scale=uscales[x_unit[m]][:, P * g : P * (g + 1)],
-                    rhs=ucodes[s][:, c0 : c0 + rows].bitcast(FP8X4),
-                    rhs_scale=uscales[s][:, c0 : c0 + rows],
-                    start=(g == 0),
-                    stop=(g == PASSES - 1),
+                    out=ps[:, i, :],
+                    lhsT=h_codes[2 * j + i][:].bitcast(FP8X4),
+                    lhsT_scale=h_scales[2 * j + i][:],
+                    rhs=b_codes[ci][:].bitcast(FP8X4),
+                    rhs_scale=b_scales[ci][:],
+                    start=True,
+                    stop=True,
                 )
+            for i in range(2):
+                m = 2 * j + i
+                nc.scalar.activation(out=y[j, ci][:, i, :], in_=ps[:, i, :], func=COPY, scale=c_f[:, m : m + 1])
 
-        def finish(m, ci):
-            n0, rows = CHUNKS[ci]
-            yt = y[m, n0 // 512][:, n0 % 512 : n0 % 512 + rows]
-            nc.vector.tensor_tensor(out=yt, in0=bps[m, ci][:, :rows], in1=yt, op=ADD)
-            nc.sync.dma_start(out=out_view[:, m, n0 : n0 + rows], in_=yt)
+        def base(j, ci):
+            ps = ps_b.tile([P, 2, WIDTH], F32, name="base")
+            bps[j, ci] = ps
+            for i in range(2):
+                xu = x_unit[2 * j + i]
+                for g in range(PASSES):
+                    s, c0 = w_unit[ci] + g // 2, WIDTH * (g % 2)
+                    nc.tensor.matmul_mx(
+                        out=ps[:, i, :],
+                        lhsT=ucodes[xu][:, P * g : P * (g + 1)].bitcast(FP8X4),
+                        lhsT_scale=uscales[xu][:, P * g : P * (g + 1)],
+                        rhs=ucodes[s][:, c0 : c0 + WIDTH].bitcast(FP8X4),
+                        rhs_scale=uscales[s][:, c0 : c0 + WIDTH],
+                        start=(g == 0),
+                        stop=(g == PASSES - 1),
+                    )
 
-        jobs = {}
+        def finish(j, ci):
+            yt = y[j, ci][:].rearrange("p i n -> p (i n)")
+            nc.vector.tensor_tensor(out=yt, in0=bps[j, ci][:].rearrange("p i n -> p (i n)"), in1=yt, op=ADD)
+            nc.sync.dma_start(out=out_view[:, 2 * j : 2 * j + 2, WIDTH * ci : WIDTH * (ci + 1)], in_=y[j, ci][:])
 
-        def at(s, fn, *args):
-            jobs.setdefault(s, []).append((fn, args))
+        def pieces(st, scalar):
+            if st >= len(stages):
+                return []
+            return [(u, i) for u in stages[st] for i in range(4) if (i >= 4 - on_scalar[u]) == scalar]
 
-        for g in range(4):
-            at(g, inter_a, g, AIL[g])
-            at(g + 1, quant_a, g)
-        for i in range(3):
-            at(6 + i, inter_b, i, BIL[i])
-            at(6 + 2 + i, quant_b, i)
-        ready_h = {}
-        for m in range(XT):
-            s = max(x_unit[m] + 3, 5 + (m + 1) // 2)
-            at(s, down, m)
-            at(s + 1, scale_h, m)
-            at(s + 2, quant_h, m)
-            ready_h[m] = s + 2
-        ready_u = {}
-        load = {}
-        todo = []
-        for ci in range(len(CHUNKS)):
-            w_ready = w_unit[ci] + CHUNKS[ci][1] // P - 1 + 3
-            for m in range(XT):
-                todo.append((max(w_ready, x_unit[m] + 3), ci, m))
-        todo = sorted(todo)
-        for s, ci, m in todo:
-            i = CHUNKS[ci][0] // 512
-            s = max(s, ready_h[m] + 2, 6 + 4 + i + 1)
-            cost = CHUNKS[ci][1] // 256
-            while load.get(s, 0) + cost > 6:
-                s += 1
-            load[s] = load.get(s, 0) + cost
-            if (m, i) not in ready_u:
-                ready_u[m, i] = s
-                at(s - 1, up, m, i)
-            at(s, base, m, ci)
-            at(s, finish, m, ci)
-        last = max(jobs)
-        for s in range(last + 1):
-            if s < SLOTS:
-                widen(s)
-            if 0 <= s - 2 < SLOTS:
-                quant(s - 2)
-            if 0 <= s - 1 < SLOTS:
-                turn(s - 1)
-            for fn, args in jobs.get(s, []):
-                if fn == up:
-                    fn(*args)
-            for fn, args in jobs.get(s, []):
-                if fn != up:
-                    fn(*args)
+        for piece in pieces(0, False) + pieces(0, True):
+            widen(*piece)
+        todo = [(j, ci) for ci in range(CHUNKS) for j in range(XT // 2)]
+        left = []
+        for s in range(len(stages) + 1):
+            for u in stages[s] if s < len(stages) else []:
+                turn(u, 0)
+                turn(u, 1)
+            for g in range(PASSES):
+                if A_STEP[g] == s:
+                    inter_a(g)
+            if s == 0:
+                nc.scalar.activation(out=lam_f[:], in_=lam_b[:], func=COPY)
+                for piece in pieces(1, True):
+                    widen(*piece)
+            if s == 2:
+                nc.scalar.activation(out=c_f[:], in_=c_b[:], func=COPY)
+            for piece in pieces(s + 2, True):
+                widen(*piece)
+            hs = [m for m in range(XT) if DOWN[m] == s - 1]
+            for job in left:
+                finish(*job)
+            left = []
+            for m in hs:
+                scale_h(m)
+            vec = pieces(s + 1, False)
+            jobs = [(j, ci) for j, ci in todo if w_stage[ci] < s and DOWN[2 * j + 1] + 1 <= s]
+            for job in jobs:
+                todo.remove(job)
+            mine = stages[s] if s < len(stages) else []
+            bs = [ci for ci in range(CHUNKS) if w_stage[ci] == s]
+            downs = [m for m in range(XT) if DOWN[m] == s]
+            if len(jobs) == 0:
+                for piece in vec:
+                    widen(*piece)
+                for m in hs:
+                    quant_h(m)
+                for g in range(PASSES):
+                    if A_STEP[g] == s:
+                        quant_a(g)
+                for m in downs:
+                    down(m)
+                for ci in bs:
+                    inter_b(ci)
+                for u in mine:
+                    quant(u)
+                for ci in bs:
+                    quant_b(ci)
+                continue
+            for piece in vec[:4]:
+                widen(*piece)
+            for m in hs:
+                quant_h(m)
+            for m in downs:
+                down(m)
+            for u in mine:
+                quant(u)
+            vec = vec[4:]
+            for n, job in enumerate(jobs):
+                if n == 0:
+                    up(*job)
+                if n + 1 < len(jobs):
+                    up(*jobs[n + 1])
+                if n == 1:
+                    for ci in bs:
+                        inter_b(ci)
+                base(*job)
+                for piece in vec[2 * n : 2 * n + 2]:
+                    widen(*piece)
+                if n == 2:
+                    for ci in bs:
+                        quant_b(ci)
+                if n + 1 < len(jobs) or s == len(stages):
+                    finish(*job)
+                else:
+                    left.append(job)

@@ -21,15 +21,16 @@ XT = T // P
 PASSES = K // 512
 WIDTH = 256
 CHUNKS = N // WIDTH
-ORDER = "x0 x1 x2 x3 x4 x5 x6 x7 w0 w1 w2 w3 w4 w5"
-LOADS = "xs x0 a0 a1 x1 a2 lam a3 x2 x3 x4 ws x5 c x6 x7 w0 b0 w1 b1 w2 b2 w3 b3 w4 b4 w5 b5"
+ORDER = "x0 x1 x2 x3 x4 x5 w0 x6 x7 w1 w2 w3 w4 w5"
+LOADS = "xs x0 x1 a0 a1 a2 a3 lam x2 x3 x4 x5 ws w0 c b0 x6 x7 w1 b1 w2 b2 w3 b3 w4 b4 w5 b5"
 SX = (2, 2, 2, 2, 2, 2, 2, 2)
-SW = (1, 0, 0, 0, 0, 0)
+SW = ((1, 1), (1, 1), (1, 0), (1, 0), (1, 0), (1, 0))
 A_ENG = "VSVV"
-A_STEP = (0, 0, 1, 1)
-DOWN = (2, 2, 3, 4, 5, 6, 7, 8)
 TB, HB, BB = 4, 2, 2
-WIDE, GROUP, YB = 5, 3, 4
+WIDE, GROUP, INTER, YB = 6, 3, 4, 4
+WARM = 0
+FILL = (1, 1, 1, 1, 1, 0, 1, 1, 1, 1, 1, 0, 1, 1, 0, 1, 2, 2, 1, 1, 1, 1)
+SFILL = (2, 2, 2, 3, 1, 1, 1, 0, 2, 1)
 
 
 def tile_fp8_base_lora_d2_kernel(tc, x_bytes, x_scale, w_bytes, w_scale, a, lam, b, c, out):
@@ -107,8 +108,8 @@ def tile_fp8_base_lora_d2_kernel(tc, x_bytes, x_scale, w_bytes, w_scale, a, lam,
                 blocks = [("w", 2 * idx + r, g) for g in range(PASSES) for r in range(2)]
                 for i in range(0, len(blocks), 4):
                     units.append(blocks[i : i + 4])
-                    on_scalar.append(SW[idx])
-        wide, grouped, ucodes, uscales = {}, {}, {}, {}
+                    on_scalar.append(SW[idx][i // 4])
+        wide, turned, grouped, ucodes, uscales = {}, {}, {}, {}, {}
 
         def widen(s, i):
             if s not in wide:
@@ -134,9 +135,8 @@ def tile_fp8_base_lora_d2_kernel(tc, x_bytes, x_scale, w_bytes, w_scale, a, lam,
                     )
 
         def turn(s, h):
-            if h == 0:
-                grouped[s] = groupp.tile([P, 4, P, 4], BF16, name="grouped", align_bytes=64)
             xt = ps_t.tile([P, 4, P], F32, name="xt")
+            turned[s, h] = xt
             for i in range(2):
                 for u in range(2):
                     if 2 * h + i >= 4 - on_scalar[s]:
@@ -144,6 +144,11 @@ def tile_fp8_base_lora_d2_kernel(tc, x_bytes, x_scale, w_bytes, w_scale, a, lam,
                     else:
                         words = wide[s][:, 2 * h + i, u, :, :].rearrange("p w e -> p (w e)").bitcast(F32)
                     nc.tensor.transpose(xt[:, 2 * i + u, :], words, ident[:])
+
+        def empty(s, h):
+            if h == 0:
+                grouped[s] = groupp.tile([P, 4, P, 4], BF16, name="grouped", align_bytes=64)
+            xt = turned[s, h]
             nc.scalar.copy(
                 out=grouped[s][:, 2 * h : 2 * h + 2, :, :].rearrange("p i w t -> p (i w t)").bitcast(F32).rearrange("p (i w u) -> p i w u", i=2, u=2),
                 in_=xt[:].rearrange("p (i u) w -> p i w u", u=2),
@@ -160,7 +165,7 @@ def tile_fp8_base_lora_d2_kernel(tc, x_bytes, x_scale, w_bytes, w_scale, a, lam,
         b_int, b_codes, b_scales = {}, {}, {}
 
         def inter_a(g):
-            a_int[g] = groupp.tile([P, 4, P, 4], BF16, name="ab_int", align_bytes=64)
+            a_int[g] = groupp.tile([P, 4, P, 4], BF16, name="ab_int", bufs=INTER, align_bytes=64)
             (nc.scalar.copy if A_ENG[g] == "S" else nc.vector.tensor_copy)(
                 out=a_int[g][:], in_=araw[g][:].rearrange("p j (m t) -> p t m j", t=4)
             )
@@ -173,7 +178,7 @@ def tile_fp8_base_lora_d2_kernel(tc, x_bytes, x_scale, w_bytes, w_scale, a, lam,
             )
 
         def inter_b(ci):
-            b_int[ci] = groupp.tile([P, WIDTH, 4], BF16, name="ab_int", align_bytes=64)
+            b_int[ci] = groupp.tile([P, WIDTH, 4], BF16, name="ab_int", bufs=INTER, align_bytes=64)
             nc.scalar.copy(out=b_int[ci][:], in_=braw[ci][:].rearrange("p j n -> p n j"))
 
         def quant_b(ci):
@@ -215,12 +220,12 @@ def tile_fp8_base_lora_d2_kernel(tc, x_bytes, x_scale, w_bytes, w_scale, a, lam,
                 out=h_codes[m][:].bitcast(FP8X4), scales=h_scales[m][:], in_=hg[m][:].rearrange("p w t -> p (w t)")
             )
 
-        y, bps = {}, {}
+        y, bps, dps, warm_ps = {}, {}, {}, {}
         out_view = out.rearrange("(p m) n -> p m n", m=XT)
 
         def up(j, ci):
             ps = ps_h.tile([P, 2, WIDTH], F32, name="hd")
-            y[j, ci] = ypool.tile([P, 2, WIDTH], F32, name="y", align_bytes=64)
+            dps[j, ci] = ps
             for i in range(2):
                 nc.tensor.matmul_mx(
                     out=ps[:, i, :],
@@ -231,9 +236,12 @@ def tile_fp8_base_lora_d2_kernel(tc, x_bytes, x_scale, w_bytes, w_scale, a, lam,
                     start=True,
                     stop=True,
                 )
+
+        def scale_d(j, ci):
+            y[j, ci] = ypool.tile([P, 2, WIDTH], F32, name="y", align_bytes=64)
             for i in range(2):
                 m = 2 * j + i
-                nc.scalar.activation(out=y[j, ci][:, i, :], in_=ps[:, i, :], func=COPY, scale=c_f[:, m : m + 1])
+                nc.scalar.activation(out=y[j, ci][:, i, :], in_=dps[j, ci][:, i, :], func=COPY, scale=c_f[:, m : m + 1])
 
         def base(j, ci):
             ps = ps_b.tile([P, 2, WIDTH], F32, name="base")
@@ -257,84 +265,141 @@ def tile_fp8_base_lora_d2_kernel(tc, x_bytes, x_scale, w_bytes, w_scale, a, lam,
             nc.vector.tensor_tensor(out=yt, in0=bps[j, ci][:].rearrange("p i n -> p (i n)"), in1=yt, op=ADD)
             nc.sync.dma_start(out=out_view[:, 2 * j : 2 * j + 2, WIDTH * ci : WIDTH * (ci + 1)], in_=y[j, ci][:])
 
-        def pieces(st, scalar):
-            if st >= len(stages):
-                return []
-            return [(u, i) for u in stages[st] for i in range(4) if (i >= 4 - on_scalar[u]) == scalar]
-
-        for piece in pieces(0, False) + pieces(0, True):
-            widen(*piece)
-        todo = [(j, ci) for ci in range(CHUNKS) for j in range(XT // 2)]
-        left = []
-        for s in range(len(stages) + 1):
-            for u in stages[s] if s < len(stages) else []:
-                turn(u, 0)
-                turn(u, 1)
-            for g in range(PASSES):
-                if A_STEP[g] == s:
-                    inter_a(g)
-            if s == 0:
+        def small(which):
+            if which == "lam":
                 nc.scalar.activation(out=lam_f[:], in_=lam_b[:], func=COPY)
-                for piece in pieces(1, True):
-                    widen(*piece)
-            if s == 2:
+            else:
                 nc.scalar.activation(out=c_f[:], in_=c_b[:], func=COPY)
-            for piece in pieces(s + 2, True):
-                widen(*piece)
-            hs = [m for m in range(XT) if DOWN[m] == s - 1]
-            for job in left:
-                finish(*job)
-            left = []
-            for m in hs:
-                scale_h(m)
-            vec = pieces(s + 1, False)
-            jobs = [(j, ci) for j, ci in todo if w_stage[ci] < s and DOWN[2 * j + 1] + 1 <= s]
-            for job in jobs:
-                todo.remove(job)
-            mine = stages[s] if s < len(stages) else []
-            bs = [ci for ci in range(CHUNKS) if w_stage[ci] == s]
-            downs = [m for m in range(XT) if DOWN[m] == s]
-            if len(jobs) == 0:
-                for piece in vec:
-                    widen(*piece)
-                for m in hs:
-                    quant_h(m)
-                for g in range(PASSES):
-                    if A_STEP[g] == s:
-                        quant_a(g)
-                for m in downs:
-                    down(m)
-                for ci in bs:
-                    inter_b(ci)
-                for u in mine:
-                    quant(u)
-                for ci in bs:
-                    quant_b(ci)
-                continue
-            for piece in vec[:4]:
-                widen(*piece)
-            for m in hs:
-                quant_h(m)
-            for m in downs:
-                down(m)
-            for u in mine:
-                quant(u)
-            vec = vec[4:]
-            for n, job in enumerate(jobs):
-                if n == 0:
-                    up(*job)
-                if n + 1 < len(jobs):
-                    up(*jobs[n + 1])
-                if n == 1:
-                    for ci in bs:
-                        inter_b(ci)
-                base(*job)
-                for piece in vec[2 * n : 2 * n + 2]:
-                    widen(*piece)
-                if n == 2:
-                    for ci in bs:
-                        quant_b(ci)
-                if n + 1 < len(jobs) or s == len(stages):
-                    finish(*job)
-                else:
-                    left.append(job)
+
+        def warm(i):
+            if i == 0:
+                warm_ps[0] = ps_b.tile([P, 2, WIDTH], F32, name="base")
+            flat = a_int[2][:].rearrange("p t m j -> p (t m j)")
+            nc.tensor.matmul(warm_ps[0][:].rearrange("p i n -> p (i n)"), lhsT=flat[:, :P], rhs=flat[:, :512], start=True, stop=True)
+
+        def both(fn, u):
+            return [(fn, u, 0), (fn, u, 1)]
+
+        def vp(u):
+            return [(widen, u, i) for i in range(4 - on_scalar[u])]
+
+        def sp(u):
+            return [(widen, u, i) for i in range(4 - on_scalar[u], 4)]
+
+        X = x_unit
+        W = w_unit
+        pe = both(turn, X[0]) + both(turn, X[1]) + [(warm, i) for i in range(WARM)]
+        for m in range(2, 6):
+            pe += [(down, m - 2)] + both(turn, X[m])
+        pe += [(down, 4)] + both(turn, W[0]) + both(turn, W[0] + 1) + [(down, 5)] + both(turn, X[6])
+        pe += [(up, 0, 0), (up, 1, 0), (base, 0, 0)] + both(turn, X[7]) + [(down, 6), (base, 1, 0), (up, 2, 0), (down, 7), (base, 2, 0)]
+        pe += both(turn, W[1]) + both(turn, W[1] + 1) + [(up, 3, 0), (up, 0, 1)]
+        jobs = [(j, ci) for ci in range(CHUNKS) for j in range(4)]
+        for n in range(3, len(jobs)):
+            j, ci = jobs[n]
+            if j == 2 and ci + 1 < CHUNKS:
+                pe += both(turn, W[ci + 1]) + both(turn, W[ci + 1] + 1)
+            pe += [(base, j, ci)]
+            if n + 2 < len(jobs):
+                pe += [(up,) + jobs[n + 2]]
+        ve = vp(X[0]) + vp(X[1]) + [(inter_a, 0), (quant, X[0]), (quant_a, 0), (inter_a, 2), (inter_a, 3), (quant_a, 1), (quant_a, 2), (quant_a, 3)]
+        ve += vp(X[2]) + [(quant, X[1])] + vp(X[3])
+        fill = vp(X[4]) + vp(X[5]) + vp(W[0]) + vp(W[0] + 1) + vp(X[6]) + vp(X[7]) + vp(W[1]) + vp(W[1] + 1)
+        marks = []
+        for m in range(5):
+            marks += [[(scale_h, m)], [(quant_h, m)], [(quant, X[m + 2])] if m < 4 else [(quant_b, 0), (quant, W[0])]]
+        marks += [[(scale_h, 5), (quant, W[0] + 1)], [(quant_h, 5), (quant, X[6])], [(finish, 0, 0), (quant, X[7])], [(scale_h, 6)], [(quant_h, 6), (finish, 1, 0)], [(scale_h, 7)], [(quant_h, 7), (quant_b, 1)]]
+        for n, mark in enumerate(marks):
+            ve += mark
+            for k in range(FILL[n]):
+                ve += fill[:1]
+                fill = fill[1:]
+        ve += fill
+        for ci in range(1, CHUNKS + 1):
+            nxt = vp(W[ci + 1]) + vp(W[ci + 1] + 1) if ci + 1 < CHUNKS else []
+            if ci == 1:
+                ve += [(finish, 2, 0)] + nxt[:2] + [(quant, W[ci])] + nxt[2:3] + [(quant, W[ci] + 1), (finish, 3, 0)] + nxt[3:5]
+            elif ci < CHUNKS:
+                ve += nxt[:2] + [(quant, W[ci]), (finish, 2, ci - 1), (quant, W[ci] + 1)] + nxt[2:3] + [(finish, 3, ci - 1)] + nxt[3:5]
+            if ci < CHUNKS:
+                ve += [(finish, 0, ci)] + nxt[5:]
+                if ci + 1 < CHUNKS:
+                    ve += [(quant_b, ci + 1)]
+                ve += [(finish, 1, ci)]
+            else:
+                ve += [(finish, 2, ci - 1), (finish, 3, ci - 1)]
+        sc = sp(X[0]) + sp(X[1]) + both(empty, X[0]) + [(inter_a, 1)] + both(empty, X[1]) + [(small, "lam")] + sp(X[2]) + sp(X[3])
+        fill = sp(X[4]) + sp(X[5]) + sp(W[0]) + sp(W[0] + 1) + [(small, "c"), (inter_b, 0)] + sp(X[6]) + sp(X[7]) + sp(W[1]) + sp(W[1] + 1) + [(inter_b, 1)]
+        marks = [both(empty, X[m]) for m in range(2, 6)] + [both(empty, W[0]), both(empty, W[0] + 1), both(empty, X[6]), [(scale_d, 0, 0), (scale_d, 1, 0)], both(empty, X[7]), [(scale_d, 2, 0)]]
+        for n, mark in enumerate(marks):
+            sc += mark
+            for k in range(SFILL[n]):
+                sc += fill[:1]
+                fill = fill[1:]
+        sc += fill
+        for ci in range(1, CHUNKS):
+            sc += both(empty, W[ci]) + both(empty, W[ci] + 1)
+            if ci == 1:
+                sc += [(scale_d, 3, 0)]
+            sc += [(scale_d, 0, ci), (scale_d, 1, ci)]
+            if ci + 1 < CHUNKS:
+                sc += [(inter_b, ci + 1)] + sp(W[ci + 1]) + sp(W[ci + 1] + 1)
+            sc += [(scale_d, 2, ci), (scale_d, 3, ci)]
+
+        def users(fns, prog):
+            return [step for step in prog if step[0] in fns]
+
+        turns = users((turn,), pe)
+        hd = users((down, up), pe)
+        bases = users((base,), pe)
+        scaled = users((scale_d,), sc)
+        inter = [(inter_a, g) for g in range(PASSES)] + [(inter_b, ci) for ci in range(CHUNKS)]
+
+        def needs(step):
+            fn = step[0]
+            if fn == widen:
+                return both(turn, step[1] - WIDE) if step[1] >= WIDE else []
+            if fn == turn:
+                n = turns.index(step)
+                return [(widen, step[1], 2 * step[2]), (widen, step[1], 2 * step[2] + 1)] + [(empty,) + t[1:] for t in turns[max(n - TB, 0) : max(n - TB + 1, 0)]]
+            if fn == empty:
+                return [(turn,) + step[1:]] + ([(quant, step[1] - GROUP)] if step[1] >= GROUP else [])
+            if fn == quant:
+                return both(empty, step[1])
+            if fn in (inter_a, inter_b):
+                n = inter.index(step) - INTER
+                return [] if n < 0 else [(quant_a if n < PASSES else quant_b, inter[n][1])]
+            if fn == warm:
+                return [(inter_a, 2)]
+            if fn == quant_a:
+                return [(inter_a, step[1])]
+            if fn == quant_b:
+                return [(inter_b, step[1])]
+            if fn in (down, up):
+                n = hd.index(step) - HB
+                slot = [] if n < 0 else [(scale_h if hd[n][0] == down else scale_d,) + hd[n][1:]]
+                if fn == down:
+                    return slot + [(quant, X[step[1]])] + [(quant_a, g) for g in range(PASSES)]
+                return slot + [(quant_h, 2 * step[1]), (quant_h, 2 * step[1] + 1), (quant_b, step[2])]
+            if fn == scale_h:
+                return [(down, step[1]), (small, "lam")] + ([(quant_h, step[1] - 2)] if step[1] >= 2 else [])
+            if fn == quant_h:
+                return [(scale_h, step[1])]
+            if fn == scale_d:
+                n = scaled.index(step) - YB
+                return [(up,) + step[1:], (small, "c")] + ([] if n < 0 else [(finish,) + scaled[n][1:]])
+            if fn == base:
+                n = bases.index(step) - BB
+                return [(quant, X[2 * step[1]]), (quant, X[2 * step[1] + 1]), (quant, W[step[2]]), (quant, W[step[2]] + 1)] + ([] if n < 0 else [(finish,) + bases[n][1:]])
+            if fn == finish:
+                return [(base,) + step[1:], (scale_d,) + step[1:]]
+            return []
+
+        written = set()
+        progs = [pe, ve, sc]
+        while any(progs):
+            ready = [prog for prog in progs if prog and all(need in written for need in needs(prog[0]))]
+            step = ready[0][0]
+            step[0](*step[1:])
+            written.add(step)
+            progs = [prog[1:] if prog and prog[0] == step else prog for prog in progs]

@@ -21,16 +21,18 @@ XT = T // P
 PASSES = K // 512
 WIDTH = 256
 CHUNKS = N // WIDTH
+LAST = (XT // 2 - 1, CHUNKS - 1)
 ORDER = "x0 x1 x2 x3 x4 x5 w0 x6 x7 w1 w2 w3 w4 w5"
-LOADS = "xs x0 x1 a0 a1 a2 a3 lam x2 x3 x4 x5 ws w0 c b0 x6 x7 w1 b1 w2 b2 w3 b3 w4 b4 w5 b5"
+LOADS = "xs x0 x1 a0 a1 a2 a3 x2 x3 lam x4 x5 ws w0 c b0 x6 x7 w1 b1 w2 b2 w3 b3 w4 b4 w5 b5"
 SX = (2, 2, 2, 2, 2, 2, 2, 2)
-SW = ((1, 1), (1, 1), (1, 0), (1, 0), (1, 0), (1, 0))
+SW = ((1, 1), (1, 1), (0, 0), (0, 0), (0, 0), (0, 0))
 A_ENG = "VSVV"
 TB, HB, BB = 4, 2, 2
-WIDE, GROUP, INTER, YB = 6, 3, 4, 4
-WARM = 0
-FILL = (1, 1, 1, 1, 1, 0, 1, 1, 1, 1, 1, 0, 1, 1, 0, 1, 2, 2, 1, 1, 1, 1)
-SFILL = (2, 2, 2, 3, 1, 1, 1, 0, 2, 1)
+WIDE, GROUP, INTER, YB = 7, 3, 4, 4
+WARM = 5
+PAIR = 0
+FILL = (1,) * 22
+SFILL = (2, 2, 2, 1, 1, 1, 1, 1, 1, 1)
 
 
 def tile_fp8_base_lora_d2_kernel(tc, x_bytes, x_scale, w_bytes, w_scale, a, lam, b, c, out):
@@ -57,6 +59,10 @@ def tile_fp8_base_lora_d2_kernel(tc, x_bytes, x_scale, w_bytes, w_scale, a, lam,
         ident = const.tile([P, P], F32, name="ident")
         make_identity(nc, ident[:])
 
+        seed = const.tile([P, 8], F32, name="seed")
+        nc.vector.memset(seed[:], 0.0)
+        unread = const.tile([P, 8], F32, name="unread")
+        nc.scalar.activation(out=unread[:], in_=seed[:], func=COPY)
         xs = const.tile([P, XT * 16], F32, name="xs")
         lam_b = const.tile([P, 4], BF16, name="lam_b")
         c_b = const.tile([P, XT], BF16, name="c_b")
@@ -244,9 +250,13 @@ def tile_fp8_base_lora_d2_kernel(tc, x_bytes, x_scale, w_bytes, w_scale, a, lam,
                 nc.scalar.activation(out=y[j, ci][:, i, :], in_=dps[j, ci][:, i, :], func=COPY, scale=c_f[:, m : m + 1])
 
         def base(j, ci):
-            ps = ps_b.tile([P, 2, WIDTH], F32, name="base")
-            bps[j, ci] = ps
+            if (j, ci) == LAST:
+                banks = [ps_t.tile([P, 2, WIDTH], F32, name="xt") for i in range(2)]
+            else:
+                banks = [ps_b.tile([P, 2, WIDTH], F32, name="base")] * 2
+            bps[j, ci] = banks
             for i in range(2):
+                ps = banks[i]
                 xu = x_unit[2 * j + i]
                 for g in range(PASSES):
                     s, c0 = w_unit[ci] + g // 2, WIDTH * (g % 2)
@@ -261,8 +271,13 @@ def tile_fp8_base_lora_d2_kernel(tc, x_bytes, x_scale, w_bytes, w_scale, a, lam,
                     )
 
         def finish(j, ci):
+            if (j, ci) == LAST:
+                for i in range(2):
+                    nc.vector.tensor_tensor(out=y[j, ci][:, i, :], in0=bps[j, ci][i][:, i, :], in1=y[j, ci][:, i, :], op=ADD)
+                    nc.sync.dma_start(out=out_view[:, 2 * j + i, WIDTH * ci : WIDTH * (ci + 1)], in_=y[j, ci][:, i, :])
+                return
             yt = y[j, ci][:].rearrange("p i n -> p (i n)")
-            nc.vector.tensor_tensor(out=yt, in0=bps[j, ci][:].rearrange("p i n -> p (i n)"), in1=yt, op=ADD)
+            nc.vector.tensor_tensor(out=yt, in0=bps[j, ci][0][:].rearrange("p i n -> p (i n)"), in1=yt, op=ADD)
             nc.sync.dma_start(out=out_view[:, 2 * j : 2 * j + 2, WIDTH * ci : WIDTH * (ci + 1)], in_=y[j, ci][:])
 
         def small(which):
@@ -289,10 +304,17 @@ def tile_fp8_base_lora_d2_kernel(tc, x_bytes, x_scale, w_bytes, w_scale, a, lam,
         X = x_unit
         W = w_unit
         pe = both(turn, X[0]) + both(turn, X[1]) + [(warm, i) for i in range(WARM)]
-        for m in range(2, 6):
-            pe += [(down, m - 2)] + both(turn, X[m])
-        pe += [(down, 4)] + both(turn, W[0]) + both(turn, W[0] + 1) + [(down, 5)] + both(turn, X[6])
-        pe += [(up, 0, 0), (up, 1, 0), (base, 0, 0)] + both(turn, X[7]) + [(down, 6), (base, 1, 0), (up, 2, 0), (down, 7), (base, 2, 0)]
+        if PAIR:
+            pe += [(down, 0)]
+            for m in (2, 4):
+                pe += both(turn, X[m]) + both(turn, X[m + 1]) + [(down, m - 1), (down, m)]
+            pe += both(turn, W[0]) + both(turn, W[0] + 1) + [(down, 5), (up, 0, 0)] + both(turn, X[6]) + both(turn, X[7])
+            pe += [(up, 1, 0), (base, 0, 0), (down, 6), (base, 1, 0), (up, 2, 0), (down, 7), (base, 2, 0)]
+        else:
+            for m in range(2, 6):
+                pe += [(down, m - 2)] + both(turn, X[m])
+            pe += [(down, 4)] + both(turn, W[0]) + both(turn, W[0] + 1) + [(down, 5)] + both(turn, X[6])
+            pe += [(up, 0, 0), (up, 1, 0), (base, 0, 0)] + both(turn, X[7]) + [(down, 6), (base, 1, 0), (up, 2, 0), (down, 7), (base, 2, 0)]
         pe += both(turn, W[1]) + both(turn, W[1] + 1) + [(up, 3, 0), (up, 0, 1)]
         jobs = [(j, ci) for ci in range(CHUNKS) for j in range(4)]
         for n in range(3, len(jobs)):
@@ -328,8 +350,8 @@ def tile_fp8_base_lora_d2_kernel(tc, x_bytes, x_scale, w_bytes, w_scale, a, lam,
                 ve += [(finish, 1, ci)]
             else:
                 ve += [(finish, 2, ci - 1), (finish, 3, ci - 1)]
-        sc = sp(X[0]) + sp(X[1]) + both(empty, X[0]) + [(inter_a, 1)] + both(empty, X[1]) + [(small, "lam")] + sp(X[2]) + sp(X[3])
-        fill = sp(X[4]) + sp(X[5]) + sp(W[0]) + sp(W[0] + 1) + [(small, "c"), (inter_b, 0)] + sp(X[6]) + sp(X[7]) + sp(W[1]) + sp(W[1] + 1) + [(inter_b, 1)]
+        sc = sp(X[0]) + sp(X[1]) + both(empty, X[0]) + [(inter_a, 1)] + both(empty, X[1]) + sp(X[2]) + sp(X[3]) + [(small, "lam")] + sp(X[4])
+        fill = sp(X[5]) + sp(W[0]) + sp(W[0] + 1) + [(small, "c"), (inter_b, 0)] + sp(X[6]) + sp(X[7]) + sp(W[1]) + sp(W[1] + 1) + [(inter_b, 1)]
         marks = [both(empty, X[m]) for m in range(2, 6)] + [both(empty, W[0]), both(empty, W[0] + 1), both(empty, X[6]), [(scale_d, 0, 0), (scale_d, 1, 0)], both(empty, X[7]), [(scale_d, 2, 0)]]
         for n, mark in enumerate(marks):
             sc += mark

@@ -24,14 +24,14 @@ CHUNKS = N // WIDTH
 LAST = (XT // 2 - 1, CHUNKS - 1)
 ORDER = "x0 x1 x2 x3 x4 x5 w0 x6 x7 w1 w2 w3 w4 w5"
 LOADS = "xs x0 x1 a0 a1 a2 a3 x2 x3 lam x4 x5 ws w0 c b0 x6 x7 w1 b1 w2 b2 w3 b3 w4 b4 w5 b5"
-SX = (2, 2, 2, 2, 2, 2, 2, 2)
-SW = ((1, 1), (1, 1), (0, 0), (0, 0), (0, 0), (0, 0))
+SX = (2, 2, 2, 2, 2, 2, 1, 1)
+SW = ((2, 2), (1, 1), (0, 0), (0, 0), (0, 0), (0, 0))
 A_ENG = "VSVV"
 TB, HB, BB = 4, 2, 2
 WIDE, GROUP, INTER, YB = 7, 3, 4, 4
 WARM = 5
 PAIR = 0
-FILL = (1,) * 22
+FILL = (1,) * 23
 SFILL = (2, 2, 2, 1, 1, 1, 1, 1, 1, 1)
 
 
@@ -173,7 +173,8 @@ def tile_fp8_base_lora_d2_kernel(tc, x_bytes, x_scale, w_bytes, w_scale, a, lam,
         def inter_a(g):
             a_int[g] = groupp.tile([P, 4, P, 4], BF16, name="ab_int", bufs=INTER, align_bytes=64)
             (nc.scalar.copy if A_ENG[g] == "S" else nc.vector.tensor_copy)(
-                out=a_int[g][:], in_=araw[g][:].rearrange("p j (m t) -> p t m j", t=4)
+                out=a_int[g][:].rearrange("p t (q m) j -> p q t m j", m=2),
+                in_=araw[g][:].rearrange("p j (q m t) -> p q t m j", m=2, t=4),
             )
 
         def quant_a(g):
@@ -185,7 +186,9 @@ def tile_fp8_base_lora_d2_kernel(tc, x_bytes, x_scale, w_bytes, w_scale, a, lam,
 
         def inter_b(ci):
             b_int[ci] = groupp.tile([P, WIDTH, 4], BF16, name="ab_int", bufs=INTER, align_bytes=64)
-            nc.scalar.copy(out=b_int[ci][:], in_=braw[ci][:].rearrange("p j n -> p n j"))
+            nc.scalar.copy(
+                out=b_int[ci][:].rearrange("p (n i) j -> p n j i", i=4), in_=braw[ci][:].rearrange("p j (n i) -> p n j i", i=4)
+            )
 
         def quant_b(ci):
             b_codes[ci] = codes.tile([P, WIDTH], U32, name="bcodes%d" % ci, align_bytes=64)
@@ -304,17 +307,11 @@ def tile_fp8_base_lora_d2_kernel(tc, x_bytes, x_scale, w_bytes, w_scale, a, lam,
         X = x_unit
         W = w_unit
         pe = both(turn, X[0]) + both(turn, X[1]) + [(warm, i) for i in range(WARM)]
-        if PAIR:
-            pe += [(down, 0)]
-            for m in (2, 4):
-                pe += both(turn, X[m]) + both(turn, X[m + 1]) + [(down, m - 1), (down, m)]
-            pe += both(turn, W[0]) + both(turn, W[0] + 1) + [(down, 5), (up, 0, 0)] + both(turn, X[6]) + both(turn, X[7])
-            pe += [(up, 1, 0), (base, 0, 0), (down, 6), (base, 1, 0), (up, 2, 0), (down, 7), (base, 2, 0)]
-        else:
-            for m in range(2, 6):
-                pe += [(down, m - 2)] + both(turn, X[m])
-            pe += [(down, 4)] + both(turn, W[0]) + both(turn, W[0] + 1) + [(down, 5)] + both(turn, X[6])
-            pe += [(up, 0, 0), (up, 1, 0), (base, 0, 0)] + both(turn, X[7]) + [(down, 6), (base, 1, 0), (up, 2, 0), (down, 7), (base, 2, 0)]
+        pe += [(down, 0)]
+        for m in (2, 4):
+            pe += both(turn, X[m]) + both(turn, X[m + 1]) + [(down, m - 1), (down, m)]
+        pe += both(turn, W[0]) + both(turn, W[0] + 1) + [(down, 5)] + both(turn, X[6])
+        pe += [(up, 0, 0), (up, 1, 0), (base, 0, 0)] + both(turn, X[7]) + [(down, 6), (base, 1, 0), (up, 2, 0), (down, 7), (base, 2, 0)]
         pe += both(turn, W[1]) + both(turn, W[1] + 1) + [(up, 3, 0), (up, 0, 1)]
         jobs = [(j, ci) for ci in range(CHUNKS) for j in range(4)]
         for n in range(3, len(jobs)):
@@ -324,13 +321,12 @@ def tile_fp8_base_lora_d2_kernel(tc, x_bytes, x_scale, w_bytes, w_scale, a, lam,
             pe += [(base, j, ci)]
             if n + 2 < len(jobs):
                 pe += [(up,) + jobs[n + 2]]
-        ve = vp(X[0]) + vp(X[1]) + [(inter_a, 0), (quant, X[0]), (quant_a, 0), (inter_a, 2), (inter_a, 3), (quant_a, 1), (quant_a, 2), (quant_a, 3)]
-        ve += vp(X[2]) + [(quant, X[1])] + vp(X[3])
-        fill = vp(X[4]) + vp(X[5]) + vp(W[0]) + vp(W[0] + 1) + vp(X[6]) + vp(X[7]) + vp(W[1]) + vp(W[1] + 1)
-        marks = []
-        for m in range(5):
-            marks += [[(scale_h, m)], [(quant_h, m)], [(quant, X[m + 2])] if m < 4 else [(quant_b, 0), (quant, W[0])]]
-        marks += [[(scale_h, 5), (quant, W[0] + 1)], [(quant_h, 5), (quant, X[6])], [(finish, 0, 0), (quant, X[7])], [(scale_h, 6)], [(quant_h, 6), (finish, 1, 0)], [(scale_h, 7)], [(quant_h, 7), (quant_b, 1)]]
+        ve = vp(X[0]) + vp(X[1]) + [(inter_a, 0), (quant_a, 0), (quant, X[0]), (inter_a, 2), (inter_a, 3), (quant_a, 1), (quant_a, 2), (quant_a, 3)]
+        ve += vp(X[2]) + [(quant, X[1])]
+        fill = vp(X[3]) + vp(X[4]) + vp(X[5]) + vp(W[0]) + vp(W[0] + 1) + vp(X[6]) + vp(X[7]) + vp(W[1]) + vp(W[1] + 1)
+        marks = [[], [(scale_h, 0)], [(quant_h, 0)], [(quant, X[2])], [], [(quant, X[3]), (scale_h, 1)], [(quant_h, 1), (scale_h, 2)], [(quant_h, 2)]]
+        marks += [[(quant, X[4])], [(quant, X[5]), (scale_h, 3)], [(quant_h, 3), (scale_h, 4)], [(quant_h, 4), (quant_b, 0)], [(quant, W[0])], [(quant, W[0] + 1), (scale_h, 5)]]
+        marks += [[(quant_h, 5)], [(quant, X[6])], [(finish, 0, 0)], [], [], [(scale_h, 6), (quant, X[7]), (quant_h, 6), (finish, 1, 0)], [], [], [(scale_h, 7), (quant_b, 1), (quant_h, 7)]]
         for n, mark in enumerate(marks):
             ve += mark
             for k in range(FILL[n]):
@@ -351,14 +347,10 @@ def tile_fp8_base_lora_d2_kernel(tc, x_bytes, x_scale, w_bytes, w_scale, a, lam,
             else:
                 ve += [(finish, 2, ci - 1), (finish, 3, ci - 1)]
         sc = sp(X[0]) + sp(X[1]) + both(empty, X[0]) + [(inter_a, 1)] + both(empty, X[1]) + sp(X[2]) + sp(X[3]) + [(small, "lam")] + sp(X[4])
-        fill = sp(X[5]) + sp(W[0]) + sp(W[0] + 1) + [(small, "c"), (inter_b, 0)] + sp(X[6]) + sp(X[7]) + sp(W[1]) + sp(W[1] + 1) + [(inter_b, 1)]
-        marks = [both(empty, X[m]) for m in range(2, 6)] + [both(empty, W[0]), both(empty, W[0] + 1), both(empty, X[6]), [(scale_d, 0, 0), (scale_d, 1, 0)], both(empty, X[7]), [(scale_d, 2, 0)]]
-        for n, mark in enumerate(marks):
-            sc += mark
-            for k in range(SFILL[n]):
-                sc += fill[:1]
-                fill = fill[1:]
-        sc += fill
+        sc += both(empty, X[2]) + both(empty, X[3]) + sp(X[5]) + [(inter_b, 0)] + sp(W[0])[:1]
+        sc += both(empty, X[4]) + both(empty, X[5]) + sp(W[0])[1:] + sp(W[0] + 1)
+        sc += both(empty, W[0]) + both(empty, W[0] + 1) + sp(X[6]) + [(small, "c")] + sp(X[7])
+        sc += both(empty, X[6]) + [(scale_d, 0, 0), (scale_d, 1, 0)] + both(empty, X[7]) + sp(W[1]) + sp(W[1] + 1) + [(scale_d, 2, 0), (inter_b, 1)]
         for ci in range(1, CHUNKS):
             sc += both(empty, W[ci]) + both(empty, W[ci] + 1)
             if ci == 1:

@@ -23,14 +23,21 @@ WIDTH = 256
 CHUNKS = N // WIDTH
 LAST = (XT // 2 - 1, CHUNKS - 1)
 ORDER = "x0 x1 x2 x3 x4 x5 w0 x6 x7 w1 w2 w3 w4 w5"
-LOADS = "xs x0 x1 a0 a1 a2 a3 x2 x3 lam x4 x5 ws w0 c b0 x6 x7 w1 b1 w2 b2 w3 b3 w4 b4 w5 b5"
-SX = (2, 2, 2, 2, 2, 2, 1, 1)
-SW = ((2, 2), (1, 1), (0, 0), (0, 0), (0, 0), (0, 0))
+LOADS = "xs x0 x1 a0 a1 a2 a3 x2 x3 lam x4 x5 ws w0 c x6 x7 w1 b1 b0 w2 b2 w3 b3 w4 b4 w5 b5"
+SX = (2, 2, 2, 2, 2, 2, 2, 1)
+SW = ((2, 2), (0, 1), (0, 0), (0, 0), (0, 0), (0, 0))
 A_ENG = "VSVV"
 TB, HB, BB = 4, 2, 2
 WIDE, GROUP, INTER, YB = 7, 3, 4, 4
 WARM = 5
-PAIR = 0
+PAIR = 1
+LATE = 1
+L0 = 18
+FINE = 1
+ENDING = ((0, 0, 256), (1, 0, 128), (1, 128, 256))
+SPLIT = 1
+SCUT, GAP1, GAP2, GAP3 = 2, 2, 1, 1
+EXTRA = 2
 FILL = (1,) * 23
 SFILL = (2, 2, 2, 1, 1, 1, 1, 1, 1, 1)
 
@@ -41,13 +48,17 @@ def tile_fp8_base_lora_d2_kernel(tc, x_bytes, x_scale, w_bytes, w_scale, a, lam,
         const = ctx.enter_context(tc.tile_pool(name="const", bufs=1))
         codes = ctx.enter_context(tc.tile_pool(name="codes", bufs=1))
         loads = ctx.enter_context(tc.tile_pool(name="loads", bufs=1))
-        widep = ctx.enter_context(tc.tile_pool(name="widep", bufs=WIDE))
-        groupp = ctx.enter_context(tc.tile_pool(name="groupp", bufs=GROUP))
-        hpool = ctx.enter_context(tc.tile_pool(name="hpool", bufs=2))
-        ypool = ctx.enter_context(tc.tile_pool(name="ypool", bufs=YB))
-        ps_t = ctx.enter_context(tc.psum_pool(name="ps_t", bufs=TB))
-        ps_h = ctx.enter_context(tc.psum_pool(name="ps_h", bufs=HB))
-        ps_b = ctx.enter_context(tc.psum_pool(name="ps_b", bufs=BB))
+        work = ctx.enter_context(tc.tile_pool(name="work", bufs=1))
+        psum = ctx.enter_context(tc.psum_pool(name="psum", bufs=1))
+        taken = {}
+
+        def ring(pool, what, depth, shape, dtype):
+            n = taken.get(what, 0)
+            taken[what] = n + 1
+            if pool == psum:
+                return pool.tile(shape, dtype, name="%s%d" % (what, n % depth))
+            return pool.tile(shape, dtype, name="%s%d" % (what, n % depth), align_bytes=64)
+
         ctx.enter_context(tc.manual_schedule())
 
         x_view = x_bytes.rearrange("(p m) k -> p m k", m=XT)
@@ -119,7 +130,7 @@ def tile_fp8_base_lora_d2_kernel(tc, x_bytes, x_scale, w_bytes, w_scale, a, lam,
 
         def widen(s, i):
             if s not in wide:
-                wide[s] = widep.tile([P, 4, 2, P, 2], BF16, name="wide", align_bytes=64)
+                wide[s] = ring(work, "wide", WIDE, [P, 4, 2, P, 2], BF16)
             kind, row, g = units[s][i]
             src = xb[row] if kind == "x" else wb[row]
             sc = xs if kind == "x" else ws
@@ -141,7 +152,7 @@ def tile_fp8_base_lora_d2_kernel(tc, x_bytes, x_scale, w_bytes, w_scale, a, lam,
                     )
 
         def turn(s, h):
-            xt = ps_t.tile([P, 4, P], F32, name="xt")
+            xt = ring(psum, "xt", TB, [P, 4, P], F32)
             turned[s, h] = xt
             for i in range(2):
                 for u in range(2):
@@ -153,7 +164,7 @@ def tile_fp8_base_lora_d2_kernel(tc, x_bytes, x_scale, w_bytes, w_scale, a, lam,
 
         def empty(s, h):
             if h == 0:
-                grouped[s] = groupp.tile([P, 4, P, 4], BF16, name="grouped", align_bytes=64)
+                grouped[s] = ring(work, "grouped", GROUP, [P, 4, P, 4], BF16)
             xt = turned[s, h]
             nc.scalar.copy(
                 out=grouped[s][:, 2 * h : 2 * h + 2, :, :].rearrange("p i w t -> p (i w t)").bitcast(F32).rearrange("p (i w u) -> p i w u", i=2, u=2),
@@ -170,22 +181,26 @@ def tile_fp8_base_lora_d2_kernel(tc, x_bytes, x_scale, w_bytes, w_scale, a, lam,
         a_int, a_codes, a_scales = {}, {}, {}
         b_int, b_codes, b_scales = {}, {}, {}
 
-        def inter_a(g):
-            a_int[g] = groupp.tile([P, 4, P, 4], BF16, name="ab_int", bufs=INTER, align_bytes=64)
+        def inter_a(g, t0, t1):
+            if t0 == 0:
+                a_int[g] = ring(work, "ab_int", INTER, [P, 4, P, 4], BF16)
             (nc.scalar.copy if A_ENG[g] == "S" else nc.vector.tensor_copy)(
-                out=a_int[g][:].rearrange("p t (q m) j -> p q t m j", m=2),
-                in_=araw[g][:].rearrange("p j (q m t) -> p q t m j", m=2, t=4),
+                out=a_int[g][:, t0:t1, :, :].rearrange("p t (q m) j -> p q t m j", m=2),
+                in_=araw[g][:].rearrange("p j (q m t) -> p q t m j", m=2, t=4)[:, :, t0:t1, :, :],
             )
 
-        def quant_a(g):
-            a_codes[g] = codes.tile([P, 512], U32, name="acodes%d" % g, align_bytes=64)
-            a_scales[g] = codes.tile([P, 512], U8, name="ascales%d" % g, align_bytes=64)
+        def quant_a(g, t0, t1):
+            if t0 == 0:
+                a_codes[g] = codes.tile([P, 512], U32, name="acodes%d" % g, align_bytes=64)
+                a_scales[g] = codes.tile([P, 512], U8, name="ascales%d" % g, align_bytes=64)
             nc.vector.quantize_mx(
-                out=a_codes[g][:].bitcast(FP8X4), scales=a_scales[g][:], in_=a_int[g][:].rearrange("p t m j -> p (t m j)")
+                out=a_codes[g][:, P * t0 : P * t1].bitcast(FP8X4),
+                scales=a_scales[g][:, P * t0 : P * t1],
+                in_=a_int[g][:, t0:t1, :, :].rearrange("p t m j -> p (t m j)"),
             )
 
         def inter_b(ci):
-            b_int[ci] = groupp.tile([P, WIDTH, 4], BF16, name="ab_int", bufs=INTER, align_bytes=64)
+            b_int[ci] = ring(work, "b_int", 3, [P, WIDTH, 4], BF16)
             nc.scalar.copy(
                 out=b_int[ci][:].rearrange("p (n i) j -> p n j i", i=4), in_=braw[ci][:].rearrange("p j (n i) -> p n j i", i=4)
             )
@@ -200,7 +215,7 @@ def tile_fp8_base_lora_d2_kernel(tc, x_bytes, x_scale, w_bytes, w_scale, a, lam,
         hps, hg, h_codes, h_scales = {}, {}, {}, {}
 
         def down(m):
-            hps[m] = ps_h.tile([P, 4, P], F32, name="hd")
+            hps[m] = ring(psum, "hd", HB, [P, 4, P], F32)
             for t in range(4):
                 for g in range(PASSES):
                     nc.tensor.matmul_mx(
@@ -214,32 +229,36 @@ def tile_fp8_base_lora_d2_kernel(tc, x_bytes, x_scale, w_bytes, w_scale, a, lam,
                     )
 
         def scale_h(m):
-            hg[m] = hpool.tile([P, P, 4], BF16, name="h_grouped", align_bytes=64)
+            if m % 2 == 0:
+                hg[m // 2] = const.tile([P, 2, P, 4], BF16, name="h_grouped%d" % (m // 2), align_bytes=64)
             nc.vector.tensor_tensor(
-                out=hg[m][:],
+                out=hg[m // 2][:, m % 2, :, :],
                 in0=hps[m][:].rearrange("p t w -> p w t"),
                 in1=lam_f[:].unsqueeze(1).to_broadcast([P, P, 4]),
                 op=MULT,
             )
 
-        def quant_h(m):
-            h_codes[m] = codes.tile([P, P], U32, name="hcodes%d" % m, align_bytes=64)
-            h_scales[m] = codes.tile([P, P], U8, name="hscales%d" % m, align_bytes=64)
+        def quant_h(j):
+            h_codes[j] = codes.tile([P, 2 * P], U32, name="hcodes%d" % j, align_bytes=64)
+            h_scales[j] = codes.tile([P, 2 * P], U8, name="hscales%d" % j, align_bytes=64)
             nc.vector.quantize_mx(
-                out=h_codes[m][:].bitcast(FP8X4), scales=h_scales[m][:], in_=hg[m][:].rearrange("p w t -> p (w t)")
+                out=h_codes[j][:].bitcast(FP8X4), scales=h_scales[j][:], in_=hg[j][:].rearrange("p i w t -> p (i w t)")
             )
 
         y, bps, dps, warm_ps = {}, {}, {}, {}
         out_view = out.rearrange("(p m) n -> p m n", m=XT)
 
         def up(j, ci):
-            ps = ps_h.tile([P, 2, WIDTH], F32, name="hd")
+            if ci < LATE:
+                ps = ring(psum, "xt", TB, [P, 2, WIDTH], F32)
+            else:
+                ps = ring(psum, "hd", HB, [P, 2, WIDTH], F32)
             dps[j, ci] = ps
             for i in range(2):
                 nc.tensor.matmul_mx(
                     out=ps[:, i, :],
-                    lhsT=h_codes[2 * j + i][:].bitcast(FP8X4),
-                    lhsT_scale=h_scales[2 * j + i][:],
+                    lhsT=h_codes[j][:, P * i : P * (i + 1)].bitcast(FP8X4),
+                    lhsT_scale=h_scales[j][:, P * i : P * (i + 1)],
                     rhs=b_codes[ci][:].bitcast(FP8X4),
                     rhs_scale=b_scales[ci][:],
                     start=True,
@@ -247,40 +266,54 @@ def tile_fp8_base_lora_d2_kernel(tc, x_bytes, x_scale, w_bytes, w_scale, a, lam,
                 )
 
         def scale_d(j, ci):
-            y[j, ci] = ypool.tile([P, 2, WIDTH], F32, name="y", align_bytes=64)
+            y[j, ci] = ring(work, "y", YB, [P, 2, WIDTH], F32)
             for i in range(2):
                 m = 2 * j + i
                 nc.scalar.activation(out=y[j, ci][:, i, :], in_=dps[j, ci][:, i, :], func=COPY, scale=c_f[:, m : m + 1])
 
         def base(j, ci):
             if (j, ci) == LAST:
-                banks = [ps_t.tile([P, 2, WIDTH], F32, name="xt") for i in range(2)]
+                parts = [(ring(psum, "xt", TB, [P, 2, WIDTH], F32), i, n0, n1) for i, n0, n1 in ENDING]
+            elif (j + 1, ci) == LAST and FINE:
+                parts = [(ring(psum, "base", BB, [P, 2, WIDTH], F32), i, 0, WIDTH) for i in range(2)]
             else:
-                banks = [ps_b.tile([P, 2, WIDTH], F32, name="base")] * 2
-            bps[j, ci] = banks
-            for i in range(2):
-                ps = banks[i]
+                ps = ring(psum, "base", BB, [P, 2, WIDTH], F32)
+                parts = [(ps, i, 0, WIDTH) for i in range(2)]
+            bps[j, ci] = parts
+            for ps, i, n0, n1 in parts:
                 xu = x_unit[2 * j + i]
                 for g in range(PASSES):
                     s, c0 = w_unit[ci] + g // 2, WIDTH * (g % 2)
                     nc.tensor.matmul_mx(
-                        out=ps[:, i, :],
+                        out=ps[:, i, n0:n1],
                         lhsT=ucodes[xu][:, P * g : P * (g + 1)].bitcast(FP8X4),
                         lhsT_scale=uscales[xu][:, P * g : P * (g + 1)],
-                        rhs=ucodes[s][:, c0 : c0 + WIDTH].bitcast(FP8X4),
-                        rhs_scale=uscales[s][:, c0 : c0 + WIDTH],
+                        rhs=ucodes[s][:, c0 + n0 : c0 + n1].bitcast(FP8X4),
+                        rhs_scale=uscales[s][:, c0 + n0 : c0 + n1],
                         start=(g == 0),
                         stop=(g == PASSES - 1),
                     )
 
+        def park(j, ci):
+            y[j, ci] = const.tile([P, 2, WIDTH], F32, name="parked%d_%d" % (j, ci), align_bytes=64)
+            nc.scalar.copy(out=y[j, ci][:].rearrange("p i n -> p (i n)"), in_=bps[j, ci][0][0][:].rearrange("p i n -> p (i n)"))
+
+        def finish_late(j, ci):
+            for i in range(2):
+                m = 2 * j + i
+                nc.vector.scalar_tensor_tensor(
+                    out=y[j, ci][:, i, :], in0=dps[j, ci][:, i, :], scalar=c_f[:, m : m + 1], in1=y[j, ci][:, i, :], op0=MULT, op1=ADD
+                )
+            nc.sync.dma_start(out=out_view[:, 2 * j : 2 * j + 2, WIDTH * ci : WIDTH * (ci + 1)], in_=y[j, ci][:])
+
         def finish(j, ci):
-            if (j, ci) == LAST:
-                for i in range(2):
-                    nc.vector.tensor_tensor(out=y[j, ci][:, i, :], in0=bps[j, ci][i][:, i, :], in1=y[j, ci][:, i, :], op=ADD)
-                    nc.sync.dma_start(out=out_view[:, 2 * j + i, WIDTH * ci : WIDTH * (ci + 1)], in_=y[j, ci][:, i, :])
+            if (j, ci) == LAST or ((j + 1, ci) == LAST and FINE):
+                for ps, i, n0, n1 in bps[j, ci]:
+                    nc.vector.tensor_tensor(out=y[j, ci][:, i, n0:n1], in0=ps[:, i, n0:n1], in1=y[j, ci][:, i, n0:n1], op=ADD)
+                    nc.sync.dma_start(out=out_view[:, 2 * j + i, WIDTH * ci + n0 : WIDTH * ci + n1], in_=y[j, ci][:, i, n0:n1])
                 return
             yt = y[j, ci][:].rearrange("p i n -> p (i n)")
-            nc.vector.tensor_tensor(out=yt, in0=bps[j, ci][0][:].rearrange("p i n -> p (i n)"), in1=yt, op=ADD)
+            nc.vector.tensor_tensor(out=yt, in0=bps[j, ci][0][0][:].rearrange("p i n -> p (i n)"), in1=yt, op=ADD)
             nc.sync.dma_start(out=out_view[:, 2 * j : 2 * j + 2, WIDTH * ci : WIDTH * (ci + 1)], in_=y[j, ci][:])
 
         def small(which):
@@ -291,7 +324,7 @@ def tile_fp8_base_lora_d2_kernel(tc, x_bytes, x_scale, w_bytes, w_scale, a, lam,
 
         def warm(i):
             if i == 0:
-                warm_ps[0] = ps_b.tile([P, 2, WIDTH], F32, name="base")
+                warm_ps[0] = ring(psum, "base", BB, [P, 2, WIDTH], F32)
             flat = a_int[2][:].rearrange("p t m j -> p (t m j)")
             nc.tensor.matmul(warm_ps[0][:].rearrange("p i n -> p (i n)"), lhsT=flat[:, :P], rhs=flat[:, :512], start=True, stop=True)
 
@@ -306,56 +339,70 @@ def tile_fp8_base_lora_d2_kernel(tc, x_bytes, x_scale, w_bytes, w_scale, a, lam,
 
         X = x_unit
         W = w_unit
+        jobs = [(j, ci) for ci in range(CHUNKS) for j in range(4)]
+        late = jobs[:4]
         pe = both(turn, X[0]) + both(turn, X[1]) + [(warm, i) for i in range(WARM)]
         pe += [(down, 0)]
         for m in (2, 4):
             pe += both(turn, X[m]) + both(turn, X[m + 1]) + [(down, m - 1), (down, m)]
-        pe += both(turn, W[0]) + both(turn, W[0] + 1) + [(down, 5)] + both(turn, X[6])
-        pe += [(up, 0, 0), (up, 1, 0), (base, 0, 0)] + both(turn, X[7]) + [(down, 6), (base, 1, 0), (up, 2, 0), (down, 7), (base, 2, 0)]
-        pe += both(turn, W[1]) + both(turn, W[1] + 1) + [(up, 3, 0), (up, 0, 1)]
-        jobs = [(j, ci) for ci in range(CHUNKS) for j in range(4)]
-        for n in range(3, len(jobs)):
+        pe += both(turn, W[0]) + both(turn, W[0] + 1) + [(down, 5)]
+        if PAIR:
+            pe += both(turn, X[6]) + both(turn, X[7]) + [(base, 0, 0), (down, 6), (base, 1, 0), (down, 7)]
+        else:
+            pe += both(turn, X[6]) + [(base, 0, 0)] + both(turn, X[7]) + [(down, 6), (base, 1, 0), (down, 7)]
+        for n in range(2, len(jobs)):
             j, ci = jobs[n]
             if j == 2 and ci + 1 < CHUNKS:
                 pe += both(turn, W[ci + 1]) + both(turn, W[ci + 1] + 1)
             pe += [(base, j, ci)]
             if n + 2 < len(jobs):
                 pe += [(up,) + jobs[n + 2]]
-        ve = vp(X[0]) + vp(X[1]) + [(inter_a, 0), (quant_a, 0), (quant, X[0]), (inter_a, 2), (inter_a, 3), (quant_a, 1), (quant_a, 2), (quant_a, 3)]
-        ve += vp(X[2]) + [(quant, X[1])]
-        fill = vp(X[3]) + vp(X[4]) + vp(X[5]) + vp(W[0]) + vp(W[0] + 1) + vp(X[6]) + vp(X[7]) + vp(W[1]) + vp(W[1] + 1)
-        marks = [[], [(scale_h, 0)], [(quant_h, 0)], [(quant, X[2])], [], [(quant, X[3]), (scale_h, 1)], [(quant_h, 1), (scale_h, 2)], [(quant_h, 2)]]
-        marks += [[(quant, X[4])], [(quant, X[5]), (scale_h, 3)], [(quant_h, 3), (scale_h, 4)], [(quant_h, 4), (quant_b, 0)], [(quant, W[0])], [(quant, W[0] + 1), (scale_h, 5)]]
-        marks += [[(quant_h, 5)], [(quant, X[6])], [(finish, 0, 0)], [], [], [(scale_h, 6), (quant, X[7]), (quant_h, 6), (finish, 1, 0)], [], [], [(scale_h, 7), (quant_b, 1), (quant_h, 7)]]
+            if 0 <= n - L0 < 4:
+                pe += [(up,) + late[n - L0]]
+        ve = vp(X[0]) + vp(X[1]) + [(inter_a, 0, 0, 4), (quant_a, 0, 0, 4), (quant, X[0]), (inter_a, 2, 0, 4)]
+        if SPLIT:
+            ve += [(inter_a, 3, 0, 2), (quant_a, 1, 0, 4), (quant_a, 2, 0, 4), (quant_a, 3, 0, 2)]
+            ve = ve[:-2] + [(quant_a, 2, 0, 4), (quant_a, 3, 0, 2), (inter_a, 3, 2, 4), (quant_a, 3, 2, 4)] + vp(X[2])
+        else:
+            ve += [(inter_a, 3, 0, 4), (quant_a, 1, 0, 4), (quant_a, 2, 0, 4), (quant_a, 3, 0, 4)] + vp(X[2])
+        ve += vp(X[3]) + [(quant, X[1])]
+        fill = vp(X[4]) + vp(X[5]) + vp(W[0]) + vp(W[0] + 1) + vp(X[6]) + vp(X[7]) + vp(W[1]) + vp(W[1] + 1) + vp(W[2])[:EXTRA]
+        marks = [[(scale_h, 0)], [(quant, X[2])], [], [(quant, X[3])], [(scale_h, 1)], [(scale_h, 2)], [(quant, X[4])]]
+        marks += [[], [(quant, X[5])], [(scale_h, 3)], [(scale_h, 4)]] + [[]] * GAP1 + [[(quant, W[0]), (quant, W[0] + 1), (scale_h, 5)]]
+        marks += [[(quant, X[6])]] + [[]] * GAP2 + [[(quant, X[7])]] + [[]] * GAP3 + [[(scale_h, 6)], [(quant_b, 1), (quant_h, 0)], [(scale_h, 7)], [(quant_h, 1)]]
         for n, mark in enumerate(marks):
-            ve += mark
-            for k in range(FILL[n]):
-                ve += fill[:1]
-                fill = fill[1:]
+            ve += mark + fill[:1]
+            fill = fill[1:]
         ve += fill
-        for ci in range(1, CHUNKS + 1):
+        for ci in range(1, CHUNKS):
             nxt = vp(W[ci + 1]) + vp(W[ci + 1] + 1) if ci + 1 < CHUNKS else []
             if ci == 1:
-                ve += [(finish, 2, 0)] + nxt[:2] + [(quant, W[ci])] + nxt[2:3] + [(quant, W[ci] + 1), (finish, 3, 0)] + nxt[3:5]
-            elif ci < CHUNKS:
-                ve += nxt[:2] + [(quant, W[ci]), (finish, 2, ci - 1), (quant, W[ci] + 1)] + nxt[2:3] + [(finish, 3, ci - 1)] + nxt[3:5]
-            if ci < CHUNKS:
-                ve += [(finish, 0, ci)] + nxt[5:]
-                if ci + 1 < CHUNKS:
-                    ve += [(quant_b, ci + 1)]
-                ve += [(finish, 1, ci)]
-            else:
-                ve += [(finish, 2, ci - 1), (finish, 3, ci - 1)]
-        sc = sp(X[0]) + sp(X[1]) + both(empty, X[0]) + [(inter_a, 1)] + both(empty, X[1]) + sp(X[2]) + sp(X[3]) + [(small, "lam")] + sp(X[4])
-        sc += both(empty, X[2]) + both(empty, X[3]) + sp(X[5]) + [(inter_b, 0)] + sp(W[0])[:1]
-        sc += both(empty, X[4]) + both(empty, X[5]) + sp(W[0])[1:] + sp(W[0] + 1)
-        sc += both(empty, W[0]) + both(empty, W[0] + 1) + sp(X[6]) + [(small, "c")] + sp(X[7])
-        sc += both(empty, X[6]) + [(scale_d, 0, 0), (scale_d, 1, 0)] + both(empty, X[7]) + sp(W[1]) + sp(W[1] + 1) + [(scale_d, 2, 0), (inter_b, 1)]
+                nxt = nxt[EXTRA:]
+            adds = [[(finish,) + job] if job not in late else [] for job in jobs[4 * ci - 2 : 4 * ci + 2]]
+            ve += nxt[:2]
+            if ci == 2:
+                ve += [(quant_b, 0)]
+            ve += [(quant, W[ci])] + adds[0] + [(quant, W[ci] + 1)]
+            if ci == 1:
+                ve += [(quant_h, 2), (quant_h, 3)]
+            if ci == CHUNKS - 1:
+                break
+            ve += nxt[2:3] + adds[1] + nxt[3:5] + adds[2] + nxt[5:] + [(quant_b, ci + 1)] + adds[3]
+        for n in range(19, len(jobs)):
+            if 0 <= n - 1 - L0 < 4:
+                ve += [(finish_late,) + late[n - 1 - L0]]
+            ve += [(finish,) + jobs[n]]
+        sc = sp(X[0]) + sp(X[1]) + both(empty, X[0]) + [(inter_a, 1, 0, 4)] + both(empty, X[1]) + sp(X[2]) + sp(X[3]) + [(small, "lam")] + sp(X[4])
+        sc += both(empty, X[2]) + both(empty, X[3]) + sp(X[5]) + sp(W[0])
+        sc += both(empty, X[4]) + both(empty, X[5]) + sp(W[0] + 1) + sp(X[6])[:SCUT]
+        sc += both(empty, W[0]) + both(empty, W[0] + 1) + sp(X[6])[SCUT:] + sp(X[7]) + [(small, "c")]
+        sc += both(empty, X[6]) + ([(park, 0, 0)] + both(empty, X[7]) if PAIR == 0 else both(empty, X[7]) + [(park, 0, 0)]) + sp(W[1]) + sp(W[1] + 1) + [(inter_b, 1), (park, 1, 0), (inter_b, 0)]
         for ci in range(1, CHUNKS):
             sc += both(empty, W[ci]) + both(empty, W[ci] + 1)
             if ci == 1:
-                sc += [(scale_d, 3, 0)]
-            sc += [(scale_d, 0, ci), (scale_d, 1, ci)]
+                sc += [(park, 2, 0), (scale_d, 0, 1), (park, 3, 0), (scale_d, 1, 1)]
+            else:
+                sc += [(scale_d, 0, ci), (scale_d, 1, ci)]
             if ci + 1 < CHUNKS:
                 sc += [(inter_b, ci + 1)] + sp(W[ci + 1]) + sp(W[ci + 1] + 1)
             sc += [(scale_d, 2, ci), (scale_d, 3, ci)]
@@ -364,10 +411,11 @@ def tile_fp8_base_lora_d2_kernel(tc, x_bytes, x_scale, w_bytes, w_scale, a, lam,
             return [step for step in prog if step[0] in fns]
 
         turns = users((turn,), pe)
-        hd = users((down, up), pe)
+        hd = [step for step in users((down, up), pe) if step[1:] not in late]
+        xt_users = [step for step in pe if step[0] == turn or (step[0] == up and step[1:] in late)]
         bases = users((base,), pe)
         scaled = users((scale_d,), sc)
-        inter = [(inter_a, g) for g in range(PASSES)] + [(inter_b, ci) for ci in range(CHUNKS)]
+        inter = users((inter_b,), sc)
 
         def needs(step):
             fn = step[0]
@@ -380,31 +428,39 @@ def tile_fp8_base_lora_d2_kernel(tc, x_bytes, x_scale, w_bytes, w_scale, a, lam,
                 return [(turn,) + step[1:]] + ([(quant, step[1] - GROUP)] if step[1] >= GROUP else [])
             if fn == quant:
                 return both(empty, step[1])
-            if fn in (inter_a, inter_b):
-                n = inter.index(step) - INTER
-                return [] if n < 0 else [(quant_a if n < PASSES else quant_b, inter[n][1])]
+            if fn == inter_b:
+                n = inter.index(step) - 3
+                return [] if n < 0 else [(quant_b, inter[n][1])]
             if fn == warm:
-                return [(inter_a, 2)]
+                return [(inter_a, 2, 0, 4)]
             if fn == quant_a:
-                return [(inter_a, step[1])]
+                return [(inter_a,) + step[1:]]
             if fn == quant_b:
                 return [(inter_b, step[1])]
+            if fn == park:
+                return [(base,) + step[1:]]
+            if fn == finish_late:
+                return [(up,) + step[1:], (park,) + step[1:], (small, "c")]
+            if fn == up and step[1:] in late:
+                old = xt_users[xt_users.index(step) - TB]
+                slot = (empty,) + old[1:] if old[0] == turn else (finish_late,) + old[1:]
+                return [slot, (quant_h, step[1]), (quant_b, step[2])]
             if fn in (down, up):
                 n = hd.index(step) - HB
                 slot = [] if n < 0 else [(scale_h if hd[n][0] == down else scale_d,) + hd[n][1:]]
                 if fn == down:
-                    return slot + [(quant, X[step[1]])] + [(quant_a, g) for g in range(PASSES)]
-                return slot + [(quant_h, 2 * step[1]), (quant_h, 2 * step[1] + 1), (quant_b, step[2])]
+                    return slot + [(quant, X[step[1]])] + users((quant_a,), ve)
+                return slot + [(quant_h, step[1]), (quant_b, step[2])]
             if fn == scale_h:
-                return [(down, step[1]), (small, "lam")] + ([(quant_h, step[1] - 2)] if step[1] >= 2 else [])
+                return [(down, step[1]), (small, "lam")]
             if fn == quant_h:
-                return [(scale_h, step[1])]
+                return [(scale_h, 2 * step[1]), (scale_h, 2 * step[1] + 1)]
             if fn == scale_d:
                 n = scaled.index(step) - YB
                 return [(up,) + step[1:], (small, "c")] + ([] if n < 0 else [(finish,) + scaled[n][1:]])
             if fn == base:
                 n = bases.index(step) - BB
-                return [(quant, X[2 * step[1]]), (quant, X[2 * step[1] + 1]), (quant, W[step[2]]), (quant, W[step[2]] + 1)] + ([] if n < 0 else [(finish,) + bases[n][1:]])
+                return [(quant, X[2 * step[1]]), (quant, X[2 * step[1] + 1]), (quant, W[step[2]]), (quant, W[step[2]] + 1)] + ([] if n < 0 else [(park if bases[n][1:] in late else finish,) + bases[n][1:]]) + ([(finish_late,) + job for job in late[:3]] if step[1:] == LAST else []) + ([(finish,) + bases[n + 1][1:]] if step[1:] == (2, CHUNKS - 1) and FINE else [])
             if fn == finish:
                 return [(base,) + step[1:], (scale_d,) + step[1:]]
             return []

@@ -3,7 +3,7 @@ from contextlib import ExitStack
 import concourse.mybir as mybir
 from concourse.masks import make_identity
 
-T, K, N, R, G = 1024, 2048, 1536, 512, 128
+T, K, N, R = 1024, 2048, 1536, 512
 P = 128
 FLOPS = 2 * T * K * N + 2 * T * K * R + 2 * T * R * N
 
@@ -17,29 +17,28 @@ MULT = mybir.AluOpType.mult
 ADD = mybir.AluOpType.add
 COPY = mybir.ActivationFunctionType.Copy
 
-XT = T // P
+TILES = T // P
+PAIRS = TILES // 2
 PASSES = K // 512
+K_BLOCKS = K // P
 WIDTH = 256
 CHUNKS = N // WIDTH
-LAST = (XT // 2 - 1, CHUNKS - 1)
-ORDER = "x0 x1 x2 x3 x4 x5 w0 x6 x7 w1 w2 w3 w4 w5"
-LOADS = "xs x0 x1 a0 a1 a2 a3 x2 x3 lam x4 x5 ws w0 c x6 x7 w1 b1 b0 w2 b2 w3 b3 w4 b4 w5 b5"
-SX = (2, 2, 2, 2, 2, 2, 2, 1)
-SW = ((2, 2), (0, 1), (0, 0), (0, 0), (0, 0), (0, 0))
-A_ENG = "VSVV"
-TB, HB, BB = 4, 2, 2
-WIDE, GROUP, INTER, YB = 7, 3, 4, 4
-WARM = 5
-PAIR = 1
-LATE = 1
-L0 = 18
-FINE = 1
+PIECES = 4
+LAST = (PAIRS - 1, CHUNKS - 1)
+BEFORE_LAST = (PAIRS - 2, CHUNKS - 1)
+
+UNIT_ORDER = "x0 x1 x2 x3 x4 x5 w0 x6 x7 w1 w2 w3 w4 w5"
+LOAD_ORDER = "xs x0 x1 a0 a1 a2 a3 x2 x3 lam x4 x5 ws w0 c x6 x7 w1 b1 b0 w2 b2 w3 b3 w4 b4 w5 b5"
+X_ON_SCALAR = (2, 2, 2, 2, 2, 2, 2, 1)
+W_ON_SCALAR = ((1, 2), (0, 0), (0, 0), (0, 0), (0, 0), (0, 0))
+A_PASS_ON_SCALAR = 1
+TURN_BANKS, ADAPTER_BANKS, BASE_BANKS = 4, 2, 2
+WIDE_BUFS, GROUP_BUFS, A_BUFS, B_BUFS, Y_BUFS = 7, 3, 4, 3, 4
+WARM_UPS = 5
+TURN_AFTER = 2
+UP_AHEAD = 2
+LEAD = 2
 ENDING = ((0, 0, 256), (1, 0, 128), (1, 128, 256))
-SPLIT = 1
-SCUT, GAP1, GAP2, GAP3 = 2, 2, 1, 1
-EXTRA = 2
-FILL = (1,) * 23
-SFILL = (2, 2, 2, 1, 1, 1, 1, 1, 1, 1)
 
 
 def tile_fp8_base_lora_d2_kernel(tc, x_bytes, x_scale, w_bytes, w_scale, a, lam, b, c, out):
@@ -61,11 +60,12 @@ def tile_fp8_base_lora_d2_kernel(tc, x_bytes, x_scale, w_bytes, w_scale, a, lam,
 
         ctx.enter_context(tc.manual_schedule())
 
-        x_view = x_bytes.rearrange("(p m) k -> p m k", m=XT)
+        x_view = x_bytes.rearrange("(p m) k -> p m k", m=TILES)
         a_view = a.rearrange("(g p j) r -> g p j r", p=P, j=4)
         b_view = b.rearrange("(p j) n -> p j n", j=4)
         w_view = w_bytes.rearrange("(r p) k -> p r k", p=P)
-        xb, araw, braw, wb = {}, {}, {}, {}
+        out_view = out.rearrange("(p m) n -> p m n", m=TILES)
+        x_raw, a_raw, b_raw, w_raw = {}, {}, {}, {}
 
         ident = const.tile([P, P], F32, name="ident")
         make_identity(nc, ident[:])
@@ -74,108 +74,104 @@ def tile_fp8_base_lora_d2_kernel(tc, x_bytes, x_scale, w_bytes, w_scale, a, lam,
         nc.vector.memset(seed[:], 0.0)
         unread = const.tile([P, 8], F32, name="unread")
         nc.scalar.activation(out=unread[:], in_=seed[:], func=COPY)
-        xs = const.tile([P, XT * 16], F32, name="xs")
+
+        xs = const.tile([P, TILES * K_BLOCKS], F32, name="xs")
         lam_b = const.tile([P, 4], BF16, name="lam_b")
-        c_b = const.tile([P, XT], BF16, name="c_b")
-        ws = const.tile([P, 192], F32, name="ws")
-        for what in LOADS.split(" "):
+        c_b = const.tile([P, TILES], BF16, name="c_b")
+        ws = const.tile([P, (N // P) * K_BLOCKS], F32, name="ws")
+        for what in LOAD_ORDER.split(" "):
             if what == "xs":
-                nc.sync.dma_start(out=xs[:], in_=x_scale.rearrange("(p m) j -> p (m j)", m=XT))
+                nc.sync.dma_start(out=xs[:], in_=x_scale.rearrange("(p m) j -> p (m j)", m=TILES))
             elif what == "lam":
                 nc.sync.dma_start(out=lam_b[:], in_=lam.rearrange("(p t) -> p t", t=4))
             elif what == "c":
-                nc.sync.dma_start(out=c_b[:], in_=c.rearrange("(p m) -> p m", m=XT))
+                nc.sync.dma_start(out=c_b[:], in_=c.rearrange("(p m) -> p m", m=TILES))
             elif what == "ws":
                 nc.sync.dma_start(out=ws[:], in_=w_scale.rearrange("i j -> (i j)").partition_broadcast(P))
             elif what[0] == "x":
                 m = int(what[1:])
-                xb[m] = loads.tile([P, K], U8, name="x_b%d" % m, align_bytes=64)
-                nc.sync.dma_start(out=xb[m][:], in_=x_view[:, m, :])
+                x_raw[m] = loads.tile([P, K], U8, name="x_b%d" % m, align_bytes=64)
+                nc.sync.dma_start(out=x_raw[m][:], in_=x_view[:, m, :])
             elif what[0] == "a":
                 g = int(what[1:])
-                araw[g] = loads.tile([P, 4, 512], BF16, name="a_raw%d" % g, align_bytes=64)
-                nc.sync.dma_start(out=araw[g][:], in_=a_view[g])
+                a_raw[g] = loads.tile([P, 4, R], BF16, name="a_raw%d" % g, align_bytes=64)
+                nc.sync.dma_start(out=a_raw[g][:], in_=a_view[g])
             elif what[0] == "b":
                 ci = int(what[1:])
-                braw[ci] = loads.tile([P, 4, WIDTH], BF16, name="b_raw%d" % ci, align_bytes=64)
-                nc.sync.dma_start(out=braw[ci][:], in_=b_view[:, :, WIDTH * ci : WIDTH * (ci + 1)])
+                b_raw[ci] = loads.tile([P, 4, WIDTH], BF16, name="b_raw%d" % ci, align_bytes=64)
+                nc.sync.dma_start(out=b_raw[ci][:], in_=b_view[:, :, WIDTH * ci : WIDTH * (ci + 1)])
             else:
                 ci = int(what[1:])
-                for r in range(2 * ci, 2 * ci + 2):
-                    wb[r] = loads.tile([P, K], U8, name="w_b%d" % r, align_bytes=64)
-                    nc.sync.dma_start(out=wb[r][:], in_=w_view[:, r, :])
+                for row in range(2 * ci, 2 * ci + 2):
+                    w_raw[row] = loads.tile([P, K], U8, name="w_b%d" % row, align_bytes=64)
+                    nc.sync.dma_start(out=w_raw[row][:], in_=w_view[:, row, :])
 
         lam_f = const.tile([P, 4], F32, name="lam_f")
-        c_f = const.tile([P, XT], F32, name="c_f")
+        c_f = const.tile([P, TILES], F32, name="c_f")
 
-        units, on_scalar, stages = [], [], []
-        x_unit, w_unit, x_stage, w_stage = {}, {}, {}, {}
-        for what in ORDER.split(" "):
+        units, on_scalar, x_unit, w_unit = [], [], {}, {}
+        for what in UNIT_ORDER.split(" "):
             idx = int(what[1:])
             if what[0] == "x":
                 x_unit[idx] = len(units)
-                x_stage[idx] = len(stages)
-                stages.append([len(units)])
                 units.append([("x", idx, g) for g in range(PASSES)])
-                on_scalar.append(SX[idx])
+                on_scalar.append(X_ON_SCALAR[idx])
             else:
                 w_unit[idx] = len(units)
-                w_stage[idx] = len(stages)
-                stages.append([len(units), len(units) + 1])
-                blocks = [("w", 2 * idx + r, g) for g in range(PASSES) for r in range(2)]
-                for i in range(0, len(blocks), 4):
-                    units.append(blocks[i : i + 4])
-                    on_scalar.append(SW[idx][i // 4])
-        wide, turned, grouped, ucodes, uscales = {}, {}, {}, {}, {}
+                for half in range(2):
+                    units.append([("w", 2 * idx + r, g) for g in (2 * half, 2 * half + 1) for r in range(2)])
+                    on_scalar.append(W_ON_SCALAR[idx][half])
+        wide, turned, grouped, unit_codes, unit_scales = {}, {}, {}, {}, {}
 
         def widen(s, i):
             if s not in wide:
-                wide[s] = ring(work, "wide", WIDE, [P, 4, 2, P, 2], BF16)
+                wide[s] = ring(work, "wide", WIDE_BUFS, [P, PIECES, 2, P, 2], BF16)
             kind, row, g = units[s][i]
-            src = xb[row] if kind == "x" else wb[row]
-            sc = xs if kind == "x" else ws
+            src = x_raw[row] if kind == "x" else w_raw[row]
+            scales = xs if kind == "x" else ws
             for q in range(4):
                 k0 = 512 * g + P * q
-                j = 16 * row + 4 * g + q
-                if i >= 4 - on_scalar[s]:
+                j = K_BLOCKS * row + 4 * g + q
+                if i >= PIECES - on_scalar[s]:
                     flat = wide[s][:, i, :, :, :].rearrange("p u w e -> p (u w e)")
                     nc.scalar.activation(
-                        out=flat[:, P * q : P * (q + 1)], in_=src[:, k0 : k0 + P].bitcast(FP8), func=COPY, scale=sc[:, j : j + 1]
+                        out=flat[:, P * q : P * (q + 1)], in_=src[:, k0 : k0 + P].bitcast(FP8), func=COPY, scale=scales[:, j : j + 1]
                     )
                 else:
                     nc.vector.tensor_scalar(
                         out=wide[s][:, i, :, 32 * q : 32 * (q + 1), :].rearrange("p u w e -> p w u e"),
                         in0=src[:, k0 : k0 + P].bitcast(FP8).rearrange("p (w u e) -> p w u e", u=2, e=2),
-                        scalar1=sc[:, j : j + 1],
+                        scalar1=scales[:, j : j + 1],
                         scalar2=None,
                         op0=MULT,
                     )
 
-        def turn(s, h):
-            xt = ring(psum, "xt", TB, [P, 4, P], F32)
-            turned[s, h] = xt
+        def turn(s, half):
+            bank = ring(psum, "xt", TURN_BANKS, [P, 4, P], F32)
+            turned[s, half] = bank
             for i in range(2):
+                piece = wide[s][:, 2 * half + i, :, :, :]
                 for u in range(2):
-                    if 2 * h + i >= 4 - on_scalar[s]:
-                        words = wide[s][:, 2 * h + i, :, :, :].rearrange("p u w e -> p (u w e)").bitcast(F32)[:, u :: 2]
+                    if 2 * half + i >= PIECES - on_scalar[s]:
+                        words = piece.rearrange("p u w e -> p (u w e)").bitcast(F32)[:, u::2]
                     else:
-                        words = wide[s][:, 2 * h + i, u, :, :].rearrange("p w e -> p (w e)").bitcast(F32)
-                    nc.tensor.transpose(xt[:, 2 * i + u, :], words, ident[:])
+                        words = piece[:, u, :, :].rearrange("p w e -> p (w e)").bitcast(F32)
+                    nc.tensor.transpose(bank[:, 2 * i + u, :], words, ident[:])
 
-        def empty(s, h):
-            if h == 0:
-                grouped[s] = ring(work, "grouped", GROUP, [P, 4, P, 4], BF16)
-            xt = turned[s, h]
+        def empty(s, half):
+            if half == 0:
+                grouped[s] = ring(work, "grouped", GROUP_BUFS, [P, PIECES, P, 4], BF16)
+            words = grouped[s][:, 2 * half : 2 * half + 2, :, :].rearrange("p i w t -> p (i w t)").bitcast(F32)
             nc.scalar.copy(
-                out=grouped[s][:, 2 * h : 2 * h + 2, :, :].rearrange("p i w t -> p (i w t)").bitcast(F32).rearrange("p (i w u) -> p i w u", i=2, u=2),
-                in_=xt[:].rearrange("p (i u) w -> p i w u", u=2),
+                out=words.rearrange("p (i w u) -> p i w u", i=2, u=2),
+                in_=turned[s, half][:].rearrange("p (i u) w -> p i w u", u=2),
             )
 
         def quant(s):
-            ucodes[s] = codes.tile([P, 512], U32, name="codes%d" % s, align_bytes=64)
-            uscales[s] = codes.tile([P, 512], U8, name="scales%d" % s, align_bytes=64)
+            unit_codes[s] = codes.tile([P, 512], U32, name="codes%d" % s, align_bytes=64)
+            unit_scales[s] = codes.tile([P, 512], U8, name="scales%d" % s, align_bytes=64)
             nc.vector.quantize_mx(
-                out=ucodes[s][:].bitcast(FP8X4), scales=uscales[s][:], in_=grouped[s][:].rearrange("p i w t -> p (i w t)")
+                out=unit_codes[s][:].bitcast(FP8X4), scales=unit_scales[s][:], in_=grouped[s][:].rearrange("p i w t -> p (i w t)")
             )
 
         a_int, a_codes, a_scales = {}, {}, {}
@@ -183,16 +179,16 @@ def tile_fp8_base_lora_d2_kernel(tc, x_bytes, x_scale, w_bytes, w_scale, a, lam,
 
         def inter_a(g, t0, t1):
             if t0 == 0:
-                a_int[g] = ring(work, "ab_int", INTER, [P, 4, P, 4], BF16)
-            (nc.scalar.copy if A_ENG[g] == "S" else nc.vector.tensor_copy)(
+                a_int[g] = ring(work, "ab_int", A_BUFS, [P, 4, P, 4], BF16)
+            (nc.scalar.copy if g == A_PASS_ON_SCALAR else nc.vector.tensor_copy)(
                 out=a_int[g][:, t0:t1, :, :].rearrange("p t (q m) j -> p q t m j", m=2),
-                in_=araw[g][:].rearrange("p j (q m t) -> p q t m j", m=2, t=4)[:, :, t0:t1, :, :],
+                in_=a_raw[g][:].rearrange("p j (q m t) -> p q t m j", m=2, t=4)[:, :, t0:t1, :, :],
             )
 
         def quant_a(g, t0, t1):
             if t0 == 0:
-                a_codes[g] = codes.tile([P, 512], U32, name="acodes%d" % g, align_bytes=64)
-                a_scales[g] = codes.tile([P, 512], U8, name="ascales%d" % g, align_bytes=64)
+                a_codes[g] = codes.tile([P, R], U32, name="acodes%d" % g, align_bytes=64)
+                a_scales[g] = codes.tile([P, R], U8, name="ascales%d" % g, align_bytes=64)
             nc.vector.quantize_mx(
                 out=a_codes[g][:, P * t0 : P * t1].bitcast(FP8X4),
                 scales=a_scales[g][:, P * t0 : P * t1],
@@ -200,9 +196,9 @@ def tile_fp8_base_lora_d2_kernel(tc, x_bytes, x_scale, w_bytes, w_scale, a, lam,
             )
 
         def inter_b(ci):
-            b_int[ci] = ring(work, "b_int", 3, [P, WIDTH, 4], BF16)
+            b_int[ci] = ring(work, "b_int", B_BUFS, [P, WIDTH, 4], BF16)
             nc.scalar.copy(
-                out=b_int[ci][:].rearrange("p (n i) j -> p n j i", i=4), in_=braw[ci][:].rearrange("p j (n i) -> p n j i", i=4)
+                out=b_int[ci][:].rearrange("p (n i) j -> p n j i", i=4), in_=b_raw[ci][:].rearrange("p j (n i) -> p n j i", i=4)
             )
 
         def quant_b(ci):
@@ -212,28 +208,28 @@ def tile_fp8_base_lora_d2_kernel(tc, x_bytes, x_scale, w_bytes, w_scale, a, lam,
                 out=b_codes[ci][:].bitcast(FP8X4), scales=b_scales[ci][:], in_=b_int[ci][:].rearrange("p n j -> p (n j)")
             )
 
-        hps, hg, h_codes, h_scales = {}, {}, {}, {}
+        h_banks, h_grouped, h_codes, h_scales = {}, {}, {}, {}
 
         def down(m):
-            hps[m] = ring(psum, "hd", HB, [P, 4, P], F32)
+            h_banks[m] = ring(psum, "hd", ADAPTER_BANKS, [P, 4, P], F32)
             for t in range(4):
                 for g in range(PASSES):
                     nc.tensor.matmul_mx(
-                        out=hps[m][:, t, :],
+                        out=h_banks[m][:, t, :],
                         lhsT=a_codes[g][:, P * t : P * (t + 1)].bitcast(FP8X4),
                         lhsT_scale=a_scales[g][:, P * t : P * (t + 1)],
-                        rhs=ucodes[x_unit[m]][:, P * g : P * (g + 1)].bitcast(FP8X4),
-                        rhs_scale=uscales[x_unit[m]][:, P * g : P * (g + 1)],
+                        rhs=unit_codes[x_unit[m]][:, P * g : P * (g + 1)].bitcast(FP8X4),
+                        rhs_scale=unit_scales[x_unit[m]][:, P * g : P * (g + 1)],
                         start=(g == 0),
                         stop=(g == PASSES - 1),
                     )
 
         def scale_h(m):
             if m % 2 == 0:
-                hg[m // 2] = const.tile([P, 2, P, 4], BF16, name="h_grouped%d" % (m // 2), align_bytes=64)
+                h_grouped[m // 2] = const.tile([P, 2, P, 4], BF16, name="h_grouped%d" % (m // 2), align_bytes=64)
             nc.vector.tensor_tensor(
-                out=hg[m // 2][:, m % 2, :, :],
-                in0=hps[m][:].rearrange("p t w -> p w t"),
+                out=h_grouped[m // 2][:, m % 2, :, :],
+                in0=h_banks[m][:].rearrange("p t w -> p w t"),
                 in1=lam_f[:].unsqueeze(1).to_broadcast([P, P, 4]),
                 op=MULT,
             )
@@ -242,21 +238,20 @@ def tile_fp8_base_lora_d2_kernel(tc, x_bytes, x_scale, w_bytes, w_scale, a, lam,
             h_codes[j] = codes.tile([P, 2 * P], U32, name="hcodes%d" % j, align_bytes=64)
             h_scales[j] = codes.tile([P, 2 * P], U8, name="hscales%d" % j, align_bytes=64)
             nc.vector.quantize_mx(
-                out=h_codes[j][:].bitcast(FP8X4), scales=h_scales[j][:], in_=hg[j][:].rearrange("p i w t -> p (i w t)")
+                out=h_codes[j][:].bitcast(FP8X4), scales=h_scales[j][:], in_=h_grouped[j][:].rearrange("p i w t -> p (i w t)")
             )
 
-        y, bps, dps, warm_ps = {}, {}, {}, {}
-        out_view = out.rearrange("(p m) n -> p m n", m=XT)
+        y, base_parts, d_banks, warm_bank = {}, {}, {}, {}
 
         def up(j, ci):
-            if ci < LATE:
-                ps = ring(psum, "xt", TB, [P, 2, WIDTH], F32)
+            if ci == 0:
+                bank = ring(psum, "xt", TURN_BANKS, [P, 2, WIDTH], F32)
             else:
-                ps = ring(psum, "hd", HB, [P, 2, WIDTH], F32)
-            dps[j, ci] = ps
+                bank = ring(psum, "hd", ADAPTER_BANKS, [P, 2, WIDTH], F32)
+            d_banks[j, ci] = bank
             for i in range(2):
                 nc.tensor.matmul_mx(
-                    out=ps[:, i, :],
+                    out=bank[:, i, :],
                     lhsT=h_codes[j][:, P * i : P * (i + 1)].bitcast(FP8X4),
                     lhsT_scale=h_scales[j][:, P * i : P * (i + 1)],
                     rhs=b_codes[ci][:].bitcast(FP8X4),
@@ -266,210 +261,207 @@ def tile_fp8_base_lora_d2_kernel(tc, x_bytes, x_scale, w_bytes, w_scale, a, lam,
                 )
 
         def scale_d(j, ci):
-            y[j, ci] = ring(work, "y", YB, [P, 2, WIDTH], F32)
+            y[j, ci] = ring(work, "y", Y_BUFS, [P, 2, WIDTH], F32)
             for i in range(2):
                 m = 2 * j + i
-                nc.scalar.activation(out=y[j, ci][:, i, :], in_=dps[j, ci][:, i, :], func=COPY, scale=c_f[:, m : m + 1])
+                nc.scalar.activation(out=y[j, ci][:, i, :], in_=d_banks[j, ci][:, i, :], func=COPY, scale=c_f[:, m : m + 1])
 
         def base(j, ci):
             if (j, ci) == LAST:
-                parts = [(ring(psum, "xt", TB, [P, 2, WIDTH], F32), i, n0, n1) for i, n0, n1 in ENDING]
-            elif (j + 1, ci) == LAST and FINE:
-                parts = [(ring(psum, "base", BB, [P, 2, WIDTH], F32), i, 0, WIDTH) for i in range(2)]
+                parts = [(ring(psum, "xt", TURN_BANKS, [P, 2, WIDTH], F32), i, n0, n1) for i, n0, n1 in ENDING]
+            elif (j, ci) == BEFORE_LAST:
+                parts = [(ring(psum, "base", BASE_BANKS, [P, 2, WIDTH], F32), i, 0, WIDTH) for i in range(2)]
             else:
-                ps = ring(psum, "base", BB, [P, 2, WIDTH], F32)
-                parts = [(ps, i, 0, WIDTH) for i in range(2)]
-            bps[j, ci] = parts
-            for ps, i, n0, n1 in parts:
-                xu = x_unit[2 * j + i]
+                shared = ring(psum, "base", BASE_BANKS, [P, 2, WIDTH], F32)
+                parts = [(shared, i, 0, WIDTH) for i in range(2)]
+            base_parts[j, ci] = parts
+            for bank, i, n0, n1 in parts:
+                tokens = x_unit[2 * j + i]
                 for g in range(PASSES):
-                    s, c0 = w_unit[ci] + g // 2, WIDTH * (g % 2)
+                    rows, c0 = w_unit[ci] + g // 2, WIDTH * (g % 2)
                     nc.tensor.matmul_mx(
-                        out=ps[:, i, n0:n1],
-                        lhsT=ucodes[xu][:, P * g : P * (g + 1)].bitcast(FP8X4),
-                        lhsT_scale=uscales[xu][:, P * g : P * (g + 1)],
-                        rhs=ucodes[s][:, c0 + n0 : c0 + n1].bitcast(FP8X4),
-                        rhs_scale=uscales[s][:, c0 + n0 : c0 + n1],
+                        out=bank[:, i, n0:n1],
+                        lhsT=unit_codes[tokens][:, P * g : P * (g + 1)].bitcast(FP8X4),
+                        lhsT_scale=unit_scales[tokens][:, P * g : P * (g + 1)],
+                        rhs=unit_codes[rows][:, c0 + n0 : c0 + n1].bitcast(FP8X4),
+                        rhs_scale=unit_scales[rows][:, c0 + n0 : c0 + n1],
                         start=(g == 0),
                         stop=(g == PASSES - 1),
                     )
 
         def park(j, ci):
             y[j, ci] = const.tile([P, 2, WIDTH], F32, name="parked%d_%d" % (j, ci), align_bytes=64)
-            nc.scalar.copy(out=y[j, ci][:].rearrange("p i n -> p (i n)"), in_=bps[j, ci][0][0][:].rearrange("p i n -> p (i n)"))
+            nc.scalar.copy(out=y[j, ci][:].rearrange("p i n -> p (i n)"), in_=base_parts[j, ci][0][0][:].rearrange("p i n -> p (i n)"))
 
-        def finish_late(j, ci):
+        def finish_parked(j, ci):
             for i in range(2):
                 m = 2 * j + i
                 nc.vector.scalar_tensor_tensor(
-                    out=y[j, ci][:, i, :], in0=dps[j, ci][:, i, :], scalar=c_f[:, m : m + 1], in1=y[j, ci][:, i, :], op0=MULT, op1=ADD
+                    out=y[j, ci][:, i, :], in0=d_banks[j, ci][:, i, :], scalar=c_f[:, m : m + 1], in1=y[j, ci][:, i, :], op0=MULT, op1=ADD
                 )
             nc.sync.dma_start(out=out_view[:, 2 * j : 2 * j + 2, WIDTH * ci : WIDTH * (ci + 1)], in_=y[j, ci][:])
 
         def finish(j, ci):
-            if (j, ci) == LAST or ((j + 1, ci) == LAST and FINE):
-                for ps, i, n0, n1 in bps[j, ci]:
-                    nc.vector.tensor_tensor(out=y[j, ci][:, i, n0:n1], in0=ps[:, i, n0:n1], in1=y[j, ci][:, i, n0:n1], op=ADD)
+            if (j, ci) in (BEFORE_LAST, LAST):
+                for bank, i, n0, n1 in base_parts[j, ci]:
+                    nc.vector.tensor_tensor(out=y[j, ci][:, i, n0:n1], in0=bank[:, i, n0:n1], in1=y[j, ci][:, i, n0:n1], op=ADD)
                     nc.sync.dma_start(out=out_view[:, 2 * j + i, WIDTH * ci + n0 : WIDTH * ci + n1], in_=y[j, ci][:, i, n0:n1])
-                return
-            yt = y[j, ci][:].rearrange("p i n -> p (i n)")
-            nc.vector.tensor_tensor(out=yt, in0=bps[j, ci][0][0][:].rearrange("p i n -> p (i n)"), in1=yt, op=ADD)
-            nc.sync.dma_start(out=out_view[:, 2 * j : 2 * j + 2, WIDTH * ci : WIDTH * (ci + 1)], in_=y[j, ci][:])
-
-        def small(which):
-            if which == "lam":
-                nc.scalar.activation(out=lam_f[:], in_=lam_b[:], func=COPY)
             else:
-                nc.scalar.activation(out=c_f[:], in_=c_b[:], func=COPY)
+                flat = y[j, ci][:].rearrange("p i n -> p (i n)")
+                nc.vector.tensor_tensor(out=flat, in0=base_parts[j, ci][0][0][:].rearrange("p i n -> p (i n)"), in1=flat, op=ADD)
+                nc.sync.dma_start(out=out_view[:, 2 * j : 2 * j + 2, WIDTH * ci : WIDTH * (ci + 1)], in_=y[j, ci][:])
+
+        def cast_lam():
+            nc.scalar.activation(out=lam_f[:], in_=lam_b[:], func=COPY)
+
+        def cast_c():
+            nc.scalar.activation(out=c_f[:], in_=c_b[:], func=COPY)
 
         def warm(i):
             if i == 0:
-                warm_ps[0] = ring(psum, "base", BB, [P, 2, WIDTH], F32)
+                warm_bank[0] = ring(psum, "base", BASE_BANKS, [P, 2, WIDTH], F32)
             flat = a_int[2][:].rearrange("p t m j -> p (t m j)")
-            nc.tensor.matmul(warm_ps[0][:].rearrange("p i n -> p (i n)"), lhsT=flat[:, :P], rhs=flat[:, :512], start=True, stop=True)
+            nc.tensor.matmul(warm_bank[0][:].rearrange("p i n -> p (i n)"), lhsT=flat[:, :P], rhs=flat[:, :512], start=True, stop=True)
 
-        def both(fn, u):
-            return [(fn, u, 0), (fn, u, 1)]
+        def halves(fn, *some_units):
+            return [(fn, s, half) for s in some_units for half in range(2)]
 
-        def vp(u):
-            return [(widen, u, i) for i in range(4 - on_scalar[u])]
+        def by_vector(*some_units):
+            return [(widen, s, i) for s in some_units for i in range(PIECES - on_scalar[s])]
 
-        def sp(u):
-            return [(widen, u, i) for i in range(4 - on_scalar[u], 4)]
+        def by_scalar(*some_units):
+            return [(widen, s, i) for s in some_units for i in range(PIECES - on_scalar[s], PIECES)]
 
-        X = x_unit
-        W = w_unit
-        jobs = [(j, ci) for ci in range(CHUNKS) for j in range(4)]
-        late = jobs[:4]
-        pe = both(turn, X[0]) + both(turn, X[1]) + [(warm, i) for i in range(WARM)]
-        pe += [(down, 0)]
+        def chunk(ci):
+            return (w_unit[ci], w_unit[ci] + 1)
+
+        products = [(j, ci) for ci in range(CHUNKS) for j in range(PAIRS)]
+        parked = products[:PAIRS]
+        after_turns = PAIRS * (CHUNKS - 2) + TURN_AFTER
+
+        tensor = halves(turn, x_unit[0], x_unit[1]) + [(warm, i) for i in range(WARM_UPS)] + [(down, 0)]
         for m in (2, 4):
-            pe += both(turn, X[m]) + both(turn, X[m + 1]) + [(down, m - 1), (down, m)]
-        pe += both(turn, W[0]) + both(turn, W[0] + 1) + [(down, 5)]
-        if PAIR:
-            pe += both(turn, X[6]) + both(turn, X[7]) + [(base, 0, 0), (down, 6), (base, 1, 0), (down, 7)]
-        else:
-            pe += both(turn, X[6]) + [(base, 0, 0)] + both(turn, X[7]) + [(down, 6), (base, 1, 0), (down, 7)]
-        for n in range(2, len(jobs)):
-            j, ci = jobs[n]
-            if j == 2 and ci + 1 < CHUNKS:
-                pe += both(turn, W[ci + 1]) + both(turn, W[ci + 1] + 1)
-            pe += [(base, j, ci)]
-            if n + 2 < len(jobs):
-                pe += [(up,) + jobs[n + 2]]
-            if 0 <= n - L0 < 4:
-                pe += [(up,) + late[n - L0]]
-        ve = vp(X[0]) + vp(X[1]) + [(inter_a, 0, 0, 4), (quant_a, 0, 0, 4), (quant, X[0]), (inter_a, 2, 0, 4)]
-        if SPLIT:
-            ve += [(inter_a, 3, 0, 2), (quant_a, 1, 0, 4), (quant_a, 2, 0, 4), (quant_a, 3, 0, 2)]
-            ve = ve[:-2] + [(quant_a, 2, 0, 4), (quant_a, 3, 0, 2), (inter_a, 3, 2, 4), (quant_a, 3, 2, 4)] + vp(X[2])
-        else:
-            ve += [(inter_a, 3, 0, 4), (quant_a, 1, 0, 4), (quant_a, 2, 0, 4), (quant_a, 3, 0, 4)] + vp(X[2])
-        ve += vp(X[3]) + [(quant, X[1])]
-        fill = vp(X[4]) + vp(X[5]) + vp(W[0]) + vp(W[0] + 1) + vp(X[6]) + vp(X[7]) + vp(W[1]) + vp(W[1] + 1) + vp(W[2])[:EXTRA]
-        marks = [[(scale_h, 0)], [(quant, X[2])], [], [(quant, X[3])], [(scale_h, 1)], [(scale_h, 2)], [(quant, X[4])]]
-        marks += [[], [(quant, X[5])], [(scale_h, 3)], [(scale_h, 4)]] + [[]] * GAP1 + [[(quant, W[0]), (quant, W[0] + 1), (scale_h, 5)]]
-        marks += [[(quant, X[6])]] + [[]] * GAP2 + [[(quant, X[7])]] + [[]] * GAP3 + [[(scale_h, 6)], [(quant_b, 1), (quant_h, 0)], [(scale_h, 7)], [(quant_h, 1)]]
-        for n, mark in enumerate(marks):
-            ve += mark + fill[:1]
-            fill = fill[1:]
-        ve += fill
+            tensor += halves(turn, x_unit[m], x_unit[m + 1]) + [(down, m - 1), (down, m)]
+        tensor += halves(turn, *chunk(0)) + [(down, 5)]
+        tensor += halves(turn, x_unit[6], x_unit[7]) + [(base, 0, 0), (down, 6), (base, 1, 0), (down, 7)]
+        for n in range(TURN_AFTER, len(products)):
+            j, ci = products[n]
+            if j == TURN_AFTER and ci + 1 < CHUNKS:
+                tensor += halves(turn, *chunk(ci + 1))
+            tensor += [(base, j, ci)]
+            if n + UP_AHEAD < len(products):
+                tensor += [(up,) + products[n + UP_AHEAD]]
+            if 0 <= n - after_turns < PAIRS:
+                tensor += [(up,) + parked[n - after_turns]]
+
+        vector = by_vector(x_unit[0], x_unit[1]) + [(inter_a, 0, 0, 4), (quant_a, 0, 0, 4), (quant, x_unit[0]), (inter_a, 2, 0, 4), (inter_a, 3, 0, 2)]
+        vector += [(quant_a, 1, 0, 4), (quant_a, 2, 0, 4), (quant_a, 3, 0, 2), (inter_a, 3, 2, 4), (quant_a, 3, 2, 4)]
+        vector += by_vector(x_unit[2], x_unit[3]) + [(quant, x_unit[1])]
+        pieces = by_vector(x_unit[4], x_unit[5], *chunk(0), x_unit[6], x_unit[7], *chunk(1)) + by_vector(w_unit[2])[:LEAD]
+        groups = [[(scale_h, 0)], [(quant, x_unit[2])], [], [(quant, x_unit[3])], [(scale_h, 1)], [(scale_h, 2)], [(quant, x_unit[4])], []]
+        groups += [[(quant, x_unit[5])], [(scale_h, 3)], [(scale_h, 4)], [], [], [], [(quant, w_unit[0]), (quant, w_unit[0] + 1), (scale_h, 5)]]
+        groups += [[(quant, x_unit[6])], [], [(quant, x_unit[7])], [], [], [(scale_h, 6)], [(quant_b, 1), (quant_h, 0)], [(scale_h, 7)], [(quant_h, 1)]]
+        for n, group in enumerate(groups):
+            vector += group + pieces[n : n + 1]
+        vector += pieces[len(groups) :]
+        for ci in range(1, CHUNKS - 1):
+            pieces = by_vector(*chunk(ci + 1))[LEAD if ci == 1 else 0 :]
+            first = PAIRS * (ci - 1) + TURN_AFTER
+            adds = [[] if product in parked else [(finish,) + product] for product in products[first : first + PAIRS]]
+            vector += pieces[:2] + ([(quant_b, 0)] if ci == 2 else [])
+            vector += [(quant, w_unit[ci])] + adds[0] + [(quant, w_unit[ci] + 1)]
+            vector += [(quant_h, 2), (quant_h, 3)] if ci == 1 else []
+            vector += pieces[2:3] + adds[1] + pieces[3:5] + adds[2] + pieces[5:] + [(quant_b, ci + 1)] + adds[3]
+        vector += [(quant, w_unit[CHUNKS - 1]), (finish,) + products[after_turns], (quant, w_unit[CHUNKS - 1] + 1)]
+        for n in range(after_turns + 1, len(products)):
+            if n - after_turns <= PAIRS:
+                vector += [(finish_parked,) + parked[n - after_turns - 1]]
+            vector += [(finish,) + products[n]]
+
+        scalar = by_scalar(x_unit[0], x_unit[1]) + halves(empty, x_unit[0]) + [(inter_a, A_PASS_ON_SCALAR, 0, 4)] + halves(empty, x_unit[1])
+        scalar += by_scalar(x_unit[2], x_unit[3]) + [(cast_lam,)] + by_scalar(x_unit[4])
+        scalar += halves(empty, x_unit[2], x_unit[3]) + by_scalar(x_unit[5], w_unit[0])
+        scalar += halves(empty, x_unit[4], x_unit[5]) + by_scalar(w_unit[0] + 1, x_unit[6])
+        scalar += halves(empty, *chunk(0)) + by_scalar(x_unit[7]) + [(cast_c,)]
+        scalar += halves(empty, x_unit[6], x_unit[7]) + [(park, 0, 0)] + by_scalar(*chunk(1)) + [(inter_b, 1), (park, 1, 0), (inter_b, 0)]
         for ci in range(1, CHUNKS):
-            nxt = vp(W[ci + 1]) + vp(W[ci + 1] + 1) if ci + 1 < CHUNKS else []
+            scalar += halves(empty, *chunk(ci))
             if ci == 1:
-                nxt = nxt[EXTRA:]
-            adds = [[(finish,) + job] if job not in late else [] for job in jobs[4 * ci - 2 : 4 * ci + 2]]
-            ve += nxt[:2]
-            if ci == 2:
-                ve += [(quant_b, 0)]
-            ve += [(quant, W[ci])] + adds[0] + [(quant, W[ci] + 1)]
-            if ci == 1:
-                ve += [(quant_h, 2), (quant_h, 3)]
-            if ci == CHUNKS - 1:
-                break
-            ve += nxt[2:3] + adds[1] + nxt[3:5] + adds[2] + nxt[5:] + [(quant_b, ci + 1)] + adds[3]
-        for n in range(19, len(jobs)):
-            if 0 <= n - 1 - L0 < 4:
-                ve += [(finish_late,) + late[n - 1 - L0]]
-            ve += [(finish,) + jobs[n]]
-        sc = sp(X[0]) + sp(X[1]) + both(empty, X[0]) + [(inter_a, 1, 0, 4)] + both(empty, X[1]) + sp(X[2]) + sp(X[3]) + [(small, "lam")] + sp(X[4])
-        sc += both(empty, X[2]) + both(empty, X[3]) + sp(X[5]) + sp(W[0])
-        sc += both(empty, X[4]) + both(empty, X[5]) + sp(W[0] + 1) + sp(X[6])[:SCUT]
-        sc += both(empty, W[0]) + both(empty, W[0] + 1) + sp(X[6])[SCUT:] + sp(X[7]) + [(small, "c")]
-        sc += both(empty, X[6]) + ([(park, 0, 0)] + both(empty, X[7]) if PAIR == 0 else both(empty, X[7]) + [(park, 0, 0)]) + sp(W[1]) + sp(W[1] + 1) + [(inter_b, 1), (park, 1, 0), (inter_b, 0)]
-        for ci in range(1, CHUNKS):
-            sc += both(empty, W[ci]) + both(empty, W[ci] + 1)
-            if ci == 1:
-                sc += [(park, 2, 0), (scale_d, 0, 1), (park, 3, 0), (scale_d, 1, 1)]
+                scalar += [(park, 2, 0), (scale_d, 0, ci), (park, 3, 0), (scale_d, 1, ci)]
             else:
-                sc += [(scale_d, 0, ci), (scale_d, 1, ci)]
+                scalar += [(scale_d, 0, ci), (scale_d, 1, ci)]
             if ci + 1 < CHUNKS:
-                sc += [(inter_b, ci + 1)] + sp(W[ci + 1]) + sp(W[ci + 1] + 1)
-            sc += [(scale_d, 2, ci), (scale_d, 3, ci)]
+                scalar += [(inter_b, ci + 1)]
+            scalar += [(scale_d, 2, ci), (scale_d, 3, ci)]
 
-        def users(fns, prog):
-            return [step for step in prog if step[0] in fns]
+        turn_bank_users = [step for step in tensor if step[0] == turn or (step[0] == up and step[1:] in parked)]
+        adapter_bank_users = [step for step in tensor if step[0] == down or (step[0] == up and step[1:] not in parked)]
+        base_bank_users = [step for step in tensor if step[0] == base]
+        y_users = [step for step in scalar if step[0] == scale_d]
+        b_users = [step for step in scalar if step[0] == inter_b]
+        last_reader = {turn: empty, down: scale_h, scale_d: finish, inter_b: quant_b}
 
-        turns = users((turn,), pe)
-        hd = [step for step in users((down, up), pe) if step[1:] not in late]
-        xt_users = [step for step in pe if step[0] == turn or (step[0] == up and step[1:] in late)]
-        bases = users((base,), pe)
-        scaled = users((scale_d,), sc)
-        inter = users((inter_b,), sc)
+        def freed(users, step, depth):
+            n = users.index(step) - depth
+            if n < 0:
+                return []
+            fn, args = users[n][0], users[n][1:]
+            if fn == up:
+                return [(scale_d,) + args]
+            if fn == base:
+                return [(park if args in parked else finish,) + args]
+            return [(last_reader[fn],) + args]
 
         def needs(step):
-            fn = step[0]
+            fn, args = step[0], step[1:]
             if fn == widen:
-                return both(turn, step[1] - WIDE) if step[1] >= WIDE else []
+                return halves(turn, args[0] - WIDE_BUFS) if args[0] >= WIDE_BUFS else []
             if fn == turn:
-                n = turns.index(step)
-                return [(widen, step[1], 2 * step[2]), (widen, step[1], 2 * step[2] + 1)] + [(empty,) + t[1:] for t in turns[max(n - TB, 0) : max(n - TB + 1, 0)]]
+                return [(widen, args[0], 2 * args[1]), (widen, args[0], 2 * args[1] + 1)] + freed(turn_bank_users, step, TURN_BANKS)
             if fn == empty:
-                return [(turn,) + step[1:]] + ([(quant, step[1] - GROUP)] if step[1] >= GROUP else [])
+                return [(turn,) + args] + ([(quant, args[0] - GROUP_BUFS)] if args[0] >= GROUP_BUFS else [])
             if fn == quant:
-                return both(empty, step[1])
-            if fn == inter_b:
-                n = inter.index(step) - 3
-                return [] if n < 0 else [(quant_b, inter[n][1])]
+                return halves(empty, args[0])
             if fn == warm:
                 return [(inter_a, 2, 0, 4)]
             if fn == quant_a:
-                return [(inter_a,) + step[1:]]
+                return [(inter_a,) + args]
+            if fn == inter_b:
+                return freed(b_users, step, B_BUFS)
             if fn == quant_b:
-                return [(inter_b, step[1])]
-            if fn == park:
-                return [(base,) + step[1:]]
-            if fn == finish_late:
-                return [(up,) + step[1:], (park,) + step[1:], (small, "c")]
-            if fn == up and step[1:] in late:
-                old = xt_users[xt_users.index(step) - TB]
-                slot = (empty,) + old[1:] if old[0] == turn else (finish_late,) + old[1:]
-                return [slot, (quant_h, step[1]), (quant_b, step[2])]
-            if fn in (down, up):
-                n = hd.index(step) - HB
-                slot = [] if n < 0 else [(scale_h if hd[n][0] == down else scale_d,) + hd[n][1:]]
-                if fn == down:
-                    return slot + [(quant, X[step[1]])] + users((quant_a,), ve)
-                return slot + [(quant_h, step[1]), (quant_b, step[2])]
+                return [(inter_b,) + args]
+            if fn == down:
+                return freed(adapter_bank_users, step, ADAPTER_BANKS) + [(quant, x_unit[args[0]])] + [s for s in vector if s[0] == quant_a]
             if fn == scale_h:
-                return [(down, step[1]), (small, "lam")]
+                return [(down,) + args, (cast_lam,)]
             if fn == quant_h:
-                return [(scale_h, 2 * step[1]), (scale_h, 2 * step[1] + 1)]
+                return [(scale_h, 2 * args[0]), (scale_h, 2 * args[0] + 1)]
+            if fn == up:
+                users, depth = (turn_bank_users, TURN_BANKS) if args in parked else (adapter_bank_users, ADAPTER_BANKS)
+                return freed(users, step, depth) + [(quant_h, args[0]), (quant_b, args[1])]
             if fn == scale_d:
-                n = scaled.index(step) - YB
-                return [(up,) + step[1:], (small, "c")] + ([] if n < 0 else [(finish,) + scaled[n][1:]])
+                return [(up,) + args, (cast_c,)] + freed(y_users, step, Y_BUFS)
             if fn == base:
-                n = bases.index(step) - BB
-                return [(quant, X[2 * step[1]]), (quant, X[2 * step[1] + 1]), (quant, W[step[2]]), (quant, W[step[2]] + 1)] + ([] if n < 0 else [(park if bases[n][1:] in late else finish,) + bases[n][1:]]) + ([(finish_late,) + job for job in late[:3]] if step[1:] == LAST else []) + ([(finish,) + bases[n + 1][1:]] if step[1:] == (2, CHUNKS - 1) and FINE else [])
+                before = [(quant, s) for s in (x_unit[2 * args[0]], x_unit[2 * args[0] + 1]) + chunk(args[1])]
+                before += freed(base_bank_users, step, BASE_BANKS)
+                if args == BEFORE_LAST:
+                    before += freed(base_bank_users, step, 1)
+                if args == LAST:
+                    before += [(finish_parked,) + product for product in parked[: len(ENDING)]]
+                return before
+            if fn == park:
+                return [(base,) + args]
+            if fn == finish_parked:
+                return [(up,) + args, (park,) + args, (cast_c,)]
             if fn == finish:
-                return [(base,) + step[1:], (scale_d,) + step[1:]]
+                return [(base,) + args, (scale_d,) + args]
             return []
 
         written = set()
-        progs = [pe, ve, sc]
-        while any(progs):
-            ready = [prog for prog in progs if prog and all(need in written for need in needs(prog[0]))]
+        lists = [tensor, vector, scalar]
+        while any(lists):
+            ready = [steps for steps in lists if steps and all(need in written for need in needs(steps[0]))]
             step = ready[0][0]
             step[0](*step[1:])
             written.add(step)
-            progs = [prog[1:] if prog and prog[0] == step else prog for prog in progs]
+            lists = [steps[1:] if steps and steps[0] == step else steps for steps in lists]

@@ -34,7 +34,6 @@ W_ON_SCALAR = ((1, 2), (0, 0), (0, 0), (0, 0), (0, 0), (0, 0))
 A_PASS_ON_SCALAR = 1
 TURN_BANKS, ADAPTER_BANKS, BASE_BANKS = 4, 2, 2
 WIDE_BUFS, GROUP_BUFS, A_BUFS, B_BUFS, Y_BUFS = 7, 3, 4, 3, 4
-WARM_UPS = 5
 TURN_AFTER = 2
 UP_AHEAD = 2
 LEAD = 2
@@ -241,7 +240,7 @@ def tile_fp8_base_lora_d2_kernel(tc, x_bytes, x_scale, w_bytes, w_scale, a, lam,
                 out=h_codes[j][:].bitcast(FP8X4), scales=h_scales[j][:], in_=h_grouped[j][:].rearrange("p i w t -> p (i w t)")
             )
 
-        y, base_parts, d_banks, warm_bank = {}, {}, {}, {}
+        y, base_parts, d_banks = {}, {}, {}
 
         def up(j, ci):
             if ci == 0:
@@ -317,12 +316,6 @@ def tile_fp8_base_lora_d2_kernel(tc, x_bytes, x_scale, w_bytes, w_scale, a, lam,
         def cast_c():
             nc.scalar.activation(out=c_f[:], in_=c_b[:], func=COPY)
 
-        def warm(i):
-            if i == 0:
-                warm_bank[0] = ring(psum, "base", BASE_BANKS, [P, 2, WIDTH], F32)
-            flat = a_int[2][:].rearrange("p t m j -> p (t m j)")
-            nc.tensor.matmul(warm_bank[0][:].rearrange("p i n -> p (i n)"), lhsT=flat[:, :P], rhs=flat[:, :512], start=True, stop=True)
-
         def halves(fn, *some_units):
             return [(fn, s, half) for s in some_units for half in range(2)]
 
@@ -339,7 +332,7 @@ def tile_fp8_base_lora_d2_kernel(tc, x_bytes, x_scale, w_bytes, w_scale, a, lam,
         parked = products[:PAIRS]
         after_turns = PAIRS * (CHUNKS - 2) + TURN_AFTER
 
-        tensor = halves(turn, x_unit[0], x_unit[1]) + [(warm, i) for i in range(WARM_UPS)] + [(down, 0)]
+        tensor = halves(turn, x_unit[0], x_unit[1]) + [(down, 0)]
         for m in (2, 4):
             tensor += halves(turn, x_unit[m], x_unit[m + 1]) + [(down, m - 1), (down, m)]
         tensor += halves(turn, *chunk(0)) + [(down, 5)]
@@ -422,8 +415,6 @@ def tile_fp8_base_lora_d2_kernel(tc, x_bytes, x_scale, w_bytes, w_scale, a, lam,
                 return [(turn,) + args] + ([(quant, args[0] - GROUP_BUFS)] if args[0] >= GROUP_BUFS else [])
             if fn == quant:
                 return halves(empty, args[0])
-            if fn == warm:
-                return [(inter_a, 2, 0, 4)]
             if fn == quant_a:
                 return [(inter_a,) + args]
             if fn == inter_b:

@@ -27,13 +27,12 @@ PIECES = 4
 LAST = (PAIRS - 1, CHUNKS - 1)
 BEFORE_LAST = (PAIRS - 2, CHUNKS - 1)
 
-UNIT_ORDER = "x0 x1 x2 x3 x4 x5 w0 x6 x7 w1 w2 w3 w4 w5"
 LOAD_ORDER = "xs x0 x1 a0 a1 a2 a3 x2 x3 lam x4 x5 ws w0 c x6 x7 w1 b1 b0 w2 b2 w3 b3 w4 b4 w5 b5"
-X_ON_SCALAR = (2, 2, 2, 2, 2, 2, 2, 1)
-W_ON_SCALAR = ((1, 2), (0, 0), (0, 0), (0, 0), (0, 0), (0, 0))
-A_PASS_ON_SCALAR = 1
+UNIT_ORDER = "x0 x1 x2 x3 x4 x5 w0 x6 x7 w1 w2 w3 w4 w5"
+PAIR_PASSES = (0,1,2,3)
+WARM = 4
 TURN_BANKS, ADAPTER_BANKS, BASE_BANKS = 4, 2, 2
-WIDE_BUFS, GROUP_BUFS, A_BUFS, B_BUFS, Y_BUFS = 7, 3, 4, 3, 4
+WIDE_BUFS, GROUP_BUFS, A_BUFS, B_BUFS, Y_BUFS = 7, 3, 4, 2, 4
 TURN_AFTER = 2
 UP_AHEAD = 2
 LEAD = 2
@@ -105,44 +104,55 @@ def tile_fp8_base_lora_d2_kernel(tc, x_bytes, x_scale, w_bytes, w_scale, a, lam,
                     w_raw[row] = loads.tile([P, K], U8, name="w_b%d" % row, align_bytes=64)
                     nc.sync.dma_start(out=w_raw[row][:], in_=w_view[:, row, :])
 
+        ws2 = const.tile([P, CHUNKS, K_BLOCKS], F32, name="ws2")
         lam_f = const.tile([P, 4], F32, name="lam_f")
         c_f = const.tile([P, TILES], F32, name="c_f")
 
-        units, on_scalar, x_unit, w_unit = [], [], {}, {}
+        units, x_unit, w_unit = [], {}, {}
         for what in UNIT_ORDER.split(" "):
             idx = int(what[1:])
             if what[0] == "x":
                 x_unit[idx] = len(units)
                 units.append([("x", idx, g) for g in range(PASSES)])
-                on_scalar.append(X_ON_SCALAR[idx])
             else:
                 w_unit[idx] = len(units)
                 for half in range(2):
-                    units.append([("w", 2 * idx + r, g) for g in (2 * half, 2 * half + 1) for r in range(2)])
-                    on_scalar.append(W_ON_SCALAR[idx][half])
+                    units.append([("w", idx, g) for g in (2 * half, 2 * half + 1) for r in range(2)])
         wide, turned, grouped, unit_codes, unit_scales = {}, {}, {}, {}, {}
 
         def widen(s, i):
             if s not in wide:
                 wide[s] = ring(work, "wide", WIDE_BUFS, [P, PIECES, 2, P, 2], BF16)
             kind, row, g = units[s][i]
-            src = x_raw[row] if kind == "x" else w_raw[row]
-            scales = xs if kind == "x" else ws
+            if kind == "w" and g not in PAIR_PASSES:
+                for q in (2 * (i % 2), 2 * (i % 2) + 1):
+                    nc.vector.tensor_scalar(
+                        out=wide[s][:, i - i % 2 : i - i % 2 + 2, :, 32 * q : 32 * (q + 1), :].rearrange("p r u w e -> p r (w e) u"),
+                        in0=w_raw[row][:, 4 * g + q, :, :].bitcast(FP8).rearrange("p r (v u) -> p r v u", u=2),
+                        scalar1=ws2[:, row, 4 * g + q : 4 * g + q + 1],
+                        scalar2=None,
+                        op0=MULT,
+                    )
+                return
             for q in range(4):
-                k0 = 512 * g + P * q
-                j = K_BLOCKS * row + 4 * g + q
-                if i >= PIECES - on_scalar[s]:
+                j = 4 * g + q
+                if kind == "x":
+                    src, scale = x_raw[row][:, P * j : P * (j + 1)].bitcast(FP8), xs[:, K_BLOCKS * row + j : K_BLOCKS * row + j + 1]
+                else:
+                    wr = 2 * row + i % 2
+                    src, scale = w_raw[wr][:, P * j : P * (j + 1)].bitcast(FP8), ws[:, K_BLOCKS * wr + j : K_BLOCKS * wr + j + 1]
+                part = wide[s][:, i, :, 32 * q : 32 * (q + 1), :]
+                if (widen, s, i) in scalar:
+                    assert g in PAIR_PASSES
                     flat = wide[s][:, i, :, :, :].rearrange("p u w e -> p (u w e)")
-                    nc.scalar.activation(
-                        out=flat[:, P * q : P * (q + 1)], in_=src[:, k0 : k0 + P].bitcast(FP8), func=COPY, scale=scales[:, j : j + 1]
+                    nc.scalar.activation(out=flat[:, P * q : P * (q + 1)], in_=src, func=COPY, scale=scale)
+                elif g in PAIR_PASSES:
+                    nc.vector.tensor_scalar(
+                        out=part.rearrange("p u w e -> p w u e"), in0=src.rearrange("p (w u e) -> p w u e", u=2, e=2), scalar1=scale, scalar2=None, op0=MULT
                     )
                 else:
                     nc.vector.tensor_scalar(
-                        out=wide[s][:, i, :, 32 * q : 32 * (q + 1), :].rearrange("p u w e -> p w u e"),
-                        in0=src[:, k0 : k0 + P].bitcast(FP8).rearrange("p (w u e) -> p w u e", u=2, e=2),
-                        scalar1=scales[:, j : j + 1],
-                        scalar2=None,
-                        op0=MULT,
+                        out=part.rearrange("p u w e -> p (w e) u"), in0=src.rearrange("p (v u) -> p v u", u=2), scalar1=scale, scalar2=None, op0=MULT
                     )
 
         def turn(s, half):
@@ -151,7 +161,7 @@ def tile_fp8_base_lora_d2_kernel(tc, x_bytes, x_scale, w_bytes, w_scale, a, lam,
             for i in range(2):
                 piece = wide[s][:, 2 * half + i, :, :, :]
                 for u in range(2):
-                    if 2 * half + i >= PIECES - on_scalar[s]:
+                    if (widen, s, 2 * half + i) in scalar:
                         words = piece.rearrange("p u w e -> p (u w e)").bitcast(F32)[:, u::2]
                     else:
                         words = piece[:, u, :, :].rearrange("p w e -> p (w e)").bitcast(F32)
@@ -161,10 +171,14 @@ def tile_fp8_base_lora_d2_kernel(tc, x_bytes, x_scale, w_bytes, w_scale, a, lam,
             if half == 0:
                 grouped[s] = ring(work, "grouped", GROUP_BUFS, [P, PIECES, P, 4], BF16)
             words = grouped[s][:, 2 * half : 2 * half + 2, :, :].rearrange("p i w t -> p (i w t)").bitcast(F32)
-            nc.scalar.copy(
-                out=words.rearrange("p (i w u) -> p i w u", i=2, u=2),
-                in_=turned[s, half][:].rearrange("p (i u) w -> p i w u", u=2),
-            )
+            copy = nc.scalar.copy if (empty, s, half) in scalar else nc.vector.tensor_copy
+            if units[s][0][0] in "xw":
+                copy(
+                    out=words.rearrange("p (i w u) -> p i w u", i=2, u=2),
+                    in_=turned[s, half][:].rearrange("p (i u) w -> p i w u", u=2),
+                )
+            else:
+                copy(out=words.rearrange("p (w v) -> p w v", v=4), in_=turned[s, half][:].rearrange("p v w -> p w v"))
 
         def quant(s):
             unit_codes[s] = codes.tile([P, 512], U32, name="codes%d" % s, align_bytes=64)
@@ -179,10 +193,40 @@ def tile_fp8_base_lora_d2_kernel(tc, x_bytes, x_scale, w_bytes, w_scale, a, lam,
         def inter_a(g, t0, t1):
             if t0 == 0:
                 a_int[g] = ring(work, "ab_int", A_BUFS, [P, 4, P, 4], BF16)
-            (nc.scalar.copy if g == A_PASS_ON_SCALAR else nc.vector.tensor_copy)(
-                out=a_int[g][:, t0:t1, :, :].rearrange("p t (q m) j -> p q t m j", m=2),
-                in_=a_raw[g][:].rearrange("p j (q m t) -> p q t m j", m=2, t=4)[:, :, t0:t1, :, :],
-            )
+            copy = nc.scalar.copy if (inter_a, g, t0, t1) in scalar else nc.vector.tensor_copy
+            if g in PAIR_PASSES:
+                copy(
+                    out=a_int[g][:, t0:t1, :, :].rearrange("p t (q m) j -> p q t m j", m=2),
+                    in_=a_raw[g][:].rearrange("p j (q m t) -> p q t m j", m=2, t=4)[:, :, t0:t1, :, :],
+                )
+            else:
+                copy(
+                    out=a_int[g][:, t0:t1, :, :].rearrange("p t m (u e) -> p m t u e", u=2),
+                    in_=a_raw[g][:].rearrange("p (e u) (m t) -> p m t u e", u=2, t=4)[:, :, t0:t1, :, :],
+                )
+
+        mixed = {}
+
+        def mix_a(g, half):
+            return None
+
+        def warm(n):
+            bank = ring(psum, "hd", 2, [P, R], F32)
+            rows = a_int[n][:].rearrange("p t m j -> p t (m j)")
+            for i in range(WARM):
+                nc.tensor.matmul(out=bank[:], lhsT=rows[:, 0, 0:P], rhs=rows[:, i % 2, :], start=True, stop=True)
+
+        def copy_a(g, half):
+            copy = nc.scalar.copy if (copy_a, g, half) in scalar else nc.vector.tensor_copy
+            if half == 0:
+                a_int[g] = ring(work, "ab_int", A_BUFS, [P, 4, P, 4], BF16)
+            if g in PAIR_PASSES:
+                copy(out=a_int[g][:, 2 * half : 2 * half + 2, :, :].rearrange("p t m j -> p (t m j)"), in_=mixed[g, half][:])
+            else:
+                copy(
+                    out=a_int[g][:, :, 64 * half : 64 * (half + 1), :].rearrange("p t m j -> p t (m j)"),
+                    in_=mixed[g, half][:].rearrange("p (t v) -> p t v", t=4),
+                )
 
         def quant_a(g, t0, t1):
             if t0 == 0:
@@ -224,13 +268,29 @@ def tile_fp8_base_lora_d2_kernel(tc, x_bytes, x_scale, w_bytes, w_scale, a, lam,
                     )
 
         def scale_h(m):
-            if m % 2 == 0:
+            if m // 2 not in h_grouped:
                 h_grouped[m // 2] = const.tile([P, 2, P, 4], BF16, name="h_grouped%d" % (m // 2), align_bytes=64)
             nc.vector.tensor_tensor(
                 out=h_grouped[m // 2][:, m % 2, :, :],
                 in0=h_banks[m][:].rearrange("p t w -> p w t"),
                 in1=lam_f[:].unsqueeze(1).to_broadcast([P, P, 4]),
                 op=MULT,
+            )
+
+        h_planes = {}
+
+        def plane_h(m):
+            if m // 2 not in h_planes:
+                h_planes[m // 2] = ring(work, "ab_int", A_BUFS, [P, 2, 4, P], BF16)
+            for t in range(4):
+                nc.scalar.activation(out=h_planes[m // 2][:, m % 2, t, :], in_=h_banks[m][:, t, :], func=COPY, scale=lam_f[:, t : t + 1])
+
+        def inter_h(m):
+            if m // 2 not in h_grouped:
+                h_grouped[m // 2] = const.tile([P, 2, P, 4], BF16, name="h_grouped%d" % (m // 2), align_bytes=64)
+            (nc.scalar.copy if (inter_h, m) in scalar else nc.vector.tensor_copy)(
+                out=h_grouped[m // 2][:, m % 2, :, :].rearrange("p (n i) t -> p n t i", i=4),
+                in_=h_planes[m // 2][:, m % 2, :, :].rearrange("p t (n i) -> p n t i", i=4),
             )
 
         def quant_h(j):
@@ -243,7 +303,7 @@ def tile_fp8_base_lora_d2_kernel(tc, x_bytes, x_scale, w_bytes, w_scale, a, lam,
         y, base_parts, d_banks = {}, {}, {}
 
         def up(j, ci):
-            if ci == 0:
+            if (up, j, ci) in turn_bank_users:
                 bank = ring(psum, "xt", TURN_BANKS, [P, 2, WIDTH], F32)
             else:
                 bank = ring(psum, "hd", ADAPTER_BANKS, [P, 2, WIDTH], F32)
@@ -313,86 +373,35 @@ def tile_fp8_base_lora_d2_kernel(tc, x_bytes, x_scale, w_bytes, w_scale, a, lam,
         def cast_lam():
             nc.scalar.activation(out=lam_f[:], in_=lam_b[:], func=COPY)
 
+        def pick_ws():
+            for h in range(2):
+                rows = slice(64 * h, 64 * (h + 1))
+                nc.scalar.copy(out=ws2[rows, :, :], in_=ws[rows, :].rearrange("p (c h j) -> p c h j", h=2, j=K_BLOCKS)[:, :, h, :])
+
         def cast_c():
             nc.scalar.activation(out=c_f[:], in_=c_b[:], func=COPY)
 
         def halves(fn, *some_units):
             return [(fn, s, half) for s in some_units for half in range(2)]
 
-        def by_vector(*some_units):
-            return [(widen, s, i) for s in some_units for i in range(PIECES - on_scalar[s])]
-
-        def by_scalar(*some_units):
-            return [(widen, s, i) for s in some_units for i in range(PIECES - on_scalar[s], PIECES)]
-
         def chunk(ci):
             return (w_unit[ci], w_unit[ci] + 1)
 
         products = [(j, ci) for ci in range(CHUNKS) for j in range(PAIRS)]
-        parked = products[:PAIRS]
         after_turns = PAIRS * (CHUNKS - 2) + TURN_AFTER
 
-        tensor = halves(turn, x_unit[0], x_unit[1]) + [(down, 0)]
-        for m in (2, 4):
-            tensor += halves(turn, x_unit[m], x_unit[m + 1]) + [(down, m - 1), (down, m)]
-        tensor += halves(turn, *chunk(0)) + [(down, 5)]
-        tensor += halves(turn, x_unit[6], x_unit[7]) + [(base, 0, 0), (down, 6), (base, 1, 0), (down, 7)]
-        for n in range(TURN_AFTER, len(products)):
-            j, ci = products[n]
-            if j == TURN_AFTER and ci + 1 < CHUNKS:
-                tensor += halves(turn, *chunk(ci + 1))
-            tensor += [(base, j, ci)]
-            if n + UP_AHEAD < len(products):
-                tensor += [(up,) + products[n + UP_AHEAD]]
-            if 0 <= n - after_turns < PAIRS:
-                tensor += [(up,) + parked[n - after_turns]]
+        tensor = [(turn, x_unit[0], 0), (turn, x_unit[0], 1), (turn, x_unit[1], 0), (turn, x_unit[1], 1), (down, 0), (turn, x_unit[2], 0), (turn, x_unit[2], 1), (turn, x_unit[3], 0), (turn, x_unit[3], 1), (down, 1), (down, 2), (turn, x_unit[4], 0), (turn, x_unit[4], 1), (turn, x_unit[5], 0), (turn, x_unit[5], 1), (down, 3), (down, 4), (turn, w_unit[0] + 0, 0), (turn, w_unit[0] + 0, 1), (turn, w_unit[0] + 1, 0), (turn, w_unit[0] + 1, 1), (down, 5), (turn, x_unit[6], 0), (turn, x_unit[6], 1), (turn, x_unit[7], 0), (turn, x_unit[7], 1), (base, 0, 0), (down, 6), (base, 1, 0), (down, 7), (turn, w_unit[1] + 0, 0), (turn, w_unit[1] + 0, 1), (turn, w_unit[1] + 1, 0), (turn, w_unit[1] + 1, 1), (base, 2, 0), (up, 0, 1), (base, 3, 0), (up, 1, 1), (base, 0, 1), (up, 2, 1), (base, 1, 1), (up, 3, 1), (turn, w_unit[2] + 0, 0), (turn, w_unit[2] + 0, 1), (turn, w_unit[2] + 1, 0), (turn, w_unit[2] + 1, 1), (base, 2, 1), (up, 0, 2), (base, 3, 1), (up, 1, 2), (base, 0, 2), (up, 2, 2), (base, 1, 2), (up, 3, 2), (turn, w_unit[3] + 0, 0), (turn, w_unit[3] + 0, 1), (turn, w_unit[3] + 1, 0), (turn, w_unit[3] + 1, 1), (base, 2, 2), (up, 0, 3), (base, 3, 2), (up, 1, 3), (base, 0, 3), (up, 2, 3), (base, 1, 3), (up, 3, 3), (turn, w_unit[4] + 0, 0), (turn, w_unit[4] + 0, 1), (turn, w_unit[4] + 1, 0), (turn, w_unit[4] + 1, 1), (base, 2, 3), (up, 0, 4), (base, 3, 3), (up, 1, 4), (base, 0, 4), (up, 2, 4), (base, 1, 4), (up, 3, 4), (turn, w_unit[5] + 0, 0), (turn, w_unit[5] + 0, 1), (turn, w_unit[5] + 1, 0), (turn, w_unit[5] + 1, 1), (base, 2, 4), (up, 0, 5), (up, 0, 0), (base, 3, 4), (up, 1, 5), (up, 1, 0), (base, 0, 5), (up, 2, 5), (up, 2, 0), (base, 1, 5), (up, 3, 5), (up, 3, 0), (base, 2, 5), (base, 3, 5)]
+        vector = [(widen, x_unit[0], 0), (widen, x_unit[0], 1), (widen, x_unit[1], 0), (widen, x_unit[1], 1), (widen, x_unit[1], 2), (inter_a, 0, 0, 4), (quant, x_unit[0]), (quant_a, 0, 0, 4), (inter_a, 2, 0, 4), (inter_a, 3, 0, 2), (quant_a, 1, 0, 2), (quant_a, 2, 0, 2), (quant_a, 3, 0, 2), (inter_a, 3, 2, 4), (quant_a, 1, 2, 4), (quant_a, 2, 2, 4), (quant_a, 3, 2, 4), (widen, x_unit[2], 0), (widen, x_unit[2], 1), (widen, x_unit[3], 0), (widen, x_unit[3], 1), (quant, x_unit[1]), (scale_h, 0), (widen, x_unit[4], 0), (quant, x_unit[2]), (widen, x_unit[4], 1), (widen, x_unit[5], 0), (quant, x_unit[3]), (widen, x_unit[5], 1), (scale_h, 1), (widen, w_unit[0] + 0, 0), (scale_h, 2), (widen, w_unit[0] + 0, 1), (quant, x_unit[4]), (widen, w_unit[0] + 1, 0), (quant, x_unit[5]), (widen, w_unit[0] + 1, 1), (scale_h, 3), (widen, x_unit[6], 0), (scale_h, 4), (widen, x_unit[6], 1), (widen, x_unit[7], 0), (widen, x_unit[7], 1), (widen, x_unit[7], 2), (quant, w_unit[0] + 0), (quant, w_unit[0] + 1), (scale_h, 5), (quant, x_unit[6]), (widen, w_unit[1] + 0, 0), (widen, w_unit[1] + 0, 1), (widen, w_unit[1] + 0, 2), (quant, x_unit[7]), (widen, w_unit[1] + 0, 3), (widen, w_unit[1] + 1, 0), (widen, w_unit[1] + 1, 1), (scale_h, 6), (quant_b, 1), (quant_h, 0), (widen, w_unit[2] + 0, 0), (scale_h, 7), (widen, w_unit[2] + 0, 1), (widen, w_unit[2] + 0, 2), (quant_h, 1), (quant, w_unit[1] + 0), (widen, w_unit[2] + 0, 3), (quant, w_unit[1] + 1), (quant_h, 2), (quant_h, 3), (widen, w_unit[2] + 1, 0), (widen, w_unit[2] + 1, 1), (widen, w_unit[2] + 1, 2), (finish, 0, 1), (widen, w_unit[2] + 1, 3), (quant_b, 2), (finish, 1, 1), (widen, w_unit[3] + 0, 0), (widen, w_unit[3] + 0, 1), (quant, w_unit[2] + 0), (finish, 2, 1), (quant, w_unit[2] + 1), (widen, w_unit[3] + 0, 2), (finish, 3, 1), (widen, w_unit[3] + 0, 3), (widen, w_unit[3] + 1, 0), (finish, 0, 2), (widen, w_unit[3] + 1, 1), (widen, w_unit[3] + 1, 2), (widen, w_unit[3] + 1, 3), (quant_b, 3), (finish, 1, 2), (widen, w_unit[4] + 0, 0), (widen, w_unit[4] + 0, 1), (quant, w_unit[3] + 0), (finish, 2, 2), (quant, w_unit[3] + 1), (widen, w_unit[4] + 0, 2), (finish, 3, 2), (widen, w_unit[4] + 0, 3), (widen, w_unit[4] + 1, 0), (finish, 0, 3), (widen, w_unit[4] + 1, 1), (widen, w_unit[4] + 1, 2), (widen, w_unit[4] + 1, 3), (quant_b, 4), (finish, 1, 3), (widen, w_unit[5] + 0, 0), (widen, w_unit[5] + 0, 1), (quant, w_unit[4] + 0), (finish, 2, 3), (quant, w_unit[4] + 1), (widen, w_unit[5] + 0, 2), (finish, 3, 3), (widen, w_unit[5] + 0, 3), (widen, w_unit[5] + 1, 0), (finish, 0, 4), (widen, w_unit[5] + 1, 1), (widen, w_unit[5] + 1, 2), (widen, w_unit[5] + 1, 3), (quant_b, 5), (finish, 1, 4), (quant_b, 0), (quant, w_unit[5] + 0), (finish, 2, 4), (quant, w_unit[5] + 1), (finish_parked, 0, 0), (finish, 3, 4), (finish_parked, 1, 0), (finish, 0, 5), (finish_parked, 2, 0), (finish, 1, 5), (finish_parked, 3, 0), (finish, 2, 5), (finish, 3, 5)]
+        scalar = [(widen, x_unit[0], 2), (widen, x_unit[0], 3), (widen, x_unit[1], 3), (empty, x_unit[0], 0), (empty, x_unit[0], 1), (inter_a, 1, 0, 4), (empty, x_unit[1], 0), (empty, x_unit[1], 1), (widen, x_unit[2], 2), (widen, x_unit[2], 3), (widen, x_unit[3], 2), (widen, x_unit[3], 3), (cast_lam,), (widen, x_unit[4], 2), (widen, x_unit[4], 3), (empty, x_unit[2], 0), (empty, x_unit[2], 1), (empty, x_unit[3], 0), (empty, x_unit[3], 1), (widen, x_unit[5], 2), (widen, x_unit[5], 3), (widen, w_unit[0] + 0, 2), (widen, w_unit[0] + 0, 3), (empty, x_unit[4], 0), (empty, x_unit[4], 1), (empty, x_unit[5], 0), (empty, x_unit[5], 1), (widen, w_unit[0] + 1, 2), (widen, w_unit[0] + 1, 3), (widen, x_unit[6], 2), (widen, x_unit[6], 3), (empty, w_unit[0] + 0, 0), (empty, w_unit[0] + 0, 1), (empty, w_unit[0] + 1, 0), (empty, w_unit[0] + 1, 1), (widen, x_unit[7], 3), (cast_c,), (empty, x_unit[6], 0), (empty, x_unit[6], 1), (empty, x_unit[7], 0), (empty, x_unit[7], 1), (park, 0, 0), (inter_b, 1), (widen, w_unit[1] + 1, 2), (widen, w_unit[1] + 1, 3), (park, 1, 0), (empty, w_unit[1] + 0, 0), (empty, w_unit[1] + 0, 1), (empty, w_unit[1] + 1, 0), (empty, w_unit[1] + 1, 1), (park, 2, 0), (scale_d, 0, 1), (park, 3, 0), (scale_d, 1, 1), (inter_b, 2), (scale_d, 2, 1), (empty, w_unit[2] + 0, 0), (empty, w_unit[2] + 0, 1), (empty, w_unit[2] + 1, 0), (empty, w_unit[2] + 1, 1), (scale_d, 3, 1), (scale_d, 0, 2), (scale_d, 1, 2), (inter_b, 3), (scale_d, 2, 2), (empty, w_unit[3] + 0, 0), (empty, w_unit[3] + 0, 1), (empty, w_unit[3] + 1, 0), (empty, w_unit[3] + 1, 1), (scale_d, 3, 2), (scale_d, 0, 3), (scale_d, 1, 3), (inter_b, 4), (scale_d, 2, 3), (empty, w_unit[4] + 0, 0), (empty, w_unit[4] + 0, 1), (empty, w_unit[4] + 1, 0), (empty, w_unit[4] + 1, 1), (scale_d, 3, 3), (scale_d, 0, 4), (inter_b, 0), (scale_d, 1, 4), (inter_b, 5), (scale_d, 2, 4), (empty, w_unit[5] + 0, 0), (empty, w_unit[5] + 0, 1), (empty, w_unit[5] + 1, 0), (empty, w_unit[5] + 1, 1), (scale_d, 3, 4), (scale_d, 0, 5), (scale_d, 1, 5), (scale_d, 2, 5), (scale_d, 3, 5)]
 
-        vector = by_vector(x_unit[0], x_unit[1]) + [(inter_a, 0, 0, 4), (quant_a, 0, 0, 4), (quant, x_unit[0]), (inter_a, 2, 0, 4), (inter_a, 3, 0, 2)]
-        vector += [(quant_a, 1, 0, 4), (quant_a, 2, 0, 4), (quant_a, 3, 0, 2), (inter_a, 3, 2, 4), (quant_a, 3, 2, 4)]
-        vector += by_vector(x_unit[2], x_unit[3]) + [(quant, x_unit[1])]
-        pieces = by_vector(x_unit[4], x_unit[5], *chunk(0), x_unit[6], x_unit[7], *chunk(1)) + by_vector(w_unit[2])[:LEAD]
-        groups = [[(scale_h, 0)], [(quant, x_unit[2])], [], [(quant, x_unit[3])], [(scale_h, 1)], [(scale_h, 2)], [(quant, x_unit[4])], []]
-        groups += [[(quant, x_unit[5])], [(scale_h, 3)], [(scale_h, 4)], [], [], [], [(quant, w_unit[0]), (quant, w_unit[0] + 1), (scale_h, 5)]]
-        groups += [[(quant, x_unit[6])], [], [(quant, x_unit[7])], [], [], [(scale_h, 6)], [(quant_b, 1), (quant_h, 0)], [(scale_h, 7)], [(quant_h, 1)]]
-        for n, group in enumerate(groups):
-            vector += group + pieces[n : n + 1]
-        vector += pieces[len(groups) :]
-        for ci in range(1, CHUNKS - 1):
-            pieces = by_vector(*chunk(ci + 1))[LEAD if ci == 1 else 0 :]
-            first = PAIRS * (ci - 1) + TURN_AFTER
-            adds = [[] if product in parked else [(finish,) + product] for product in products[first : first + PAIRS]]
-            vector += pieces[:2] + ([(quant_b, 0)] if ci == 2 else [])
-            vector += [(quant, w_unit[ci])] + adds[0] + [(quant, w_unit[ci] + 1)]
-            vector += [(quant_h, 2), (quant_h, 3)] if ci == 1 else []
-            vector += pieces[2:3] + adds[1] + pieces[3:5] + adds[2] + pieces[5:] + [(quant_b, ci + 1)] + adds[3]
-        vector += [(quant, w_unit[CHUNKS - 1]), (finish,) + products[after_turns], (quant, w_unit[CHUNKS - 1] + 1)]
-        for n in range(after_turns + 1, len(products)):
-            if n - after_turns <= PAIRS:
-                vector += [(finish_parked,) + parked[n - after_turns - 1]]
-            vector += [(finish,) + products[n]]
-
-        scalar = by_scalar(x_unit[0], x_unit[1]) + halves(empty, x_unit[0]) + [(inter_a, A_PASS_ON_SCALAR, 0, 4)] + halves(empty, x_unit[1])
-        scalar += by_scalar(x_unit[2], x_unit[3]) + [(cast_lam,)] + by_scalar(x_unit[4])
-        scalar += halves(empty, x_unit[2], x_unit[3]) + by_scalar(x_unit[5], w_unit[0])
-        scalar += halves(empty, x_unit[4], x_unit[5]) + by_scalar(w_unit[0] + 1, x_unit[6])
-        scalar += halves(empty, *chunk(0)) + by_scalar(x_unit[7]) + [(cast_c,)]
-        scalar += halves(empty, x_unit[6], x_unit[7]) + [(park, 0, 0)] + by_scalar(*chunk(1)) + [(inter_b, 1), (park, 1, 0), (inter_b, 0)]
-        for ci in range(1, CHUNKS):
-            scalar += halves(empty, *chunk(ci))
-            if ci == 1:
-                scalar += [(park, 2, 0), (scale_d, 0, ci), (park, 3, 0), (scale_d, 1, ci)]
-            else:
-                scalar += [(scale_d, 0, ci), (scale_d, 1, ci)]
-            if ci + 1 < CHUNKS:
-                scalar += [(inter_b, ci + 1)]
-            scalar += [(scale_d, 2, ci), (scale_d, 3, ci)]
-
-        turn_bank_users = [step for step in tensor if step[0] == turn or (step[0] == up and step[1:] in parked)]
-        adapter_bank_users = [step for step in tensor if step[0] == down or (step[0] == up and step[1:] not in parked)]
-        base_bank_users = [step for step in tensor if step[0] == base]
+        parked = [p for p in products if tensor.index((base,) + p) < tensor.index((up,) + p)]
+        last_turn = tensor.index((turn, w_unit[CHUNKS - 1] + 1, 1))
+        turn_bank_users = [step for n, step in enumerate(tensor) if step[0] == turn or (step[0] == up and step[1:] in parked and n > last_turn)]
+        adapter_bank_users = [step for step in tensor if (step[0] in (down, warm, up) and step not in turn_bank_users) or (step[0] == mix_a and step[1] % 2 == 0)]
+        base_bank_users = [step for step in tensor if step[0] == base or (step[0] == mix_a and step[1] % 2 == 1)]
         y_users = [step for step in scalar if step[0] == scale_d]
         b_users = [step for step in scalar if step[0] == inter_b]
-        last_reader = {turn: empty, down: scale_h, scale_d: finish, inter_b: quant_b}
+        last_reader = {turn: empty, mix_a: copy_a, scale_d: finish, inter_b: quant_b}
 
         def freed(users, step, depth):
             n = users.index(step) - depth
@@ -400,7 +409,11 @@ def tile_fp8_base_lora_d2_kernel(tc, x_bytes, x_scale, w_bytes, w_scale, a, lam,
                 return []
             fn, args = users[n][0], users[n][1:]
             if fn == up:
-                return [(scale_d,) + args]
+                return [(finish_parked if args in parked else scale_d,) + args]
+            if fn == warm:
+                return []
+            if fn == down:
+                return [(plane_h if (plane_h,) + args in scalar else scale_h,) + args]
             if fn == base:
                 return [(park if args in parked else finish,) + args]
             return [(last_reader[fn],) + args]
@@ -408,15 +421,30 @@ def tile_fp8_base_lora_d2_kernel(tc, x_bytes, x_scale, w_bytes, w_scale, a, lam,
         def needs(step):
             fn, args = step[0], step[1:]
             if fn == widen:
-                return halves(turn, args[0] - WIDE_BUFS) if args[0] >= WIDE_BUFS else []
+                first = []
+                return first + (halves(turn, args[0] - WIDE_BUFS) if args[0] >= WIDE_BUFS else [])
             if fn == turn:
                 return [(widen, args[0], 2 * args[1]), (widen, args[0], 2 * args[1] + 1)] + freed(turn_bank_users, step, TURN_BANKS)
             if fn == empty:
                 return [(turn,) + args] + ([(quant, args[0] - GROUP_BUFS)] if args[0] >= GROUP_BUFS else [])
             if fn == quant:
                 return halves(empty, args[0])
+            if fn == mix_a:
+                return freed(adapter_bank_users if args[0] % 2 == 0 else base_bank_users, step, 2)
+            if fn == copy_a:
+                return [(mix_a,) + args]
             if fn == quant_a:
-                return [(inter_a,) + args]
+                if (mix_a, args[0], 0) not in tensor:
+                    return [s for s in vector + scalar if s[0] == inter_a and s[1] == args[0] and s[2] < args[2] and s[3] > args[1]]
+                if args[0] in PAIR_PASSES:
+                    return [(copy_a, args[0], half) for half in range(args[1] // 2, args[2] // 2)]
+                return halves(copy_a, args[0])
+            if fn == warm:
+                return [s for s in vector + scalar if s[:3] == (inter_a, args[0], 0)]
+            if fn == plane_h:
+                return [(down,) + args, (cast_lam,)]
+            if fn == inter_h:
+                return [(plane_h,) + args]
             if fn == inter_b:
                 return freed(b_users, step, B_BUFS)
             if fn == quant_b:
@@ -426,9 +454,9 @@ def tile_fp8_base_lora_d2_kernel(tc, x_bytes, x_scale, w_bytes, w_scale, a, lam,
             if fn == scale_h:
                 return [(down,) + args, (cast_lam,)]
             if fn == quant_h:
-                return [(scale_h, 2 * args[0]), (scale_h, 2 * args[0] + 1)]
+                return [(inter_h if (plane_h, m) in scalar else scale_h, m) for m in (2 * args[0], 2 * args[0] + 1)]
             if fn == up:
-                users, depth = (turn_bank_users, TURN_BANKS) if args in parked else (adapter_bank_users, ADAPTER_BANKS)
+                users, depth = (turn_bank_users, TURN_BANKS) if step in turn_bank_users else (adapter_bank_users, ADAPTER_BANKS)
                 return freed(users, step, depth) + [(quant_h, args[0]), (quant_b, args[1])]
             if fn == scale_d:
                 return [(up,) + args, (cast_c,)] + freed(y_users, step, Y_BUFS)
@@ -438,7 +466,7 @@ def tile_fp8_base_lora_d2_kernel(tc, x_bytes, x_scale, w_bytes, w_scale, a, lam,
                 if args == BEFORE_LAST:
                     before += freed(base_bank_users, step, 1)
                 if args == LAST:
-                    before += [(finish_parked,) + product for product in parked[: len(ENDING)]]
+                    before += halves(empty, *chunk(CHUNKS - 1)) + [(finish_parked,) + s[1:] for s in turn_bank_users[-TURN_BANKS:][: len(ENDING)] if s[0] == up]
                 return before
             if fn == park:
                 return [(base,) + args]
@@ -451,6 +479,7 @@ def tile_fp8_base_lora_d2_kernel(tc, x_bytes, x_scale, w_bytes, w_scale, a, lam,
         written = set()
         lists = [tensor, vector, scalar]
         while any(lists):
+            assert any(steps and all(need in written for need in needs(steps[0])) for steps in lists), [(steps[0], [n for n in needs(steps[0]) if n not in written]) for steps in lists if steps]
             ready = [steps for steps in lists if steps and all(need in written for need in needs(steps[0]))]
             step = ready[0][0]
             step[0](*step[1:])

@@ -27,15 +27,18 @@ PIECES = 4
 LAST = (PAIRS - 1, CHUNKS - 1)
 BEFORE_LAST = (PAIRS - 2, CHUNKS - 1)
 
-LOAD_ORDER = "xs x0 x1 a0 a1 a2 a3 x2 x3 lam x4 x5 ws w0 c x6 x7 w1 b1 b0 w2 b2 w3 b3 w4 b4 w5 b5"
 UNIT_ORDER = "x0 x1 x2 x3 x4 x5 w0 x6 x7 w1 w2 w3 w4 w5"
-PAIR_PASSES = (0,1,2,3)
-WARM = 4
+LOAD_ORDER = "xs x0 x1 a0 a1 a2 a3 x2 x3 lam x4 x5 ws w0 c x6 x7 w1 b1 b0 w2 b2 w3 b3 w4 b4 w5 b5"
+X_ON_SCALAR = (2, 1, 2, 2, 2, 2, 2, 1)
+W_ON_SCALAR = ((1, 2), (0, 1), (0, 0), (0, 0), (0, 0), (0, 0))
+A_PASS_ON_SCALAR = 1
 TURN_BANKS, ADAPTER_BANKS, BASE_BANKS = 4, 2, 2
 WIDE_BUFS, GROUP_BUFS, A_BUFS, B_BUFS, Y_BUFS = 7, 3, 4, 2, 4
 TURN_AFTER = 2
 UP_AHEAD = 2
-LEAD = 2
+FIRST_UNPARK = 2
+SCALE_PAD = 64
+SCALE_ROW = {"w": 4, "b": 4, "x": 8, "h": 8, "a": 12}
 ENDING = ((0, 0, 256), (1, 0, 128), (1, 128, 256))
 
 
@@ -55,6 +58,11 @@ def tile_fp8_base_lora_d2_kernel(tc, x_bytes, x_scale, w_bytes, w_scale, a, lam,
             if pool == psum:
                 return pool.tile(shape, dtype, name="%s%d" % (what, n % depth))
             return pool.tile(shape, dtype, name="%s%d" % (what, n % depth), align_bytes=64)
+
+        def mx_operand(what, index, width):
+            words = codes.tile([P, width], U32, name="%s_codes%d" % (what, index), align_bytes=64)
+            plane = codes.tile([P, SCALE_PAD + width], U8, name="%s_scales%d" % (what, index), align_bytes=64)
+            return words, plane[SCALE_ROW[what] :, SCALE_PAD:]
 
         ctx.enter_context(tc.manual_schedule())
 
@@ -104,55 +112,44 @@ def tile_fp8_base_lora_d2_kernel(tc, x_bytes, x_scale, w_bytes, w_scale, a, lam,
                     w_raw[row] = loads.tile([P, K], U8, name="w_b%d" % row, align_bytes=64)
                     nc.sync.dma_start(out=w_raw[row][:], in_=w_view[:, row, :])
 
-        ws2 = const.tile([P, CHUNKS, K_BLOCKS], F32, name="ws2")
         lam_f = const.tile([P, 4], F32, name="lam_f")
         c_f = const.tile([P, TILES], F32, name="c_f")
 
-        units, x_unit, w_unit = [], {}, {}
+        units, on_scalar, x_unit, w_unit = [], [], {}, {}
         for what in UNIT_ORDER.split(" "):
             idx = int(what[1:])
             if what[0] == "x":
                 x_unit[idx] = len(units)
                 units.append([("x", idx, g) for g in range(PASSES)])
+                on_scalar.append(X_ON_SCALAR[idx])
             else:
                 w_unit[idx] = len(units)
                 for half in range(2):
-                    units.append([("w", idx, g) for g in (2 * half, 2 * half + 1) for r in range(2)])
+                    units.append([("w", 2 * idx + r, g) for g in (2 * half, 2 * half + 1) for r in range(2)])
+                    on_scalar.append(W_ON_SCALAR[idx][half])
         wide, turned, grouped, unit_codes, unit_scales = {}, {}, {}, {}, {}
 
         def widen(s, i):
             if s not in wide:
                 wide[s] = ring(work, "wide", WIDE_BUFS, [P, PIECES, 2, P, 2], BF16)
             kind, row, g = units[s][i]
-            if kind == "w" and g not in PAIR_PASSES:
-                for q in (2 * (i % 2), 2 * (i % 2) + 1):
+            src = x_raw[row] if kind == "x" else w_raw[row]
+            scales = xs if kind == "x" else ws
+            for q in range(4):
+                k0 = 512 * g + P * q
+                j = K_BLOCKS * row + 4 * g + q
+                if i >= PIECES - on_scalar[s]:
+                    flat = wide[s][:, i, :, :, :].rearrange("p u w e -> p (u w e)")
+                    nc.scalar.activation(
+                        out=flat[:, P * q : P * (q + 1)], in_=src[:, k0 : k0 + P].bitcast(FP8), func=COPY, scale=scales[:, j : j + 1]
+                    )
+                else:
                     nc.vector.tensor_scalar(
-                        out=wide[s][:, i - i % 2 : i - i % 2 + 2, :, 32 * q : 32 * (q + 1), :].rearrange("p r u w e -> p r (w e) u"),
-                        in0=w_raw[row][:, 4 * g + q, :, :].bitcast(FP8).rearrange("p r (v u) -> p r v u", u=2),
-                        scalar1=ws2[:, row, 4 * g + q : 4 * g + q + 1],
+                        out=wide[s][:, i, :, 32 * q : 32 * (q + 1), :].rearrange("p u w e -> p w u e"),
+                        in0=src[:, k0 : k0 + P].bitcast(FP8).rearrange("p (w u e) -> p w u e", u=2, e=2),
+                        scalar1=scales[:, j : j + 1],
                         scalar2=None,
                         op0=MULT,
-                    )
-                return
-            for q in range(4):
-                j = 4 * g + q
-                if kind == "x":
-                    src, scale = x_raw[row][:, P * j : P * (j + 1)].bitcast(FP8), xs[:, K_BLOCKS * row + j : K_BLOCKS * row + j + 1]
-                else:
-                    wr = 2 * row + i % 2
-                    src, scale = w_raw[wr][:, P * j : P * (j + 1)].bitcast(FP8), ws[:, K_BLOCKS * wr + j : K_BLOCKS * wr + j + 1]
-                part = wide[s][:, i, :, 32 * q : 32 * (q + 1), :]
-                if (widen, s, i) in scalar:
-                    assert g in PAIR_PASSES
-                    flat = wide[s][:, i, :, :, :].rearrange("p u w e -> p (u w e)")
-                    nc.scalar.activation(out=flat[:, P * q : P * (q + 1)], in_=src, func=COPY, scale=scale)
-                elif g in PAIR_PASSES:
-                    nc.vector.tensor_scalar(
-                        out=part.rearrange("p u w e -> p w u e"), in0=src.rearrange("p (w u e) -> p w u e", u=2, e=2), scalar1=scale, scalar2=None, op0=MULT
-                    )
-                else:
-                    nc.vector.tensor_scalar(
-                        out=part.rearrange("p u w e -> p (w e) u"), in0=src.rearrange("p (v u) -> p v u", u=2), scalar1=scale, scalar2=None, op0=MULT
                     )
 
         def turn(s, half):
@@ -161,7 +158,7 @@ def tile_fp8_base_lora_d2_kernel(tc, x_bytes, x_scale, w_bytes, w_scale, a, lam,
             for i in range(2):
                 piece = wide[s][:, 2 * half + i, :, :, :]
                 for u in range(2):
-                    if (widen, s, 2 * half + i) in scalar:
+                    if 2 * half + i >= PIECES - on_scalar[s]:
                         words = piece.rearrange("p u w e -> p (u w e)").bitcast(F32)[:, u::2]
                     else:
                         words = piece[:, u, :, :].rearrange("p w e -> p (w e)").bitcast(F32)
@@ -171,20 +168,15 @@ def tile_fp8_base_lora_d2_kernel(tc, x_bytes, x_scale, w_bytes, w_scale, a, lam,
             if half == 0:
                 grouped[s] = ring(work, "grouped", GROUP_BUFS, [P, PIECES, P, 4], BF16)
             words = grouped[s][:, 2 * half : 2 * half + 2, :, :].rearrange("p i w t -> p (i w t)").bitcast(F32)
-            copy = nc.scalar.copy if (empty, s, half) in scalar else nc.vector.tensor_copy
-            if units[s][0][0] in "xw":
-                copy(
-                    out=words.rearrange("p (i w u) -> p i w u", i=2, u=2),
-                    in_=turned[s, half][:].rearrange("p (i u) w -> p i w u", u=2),
-                )
-            else:
-                copy(out=words.rearrange("p (w v) -> p w v", v=4), in_=turned[s, half][:].rearrange("p v w -> p w v"))
+            nc.scalar.copy(
+                out=words.rearrange("p (i w u) -> p i w u", i=2, u=2),
+                in_=turned[s, half][:].rearrange("p (i u) w -> p i w u", u=2),
+            )
 
         def quant(s):
-            unit_codes[s] = codes.tile([P, 512], U32, name="codes%d" % s, align_bytes=64)
-            unit_scales[s] = codes.tile([P, 512], U8, name="scales%d" % s, align_bytes=64)
+            unit_codes[s], unit_scales[s] = mx_operand(units[s][0][0], s, PIECES * P)
             nc.vector.quantize_mx(
-                out=unit_codes[s][:].bitcast(FP8X4), scales=unit_scales[s][:], in_=grouped[s][:].rearrange("p i w t -> p (i w t)")
+                out=unit_codes[s][:].bitcast(FP8X4), scales=unit_scales[s], in_=grouped[s][:].rearrange("p i w t -> p (i w t)")
             )
 
         a_int, a_codes, a_scales = {}, {}, {}
@@ -193,45 +185,14 @@ def tile_fp8_base_lora_d2_kernel(tc, x_bytes, x_scale, w_bytes, w_scale, a, lam,
         def inter_a(g, t0, t1):
             if t0 == 0:
                 a_int[g] = ring(work, "ab_int", A_BUFS, [P, 4, P, 4], BF16)
-            copy = nc.scalar.copy if (inter_a, g, t0, t1) in scalar else nc.vector.tensor_copy
-            if g in PAIR_PASSES:
-                copy(
-                    out=a_int[g][:, t0:t1, :, :].rearrange("p t (q m) j -> p q t m j", m=2),
-                    in_=a_raw[g][:].rearrange("p j (q m t) -> p q t m j", m=2, t=4)[:, :, t0:t1, :, :],
-                )
-            else:
-                copy(
-                    out=a_int[g][:, t0:t1, :, :].rearrange("p t m (u e) -> p m t u e", u=2),
-                    in_=a_raw[g][:].rearrange("p (e u) (m t) -> p m t u e", u=2, t=4)[:, :, t0:t1, :, :],
-                )
-
-        mixed = {}
-
-        def mix_a(g, half):
-            return None
-
-        def warm(n):
-            bank = ring(psum, "hd", 2, [P, R], F32)
-            rows = a_int[n][:].rearrange("p t m j -> p t (m j)")
-            for i in range(WARM):
-                nc.tensor.matmul(out=bank[:], lhsT=rows[:, 0, 0:P], rhs=rows[:, i % 2, :], start=True, stop=True)
-
-        def copy_a(g, half):
-            copy = nc.scalar.copy if (copy_a, g, half) in scalar else nc.vector.tensor_copy
-            if half == 0:
-                a_int[g] = ring(work, "ab_int", A_BUFS, [P, 4, P, 4], BF16)
-            if g in PAIR_PASSES:
-                copy(out=a_int[g][:, 2 * half : 2 * half + 2, :, :].rearrange("p t m j -> p (t m j)"), in_=mixed[g, half][:])
-            else:
-                copy(
-                    out=a_int[g][:, :, 64 * half : 64 * (half + 1), :].rearrange("p t m j -> p t (m j)"),
-                    in_=mixed[g, half][:].rearrange("p (t v) -> p t v", t=4),
-                )
+            (nc.scalar.copy if g == A_PASS_ON_SCALAR else nc.vector.tensor_copy)(
+                out=a_int[g][:, t0:t1, :, :].rearrange("p t (q m) j -> p q t m j", m=2),
+                in_=a_raw[g][:].rearrange("p j (q m t) -> p q t m j", m=2, t=4)[:, :, t0:t1, :, :],
+            )
 
         def quant_a(g, t0, t1):
             if t0 == 0:
-                a_codes[g] = codes.tile([P, R], U32, name="acodes%d" % g, align_bytes=64)
-                a_scales[g] = codes.tile([P, R], U8, name="ascales%d" % g, align_bytes=64)
+                a_codes[g], a_scales[g] = mx_operand("a", g, R)
             nc.vector.quantize_mx(
                 out=a_codes[g][:, P * t0 : P * t1].bitcast(FP8X4),
                 scales=a_scales[g][:, P * t0 : P * t1],
@@ -245,10 +206,9 @@ def tile_fp8_base_lora_d2_kernel(tc, x_bytes, x_scale, w_bytes, w_scale, a, lam,
             )
 
         def quant_b(ci):
-            b_codes[ci] = codes.tile([P, WIDTH], U32, name="bcodes%d" % ci, align_bytes=64)
-            b_scales[ci] = codes.tile([P, WIDTH], U8, name="bscales%d" % ci, align_bytes=64)
+            b_codes[ci], b_scales[ci] = mx_operand("b", ci, WIDTH)
             nc.vector.quantize_mx(
-                out=b_codes[ci][:].bitcast(FP8X4), scales=b_scales[ci][:], in_=b_int[ci][:].rearrange("p n j -> p (n j)")
+                out=b_codes[ci][:].bitcast(FP8X4), scales=b_scales[ci], in_=b_int[ci][:].rearrange("p n j -> p (n j)")
             )
 
         h_banks, h_grouped, h_codes, h_scales = {}, {}, {}, {}
@@ -268,7 +228,7 @@ def tile_fp8_base_lora_d2_kernel(tc, x_bytes, x_scale, w_bytes, w_scale, a, lam,
                     )
 
         def scale_h(m):
-            if m // 2 not in h_grouped:
+            if m % 2 == 0:
                 h_grouped[m // 2] = const.tile([P, 2, P, 4], BF16, name="h_grouped%d" % (m // 2), align_bytes=64)
             nc.vector.tensor_tensor(
                 out=h_grouped[m // 2][:, m % 2, :, :],
@@ -277,36 +237,16 @@ def tile_fp8_base_lora_d2_kernel(tc, x_bytes, x_scale, w_bytes, w_scale, a, lam,
                 op=MULT,
             )
 
-        h_planes = {}
-
-        def plane_h(m):
-            if m // 2 not in h_planes:
-                h_planes[m // 2] = ring(work, "ab_int", A_BUFS, [P, 2, 4, P], BF16)
-            for t in range(4):
-                nc.scalar.activation(out=h_planes[m // 2][:, m % 2, t, :], in_=h_banks[m][:, t, :], func=COPY, scale=lam_f[:, t : t + 1])
-
-        def inter_h(m):
-            if m // 2 not in h_grouped:
-                h_grouped[m // 2] = const.tile([P, 2, P, 4], BF16, name="h_grouped%d" % (m // 2), align_bytes=64)
-            (nc.scalar.copy if (inter_h, m) in scalar else nc.vector.tensor_copy)(
-                out=h_grouped[m // 2][:, m % 2, :, :].rearrange("p (n i) t -> p n t i", i=4),
-                in_=h_planes[m // 2][:, m % 2, :, :].rearrange("p t (n i) -> p n t i", i=4),
-            )
-
         def quant_h(j):
-            h_codes[j] = codes.tile([P, 2 * P], U32, name="hcodes%d" % j, align_bytes=64)
-            h_scales[j] = codes.tile([P, 2 * P], U8, name="hscales%d" % j, align_bytes=64)
+            h_codes[j], h_scales[j] = mx_operand("h", j, 2 * P)
             nc.vector.quantize_mx(
-                out=h_codes[j][:].bitcast(FP8X4), scales=h_scales[j][:], in_=h_grouped[j][:].rearrange("p i w t -> p (i w t)")
+                out=h_codes[j][:].bitcast(FP8X4), scales=h_scales[j], in_=h_grouped[j][:].rearrange("p i w t -> p (i w t)")
             )
 
         y, base_parts, d_banks = {}, {}, {}
 
         def up(j, ci):
-            if (up, j, ci) in turn_bank_users:
-                bank = ring(psum, "xt", TURN_BANKS, [P, 2, WIDTH], F32)
-            else:
-                bank = ring(psum, "hd", ADAPTER_BANKS, [P, 2, WIDTH], F32)
+            bank = ring(psum, "hd", ADAPTER_BANKS, [P, 2, WIDTH], F32)
             d_banks[j, ci] = bank
             for i in range(2):
                 nc.tensor.matmul_mx(
@@ -314,7 +254,7 @@ def tile_fp8_base_lora_d2_kernel(tc, x_bytes, x_scale, w_bytes, w_scale, a, lam,
                     lhsT=h_codes[j][:, P * i : P * (i + 1)].bitcast(FP8X4),
                     lhsT_scale=h_scales[j][:, P * i : P * (i + 1)],
                     rhs=b_codes[ci][:].bitcast(FP8X4),
-                    rhs_scale=b_scales[ci][:],
+                    rhs_scale=b_scales[ci],
                     start=True,
                     stop=True,
                 )
@@ -329,7 +269,8 @@ def tile_fp8_base_lora_d2_kernel(tc, x_bytes, x_scale, w_bytes, w_scale, a, lam,
             if (j, ci) == LAST:
                 parts = [(ring(psum, "xt", TURN_BANKS, [P, 2, WIDTH], F32), i, n0, n1) for i, n0, n1 in ENDING]
             elif (j, ci) == BEFORE_LAST:
-                parts = [(ring(psum, "base", BASE_BANKS, [P, 2, WIDTH], F32), i, 0, WIDTH) for i in range(2)]
+                parts = [(ring(psum, "base", BASE_BANKS, [P, 2, WIDTH], F32), 0, 0, WIDTH)]
+                parts += [(ring(psum, "xt", TURN_BANKS, [P, 2, WIDTH], F32), 1, 0, WIDTH)]
             else:
                 shared = ring(psum, "base", BASE_BANKS, [P, 2, WIDTH], F32)
                 parts = [(shared, i, 0, WIDTH) for i in range(2)]
@@ -373,35 +314,89 @@ def tile_fp8_base_lora_d2_kernel(tc, x_bytes, x_scale, w_bytes, w_scale, a, lam,
         def cast_lam():
             nc.scalar.activation(out=lam_f[:], in_=lam_b[:], func=COPY)
 
-        def pick_ws():
-            for h in range(2):
-                rows = slice(64 * h, 64 * (h + 1))
-                nc.scalar.copy(out=ws2[rows, :, :], in_=ws[rows, :].rearrange("p (c h j) -> p c h j", h=2, j=K_BLOCKS)[:, :, h, :])
-
         def cast_c():
             nc.scalar.activation(out=c_f[:], in_=c_b[:], func=COPY)
 
         def halves(fn, *some_units):
             return [(fn, s, half) for s in some_units for half in range(2)]
 
+        def by_vector(*some_units):
+            return [(widen, s, i) for s in some_units for i in range(PIECES - on_scalar[s])]
+
+        def by_scalar(*some_units):
+            return [(widen, s, i) for s in some_units for i in range(PIECES - on_scalar[s], PIECES)]
+
         def chunk(ci):
             return (w_unit[ci], w_unit[ci] + 1)
 
         products = [(j, ci) for ci in range(CHUNKS) for j in range(PAIRS)]
-        after_turns = PAIRS * (CHUNKS - 2) + TURN_AFTER
+        parked = products[:PAIRS]
 
-        tensor = [(turn, x_unit[0], 0), (turn, x_unit[0], 1), (turn, x_unit[1], 0), (turn, x_unit[1], 1), (down, 0), (turn, x_unit[2], 0), (turn, x_unit[2], 1), (turn, x_unit[3], 0), (turn, x_unit[3], 1), (down, 1), (down, 2), (turn, x_unit[4], 0), (turn, x_unit[4], 1), (turn, x_unit[5], 0), (turn, x_unit[5], 1), (down, 3), (down, 4), (turn, w_unit[0] + 0, 0), (turn, w_unit[0] + 0, 1), (turn, w_unit[0] + 1, 0), (turn, w_unit[0] + 1, 1), (down, 5), (turn, x_unit[6], 0), (turn, x_unit[6], 1), (turn, x_unit[7], 0), (turn, x_unit[7], 1), (base, 0, 0), (down, 6), (base, 1, 0), (down, 7), (turn, w_unit[1] + 0, 0), (turn, w_unit[1] + 0, 1), (turn, w_unit[1] + 1, 0), (turn, w_unit[1] + 1, 1), (base, 2, 0), (up, 0, 1), (base, 3, 0), (up, 1, 1), (base, 0, 1), (up, 2, 1), (base, 1, 1), (up, 3, 1), (turn, w_unit[2] + 0, 0), (turn, w_unit[2] + 0, 1), (turn, w_unit[2] + 1, 0), (turn, w_unit[2] + 1, 1), (base, 2, 1), (up, 0, 2), (base, 3, 1), (up, 1, 2), (base, 0, 2), (up, 2, 2), (base, 1, 2), (up, 3, 2), (turn, w_unit[3] + 0, 0), (turn, w_unit[3] + 0, 1), (turn, w_unit[3] + 1, 0), (turn, w_unit[3] + 1, 1), (base, 2, 2), (up, 0, 3), (base, 3, 2), (up, 1, 3), (base, 0, 3), (up, 2, 3), (base, 1, 3), (up, 3, 3), (turn, w_unit[4] + 0, 0), (turn, w_unit[4] + 0, 1), (turn, w_unit[4] + 1, 0), (turn, w_unit[4] + 1, 1), (base, 2, 3), (up, 0, 4), (base, 3, 3), (up, 1, 4), (base, 0, 4), (up, 2, 4), (base, 1, 4), (up, 3, 4), (turn, w_unit[5] + 0, 0), (turn, w_unit[5] + 0, 1), (turn, w_unit[5] + 1, 0), (turn, w_unit[5] + 1, 1), (base, 2, 4), (up, 0, 5), (up, 0, 0), (base, 3, 4), (up, 1, 5), (up, 1, 0), (base, 0, 5), (up, 2, 5), (up, 2, 0), (base, 1, 5), (up, 3, 5), (up, 3, 0), (base, 2, 5), (base, 3, 5)]
-        vector = [(widen, x_unit[0], 0), (widen, x_unit[0], 1), (widen, x_unit[1], 0), (widen, x_unit[1], 1), (widen, x_unit[1], 2), (inter_a, 0, 0, 4), (quant, x_unit[0]), (quant_a, 0, 0, 4), (inter_a, 2, 0, 4), (inter_a, 3, 0, 2), (quant_a, 1, 0, 2), (quant_a, 2, 0, 2), (quant_a, 3, 0, 2), (inter_a, 3, 2, 4), (quant_a, 1, 2, 4), (quant_a, 2, 2, 4), (quant_a, 3, 2, 4), (widen, x_unit[2], 0), (widen, x_unit[2], 1), (widen, x_unit[3], 0), (widen, x_unit[3], 1), (quant, x_unit[1]), (scale_h, 0), (widen, x_unit[4], 0), (quant, x_unit[2]), (widen, x_unit[4], 1), (widen, x_unit[5], 0), (quant, x_unit[3]), (widen, x_unit[5], 1), (scale_h, 1), (widen, w_unit[0] + 0, 0), (scale_h, 2), (widen, w_unit[0] + 0, 1), (quant, x_unit[4]), (widen, w_unit[0] + 1, 0), (quant, x_unit[5]), (widen, w_unit[0] + 1, 1), (scale_h, 3), (widen, x_unit[6], 0), (scale_h, 4), (widen, x_unit[6], 1), (widen, x_unit[7], 0), (widen, x_unit[7], 1), (widen, x_unit[7], 2), (quant, w_unit[0] + 0), (quant, w_unit[0] + 1), (scale_h, 5), (quant, x_unit[6]), (widen, w_unit[1] + 0, 0), (widen, w_unit[1] + 0, 1), (widen, w_unit[1] + 0, 2), (quant, x_unit[7]), (widen, w_unit[1] + 0, 3), (widen, w_unit[1] + 1, 0), (widen, w_unit[1] + 1, 1), (scale_h, 6), (quant_b, 1), (quant_h, 0), (widen, w_unit[2] + 0, 0), (scale_h, 7), (widen, w_unit[2] + 0, 1), (widen, w_unit[2] + 0, 2), (quant_h, 1), (quant, w_unit[1] + 0), (widen, w_unit[2] + 0, 3), (quant, w_unit[1] + 1), (quant_h, 2), (quant_h, 3), (widen, w_unit[2] + 1, 0), (widen, w_unit[2] + 1, 1), (widen, w_unit[2] + 1, 2), (finish, 0, 1), (widen, w_unit[2] + 1, 3), (quant_b, 2), (finish, 1, 1), (widen, w_unit[3] + 0, 0), (widen, w_unit[3] + 0, 1), (quant, w_unit[2] + 0), (finish, 2, 1), (quant, w_unit[2] + 1), (widen, w_unit[3] + 0, 2), (finish, 3, 1), (widen, w_unit[3] + 0, 3), (widen, w_unit[3] + 1, 0), (finish, 0, 2), (widen, w_unit[3] + 1, 1), (widen, w_unit[3] + 1, 2), (widen, w_unit[3] + 1, 3), (quant_b, 3), (finish, 1, 2), (widen, w_unit[4] + 0, 0), (widen, w_unit[4] + 0, 1), (quant, w_unit[3] + 0), (finish, 2, 2), (quant, w_unit[3] + 1), (widen, w_unit[4] + 0, 2), (finish, 3, 2), (widen, w_unit[4] + 0, 3), (widen, w_unit[4] + 1, 0), (finish, 0, 3), (widen, w_unit[4] + 1, 1), (widen, w_unit[4] + 1, 2), (widen, w_unit[4] + 1, 3), (quant_b, 4), (finish, 1, 3), (widen, w_unit[5] + 0, 0), (widen, w_unit[5] + 0, 1), (quant, w_unit[4] + 0), (finish, 2, 3), (quant, w_unit[4] + 1), (widen, w_unit[5] + 0, 2), (finish, 3, 3), (widen, w_unit[5] + 0, 3), (widen, w_unit[5] + 1, 0), (finish, 0, 4), (widen, w_unit[5] + 1, 1), (widen, w_unit[5] + 1, 2), (widen, w_unit[5] + 1, 3), (quant_b, 5), (finish, 1, 4), (quant_b, 0), (quant, w_unit[5] + 0), (finish, 2, 4), (quant, w_unit[5] + 1), (finish_parked, 0, 0), (finish, 3, 4), (finish_parked, 1, 0), (finish, 0, 5), (finish_parked, 2, 0), (finish, 1, 5), (finish_parked, 3, 0), (finish, 2, 5), (finish, 3, 5)]
-        scalar = [(widen, x_unit[0], 2), (widen, x_unit[0], 3), (widen, x_unit[1], 3), (empty, x_unit[0], 0), (empty, x_unit[0], 1), (inter_a, 1, 0, 4), (empty, x_unit[1], 0), (empty, x_unit[1], 1), (widen, x_unit[2], 2), (widen, x_unit[2], 3), (widen, x_unit[3], 2), (widen, x_unit[3], 3), (cast_lam,), (widen, x_unit[4], 2), (widen, x_unit[4], 3), (empty, x_unit[2], 0), (empty, x_unit[2], 1), (empty, x_unit[3], 0), (empty, x_unit[3], 1), (widen, x_unit[5], 2), (widen, x_unit[5], 3), (widen, w_unit[0] + 0, 2), (widen, w_unit[0] + 0, 3), (empty, x_unit[4], 0), (empty, x_unit[4], 1), (empty, x_unit[5], 0), (empty, x_unit[5], 1), (widen, w_unit[0] + 1, 2), (widen, w_unit[0] + 1, 3), (widen, x_unit[6], 2), (widen, x_unit[6], 3), (empty, w_unit[0] + 0, 0), (empty, w_unit[0] + 0, 1), (empty, w_unit[0] + 1, 0), (empty, w_unit[0] + 1, 1), (widen, x_unit[7], 3), (cast_c,), (empty, x_unit[6], 0), (empty, x_unit[6], 1), (empty, x_unit[7], 0), (empty, x_unit[7], 1), (park, 0, 0), (inter_b, 1), (widen, w_unit[1] + 1, 2), (widen, w_unit[1] + 1, 3), (park, 1, 0), (empty, w_unit[1] + 0, 0), (empty, w_unit[1] + 0, 1), (empty, w_unit[1] + 1, 0), (empty, w_unit[1] + 1, 1), (park, 2, 0), (scale_d, 0, 1), (park, 3, 0), (scale_d, 1, 1), (inter_b, 2), (scale_d, 2, 1), (empty, w_unit[2] + 0, 0), (empty, w_unit[2] + 0, 1), (empty, w_unit[2] + 1, 0), (empty, w_unit[2] + 1, 1), (scale_d, 3, 1), (scale_d, 0, 2), (scale_d, 1, 2), (inter_b, 3), (scale_d, 2, 2), (empty, w_unit[3] + 0, 0), (empty, w_unit[3] + 0, 1), (empty, w_unit[3] + 1, 0), (empty, w_unit[3] + 1, 1), (scale_d, 3, 2), (scale_d, 0, 3), (scale_d, 1, 3), (inter_b, 4), (scale_d, 2, 3), (empty, w_unit[4] + 0, 0), (empty, w_unit[4] + 0, 1), (empty, w_unit[4] + 1, 0), (empty, w_unit[4] + 1, 1), (scale_d, 3, 3), (scale_d, 0, 4), (inter_b, 0), (scale_d, 1, 4), (inter_b, 5), (scale_d, 2, 4), (empty, w_unit[5] + 0, 0), (empty, w_unit[5] + 0, 1), (empty, w_unit[5] + 1, 0), (empty, w_unit[5] + 1, 1), (scale_d, 3, 4), (scale_d, 0, 5), (scale_d, 1, 5), (scale_d, 2, 5), (scale_d, 3, 5)]
+        tensor = halves(turn, x_unit[0], x_unit[1]) + [(down, 0)]
+        for m in (2, 4):
+            tensor += halves(turn, x_unit[m], x_unit[m + 1]) + [(down, m - 1), (down, m)]
+        tensor += halves(turn, *chunk(0)) + [(down, 5)]
+        tensor += halves(turn, x_unit[6], x_unit[7]) + [(base, 0, 0), (down, 6), (base, 1, 0), (down, 7)]
+        for n in range(TURN_AFTER, len(products)):
+            j, ci = products[n]
+            if j == TURN_AFTER and ci + 1 < CHUNKS:
+                tensor += halves(turn, *chunk(ci + 1))
+            tensor += [(base, j, ci)]
+            if n + UP_AHEAD < len(products):
+                tensor += [(up,) + products[n + UP_AHEAD]]
+            if j == 0 and ci >= FIRST_UNPARK:
+                tensor += [(up,) + parked[ci - FIRST_UNPARK]]
 
-        parked = [p for p in products if tensor.index((base,) + p) < tensor.index((up,) + p)]
-        last_turn = tensor.index((turn, w_unit[CHUNKS - 1] + 1, 1))
-        turn_bank_users = [step for n, step in enumerate(tensor) if step[0] == turn or (step[0] == up and step[1:] in parked and n > last_turn)]
-        adapter_bank_users = [step for step in tensor if (step[0] in (down, warm, up) and step not in turn_bank_users) or (step[0] == mix_a and step[1] % 2 == 0)]
-        base_bank_users = [step for step in tensor if step[0] == base or (step[0] == mix_a and step[1] % 2 == 1)]
+        vector = by_vector(x_unit[0], x_unit[1]) + [(inter_a, 0, 0, 4), (quant, x_unit[0]), (quant_a, 0, 0, 4), (inter_a, 2, 0, 4)]
+        for t0 in (0, 2):
+            vector += [(inter_a, 3, t0, t0 + 2)] + [(quant_a, g, t0, t0 + 2) for g in (1, 2, 3)]
+        vector += by_vector(x_unit[2], x_unit[3]) + [(quant, x_unit[1])]
+
+        def weave(results, pieces, counts):
+            steps, done = [], 0
+            for result, count in zip(results, counts):
+                steps += result + pieces[done : done + count]
+                done += count
+            return steps
+
+        results = [(scale_h, 0), (quant, x_unit[2]), (quant, x_unit[3]), (scale_h, 1), (scale_h, 2)]
+        results += [(quant, x_unit[4]), (quant, x_unit[5]), (scale_h, 3), (scale_h, 4)]
+        pieces = by_vector(x_unit[4], x_unit[5], *chunk(0), x_unit[6], x_unit[7])
+        vector += weave([[step] for step in results], pieces, (1, 2, 1, 1, 1, 2, 1, 1, 4))
+        results = [[(quant, w_unit[0]), (quant, w_unit[0] + 1), (scale_h, 5), (quant, x_unit[6])], [(quant, x_unit[7])]]
+        vector += weave(results, by_vector(*chunk(1)), (3, 4))
+        results = [[(scale_h, 6), (quant_b, 1), (quant_h, 0)], [(scale_h, 7)], [(quant_h, 1), (quant, w_unit[1])]]
+        results += [[(quant, w_unit[1] + 1), (quant_h, 2), (quant_h, 3)], [(finish, 0, 1)]]
+        vector += weave(results, by_vector(*chunk(2)), (1, 2, 1, 3, 1)) + [(quant_b, 2), (finish, 1, 1)]
+        for ci in range(FIRST_UNPARK, CHUNKS):
+            late_b = [(quant_b, 0)] if ci == FIRST_UNPARK else []
+            results = [[], [(quant, w_unit[ci]), (finish, 2, ci - 1)] + late_b + [(quant, w_unit[ci] + 1)], [(finish, 3, ci - 1)]]
+            results += [[(finish, 0, ci), (finish_parked,) + parked[ci - FIRST_UNPARK]]]
+            if ci + 1 < CHUNKS:
+                vector += weave(results, by_vector(*chunk(ci + 1)), (2, 1, 2, 3)) + [(quant_b, ci + 1), (finish, 1, ci)]
+            else:
+                vector += weave(results, [], (0, 0, 0, 0)) + [(finish, j, ci) for j in range(1, PAIRS)]
+
+        scalar = by_scalar(x_unit[0], x_unit[1]) + halves(empty, x_unit[0]) + [(inter_a, A_PASS_ON_SCALAR, 0, 4)] + halves(empty, x_unit[1])
+        scalar += by_scalar(x_unit[2], x_unit[3]) + [(cast_lam,)] + by_scalar(x_unit[4])
+        scalar += halves(empty, x_unit[2], x_unit[3]) + by_scalar(x_unit[5], w_unit[0])
+        scalar += halves(empty, x_unit[4], x_unit[5]) + by_scalar(w_unit[0] + 1, x_unit[6])
+        scalar += halves(empty, *chunk(0)) + by_scalar(x_unit[7]) + [(cast_c,)]
+        scalar += halves(empty, x_unit[6], x_unit[7]) + [(park, 0, 0), (inter_b, 1)] + by_scalar(*chunk(1)) + [(park, 1, 0)]
+        scalar += halves(empty, *chunk(1)) + [(park, 2, 0), (scale_d, 0, 1), (park, 3, 0), (scale_d, 1, 1), (inter_b, 2), (scale_d, 2, 1), (inter_b, 0)]
+        for ci in range(2, CHUNKS):
+            scalar += halves(empty, *chunk(ci)) + [(scale_d, 3, ci - 1), (scale_d, 0, ci), (scale_d, 1, ci)]
+            if ci + 1 < CHUNKS:
+                scalar += [(inter_b, ci + 1)]
+            scalar += [(scale_d, 2, ci)]
+        scalar += [(scale_d,) + LAST]
+
+        turn_bank_users = [step for step in tensor if step[0] == turn]
+        adapter_bank_users = [step for step in tensor if step[0] in (down, up)]
+        base_bank_users = [step for step in tensor if step[0] == base]
         y_users = [step for step in scalar if step[0] == scale_d]
         b_users = [step for step in scalar if step[0] == inter_b]
-        last_reader = {turn: empty, mix_a: copy_a, scale_d: finish, inter_b: quant_b}
+        last_reader = {turn: empty, down: scale_h, scale_d: finish, inter_b: quant_b}
 
         def freed(users, step, depth):
             n = users.index(step) - depth
@@ -410,10 +405,6 @@ def tile_fp8_base_lora_d2_kernel(tc, x_bytes, x_scale, w_bytes, w_scale, a, lam,
             fn, args = users[n][0], users[n][1:]
             if fn == up:
                 return [(finish_parked if args in parked else scale_d,) + args]
-            if fn == warm:
-                return []
-            if fn == down:
-                return [(plane_h if (plane_h,) + args in scalar else scale_h,) + args]
             if fn == base:
                 return [(park if args in parked else finish,) + args]
             return [(last_reader[fn],) + args]
@@ -421,30 +412,15 @@ def tile_fp8_base_lora_d2_kernel(tc, x_bytes, x_scale, w_bytes, w_scale, a, lam,
         def needs(step):
             fn, args = step[0], step[1:]
             if fn == widen:
-                first = []
-                return first + (halves(turn, args[0] - WIDE_BUFS) if args[0] >= WIDE_BUFS else [])
+                return halves(turn, args[0] - WIDE_BUFS) if args[0] >= WIDE_BUFS else []
             if fn == turn:
                 return [(widen, args[0], 2 * args[1]), (widen, args[0], 2 * args[1] + 1)] + freed(turn_bank_users, step, TURN_BANKS)
             if fn == empty:
                 return [(turn,) + args] + ([(quant, args[0] - GROUP_BUFS)] if args[0] >= GROUP_BUFS else [])
             if fn == quant:
                 return halves(empty, args[0])
-            if fn == mix_a:
-                return freed(adapter_bank_users if args[0] % 2 == 0 else base_bank_users, step, 2)
-            if fn == copy_a:
-                return [(mix_a,) + args]
             if fn == quant_a:
-                if (mix_a, args[0], 0) not in tensor:
-                    return [s for s in vector + scalar if s[0] == inter_a and s[1] == args[0] and s[2] < args[2] and s[3] > args[1]]
-                if args[0] in PAIR_PASSES:
-                    return [(copy_a, args[0], half) for half in range(args[1] // 2, args[2] // 2)]
-                return halves(copy_a, args[0])
-            if fn == warm:
-                return [s for s in vector + scalar if s[:3] == (inter_a, args[0], 0)]
-            if fn == plane_h:
-                return [(down,) + args, (cast_lam,)]
-            if fn == inter_h:
-                return [(plane_h,) + args]
+                return [s for s in vector + scalar if s[:2] == (inter_a, args[0]) and s[2] <= args[1] < s[3]]
             if fn == inter_b:
                 return freed(b_users, step, B_BUFS)
             if fn == quant_b:
@@ -454,19 +430,16 @@ def tile_fp8_base_lora_d2_kernel(tc, x_bytes, x_scale, w_bytes, w_scale, a, lam,
             if fn == scale_h:
                 return [(down,) + args, (cast_lam,)]
             if fn == quant_h:
-                return [(inter_h if (plane_h, m) in scalar else scale_h, m) for m in (2 * args[0], 2 * args[0] + 1)]
+                return [(scale_h, 2 * args[0]), (scale_h, 2 * args[0] + 1)]
             if fn == up:
-                users, depth = (turn_bank_users, TURN_BANKS) if step in turn_bank_users else (adapter_bank_users, ADAPTER_BANKS)
-                return freed(users, step, depth) + [(quant_h, args[0]), (quant_b, args[1])]
+                return freed(adapter_bank_users, step, ADAPTER_BANKS) + [(quant_h, args[0]), (quant_b, args[1])]
             if fn == scale_d:
                 return [(up,) + args, (cast_c,)] + freed(y_users, step, Y_BUFS)
             if fn == base:
                 before = [(quant, s) for s in (x_unit[2 * args[0]], x_unit[2 * args[0] + 1]) + chunk(args[1])]
                 before += freed(base_bank_users, step, BASE_BANKS)
                 if args == BEFORE_LAST:
-                    before += freed(base_bank_users, step, 1)
-                if args == LAST:
-                    before += halves(empty, *chunk(CHUNKS - 1)) + [(finish_parked,) + s[1:] for s in turn_bank_users[-TURN_BANKS:][: len(ENDING)] if s[0] == up]
+                    before += halves(empty, *chunk(CHUNKS - 1))
                 return before
             if fn == park:
                 return [(base,) + args]
@@ -479,7 +452,6 @@ def tile_fp8_base_lora_d2_kernel(tc, x_bytes, x_scale, w_bytes, w_scale, a, lam,
         written = set()
         lists = [tensor, vector, scalar]
         while any(lists):
-            assert any(steps and all(need in written for need in needs(steps[0])) for steps in lists), [(steps[0], [n for n in needs(steps[0]) if n not in written]) for steps in lists if steps]
             ready = [steps for steps in lists if steps and all(need in written for need in needs(steps[0]))]
             step = ready[0][0]
             step[0](*step[1:])

@@ -336,7 +336,7 @@ def tile_fp8_base_lora_d2_kernel(tc, x_bytes, x_scale, w_bytes, w_scale, a, lam,
         for m in (2, 4):
             tensor += halves(turn, x_unit[m], x_unit[m + 1]) + [(down, m - 1), (down, m)]
         tensor += halves(turn, *chunk(0)) + [(down, 5)]
-        tensor += halves(turn, x_unit[6], x_unit[7]) + [(base, 0, 0), (down, 6), (base, 1, 0), (down, 7)]
+        tensor += halves(turn, x_unit[6], x_unit[7]) + [(base, 0, 0), (base, 1, 0), (down, 6), (down, 7)]
         for n in range(TURN_AFTER, len(products)):
             j, ci = products[n]
             if j == TURN_AFTER and ci + 1 < CHUNKS:
@@ -352,38 +352,37 @@ def tile_fp8_base_lora_d2_kernel(tc, x_bytes, x_scale, w_bytes, w_scale, a, lam,
             vector += [(inter_a, 3, t0, t0 + 2)] + [(quant_a, g, t0, t0 + 2) for g in (1, 2, 3)]
         vector += by_vector(x_unit[2], x_unit[3]) + [(quant, x_unit[1])]
 
-        def weave(results, pieces, counts):
-            steps, done = [], 0
-            for result, count in zip(results, counts):
-                steps += result + pieces[done : done + count]
-                done += count
+        def weave(results, pieces):
+            steps = []
+            for n, result in enumerate(results):
+                steps += result + pieces[n * len(pieces) // len(results) : (n + 1) * len(pieces) // len(results)]
             return steps
 
         results = [(scale_h, 0), (quant, x_unit[2]), (quant, x_unit[3]), (scale_h, 1), (scale_h, 2)]
         results += [(quant, x_unit[4]), (quant, x_unit[5]), (scale_h, 3), (scale_h, 4)]
         pieces = by_vector(x_unit[4], x_unit[5], *chunk(0), x_unit[6], x_unit[7])
-        vector += weave([[step] for step in results], pieces, (1, 2, 1, 1, 1, 2, 1, 1, 4))
+        vector += weave([[step] for step in results], pieces)
         results = [[(quant, w_unit[0]), (quant, w_unit[0] + 1), (scale_h, 5), (quant, x_unit[6])], [(quant, x_unit[7])]]
-        vector += weave(results, by_vector(*chunk(1)), (3, 4))
+        vector += weave(results, by_vector(*chunk(1)))
         results = [[(scale_h, 6), (quant_b, 1), (quant_h, 0)], [(scale_h, 7)], [(quant_h, 1), (quant, w_unit[1])]]
         results += [[(quant, w_unit[1] + 1), (quant_h, 2), (quant_h, 3)], [(finish, 0, 1)]]
-        vector += weave(results, by_vector(*chunk(2)), (1, 2, 1, 3, 1)) + [(quant_b, 2), (finish, 1, 1)]
+        vector += weave(results, by_vector(*chunk(2))) + [(quant_b, 2), (finish, 1, 1)]
         for ci in range(FIRST_UNPARK, CHUNKS):
             late_b = [(quant_b, 0)] if ci == FIRST_UNPARK else []
             results = [[], [(quant, w_unit[ci]), (finish, 2, ci - 1)] + late_b + [(quant, w_unit[ci] + 1)], [(finish, 3, ci - 1)]]
             results += [[(finish, 0, ci), (finish_parked,) + parked[ci - FIRST_UNPARK]]]
             if ci + 1 < CHUNKS:
-                vector += weave(results, by_vector(*chunk(ci + 1)), (2, 1, 2, 3)) + [(quant_b, ci + 1), (finish, 1, ci)]
+                vector += weave(results, by_vector(*chunk(ci + 1))) + [(quant_b, ci + 1), (finish, 1, ci)]
             else:
-                vector += weave(results, [], (0, 0, 0, 0)) + [(finish, j, ci) for j in range(1, PAIRS)]
+                vector += weave(results, []) + [(finish, j, ci) for j in range(1, PAIRS)]
 
         scalar = by_scalar(x_unit[0], x_unit[1]) + halves(empty, x_unit[0]) + [(inter_a, A_PASS_ON_SCALAR, 0, 4)] + halves(empty, x_unit[1])
         scalar += by_scalar(x_unit[2], x_unit[3]) + [(cast_lam,)] + by_scalar(x_unit[4])
         scalar += halves(empty, x_unit[2], x_unit[3]) + by_scalar(x_unit[5], w_unit[0])
         scalar += halves(empty, x_unit[4], x_unit[5]) + by_scalar(w_unit[0] + 1, x_unit[6])
         scalar += halves(empty, *chunk(0)) + by_scalar(x_unit[7]) + [(cast_c,)]
-        scalar += halves(empty, x_unit[6], x_unit[7]) + [(park, 0, 0), (inter_b, 1)] + by_scalar(*chunk(1)) + [(park, 1, 0)]
-        scalar += halves(empty, *chunk(1)) + [(park, 2, 0), (scale_d, 0, 1), (park, 3, 0), (scale_d, 1, 1), (inter_b, 2), (scale_d, 2, 1), (inter_b, 0)]
+        scalar += halves(empty, x_unit[6], x_unit[7]) + [(park, 0, 0), (park, 1, 0), (inter_b, 1)] + by_scalar(*chunk(1)) + [(inter_b, 0)]
+        scalar += halves(empty, *chunk(1)) + [(park, 2, 0), (scale_d, 0, 1), (park, 3, 0), (scale_d, 1, 1), (inter_b, 2), (scale_d, 2, 1)]
         for ci in range(2, CHUNKS):
             scalar += halves(empty, *chunk(ci)) + [(scale_d, 3, ci - 1), (scale_d, 0, ci), (scale_d, 1, ci)]
             if ci + 1 < CHUNKS:

@@ -30,9 +30,11 @@ BEFORE_LAST = (PAIRS - 2, CHUNKS - 1)
 UNIT_ORDER = "x0 x1 x2 x3 x4 x5 w0 x6 x7 w1 w2 w3 w4 w5"
 LOAD_ORDER = "xs x0 x1 a0 a1 a2 a3 x2 x3 lam x4 x5 ws w0 c x6 x7 w1 b1 b0 w2 b2 w3 b3 w4 b4 w5 b5"
 X_ON_SCALAR = (2, 1, 2, 2, 2, 2, 2, 1)
-W_ON_SCALAR = ((1, 2), (0, 1), (0, 0), (0, 0), (0, 0), (0, 0))
+W_ON_SCALAR = ((0, 2), (0, 1), (0, 0), (0, 0), (0, 0), (0, 0))
+SPLIT_PASSES = 2
+PAIRED_CHUNKS = 5
 A_PASS_ON_SCALAR = 1
-TURN_BANKS, ADAPTER_BANKS, BASE_BANKS = 4, 2, 2
+BANKS = 8
 WIDE_BUFS, GROUP_BUFS, A_BUFS, B_BUFS, Y_BUFS = 7, 3, 4, 2, 4
 TURN_AFTER = 2
 UP_AHEAD = 2
@@ -71,7 +73,7 @@ def tile_fp8_base_lora_d2_kernel(tc, x_bytes, x_scale, w_bytes, w_scale, a, lam,
         b_view = b.rearrange("(p j) n -> p j n", j=4)
         w_view = w_bytes.rearrange("(r p) k -> p r k", p=P)
         out_view = out.rearrange("(p m) n -> p m n", m=TILES)
-        x_raw, a_raw, b_raw, w_raw = {}, {}, {}, {}
+        x_raw, a_raw, b_raw, w_raw, w_blocks, w_rest = {}, {}, {}, {}, {}, {}
 
         ident = const.tile([P, P], F32, name="ident")
         make_identity(nc, ident[:])
@@ -84,7 +86,8 @@ def tile_fp8_base_lora_d2_kernel(tc, x_bytes, x_scale, w_bytes, w_scale, a, lam,
         xs = const.tile([P, TILES * K_BLOCKS], F32, name="xs")
         lam_b = const.tile([P, 4], BF16, name="lam_b")
         c_b = const.tile([P, TILES], BF16, name="c_b")
-        ws = const.tile([P, (N // P) * K_BLOCKS], F32, name="ws")
+        ws = const.tile([P, 2 * (CHUNKS - PAIRED_CHUNKS) * K_BLOCKS], F32, name="ws")
+        ws_paired = const.tile([P, (2 * PAIRED_CHUNKS - 1) * K_BLOCKS], F32, name="ws_paired")
         for what in LOAD_ORDER.split(" "):
             if what == "xs":
                 nc.sync.dma_start(out=xs[:], in_=x_scale.rearrange("(p m) j -> p (m j)", m=TILES))
@@ -93,7 +96,11 @@ def tile_fp8_base_lora_d2_kernel(tc, x_bytes, x_scale, w_bytes, w_scale, a, lam,
             elif what == "c":
                 nc.sync.dma_start(out=c_b[:], in_=c.rearrange("(p m) -> p m", m=TILES))
             elif what == "ws":
-                nc.sync.dma_start(out=ws[:], in_=w_scale.rearrange("i j -> (i j)").partition_broadcast(P))
+                last = w_scale[2 * PAIRED_CHUNKS :, :]
+                nc.sync.dma_start(out=ws[:], in_=last.rearrange("i j -> (i j)").partition_broadcast(P))
+                for h in range(2):
+                    mine = w_scale[h : h + 2 * PAIRED_CHUNKS - 1, :].rearrange("i j -> (i j)")
+                    nc.sync.dma_start(out=ws_paired[P // 2 * h : P // 2 * (h + 1), :], in_=mine.partition_broadcast(P // 2))
             elif what[0] == "x":
                 m = int(what[1:])
                 x_raw[m] = loads.tile([P, K], U8, name="x_b%d" % m, align_bytes=64)
@@ -101,16 +108,30 @@ def tile_fp8_base_lora_d2_kernel(tc, x_bytes, x_scale, w_bytes, w_scale, a, lam,
             elif what[0] == "a":
                 g = int(what[1:])
                 a_raw[g] = loads.tile([P, 4, R], BF16, name="a_raw%d" % g, align_bytes=64)
-                nc.sync.dma_start(out=a_raw[g][:], in_=a_view[g])
+                if g < SPLIT_PASSES:
+                    for u in range(2):
+                        nc.sync.dma_start(out=a_raw[g][:, 2 * u : 2 * u + 2, :], in_=a_view[g][:, u::2, :])
+                else:
+                    nc.sync.dma_start(out=a_raw[g][:], in_=a_view[g])
             elif what[0] == "b":
                 ci = int(what[1:])
                 b_raw[ci] = loads.tile([P, 4, WIDTH], BF16, name="b_raw%d" % ci, align_bytes=64)
                 nc.sync.dma_start(out=b_raw[ci][:], in_=b_view[:, :, WIDTH * ci : WIDTH * (ci + 1)])
             else:
                 ci = int(what[1:])
-                for row in range(2 * ci, 2 * ci + 2):
-                    w_raw[row] = loads.tile([P, K], U8, name="w_b%d" % row, align_bytes=64)
-                    nc.sync.dma_start(out=w_raw[row][:], in_=w_view[:, row, :])
+                if ci < PAIRED_CHUNKS:
+                    rows = w_bytes[WIDTH * ci : WIDTH * (ci + 1), :].rearrange("(p r) k -> p r k", r=2)
+                    w_blocks[ci] = loads.tile([P, 4 * SPLIT_PASSES, 2, P], U8, name="w_blocks%d" % ci, align_bytes=64)
+                    for r in range(2):
+                        nc.sync.dma_start(
+                            out=w_blocks[ci][:, :, r, :], in_=rows[:, r, : 512 * SPLIT_PASSES].rearrange("p (j k) -> p j k", k=P)
+                        )
+                    w_rest[ci] = loads.tile([P, 2, K - 512 * SPLIT_PASSES], U8, name="w_rest%d" % ci, align_bytes=64)
+                    nc.sync.dma_start(out=w_rest[ci][:], in_=rows[:, :, 512 * SPLIT_PASSES :])
+                else:
+                    for row in range(2 * ci, 2 * ci + 2):
+                        w_raw[row] = loads.tile([P, K], U8, name="w_b%d" % row, align_bytes=64)
+                        nc.sync.dma_start(out=w_raw[row][:], in_=w_view[:, row, :])
 
         lam_f = const.tile([P, 4], F32, name="lam_f")
         c_f = const.tile([P, TILES], F32, name="c_f")
@@ -133,27 +154,51 @@ def tile_fp8_base_lora_d2_kernel(tc, x_bytes, x_scale, w_bytes, w_scale, a, lam,
             if s not in wide:
                 wide[s] = ring(work, "wide", WIDE_BUFS, [P, PIECES, 2, P, 2], BF16)
             kind, row, g = units[s][i]
-            src = x_raw[row] if kind == "x" else w_raw[row]
-            scales = xs if kind == "x" else ws
+            paired = kind == "w" and row // 2 < PAIRED_CHUNKS
             for q in range(4):
-                k0 = 512 * g + P * q
-                j = K_BLOCKS * row + 4 * g + q
+                j = 4 * g + q
+                if paired and g < SPLIT_PASSES:
+                    if i % 2 == 0:
+                        nc.vector.tensor_scalar(
+                            out=wide[s][:, i : i + 2, :, 32 * q : 32 * (q + 1), :].rearrange("p r u w e -> p r (w e) u"),
+                            in0=w_blocks[row // 2][:, j, :, :].bitcast(FP8).rearrange("p r (m u) -> p r m u", u=2),
+                            scalar1=ws_paired[:, K_BLOCKS * row + j : K_BLOCKS * row + j + 1],
+                            scalar2=None,
+                            op0=MULT,
+                        )
+                    continue
+                if paired:
+                    k0 = P * (j - 4 * SPLIT_PASSES)
+                    at = K_BLOCKS * (row - row % 2) + j
+                    src, scale = w_rest[row // 2][:, row % 2, k0 : k0 + P], ws_paired[:, at : at + 1]
+                elif kind == "w":
+                    at = K_BLOCKS * (row - 2 * PAIRED_CHUNKS) + j
+                    src, scale = w_raw[row][:, P * j : P * (j + 1)], ws[:, at : at + 1]
+                else:
+                    src, scale = x_raw[row][:, P * j : P * (j + 1)], xs[:, K_BLOCKS * row + j : K_BLOCKS * row + j + 1]
+                words = wide[s][:, i, :, 32 * q : 32 * (q + 1), :]
                 if i >= PIECES - on_scalar[s]:
                     flat = wide[s][:, i, :, :, :].rearrange("p u w e -> p (u w e)")
-                    nc.scalar.activation(
-                        out=flat[:, P * q : P * (q + 1)], in_=src[:, k0 : k0 + P].bitcast(FP8), func=COPY, scale=scales[:, j : j + 1]
+                    nc.scalar.activation(out=flat[:, P * q : P * (q + 1)], in_=src.bitcast(FP8), func=COPY, scale=scale)
+                elif g < SPLIT_PASSES:
+                    nc.vector.tensor_scalar(
+                        out=words.rearrange("p u w e -> p (w e) u"),
+                        in0=src.bitcast(FP8).rearrange("p (m u) -> p m u", u=2),
+                        scalar1=scale,
+                        scalar2=None,
+                        op0=MULT,
                     )
                 else:
                     nc.vector.tensor_scalar(
-                        out=wide[s][:, i, :, 32 * q : 32 * (q + 1), :].rearrange("p u w e -> p w u e"),
-                        in0=src[:, k0 : k0 + P].bitcast(FP8).rearrange("p (w u e) -> p w u e", u=2, e=2),
-                        scalar1=scales[:, j : j + 1],
+                        out=words.rearrange("p u w e -> p w u e"),
+                        in0=src.bitcast(FP8).rearrange("p (w u e) -> p w u e", u=2, e=2),
+                        scalar1=scale,
                         scalar2=None,
                         op0=MULT,
                     )
 
         def turn(s, half):
-            bank = ring(psum, "xt", TURN_BANKS, [P, 4, P], F32)
+            bank = ring(psum, "bank", BANKS, [P, 4, P], F32)
             turned[s, half] = bank
             for i in range(2):
                 piece = wide[s][:, 2 * half + i, :, :, :]
@@ -214,7 +259,7 @@ def tile_fp8_base_lora_d2_kernel(tc, x_bytes, x_scale, w_bytes, w_scale, a, lam,
         h_banks, h_grouped, h_codes, h_scales = {}, {}, {}, {}
 
         def down(m):
-            h_banks[m] = ring(psum, "hd", ADAPTER_BANKS, [P, 4, P], F32)
+            h_banks[m] = ring(psum, "bank", BANKS, [P, 4, P], F32)
             for t in range(4):
                 for g in range(PASSES):
                     nc.tensor.matmul_mx(
@@ -246,7 +291,7 @@ def tile_fp8_base_lora_d2_kernel(tc, x_bytes, x_scale, w_bytes, w_scale, a, lam,
         y, base_parts, d_banks = {}, {}, {}
 
         def up(j, ci):
-            bank = ring(psum, "hd", ADAPTER_BANKS, [P, 2, WIDTH], F32)
+            bank = ring(psum, "bank", BANKS, [P, 2, WIDTH], F32)
             d_banks[j, ci] = bank
             for i in range(2):
                 nc.tensor.matmul_mx(
@@ -267,12 +312,12 @@ def tile_fp8_base_lora_d2_kernel(tc, x_bytes, x_scale, w_bytes, w_scale, a, lam,
 
         def base(j, ci):
             if (j, ci) == LAST:
-                parts = [(ring(psum, "xt", TURN_BANKS, [P, 2, WIDTH], F32), i, n0, n1) for i, n0, n1 in ENDING]
+                parts = [(ring(psum, "bank", BANKS, [P, 2, WIDTH], F32), i, n0, n1) for i, n0, n1 in ENDING]
             elif (j, ci) == BEFORE_LAST:
-                parts = [(ring(psum, "base", BASE_BANKS, [P, 2, WIDTH], F32), 0, 0, WIDTH)]
-                parts += [(ring(psum, "xt", TURN_BANKS, [P, 2, WIDTH], F32), 1, 0, WIDTH)]
+                parts = [(ring(psum, "bank", BANKS, [P, 2, WIDTH], F32), 0, 0, WIDTH)]
+                parts += [(ring(psum, "bank", BANKS, [P, 2, WIDTH], F32), 1, 0, WIDTH)]
             else:
-                shared = ring(psum, "base", BASE_BANKS, [P, 2, WIDTH], F32)
+                shared = ring(psum, "bank", BANKS, [P, 2, WIDTH], F32)
                 parts = [(shared, i, 0, WIDTH) for i in range(2)]
             base_parts[j, ci] = parts
             for bank, i, n0, n1 in parts:
@@ -289,9 +334,15 @@ def tile_fp8_base_lora_d2_kernel(tc, x_bytes, x_scale, w_bytes, w_scale, a, lam,
                         stop=(g == PASSES - 1),
                     )
 
+        def in_order(j, ci):
+            bank = base_parts[j, ci][0][0]
+            if ci < PAIRED_CHUNKS:
+                return bank[:].rearrange("p i (r c) -> p i c r", r=2)
+            return bank[:].rearrange("p i (c r) -> p i c r", r=2)
+
         def park(j, ci):
             y[j, ci] = const.tile([P, 2, WIDTH], F32, name="parked%d_%d" % (j, ci), align_bytes=64)
-            nc.scalar.copy(out=y[j, ci][:].rearrange("p i n -> p (i n)"), in_=base_parts[j, ci][0][0][:].rearrange("p i n -> p (i n)"))
+            nc.scalar.copy(out=y[j, ci][:].rearrange("p i (c r) -> p i c r", r=2), in_=in_order(j, ci))
 
         def finish_parked(j, ci):
             for i in range(2):
@@ -307,8 +358,8 @@ def tile_fp8_base_lora_d2_kernel(tc, x_bytes, x_scale, w_bytes, w_scale, a, lam,
                     nc.vector.tensor_tensor(out=y[j, ci][:, i, n0:n1], in0=bank[:, i, n0:n1], in1=y[j, ci][:, i, n0:n1], op=ADD)
                     nc.sync.dma_start(out=out_view[:, 2 * j + i, WIDTH * ci + n0 : WIDTH * ci + n1], in_=y[j, ci][:, i, n0:n1])
             else:
-                flat = y[j, ci][:].rearrange("p i n -> p (i n)")
-                nc.vector.tensor_tensor(out=flat, in0=base_parts[j, ci][0][0][:].rearrange("p i n -> p (i n)"), in1=flat, op=ADD)
+                flat = y[j, ci][:].rearrange("p i (c r) -> p i c r", r=2)
+                nc.vector.tensor_tensor(out=flat, in0=in_order(j, ci), in1=flat, op=ADD)
                 nc.sync.dma_start(out=out_view[:, 2 * j : 2 * j + 2, WIDTH * ci : WIDTH * (ci + 1)], in_=y[j, ci][:])
 
         def cast_lam():
@@ -390,30 +441,29 @@ def tile_fp8_base_lora_d2_kernel(tc, x_bytes, x_scale, w_bytes, w_scale, a, lam,
             scalar += [(scale_d, 2, ci)]
         scalar += [(scale_d,) + LAST]
 
-        turn_bank_users = [step for step in tensor if step[0] == turn]
-        adapter_bank_users = [step for step in tensor if step[0] in (down, up)]
-        base_bank_users = [step for step in tensor if step[0] == base]
+        parts_of = {(base,) + LAST: len(ENDING), (base,) + BEFORE_LAST: 2}
+        bank_users = [step for step in tensor for n in range(parts_of.get(step, 1))]
         y_users = [step for step in scalar if step[0] == scale_d]
         b_users = [step for step in scalar if step[0] == inter_b]
         last_reader = {turn: empty, down: scale_h, scale_d: finish, inter_b: quant_b}
 
-        def freed(users, step, depth):
-            n = users.index(step) - depth
-            if n < 0:
-                return []
-            fn, args = users[n][0], users[n][1:]
+        def reader(step):
+            fn, args = step[0], step[1:]
             if fn == up:
-                return [(finish_parked if args in parked else scale_d,) + args]
+                return (finish_parked if args in parked else scale_d,) + args
             if fn == base:
-                return [(park if args in parked else finish,) + args]
-            return [(last_reader[fn],) + args]
+                return (park if args in parked else finish,) + args
+            return (last_reader[fn],) + args
+
+        def freed(users, step, depth):
+            return [reader(users[n - depth]) for n in range(depth, len(users)) if users[n] == step]
 
         def needs(step):
             fn, args = step[0], step[1:]
             if fn == widen:
                 return halves(turn, args[0] - WIDE_BUFS) if args[0] >= WIDE_BUFS else []
             if fn == turn:
-                return [(widen, args[0], 2 * args[1]), (widen, args[0], 2 * args[1] + 1)] + freed(turn_bank_users, step, TURN_BANKS)
+                return [(widen, args[0], 2 * args[1]), (widen, args[0], 2 * args[1] + 1)] + freed(bank_users, step, BANKS)
             if fn == empty:
                 return [(turn,) + args] + ([(quant, args[0] - GROUP_BUFS)] if args[0] >= GROUP_BUFS else [])
             if fn == quant:
@@ -425,21 +475,18 @@ def tile_fp8_base_lora_d2_kernel(tc, x_bytes, x_scale, w_bytes, w_scale, a, lam,
             if fn == quant_b:
                 return [(inter_b,) + args]
             if fn == down:
-                return freed(adapter_bank_users, step, ADAPTER_BANKS) + [(quant, x_unit[args[0]])] + [s for s in vector if s[0] == quant_a]
+                return freed(bank_users, step, BANKS) + [(quant, x_unit[args[0]])] + [s for s in vector if s[0] == quant_a]
             if fn == scale_h:
                 return [(down,) + args, (cast_lam,)]
             if fn == quant_h:
                 return [(scale_h, 2 * args[0]), (scale_h, 2 * args[0] + 1)]
             if fn == up:
-                return freed(adapter_bank_users, step, ADAPTER_BANKS) + [(quant_h, args[0]), (quant_b, args[1])]
+                return freed(bank_users, step, BANKS) + [(quant_h, args[0]), (quant_b, args[1])]
             if fn == scale_d:
                 return [(up,) + args, (cast_c,)] + freed(y_users, step, Y_BUFS)
             if fn == base:
                 before = [(quant, s) for s in (x_unit[2 * args[0]], x_unit[2 * args[0] + 1]) + chunk(args[1])]
-                before += freed(base_bank_users, step, BASE_BANKS)
-                if args == BEFORE_LAST:
-                    before += halves(empty, *chunk(CHUNKS - 1))
-                return before
+                return before + freed(bank_users, step, BANKS)
             if fn == park:
                 return [(base,) + args]
             if fn == finish_parked:

@@ -23,22 +23,20 @@ PASSES = K // 512
 K_BLOCKS = K // P
 WIDTH = 256
 CHUNKS = N // WIDTH
+SPAN = 2 * WIDTH
+SPANS = N // SPAN
 PIECES = 4
-LAST = (PAIRS - 1, CHUNKS - 1)
-BEFORE_LAST = (PAIRS - 2, CHUNKS - 1)
 
-UNIT_ORDER = "x0 x1 x2 x3 x4 x5 w0 x6 x7 w1 w2 w3 w4 w5"
-LOAD_ORDER = "xs x0 x1 a0 a1 a2 a3 x2 x3 lam x4 x5 ws w0 c x6 x7 w1 b1 b0 w2 b2 w3 b3 w4 b4 w5 b5"
-X_ON_SCALAR = (2, 1, 2, 2, 2, 2, 2, 1)
-W_ON_SCALAR = ((0, 2), (0, 1), (0, 0), (0, 0), (0, 0), (0, 0))
-SPLIT_PASSES = 2
-PAIRED_CHUNKS = 5
-A_PASS_ON_SCALAR = 1
+ORDER = "x0 x1 w0 x2 x3 w1 w2 w3 w4 w5"
+LOAD_ORDER = "xs x0 a0 a1 a2 a3 x1 ws w0 lam x2 x3 c w1 b0 w2 w3 b1 w4 b2 w5"
+RUNS = (2, 1, 1, 1, 1, 1, 1, 2, 2, 2, 2, 2, 2)
+ON_SCALAR = (2, 1, 4, 0, 0, 0, 0)
 BANKS = 8
-WIDE_BUFS, GROUP_BUFS, A_BUFS, B_BUFS, Y_BUFS = 7, 3, 4, 2, 4
-TURN_AFTER = 2
-UP_AHEAD = 2
-FIRST_UNPARK = 2
+UPS = ((1, 1, 1, 1), (1, 2, 3, 0), (2, 4, 4, 1), (1, 1, 1, 0))
+LEAD1, LEAD2, HELD = 3, 5, 1
+AHEAD = 1
+FILL = (0, 0, 0, 0, 0, 0, 1, 0, 3, 4, 4, 0, 0)
+WIDE_BUFS, GROUP_BUFS, INT_BUFS, W_CODE_BUFS, H_BUFS = 6, 3, 4, 6, 2
 SCALE_PAD = 64
 SCALE_ROW = {"w": 4, "b": 4, "x": 8, "h": 8, "a": 12}
 ENDING = ((0, 0, 256), (1, 0, 128), (1, 128, 256))
@@ -73,7 +71,7 @@ def tile_fp8_base_lora_d2_kernel(tc, x_bytes, x_scale, w_bytes, w_scale, a, lam,
         b_view = b.rearrange("(p j) n -> p j n", j=4)
         w_view = w_bytes.rearrange("(r p) k -> p r k", p=P)
         out_view = out.rearrange("(p m) n -> p m n", m=TILES)
-        x_raw, a_raw, b_raw, w_raw, w_blocks, w_rest = {}, {}, {}, {}, {}, {}
+        raw, a_raw, b_raw = {}, {}, {}
 
         ident = const.tile([P, P], F32, name="ident")
         make_identity(nc, ident[:])
@@ -86,8 +84,7 @@ def tile_fp8_base_lora_d2_kernel(tc, x_bytes, x_scale, w_bytes, w_scale, a, lam,
         xs = const.tile([P, TILES * K_BLOCKS], F32, name="xs")
         lam_b = const.tile([P, 4], BF16, name="lam_b")
         c_b = const.tile([P, TILES], BF16, name="c_b")
-        ws = const.tile([P, 2 * (CHUNKS - PAIRED_CHUNKS) * K_BLOCKS], F32, name="ws")
-        ws_paired = const.tile([P, (2 * PAIRED_CHUNKS - 1) * K_BLOCKS], F32, name="ws_paired")
+        ws = const.tile([P, 2 * CHUNKS * K_BLOCKS], F32, name="ws")
         for what in LOAD_ORDER.split(" "):
             if what == "xs":
                 nc.sync.dma_start(out=xs[:], in_=x_scale.rearrange("(p m) j -> p (m j)", m=TILES))
@@ -96,141 +93,98 @@ def tile_fp8_base_lora_d2_kernel(tc, x_bytes, x_scale, w_bytes, w_scale, a, lam,
             elif what == "c":
                 nc.sync.dma_start(out=c_b[:], in_=c.rearrange("(p m) -> p m", m=TILES))
             elif what == "ws":
-                last = w_scale[2 * PAIRED_CHUNKS :, :]
-                nc.sync.dma_start(out=ws[:], in_=last.rearrange("i j -> (i j)").partition_broadcast(P))
-                for h in range(2):
-                    mine = w_scale[h : h + 2 * PAIRED_CHUNKS - 1, :].rearrange("i j -> (i j)")
-                    nc.sync.dma_start(out=ws_paired[P // 2 * h : P // 2 * (h + 1), :], in_=mine.partition_broadcast(P // 2))
-            elif what[0] == "x":
-                m = int(what[1:])
-                x_raw[m] = loads.tile([P, K], U8, name="x_b%d" % m, align_bytes=64)
-                nc.sync.dma_start(out=x_raw[m][:], in_=x_view[:, m, :])
+                nc.sync.dma_start(out=ws[:], in_=w_scale.rearrange("i j -> (i j)").partition_broadcast(P))
             elif what[0] == "a":
                 g = int(what[1:])
                 a_raw[g] = loads.tile([P, 4, R], BF16, name="a_raw%d" % g, align_bytes=64)
-                if g < SPLIT_PASSES:
-                    for u in range(2):
-                        nc.sync.dma_start(out=a_raw[g][:, 2 * u : 2 * u + 2, :], in_=a_view[g][:, u::2, :])
-                else:
-                    nc.sync.dma_start(out=a_raw[g][:], in_=a_view[g])
+                nc.sync.dma_start(out=a_raw[g][:], in_=a_view[g])
             elif what[0] == "b":
-                ci = int(what[1:])
-                b_raw[ci] = loads.tile([P, 4, WIDTH], BF16, name="b_raw%d" % ci, align_bytes=64)
-                nc.sync.dma_start(out=b_raw[ci][:], in_=b_view[:, :, WIDTH * ci : WIDTH * (ci + 1)])
+                s = int(what[1:])
+                b_raw[s] = loads.tile([P, 4, SPAN], BF16, name="b_raw%d" % s, align_bytes=64)
+                nc.sync.dma_start(out=b_raw[s][:], in_=b_view[:, :, SPAN * s : SPAN * (s + 1)])
             else:
-                ci = int(what[1:])
-                if ci < PAIRED_CHUNKS:
-                    rows = w_bytes[WIDTH * ci : WIDTH * (ci + 1), :].rearrange("(p r) k -> p r k", r=2)
-                    w_blocks[ci] = loads.tile([P, 4 * SPLIT_PASSES, 2, P], U8, name="w_blocks%d" % ci, align_bytes=64)
-                    for r in range(2):
-                        nc.sync.dma_start(
-                            out=w_blocks[ci][:, :, r, :], in_=rows[:, r, : 512 * SPLIT_PASSES].rearrange("p (j k) -> p j k", k=P)
-                        )
-                    w_rest[ci] = loads.tile([P, 2, K - 512 * SPLIT_PASSES], U8, name="w_rest%d" % ci, align_bytes=64)
-                    nc.sync.dma_start(out=w_rest[ci][:], in_=rows[:, :, 512 * SPLIT_PASSES :])
+                idx = int(what[1:])
+                rows = (x_view if what[0] == "x" else w_view)[:, 2 * idx : 2 * idx + 2, :]
+                if what == "x0":
+                    for h in range(2):
+                        raw[what, h] = loads.tile([P, 2, K // 2], U8, name="%s_bytes%d" % (what, h), align_bytes=64)
+                        nc.sync.dma_start(out=raw[what, h][:], in_=rows[:, :, K // 2 * h : K // 2 * (h + 1)])
                 else:
-                    for row in range(2 * ci, 2 * ci + 2):
-                        w_raw[row] = loads.tile([P, K], U8, name="w_b%d" % row, align_bytes=64)
-                        nc.sync.dma_start(out=w_raw[row][:], in_=w_view[:, row, :])
+                    both = loads.tile([P, 2, K], U8, name="%s_bytes" % what, align_bytes=64)
+                    nc.sync.dma_start(out=both[:], in_=rows)
+                    for h in range(2):
+                        raw[what, h] = both[:, :, K // 2 * h : K // 2 * (h + 1)]
 
         lam_f = const.tile([P, 4], F32, name="lam_f")
         c_f = const.tile([P, TILES], F32, name="c_f")
 
-        units, on_scalar, x_unit, w_unit = [], [], {}, {}
-        for what in UNIT_ORDER.split(" "):
-            idx = int(what[1:])
-            if what[0] == "x":
-                x_unit[idx] = len(units)
-                units.append([("x", idx, g) for g in range(PASSES)])
-                on_scalar.append(X_ON_SCALAR[idx])
-            else:
-                w_unit[idx] = len(units)
-                for half in range(2):
-                    units.append([("w", 2 * idx + r, g) for g in (2 * half, 2 * half + 1) for r in range(2)])
-                    on_scalar.append(W_ON_SCALAR[idx][half])
+        units = [(what, h) for what in ORDER.split(" ") for h in range(2)]
+        on_scalar = {unit: (ON_SCALAR[s] if s < len(ON_SCALAR) else 0) for s, unit in enumerate(units)}
         wide, turned, grouped, unit_codes, unit_scales = {}, {}, {}, {}, {}
 
-        def widen(s, i):
-            if s not in wide:
-                wide[s] = ring(work, "wide", WIDE_BUFS, [P, PIECES, 2, P, 2], BF16)
-            kind, row, g = units[s][i]
-            paired = kind == "w" and row // 2 < PAIRED_CHUNKS
+        def widen(unit, i):
+            if unit not in wide:
+                wide[unit] = work.tile([P, PIECES, 2, P, 2], BF16, name="wide%d" % (units.index(unit) % WIDE_BUFS), align_bytes=64)
+            what, h = unit
+            g, r = divmod(i, 2)
+            row = 2 * int(what[1:]) + r
             for q in range(4):
                 j = 4 * g + q
-                if paired and g < SPLIT_PASSES:
-                    if i % 2 == 0:
-                        nc.vector.tensor_scalar(
-                            out=wide[s][:, i : i + 2, :, 32 * q : 32 * (q + 1), :].rearrange("p r u w e -> p r (w e) u"),
-                            in0=w_blocks[row // 2][:, j, :, :].bitcast(FP8).rearrange("p r (m u) -> p r m u", u=2),
-                            scalar1=ws_paired[:, K_BLOCKS * row + j : K_BLOCKS * row + j + 1],
-                            scalar2=None,
-                            op0=MULT,
-                        )
-                    continue
-                if paired:
-                    k0 = P * (j - 4 * SPLIT_PASSES)
-                    at = K_BLOCKS * (row - row % 2) + j
-                    src, scale = w_rest[row // 2][:, row % 2, k0 : k0 + P], ws_paired[:, at : at + 1]
-                elif kind == "w":
-                    at = K_BLOCKS * (row - 2 * PAIRED_CHUNKS) + j
-                    src, scale = w_raw[row][:, P * j : P * (j + 1)], ws[:, at : at + 1]
-                else:
-                    src, scale = x_raw[row][:, P * j : P * (j + 1)], xs[:, K_BLOCKS * row + j : K_BLOCKS * row + j + 1]
-                words = wide[s][:, i, :, 32 * q : 32 * (q + 1), :]
-                if i >= PIECES - on_scalar[s]:
-                    flat = wide[s][:, i, :, :, :].rearrange("p u w e -> p (u w e)")
-                    nc.scalar.activation(out=flat[:, P * q : P * (q + 1)], in_=src.bitcast(FP8), func=COPY, scale=scale)
-                elif g < SPLIT_PASSES:
-                    nc.vector.tensor_scalar(
-                        out=words.rearrange("p u w e -> p (w e) u"),
-                        in0=src.bitcast(FP8).rearrange("p (m u) -> p m u", u=2),
-                        scalar1=scale,
-                        scalar2=None,
-                        op0=MULT,
-                    )
+                src = raw[unit][:, r, P * j : P * (j + 1)].bitcast(FP8)
+                at = K_BLOCKS * row + K_BLOCKS // 2 * h + j
+                scale = (xs if what[0] == "x" else ws)[:, at : at + 1]
+                if i >= PIECES - on_scalar[unit]:
+                    flat = wide[unit][:, i, :, :, :].rearrange("p u w e -> p (u w e)")
+                    nc.scalar.activation(out=flat[:, P * q : P * (q + 1)], in_=src, func=COPY, scale=scale)
                 else:
                     nc.vector.tensor_scalar(
-                        out=words.rearrange("p u w e -> p w u e"),
-                        in0=src.bitcast(FP8).rearrange("p (w u e) -> p w u e", u=2, e=2),
+                        out=wide[unit][:, i, :, 32 * q : 32 * (q + 1), :].rearrange("p u w e -> p w u e"),
+                        in0=src.rearrange("p (w u e) -> p w u e", u=2, e=2),
                         scalar1=scale,
                         scalar2=None,
                         op0=MULT,
                     )
 
-        def turn(s, half):
+        def turn(unit, half):
             bank = ring(psum, "bank", BANKS, [P, 4, P], F32)
-            turned[s, half] = bank
+            turned[unit, half] = bank
             for i in range(2):
-                piece = wide[s][:, 2 * half + i, :, :, :]
+                piece = wide[unit][:, 2 * half + i, :, :, :]
                 for u in range(2):
-                    if 2 * half + i >= PIECES - on_scalar[s]:
+                    if 2 * half + i >= PIECES - on_scalar[unit]:
                         words = piece.rearrange("p u w e -> p (u w e)").bitcast(F32)[:, u::2]
                     else:
                         words = piece[:, u, :, :].rearrange("p w e -> p (w e)").bitcast(F32)
                     nc.tensor.transpose(bank[:, 2 * i + u, :], words, ident[:])
 
-        def empty(s, half):
+        def empty(unit, half):
             if half == 0:
-                grouped[s] = ring(work, "grouped", GROUP_BUFS, [P, PIECES, P, 4], BF16)
-            words = grouped[s][:, 2 * half : 2 * half + 2, :, :].rearrange("p i w t -> p (i w t)").bitcast(F32)
+                grouped[unit] = ring(work, "grouped", GROUP_BUFS, [P, PIECES, P, 4], BF16)
+            words = grouped[unit][:, 2 * half : 2 * half + 2, :, :].rearrange("p i w t -> p (i w t)").bitcast(F32)
             nc.scalar.copy(
                 out=words.rearrange("p (i w u) -> p i w u", i=2, u=2),
-                in_=turned[s, half][:].rearrange("p (i u) w -> p i w u", u=2),
+                in_=turned[unit, half][:].rearrange("p (i u) w -> p i w u", u=2),
             )
 
-        def quant(s):
-            unit_codes[s], unit_scales[s] = mx_operand(units[s][0][0], s, PIECES * P)
+        w_units = [unit for unit in units if unit[0][0] == "w"]
+
+        def quant(unit):
+            kind = unit[0][0]
+            index = w_units.index(unit) % W_CODE_BUFS if kind == "w" else units.index(unit)
+            unit_codes[unit], unit_scales[unit] = mx_operand(kind, index, PIECES * P)
             nc.vector.quantize_mx(
-                out=unit_codes[s][:].bitcast(FP8X4), scales=unit_scales[s], in_=grouped[s][:].rearrange("p i w t -> p (i w t)")
+                out=unit_codes[unit][:].bitcast(FP8X4),
+                scales=unit_scales[unit],
+                in_=grouped[unit][:].rearrange("p i w t -> p (i w t)"),
             )
 
         a_int, a_codes, a_scales = {}, {}, {}
         b_int, b_codes, b_scales = {}, {}, {}
 
-        def inter_a(g, t0, t1):
-            if t0 == 0:
-                a_int[g] = ring(work, "ab_int", A_BUFS, [P, 4, P, 4], BF16)
-            (nc.scalar.copy if g == A_PASS_ON_SCALAR else nc.vector.tensor_copy)(
+        def inter_a(g, t0, t1, on):
+            if g not in a_int:
+                a_int[g] = ring(work, "ab_int", INT_BUFS, [P, 4, P, 4], BF16)
+            (nc.scalar.copy if on == "s" else nc.vector.tensor_copy)(
                 out=a_int[g][:, t0:t1, :, :].rearrange("p t (q m) j -> p q t m j", m=2),
                 in_=a_raw[g][:].rearrange("p j (q m t) -> p q t m j", m=2, t=4)[:, :, t0:t1, :, :],
             )
@@ -244,123 +198,136 @@ def tile_fp8_base_lora_d2_kernel(tc, x_bytes, x_scale, w_bytes, w_scale, a, lam,
                 in_=a_int[g][:, t0:t1, :, :].rearrange("p t m j -> p (t m j)"),
             )
 
-        def inter_b(ci):
-            b_int[ci] = ring(work, "b_int", B_BUFS, [P, WIDTH, 4], BF16)
+        def inter_b(s, part):
+            if part == 0:
+                b_int[s] = ring(work, "ab_int", INT_BUFS, [P, SPAN, 4], BF16)
+            cols = slice(P * part, P * (part + 1))
             nc.scalar.copy(
-                out=b_int[ci][:].rearrange("p (n i) j -> p n j i", i=4), in_=b_raw[ci][:].rearrange("p j (n i) -> p n j i", i=4)
+                out=b_int[s][:, cols, :].rearrange("p (n i) j -> p n j i", i=4),
+                in_=b_raw[s][:, :, cols].rearrange("p j (n i) -> p n j i", i=4),
             )
 
-        def quant_b(ci):
-            b_codes[ci], b_scales[ci] = mx_operand("b", ci, WIDTH)
+        def quant_b(s):
+            b_codes[s], b_scales[s] = mx_operand("b", s, SPAN)
             nc.vector.quantize_mx(
-                out=b_codes[ci][:].bitcast(FP8X4), scales=b_scales[ci], in_=b_int[ci][:].rearrange("p n j -> p (n j)")
+                out=b_codes[s][:].bitcast(FP8X4), scales=b_scales[s], in_=b_int[s][:].rearrange("p n j -> p (n j)")
             )
 
-        h_banks, h_grouped, h_codes, h_scales = {}, {}, {}, {}
+        h_banks, h_rows, h_int, h_codes, h_scales = {}, {}, {}, {}, {}
 
-        def down(m):
-            h_banks[m] = ring(psum, "bank", BANKS, [P, 4, P], F32)
-            for t in range(4):
-                for g in range(PASSES):
+        def down(j, side, h):
+            if h == 0:
+                h_banks[j, side] = ring(psum, "bank", BANKS, [P, 2, 2 * P], F32)
+            unit = ("x%d" % j, h)
+            for g in range(2):
+                for i in range(2):
+                    t = 2 * side + i
                     nc.tensor.matmul_mx(
-                        out=h_banks[m][:, t, :],
-                        lhsT=a_codes[g][:, P * t : P * (t + 1)].bitcast(FP8X4),
-                        lhsT_scale=a_scales[g][:, P * t : P * (t + 1)],
-                        rhs=unit_codes[x_unit[m]][:, P * g : P * (g + 1)].bitcast(FP8X4),
-                        rhs_scale=unit_scales[x_unit[m]][:, P * g : P * (g + 1)],
-                        start=(g == 0),
-                        stop=(g == PASSES - 1),
+                        out=h_banks[j, side][:, i, :],
+                        lhsT=a_codes[2 * h + g][:, P * t : P * (t + 1)].bitcast(FP8X4),
+                        lhsT_scale=a_scales[2 * h + g][:, P * t : P * (t + 1)],
+                        rhs=unit_codes[unit][:, 2 * P * g : 2 * P * (g + 1)].bitcast(FP8X4),
+                        rhs_scale=unit_scales[unit][:, 2 * P * g : 2 * P * (g + 1)],
+                        start=(h == 0 and g == 0 and i == 0),
+                        stop=(h == 1 and g == 1 and i == 1),
                     )
 
-        def scale_h(m):
-            if m % 2 == 0:
-                h_grouped[m // 2] = const.tile([P, 2, P, 4], BF16, name="h_grouped%d" % (m // 2), align_bytes=64)
-            nc.vector.tensor_tensor(
-                out=h_grouped[m // 2][:, m % 2, :, :],
-                in0=h_banks[m][:].rearrange("p t w -> p w t"),
-                in1=lam_f[:].unsqueeze(1).to_broadcast([P, P, 4]),
-                op=MULT,
+        def scale_h(j, side):
+            if side == 0:
+                h_rows[j] = const.tile([P, 4, 2 * P], BF16, name="h_rows%d" % j, align_bytes=64)
+            for i in range(2):
+                t = 2 * side + i
+                nc.scalar.activation(out=h_rows[j][:, t, :], in_=h_banks[j, side][:, i, :], func=COPY, scale=lam_f[:, t : t + 1])
+
+        def inter_h(j):
+            h_int[j] = ring(work, "h_int", H_BUFS, [P, 2 * P, 4], BF16)
+            nc.vector.tensor_copy(
+                out=h_int[j][:].rearrange("p (n i) t -> p n t i", i=4), in_=h_rows[j][:].rearrange("p t (n i) -> p n t i", i=4)
             )
 
         def quant_h(j):
             h_codes[j], h_scales[j] = mx_operand("h", j, 2 * P)
             nc.vector.quantize_mx(
-                out=h_codes[j][:].bitcast(FP8X4), scales=h_scales[j], in_=h_grouped[j][:].rearrange("p i w t -> p (i w t)")
+                out=h_codes[j][:].bitcast(FP8X4), scales=h_scales[j], in_=h_int[j][:].rearrange("p w t -> p (w t)")
             )
 
         y, base_parts, d_banks = {}, {}, {}
 
-        def up(j, ci):
-            bank = ring(psum, "bank", BANKS, [P, 2, WIDTH], F32)
-            d_banks[j, ci] = bank
-            for i in range(2):
-                nc.tensor.matmul_mx(
-                    out=bank[:, i, :],
-                    lhsT=h_codes[j][:, P * i : P * (i + 1)].bitcast(FP8X4),
-                    lhsT_scale=h_scales[j][:, P * i : P * (i + 1)],
-                    rhs=b_codes[ci][:].bitcast(FP8X4),
-                    rhs_scale=b_scales[ci],
-                    start=True,
-                    stop=True,
-                )
+        def result(j, s):
+            if (j, s) not in y:
+                y[j, s] = work.tile([P, 2, SPAN], F32, name="y%d_%d" % (j, s % 2), align_bytes=64)
+            return y[j, s]
 
-        def scale_d(j, ci):
-            y[j, ci] = ring(work, "y", Y_BUFS, [P, 2, WIDTH], F32)
-            for i in range(2):
-                m = 2 * j + i
-                nc.scalar.activation(out=y[j, ci][:, i, :], in_=d_banks[j, ci][:, i, :], func=COPY, scale=c_f[:, m : m + 1])
+        def up(m, s):
+            d_banks[m, s] = ring(psum, "bank", BANKS, [P, SPAN], F32)
+            j, i = divmod(m, 2)
+            nc.tensor.matmul_mx(
+                out=d_banks[m, s][:],
+                lhsT=h_codes[j][:, P * i : P * (i + 1)].bitcast(FP8X4),
+                lhsT_scale=h_scales[j][:, P * i : P * (i + 1)],
+                rhs=b_codes[s][:].bitcast(FP8X4),
+                rhs_scale=b_scales[s],
+                start=True,
+                stop=True,
+            )
 
-        def base(j, ci):
-            if (j, ci) == LAST:
-                parts = [(ring(psum, "bank", BANKS, [P, 2, WIDTH], F32), i, n0, n1) for i, n0, n1 in ENDING]
-            elif (j, ci) == BEFORE_LAST:
-                parts = [(ring(psum, "bank", BANKS, [P, 2, WIDTH], F32), 0, 0, WIDTH)]
-                parts += [(ring(psum, "bank", BANKS, [P, 2, WIDTH], F32), 1, 0, WIDTH)]
-            else:
-                shared = ring(psum, "bank", BANKS, [P, 2, WIDTH], F32)
-                parts = [(shared, i, 0, WIDTH) for i in range(2)]
-            base_parts[j, ci] = parts
-            for bank, i, n0, n1 in parts:
-                tokens = x_unit[2 * j + i]
-                for g in range(PASSES):
-                    rows, c0 = w_unit[ci] + g // 2, WIDTH * (g % 2)
+        def base(j, ci, h):
+            if h == 0:
+                base_parts[j, ci] = ring(psum, "bank", BANKS, [P, 2, WIDTH], F32)
+            tokens, rows = ("x%d" % j, h), ("w%d" % ci, h)
+            for g in range(2):
+                for i in range(2):
+                    at = 2 * P * g + P * i
                     nc.tensor.matmul_mx(
-                        out=bank[:, i, n0:n1],
-                        lhsT=unit_codes[tokens][:, P * g : P * (g + 1)].bitcast(FP8X4),
-                        lhsT_scale=unit_scales[tokens][:, P * g : P * (g + 1)],
-                        rhs=unit_codes[rows][:, c0 + n0 : c0 + n1].bitcast(FP8X4),
-                        rhs_scale=unit_scales[rows][:, c0 + n0 : c0 + n1],
-                        start=(g == 0),
-                        stop=(g == PASSES - 1),
+                        out=base_parts[j, ci][:, i, :],
+                        lhsT=unit_codes[tokens][:, at : at + P].bitcast(FP8X4),
+                        lhsT_scale=unit_scales[tokens][:, at : at + P],
+                        rhs=unit_codes[rows][:, WIDTH * g : WIDTH * (g + 1)].bitcast(FP8X4),
+                        rhs_scale=unit_scales[rows][:, WIDTH * g : WIDTH * (g + 1)],
+                        start=(h == 0 and g == 0 and i == 0),
+                        stop=(h == 1 and g == 1 and i == 1),
                     )
 
-        def in_order(j, ci):
-            bank = base_parts[j, ci][0][0]
-            if ci < PAIRED_CHUNKS:
-                return bank[:].rearrange("p i (r c) -> p i c r", r=2)
-            return bank[:].rearrange("p i (c r) -> p i c r", r=2)
+        def base_part(j, i, n0, n1):
+            bank = ring(psum, "bank", BANKS, [P, WIDTH], F32)
+            base_parts[j, i, n0] = bank
+            for g in range(PASSES):
+                tokens, rows = ("x%d" % j, g // 2), ("w%d" % (CHUNKS - 1), g // 2)
+                at, c0 = 2 * P * (g % 2) + P * i, WIDTH * (g % 2)
+                nc.tensor.matmul_mx(
+                    out=bank[:, n0:n1],
+                    lhsT=unit_codes[tokens][:, at : at + P].bitcast(FP8X4),
+                    lhsT_scale=unit_scales[tokens][:, at : at + P],
+                    rhs=unit_codes[rows][:, c0 + n0 : c0 + n1].bitcast(FP8X4),
+                    rhs_scale=unit_scales[rows][:, c0 + n0 : c0 + n1],
+                    start=(g == 0),
+                    stop=(g == PASSES - 1),
+                )
 
         def park(j, ci):
-            y[j, ci] = const.tile([P, 2, WIDTH], F32, name="parked%d_%d" % (j, ci), align_bytes=64)
-            nc.scalar.copy(out=y[j, ci][:].rearrange("p i (c r) -> p i c r", r=2), in_=in_order(j, ci))
+            n0 = WIDTH * (ci % 2)
+            nc.scalar.copy(out=result(j, ci // 2)[:, :, n0 : n0 + WIDTH], in_=base_parts[j, ci][:])
 
-        def finish_parked(j, ci):
-            for i in range(2):
-                m = 2 * j + i
-                nc.vector.scalar_tensor_tensor(
-                    out=y[j, ci][:, i, :], in0=d_banks[j, ci][:, i, :], scalar=c_f[:, m : m + 1], in1=y[j, ci][:, i, :], op0=MULT, op1=ADD
-                )
-            nc.sync.dma_start(out=out_view[:, 2 * j : 2 * j + 2, WIDTH * ci : WIDTH * (ci + 1)], in_=y[j, ci][:])
+        def finish(m, s):
+            j, i = divmod(m, 2)
+            mine = y[j, s][:, i, :]
+            nc.vector.scalar_tensor_tensor(out=mine, in0=d_banks[m, s][:], scalar=c_f[:, m : m + 1], in1=mine, op0=MULT, op1=ADD)
+            nc.sync.dma_start(out=out_view[:, m, SPAN * s : SPAN * (s + 1)], in_=mine)
 
-        def finish(j, ci):
-            if (j, ci) in (BEFORE_LAST, LAST):
-                for bank, i, n0, n1 in base_parts[j, ci]:
-                    nc.vector.tensor_tensor(out=y[j, ci][:, i, n0:n1], in0=bank[:, i, n0:n1], in1=y[j, ci][:, i, n0:n1], op=ADD)
-                    nc.sync.dma_start(out=out_view[:, 2 * j + i, WIDTH * ci + n0 : WIDTH * ci + n1], in_=y[j, ci][:, i, n0:n1])
-            else:
-                flat = y[j, ci][:].rearrange("p i (c r) -> p i c r", r=2)
-                nc.vector.tensor_tensor(out=flat, in0=in_order(j, ci), in1=flat, op=ADD)
-                nc.sync.dma_start(out=out_view[:, 2 * j : 2 * j + 2, WIDTH * ci : WIDTH * (ci + 1)], in_=y[j, ci][:])
+        def scale_d(m, s):
+            j, i = divmod(m, 2)
+            nc.scalar.activation(out=result(j, s)[:, i, :], in_=d_banks[m, s][:], func=COPY, scale=c_f[:, m : m + 1])
+
+        def add(j, ci):
+            n0 = WIDTH * (ci % 2)
+            mine = y[j, ci // 2][:, :, n0 : n0 + WIDTH]
+            nc.vector.tensor_tensor(out=mine, in0=base_parts[j, ci][:], in1=mine, op=ADD)
+            nc.sync.dma_start(out=out_view[:, 2 * j : 2 * j + 2, WIDTH * ci : WIDTH * (ci + 1)], in_=mine)
+
+        def add_part(j, i, n0, n1):
+            mine = y[j, SPANS - 1][:, i, WIDTH + n0 : WIDTH + n1]
+            nc.vector.tensor_tensor(out=mine, in0=base_parts[j, i, n0][:, n0:n1], in1=mine, op=ADD)
+            nc.sync.dma_start(out=out_view[:, 2 * j + i, N - WIDTH + n0 : N - WIDTH + n1], in_=mine)
 
         def cast_lam():
             nc.scalar.activation(out=lam_f[:], in_=lam_b[:], func=COPY)
@@ -368,131 +335,170 @@ def tile_fp8_base_lora_d2_kernel(tc, x_bytes, x_scale, w_bytes, w_scale, a, lam,
         def cast_c():
             nc.scalar.activation(out=c_f[:], in_=c_b[:], func=COPY)
 
-        def halves(fn, *some_units):
-            return [(fn, s, half) for s in some_units for half in range(2)]
+        def halves(fn, *args):
+            return [(fn,) + args + (half,) for half in range(2)]
 
-        def by_vector(*some_units):
-            return [(widen, s, i) for s in some_units for i in range(PIECES - on_scalar[s])]
+        def each(fn, some_units):
+            return [step for unit in some_units for step in halves(fn, unit)]
 
-        def by_scalar(*some_units):
-            return [(widen, s, i) for s in some_units for i in range(PIECES - on_scalar[s], PIECES)]
+        def by_vector(some_units):
+            return [(widen, unit, i) for unit in some_units for i in range(PIECES - on_scalar[unit])]
 
-        def chunk(ci):
-            return (w_unit[ci], w_unit[ci] + 1)
-
-        products = [(j, ci) for ci in range(CHUNKS) for j in range(PAIRS)]
-        parked = products[:PAIRS]
-
-        tensor = halves(turn, x_unit[0], x_unit[1]) + [(down, 0)]
-        for m in (2, 4):
-            tensor += halves(turn, x_unit[m], x_unit[m + 1]) + [(down, m - 1), (down, m)]
-        tensor += halves(turn, *chunk(0)) + [(down, 5)]
-        tensor += halves(turn, x_unit[6], x_unit[7]) + [(base, 0, 0), (base, 1, 0), (down, 6), (down, 7)]
-        for n in range(TURN_AFTER, len(products)):
-            j, ci = products[n]
-            if j == TURN_AFTER and ci + 1 < CHUNKS:
-                tensor += halves(turn, *chunk(ci + 1))
-            tensor += [(base, j, ci)]
-            if n + UP_AHEAD < len(products):
-                tensor += [(up,) + products[n + UP_AHEAD]]
-            if j == 0 and ci >= FIRST_UNPARK:
-                tensor += [(up,) + parked[ci - FIRST_UNPARK]]
-
-        vector = by_vector(x_unit[0], x_unit[1]) + [(inter_a, 0, 0, 4), (quant, x_unit[0]), (quant_a, 0, 0, 4), (inter_a, 2, 0, 4)]
-        for t0 in (0, 2):
-            vector += [(inter_a, 3, t0, t0 + 2)] + [(quant_a, g, t0, t0 + 2) for g in (1, 2, 3)]
-        vector += by_vector(x_unit[2], x_unit[3]) + [(quant, x_unit[1])]
+        def by_scalar(some_units):
+            return [(widen, unit, i) for unit in some_units for i in range(PIECES - on_scalar[unit], PIECES)]
 
         def weave(results, pieces):
             steps = []
-            for n, result in enumerate(results):
-                steps += result + pieces[n * len(pieces) // len(results) : (n + 1) * len(pieces) // len(results)]
+            for n, result_steps in enumerate(results):
+                steps += result_steps + pieces[n * len(pieces) // len(results) : (n + 1) * len(pieces) // len(results)]
             return steps
 
-        results = [(scale_h, 0), (quant, x_unit[2]), (quant, x_unit[3]), (scale_h, 1), (scale_h, 2)]
-        results += [(quant, x_unit[4]), (quant, x_unit[5]), (scale_h, 3), (scale_h, 4)]
-        pieces = by_vector(x_unit[4], x_unit[5], *chunk(0), x_unit[6], x_unit[7])
-        vector += weave([[step] for step in results], pieces)
-        results = [[(quant, w_unit[0]), (quant, w_unit[0] + 1), (scale_h, 5), (quant, x_unit[6])], [(quant, x_unit[7])]]
-        vector += weave(results, by_vector(*chunk(1)))
-        results = [[(scale_h, 6), (quant_b, 1), (quant_h, 0)], [(scale_h, 7)], [(quant_h, 1), (quant, w_unit[1])]]
-        results += [[(quant, w_unit[1] + 1), (quant_h, 2), (quant_h, 3)], [(finish, 0, 1)]]
-        vector += weave(results, by_vector(*chunk(2))) + [(quant_b, 2), (finish, 1, 1)]
-        for ci in range(FIRST_UNPARK, CHUNKS):
-            late_b = [(quant_b, 0)] if ci == FIRST_UNPARK else []
-            results = [[], [(quant, w_unit[ci]), (finish, 2, ci - 1)] + late_b + [(quant, w_unit[ci] + 1)], [(finish, 3, ci - 1)]]
-            results += [[(finish, 0, ci), (finish_parked,) + parked[ci - FIRST_UNPARK]]]
-            if ci + 1 < CHUNKS:
-                vector += weave(results, by_vector(*chunk(ci + 1))) + [(quant_b, ci + 1), (finish, 1, ci)]
-            else:
-                vector += weave(results, []) + [(finish, j, ci) for j in range(1, PAIRS)]
+        runs = [units[sum(RUNS[:n]) : sum(RUNS[: n + 1])] for n in range(len(RUNS))]
 
-        scalar = by_scalar(x_unit[0], x_unit[1]) + halves(empty, x_unit[0]) + [(inter_a, A_PASS_ON_SCALAR, 0, 4)] + halves(empty, x_unit[1])
-        scalar += by_scalar(x_unit[2], x_unit[3]) + [(cast_lam,)] + by_scalar(x_unit[4])
-        scalar += halves(empty, x_unit[2], x_unit[3]) + by_scalar(x_unit[5], w_unit[0])
-        scalar += halves(empty, x_unit[4], x_unit[5]) + by_scalar(w_unit[0] + 1, x_unit[6])
-        scalar += halves(empty, *chunk(0)) + by_scalar(x_unit[7]) + [(cast_c,)]
-        scalar += halves(empty, x_unit[6], x_unit[7]) + [(park, 0, 0), (park, 1, 0), (inter_b, 1)] + by_scalar(*chunk(1)) + [(inter_b, 0)]
-        scalar += halves(empty, *chunk(1)) + [(park, 2, 0), (scale_d, 0, 1), (park, 3, 0), (scale_d, 1, 1), (inter_b, 2), (scale_d, 2, 1)]
+        def downs(j):
+            return [(down, j, side, h) for h in range(2) for side in range(2)]
+
+        def ups(s, m0, m1):
+            return [(up, m, s) for m in range(m0, m1)]
+
+        ending = [(PAIRS - 2, i, 0, WIDTH) for i in range(2)] + [(PAIRS - 1,) + part for part in ENDING]
+
+        def bases(ci, h, j0, j1):
+            return [(base, j, ci, h) for j in range(j0, j1)]
+
+        def whole(ci, j0, j1):
+            return [step for j in range(j0, j1) for step in halves(base, j, ci)]
+
+        after = [
+            downs(0)[:2],
+            downs(0)[2:],
+            downs(1)[:2],
+            downs(1)[2:],
+            bases(0, 0, 0, 2),
+            bases(0, 1, 0, 2),
+            downs(2)[:2] + bases(0, 0, 2, 3),
+            downs(2)[2:] + bases(0, 1, 2, 3) + downs(3)[:2],
+            downs(3)[2:] + whole(0, 3, 4) + whole(1, 0, 2),
+        ]
+        todo = ups(0, 0, TILES) + ups(2, 0, 2) + ups(1, 0, 2) + ups(2, 2, 6) + ups(1, 2, 4) + ups(2, 6, TILES) + ups(1, 4, TILES)
         for ci in range(2, CHUNKS):
-            scalar += halves(empty, *chunk(ci)) + [(scale_d, 3, ci - 1), (scale_d, 0, ci), (scale_d, 1, ci)]
-            if ci + 1 < CHUNKS:
-                scalar += [(inter_b, ci + 1)]
-            scalar += [(scale_d, 2, ci)]
-        scalar += [(scale_d,) + LAST]
+            steps = []
+            for j, chunk in ((2, ci - 1), (3, ci - 1), (0, ci), (1, ci)):
+                count = UPS[ci - 2][(j + 2) % 4]
+                steps += whole(chunk, j, j + 1) + todo[:count]
+                todo = todo[count:]
+            after.append(steps)
+        after[-1] += [(base_part,) + part for part in ending]
 
-        parts_of = {(base,) + LAST: len(ENDING), (base,) + BEFORE_LAST: 2}
-        bank_users = [step for step in tensor for n in range(parts_of.get(step, 1))]
-        y_users = [step for step in scalar if step[0] == scale_d]
-        b_users = [step for step in scalar if step[0] == inter_b]
-        last_reader = {turn: empty, down: scale_h, scale_d: finish, inter_b: quant_b}
+        tensor = []
+        for n, run in enumerate(runs):
+            tensor += each(turn, run) + after[n]
 
         def reader(step):
             fn, args = step[0], step[1:]
             if fn == up:
-                return (finish_parked if args in parked else scale_d,) + args
+                return (scale_d if args[1] == SPANS - 1 else finish,) + args
             if fn == base:
-                return (park if args in parked else finish,) + args
-            return (last_reader[fn],) + args
+                return (add if args[1] // 2 == SPANS - 1 else park,) + args[:2]
+            if fn == down:
+                return (scale_h,) + args[:2]
+            return ({turn: empty, base_part: add_part}[fn],) + args
 
-        def freed(users, step, depth):
-            return [reader(users[n - depth]) for n in range(depth, len(users)) if users[n] == step]
+        def results(n, fns):
+            done = [step for step in after[n] if step[0] in (up, base_part) or step[-1] == 1]
+            return [reader(step) for step in done if reader(step)[0] in fns]
+
+        vector = by_vector(runs[0]) + [(inter_a, 0, 0, 4, "v"), (quant, units[0]), (quant_a, 0, 0, 4)]
+        vector += [(inter_a, 2, 0, 4, "v"), (quant_a, 1, 0, 4), (inter_a, 3, 0, 4, "v"), (quant, units[1]), (quant_a, 2, 0, 4), (quant_a, 3, 0, 4)]
+        vector += by_vector(runs[1])
+        extra = {7: [(inter_h, 0)], 8: [(quant_h, 0), (inter_h, 1), (quant_h, 1), (inter_h, 2), (quant_b, 0), (quant_h, 2)], 9: [(inter_h, 3), (quant_h, 3)],
+                 10: [(quant_b, 2)]}
+        first = {11: [(quant_b, 1)]}
+        held = []
+        stream = by_vector(units[sum(RUNS[:2]) :])
+        vector += stream[:AHEAD]
+        stream = stream[AHEAD:]
+        for n in range(1, len(runs)):
+            count = len(by_vector(runs[n + 1])) if n + 1 < len(runs) else 0
+            nxt, stream = stream[:count], stream[count:]
+            rest = results(n, (finish, add, add_part))
+            more = extra.get(n, [])
+            if RUNS[n] == 1:
+                vector += nxt[:4] + [(quant, runs[n][0])] + nxt[4:] + more
+            else:
+                vector += held + first.get(n, []) + nxt[:LEAD1] + [(quant, runs[n][0])] + nxt[LEAD1:LEAD2] + [(quant, runs[n][1])]
+                keep = len(rest) - (HELD if n + 1 < len(runs) else 0)
+                mixed = more + rest[:keep]
+                vector += weave([[step] for step in mixed[:3]] or [[]], nxt[LEAD2:]) + mixed[3:]
+                held = rest[keep:]
+
+        scalar = by_scalar(runs[0]) + each(empty, runs[0][:1]) + [(inter_a, 1, 0, 4, "s")] + each(empty, runs[0][1:2])
+        scalar += by_scalar(runs[1]) + [(cast_lam,)]
+        late = []
+        fill = [(inter_b, s, part) for s in (0, 2, 1) for part in range(4)]
+        for n in range(1, len(runs)):
+            nxt = by_scalar(runs[n + 2]) if n + 2 < len(runs) else []
+            mine = results(n, (scale_h, park, scale_d))
+            keep = len(mine) - (1 if RUNS[n] == 1 and len(mine) == 2 else 0)
+            count = FILL[n]
+            scalar += each(empty, runs[n]) + late + nxt + [step for k in range(max(keep, count)) for step in mine[k : min(k + 1, keep)] + fill[k : min(k + 1, count)]]
+            fill = fill[count:]
+            late = mine[keep:]
+            if n == 2:
+                scalar += [(cast_c,)]
+
+        bank_users = [step for step in tensor if step[0] in (turn, up, base_part) or step[-1] == 0]
+        int_users = [step for step in vector if step[0] == quant_a]
 
         def needs(step):
             fn, args = step[0], step[1:]
+            n = bank_users.index(step) if step in bank_users else 0
+            bank = [reader(bank_users[n - BANKS])] if n >= BANKS else []
             if fn == widen:
-                return halves(turn, args[0] - WIDE_BUFS) if args[0] >= WIDE_BUFS else []
+                s = units.index(args[0])
+                return halves(turn, units[s - WIDE_BUFS]) if s >= WIDE_BUFS else []
             if fn == turn:
-                return [(widen, args[0], 2 * args[1]), (widen, args[0], 2 * args[1] + 1)] + freed(bank_users, step, BANKS)
+                return [(widen, args[0], 2 * args[1]), (widen, args[0], 2 * args[1] + 1)] + bank
             if fn == empty:
-                return [(turn,) + args] + ([(quant, args[0] - GROUP_BUFS)] if args[0] >= GROUP_BUFS else [])
+                s = units.index(args[0])
+                return [(turn,) + args] + ([(quant, units[s - GROUP_BUFS])] if s >= GROUP_BUFS else [])
             if fn == quant:
-                return halves(empty, args[0])
+                s = w_units.index(args[0]) if args[0] in w_units else 0
+                old = w_units[s - W_CODE_BUFS]
+                return halves(empty, args[0]) + ([(base, PAIRS - 1, int(old[0][1:]), old[1])] if s >= W_CODE_BUFS else [])
             if fn == quant_a:
                 return [s for s in vector + scalar if s[:2] == (inter_a, args[0]) and s[2] <= args[1] < s[3]]
             if fn == inter_b:
-                return freed(b_users, step, B_BUFS)
+                return int_users
             if fn == quant_b:
-                return [(inter_b,) + args]
+                return [(inter_b, args[0], part) for part in range(4)]
             if fn == down:
-                return freed(bank_users, step, BANKS) + [(quant, x_unit[args[0]])] + [s for s in vector if s[0] == quant_a]
+                j, side, h = args
+                return bank + [(quant, ("x%d" % j, h))] + [s for s in vector if s[0] == quant_a and s[1] // 2 == h and s[2] <= 2 * side < s[3]]
             if fn == scale_h:
-                return [(down,) + args, (cast_lam,)]
+                return [(down,) + args + (1,), (cast_lam,)]
+            if fn == inter_h:
+                return halves(scale_h, args[0]) + ([(quant_h, args[0] - H_BUFS)] if args[0] >= H_BUFS else [])
             if fn == quant_h:
-                return [(scale_h, 2 * args[0]), (scale_h, 2 * args[0] + 1)]
+                return [(inter_h,) + args]
             if fn == up:
-                return freed(bank_users, step, BANKS) + [(quant_h, args[0]), (quant_b, args[1])]
+                return bank + [(quant_h, args[0] // 2), (quant_b, args[1])]
             if fn == scale_d:
-                return [(up,) + args, (cast_c,)] + freed(y_users, step, Y_BUFS)
+                m, s = args
+                return [(up,) + args, (cast_c,), (finish, m - m % 2, s - 2), (finish, m - m % 2 + 1, s - 2)]
             if fn == base:
-                before = [(quant, s) for s in (x_unit[2 * args[0]], x_unit[2 * args[0] + 1]) + chunk(args[1])]
-                return before + freed(bank_users, step, BANKS)
+                return bank + [(quant, ("x%d" % args[0], args[2])), (quant, ("w%d" % args[1], args[2]))]
+            if fn == base_part:
+                return bank + [(quant, ("w%d" % (CHUNKS - 1), 1))]
             if fn == park:
-                return [(base,) + args]
-            if fn == finish_parked:
-                return [(up,) + args, (park,) + args, (cast_c,)]
+                return [(base,) + args + (1,)]
             if fn == finish:
-                return [(base,) + args, (scale_d,) + args]
+                m, s = args
+                return [(up,) + args, (park, m // 2, 2 * s), (park, m // 2, 2 * s + 1), (cast_c,)]
+            if fn == add:
+                return [(base,) + args + (1,), (scale_d, 2 * args[0], SPANS - 1), (scale_d, 2 * args[0] + 1, SPANS - 1)]
+            if fn == add_part:
+                return [(base_part,) + args, (scale_d, 2 * args[0] + args[1], SPANS - 1)]
             return []
 
         written = set()

@@ -28,18 +28,19 @@ SPANS = N // SPAN
 PIECES = 4
 
 ORDER = "x0 x1 w0 x2 x3 w1 w2 w3 w4 w5"
-LOAD_ORDER = "xs x0 a0 a1 a2 a3 x1 ws w0 lam x2 x3 c w1 b0 w2 w3 b1 w4 b2 w5"
+LOAD_ORDER = "xs x00 x01 a0 a1 a2 x10 a3 lam x11 ws w0 x2 x3 c w1 b0 w2 w3 b2 w4 b1 w5"
 RUNS = (2, 1, 1, 1, 1, 1, 1, 2, 2, 2, 2, 2, 2)
-ON_SCALAR = (2, 1, 4, 0, 0, 0, 0)
+PLAIN_PASSES = 1
+W_STEPPED = 0
+ON_SCALAR = (2, 0, 2, 0, 0, 0, 1, 0, 2)
 BANKS = 8
-UPS = ((1, 1, 1, 1), (1, 2, 3, 0), (2, 4, 4, 1), (1, 1, 1, 0))
-LEAD1, LEAD2, HELD = 3, 5, 1
-AHEAD = 1
-FILL = (0, 0, 0, 0, 0, 0, 1, 0, 3, 4, 4, 0, 0)
-WIDE_BUFS, GROUP_BUFS, INT_BUFS, W_CODE_BUFS, H_BUFS = 6, 3, 4, 6, 2
+UPS = ((0, 0, 0, 0, 0), (0, 1, 1, 1, 1), (0, 1, 5, 3, 3), (3, 2, 2, 1, 0))
+LEAD1, LEAD2, HELD = 4, 6, 1
+H_ON_SCALAR = 0
+FILL = (0, 0, 1, 1, 1, 1, 1, 0, 2, 2, 4, 3, 0)
+WIDE_BUFS, GROUP_BUFS, INT_BUFS, W_CODE_BUFS, H_BUFS = 6, 3, 4, 6, 4
 SCALE_PAD = 64
 SCALE_ROW = {"w": 4, "b": 4, "x": 8, "h": 8, "a": 12}
-ENDING = ((0, 0, 256), (1, 0, 128), (1, 128, 256))
 
 
 def tile_fp8_base_lora_d2_kernel(tc, x_bytes, x_scale, w_bytes, w_scale, a, lam, b, c, out):
@@ -69,7 +70,6 @@ def tile_fp8_base_lora_d2_kernel(tc, x_bytes, x_scale, w_bytes, w_scale, a, lam,
         x_view = x_bytes.rearrange("(p m) k -> p m k", m=TILES)
         a_view = a.rearrange("(g p j) r -> g p j r", p=P, j=4)
         b_view = b.rearrange("(p j) n -> p j n", j=4)
-        w_view = w_bytes.rearrange("(r p) k -> p r k", p=P)
         out_view = out.rearrange("(p m) n -> p m n", m=TILES)
         raw, a_raw, b_raw = {}, {}, {}
 
@@ -84,7 +84,7 @@ def tile_fp8_base_lora_d2_kernel(tc, x_bytes, x_scale, w_bytes, w_scale, a, lam,
         xs = const.tile([P, TILES * K_BLOCKS], F32, name="xs")
         lam_b = const.tile([P, 4], BF16, name="lam_b")
         c_b = const.tile([P, TILES], BF16, name="c_b")
-        ws = const.tile([P, 2 * CHUNKS * K_BLOCKS], F32, name="ws")
+        ws = const.tile([P, (2 * CHUNKS - 1) * K_BLOCKS], F32, name="ws")
         for what in LOAD_ORDER.split(" "):
             if what == "xs":
                 nc.sync.dma_start(out=xs[:], in_=x_scale.rearrange("(p m) j -> p (m j)", m=TILES))
@@ -93,22 +93,36 @@ def tile_fp8_base_lora_d2_kernel(tc, x_bytes, x_scale, w_bytes, w_scale, a, lam,
             elif what == "c":
                 nc.sync.dma_start(out=c_b[:], in_=c.rearrange("(p m) -> p m", m=TILES))
             elif what == "ws":
-                nc.sync.dma_start(out=ws[:], in_=w_scale.rearrange("i j -> (i j)").partition_broadcast(P))
+                for h in range(2):
+                    mine = w_scale[h : h + 2 * CHUNKS - 1, :].rearrange("i j -> (i j)")
+                    nc.sync.dma_start(out=ws[P // 2 * h : P // 2 * (h + 1), :], in_=mine.partition_broadcast(P // 2))
             elif what[0] == "a":
                 g = int(what[1:])
-                a_raw[g] = loads.tile([P, 4, R], BF16, name="a_raw%d" % g, align_bytes=64)
-                nc.sync.dma_start(out=a_raw[g][:], in_=a_view[g])
+                a_raw[g] = loads.tile([P, 4, R], BF16, name="a_raw%d" % g, tag="shared%d" % g, align_bytes=64)
+                if g < PLAIN_PASSES:
+                    nc.sync.dma_start(out=a_raw[g][:], in_=a_view[g])
+                else:
+                    for u in range(2):
+                        nc.sync.dma_start(out=a_raw[g][:, 2 * u : 2 * u + 2, :], in_=a_view[g][:, u::2, :])
             elif what[0] == "b":
                 s = int(what[1:])
                 b_raw[s] = loads.tile([P, 4, SPAN], BF16, name="b_raw%d" % s, align_bytes=64)
                 nc.sync.dma_start(out=b_raw[s][:], in_=b_view[:, :, SPAN * s : SPAN * (s + 1)])
-            else:
+            elif what[0] == "w":
                 idx = int(what[1:])
-                rows = (x_view if what[0] == "x" else w_view)[:, 2 * idx : 2 * idx + 2, :]
-                if what == "x0":
-                    for h in range(2):
-                        raw[what, h] = loads.tile([P, 2, K // 2], U8, name="%s_bytes%d" % (what, h), align_bytes=64)
-                        nc.sync.dma_start(out=raw[what, h][:], in_=rows[:, :, K // 2 * h : K // 2 * (h + 1)])
+                rows = w_bytes[WIDTH * idx : WIDTH * (idx + 1), :].rearrange("(p r) (j k) -> p r j k", r=2, k=P)
+                blocks = loads.tile([P, K_BLOCKS, 2, P], U8, name="%s_bytes" % what, align_bytes=64)
+                for r in range(2):
+                    nc.sync.dma_start(out=blocks[:, :, r, :], in_=rows[:, r, :, :])
+                for h in range(2):
+                    raw[what, h] = blocks[:, K_BLOCKS // 2 * h : K_BLOCKS // 2 * (h + 1), :, :]
+            else:
+                idx = int(what[1])
+                rows = x_view[:, 2 * idx : 2 * idx + 2, :]
+                if len(what) == 3:
+                    h = int(what[2])
+                    raw[what[:2], h] = loads.tile([P, 2, K // 2], U8, name="%s_bytes" % what, align_bytes=64)
+                    nc.sync.dma_start(out=raw[what[:2], h][:], in_=rows[:, :, K // 2 * h : K // 2 * (h + 1)])
                 else:
                     both = loads.tile([P, 2, K], U8, name="%s_bytes" % what, align_bytes=64)
                     nc.sync.dma_start(out=both[:], in_=rows)
@@ -127,19 +141,41 @@ def tile_fp8_base_lora_d2_kernel(tc, x_bytes, x_scale, w_bytes, w_scale, a, lam,
                 wide[unit] = work.tile([P, PIECES, 2, P, 2], BF16, name="wide%d" % (units.index(unit) % WIDE_BUFS), align_bytes=64)
             what, h = unit
             g, r = divmod(i, 2)
-            row = 2 * int(what[1:]) + r
+            plain = 2 * h + g < PLAIN_PASSES
             for q in range(4):
                 j = 4 * g + q
-                src = raw[unit][:, r, P * j : P * (j + 1)].bitcast(FP8)
-                at = K_BLOCKS * row + K_BLOCKS // 2 * h + j
-                scale = (xs if what[0] == "x" else ws)[:, at : at + 1]
-                if i >= PIECES - on_scalar[unit]:
+                paired = what[0] == "w"
+                first_row = 2 * int(what[1:])
+                at = K_BLOCKS * (first_row + (0 if paired else r)) + K_BLOCKS // 2 * h + j
+                scale = (ws if paired else xs)[:, at : at + 1]
+                if paired and (W_STEPPED or not plain):
+                    if r == 0:
+                        both = wide[unit][:, i : i + 2, :, :, :]
+                        src = raw[unit][:, j, :, :].bitcast(FP8)
+                        if plain:
+                            dst = both.rearrange("p r u w e -> p r (u w e)")[:, :, P * q : P * (q + 1)]
+                        else:
+                            dst = both[:, :, :, 32 * q : 32 * (q + 1), :].rearrange("p r u w e -> p r (w e) u")
+                            src = src.rearrange("p r (m u) -> p r m u", u=2)
+                        nc.vector.tensor_scalar(out=dst, in0=src, scalar1=scale, scalar2=None, op0=MULT)
+                    continue
+                src = (raw[unit][:, r, P * j : P * (j + 1)] if not paired else raw[unit][:, j, r, :]).bitcast(FP8)
+                words = wide[unit][:, i, :, 32 * q : 32 * (q + 1), :]
+                if i < on_scalar[unit]:
                     flat = wide[unit][:, i, :, :, :].rearrange("p u w e -> p (u w e)")
                     nc.scalar.activation(out=flat[:, P * q : P * (q + 1)], in_=src, func=COPY, scale=scale)
+                elif plain:
+                    nc.vector.tensor_scalar(
+                        out=words.rearrange("p u w e -> p w u e"),
+                        in0=src.rearrange("p (w u e) -> p w u e", u=2, e=2),
+                        scalar1=scale,
+                        scalar2=None,
+                        op0=MULT,
+                    )
                 else:
                     nc.vector.tensor_scalar(
-                        out=wide[unit][:, i, :, 32 * q : 32 * (q + 1), :].rearrange("p u w e -> p w u e"),
-                        in0=src.rearrange("p (w u e) -> p w u e", u=2, e=2),
+                        out=words.rearrange("p u w e -> p (w e) u"),
+                        in0=src.rearrange("p (m u) -> p m u", u=2),
                         scalar1=scale,
                         scalar2=None,
                         op0=MULT,
@@ -151,7 +187,7 @@ def tile_fp8_base_lora_d2_kernel(tc, x_bytes, x_scale, w_bytes, w_scale, a, lam,
             for i in range(2):
                 piece = wide[unit][:, 2 * half + i, :, :, :]
                 for u in range(2):
-                    if 2 * half + i >= PIECES - on_scalar[unit]:
+                    if 2 * half + i < on_scalar[unit] or (W_STEPPED and unit[0][0] == "w" and 2 * unit[1] + half < PLAIN_PASSES):
                         words = piece.rearrange("p u w e -> p (u w e)").bitcast(F32)[:, u::2]
                     else:
                         words = piece[:, u, :, :].rearrange("p w e -> p (w e)").bitcast(F32)
@@ -241,7 +277,7 @@ def tile_fp8_base_lora_d2_kernel(tc, x_bytes, x_scale, w_bytes, w_scale, a, lam,
 
         def inter_h(j):
             h_int[j] = ring(work, "h_int", H_BUFS, [P, 2 * P, 4], BF16)
-            nc.vector.tensor_copy(
+            (nc.scalar.copy if j < H_ON_SCALAR else nc.vector.tensor_copy)(
                 out=h_int[j][:].rearrange("p (n i) t -> p n t i", i=4), in_=h_rows[j][:].rearrange("p t (n i) -> p n t i", i=4)
             )
 
@@ -255,7 +291,10 @@ def tile_fp8_base_lora_d2_kernel(tc, x_bytes, x_scale, w_bytes, w_scale, a, lam,
 
         def result(j, s):
             if (j, s) not in y:
-                y[j, s] = work.tile([P, 2, SPAN], F32, name="y%d_%d" % (j, s % 2), align_bytes=64)
+                if s == SPANS - 1:
+                    y[j, s] = loads.tile([P, 2, SPAN], F32, name="y%d_%d" % (j, s), tag="shared%d" % j, align_bytes=64)
+                else:
+                    y[j, s] = work.tile([P, 2, SPAN], F32, name="y%d_%d" % (j, s), align_bytes=64)
             return y[j, s]
 
         def up(m, s):
@@ -306,7 +345,10 @@ def tile_fp8_base_lora_d2_kernel(tc, x_bytes, x_scale, w_bytes, w_scale, a, lam,
 
         def park(j, ci):
             n0 = WIDTH * (ci % 2)
-            nc.scalar.copy(out=result(j, ci // 2)[:, :, n0 : n0 + WIDTH], in_=base_parts[j, ci][:])
+            nc.scalar.copy(
+                out=result(j, ci // 2)[:, :, n0 : n0 + WIDTH].rearrange("p i (c r) -> p i c r", r=2),
+                in_=base_parts[j, ci][:].rearrange("p i (r c) -> p i c r", r=2),
+            )
 
         def finish(m, s):
             j, i = divmod(m, 2)
@@ -321,12 +363,14 @@ def tile_fp8_base_lora_d2_kernel(tc, x_bytes, x_scale, w_bytes, w_scale, a, lam,
         def add(j, ci):
             n0 = WIDTH * (ci % 2)
             mine = y[j, ci // 2][:, :, n0 : n0 + WIDTH]
-            nc.vector.tensor_tensor(out=mine, in0=base_parts[j, ci][:], in1=mine, op=ADD)
+            pairs = mine.rearrange("p i (c r) -> p i c r", r=2)
+            nc.vector.tensor_tensor(out=pairs, in0=base_parts[j, ci][:].rearrange("p i (r c) -> p i c r", r=2), in1=pairs, op=ADD)
             nc.sync.dma_start(out=out_view[:, 2 * j : 2 * j + 2, WIDTH * ci : WIDTH * (ci + 1)], in_=mine)
 
         def add_part(j, i, n0, n1):
             mine = y[j, SPANS - 1][:, i, WIDTH + n0 : WIDTH + n1]
-            nc.vector.tensor_tensor(out=mine, in0=base_parts[j, i, n0][:, n0:n1], in1=mine, op=ADD)
+            pairs = mine.rearrange("p (c r) -> p c r", r=2)
+            nc.vector.tensor_tensor(out=pairs, in0=base_parts[j, i, n0][:].rearrange("p (r c) -> p c r", r=2), in1=pairs, op=ADD)
             nc.sync.dma_start(out=out_view[:, 2 * j + i, N - WIDTH + n0 : N - WIDTH + n1], in_=mine)
 
         def cast_lam():
@@ -342,10 +386,10 @@ def tile_fp8_base_lora_d2_kernel(tc, x_bytes, x_scale, w_bytes, w_scale, a, lam,
             return [step for unit in some_units for step in halves(fn, unit)]
 
         def by_vector(some_units):
-            return [(widen, unit, i) for unit in some_units for i in range(PIECES - on_scalar[unit])]
+            return [(widen, unit, i) for unit in some_units for i in range(on_scalar[unit], PIECES)]
 
         def by_scalar(some_units):
-            return [(widen, unit, i) for unit in some_units for i in range(PIECES - on_scalar[unit], PIECES)]
+            return [(widen, unit, i) for unit in some_units for i in range(on_scalar[unit])]
 
         def weave(results, pieces):
             steps = []
@@ -361,7 +405,7 @@ def tile_fp8_base_lora_d2_kernel(tc, x_bytes, x_scale, w_bytes, w_scale, a, lam,
         def ups(s, m0, m1):
             return [(up, m, s) for m in range(m0, m1)]
 
-        ending = [(PAIRS - 2, i, 0, WIDTH) for i in range(2)] + [(PAIRS - 1,) + part for part in ENDING]
+        ending = [(j, i, 0, WIDTH) for j in range(PAIRS - 2, PAIRS) for i in range(2)]
 
         def bases(ci, h, j0, j1):
             return [(base, j, ci, h) for j in range(j0, j1)]
@@ -380,15 +424,18 @@ def tile_fp8_base_lora_d2_kernel(tc, x_bytes, x_scale, w_bytes, w_scale, a, lam,
             downs(2)[2:] + bases(0, 1, 2, 3) + downs(3)[:2],
             downs(3)[2:] + whole(0, 3, 4) + whole(1, 0, 2),
         ]
-        todo = ups(0, 0, TILES) + ups(2, 0, 2) + ups(1, 0, 2) + ups(2, 2, 6) + ups(1, 2, 4) + ups(2, 6, TILES) + ups(1, 4, TILES)
+        todo = ups(0, 0, 5) + ups(2, 0, 2) + ups(0, 5, 6) + ups(2, 2, 4) + ups(0, 6, 7) + ups(2, 4, 6) + ups(0, 7, TILES) + ups(1, 0, 3) + ups(2, 6, TILES) + ups(1, 3, TILES)
         for ci in range(2, CHUNKS):
-            steps = []
+            steps = todo[: UPS[ci - 2][0]]
+            todo = todo[UPS[ci - 2][0] :]
             for j, chunk in ((2, ci - 1), (3, ci - 1), (0, ci), (1, ci)):
-                count = UPS[ci - 2][(j + 2) % 4]
+                count = UPS[ci - 2][1 + (j + 2) % 4]
                 steps += whole(chunk, j, j + 1) + todo[:count]
                 todo = todo[count:]
             after.append(steps)
-        after[-1] += [(base_part,) + part for part in ending]
+        for part in ending:
+            after[-1] += [(base_part,) + part] + todo[:1]
+            todo = todo[1:]
 
         tensor = []
         for n, run in enumerate(runs):
@@ -408,44 +455,43 @@ def tile_fp8_base_lora_d2_kernel(tc, x_bytes, x_scale, w_bytes, w_scale, a, lam,
             done = [step for step in after[n] if step[0] in (up, base_part) or step[-1] == 1]
             return [reader(step) for step in done if reader(step)[0] in fns]
 
+        def alternate(first, second):
+            return [step for k in range(max(len(first), len(second))) for step in first[k : k + 1] + second[k : k + 1]]
+
         vector = by_vector(runs[0]) + [(inter_a, 0, 0, 4, "v"), (quant, units[0]), (quant_a, 0, 0, 4)]
-        vector += [(inter_a, 2, 0, 4, "v"), (quant_a, 1, 0, 4), (inter_a, 3, 0, 4, "v"), (quant, units[1]), (quant_a, 2, 0, 4), (quant_a, 3, 0, 4)]
-        vector += by_vector(runs[1])
-        extra = {7: [(inter_h, 0)], 8: [(quant_h, 0), (inter_h, 1), (quant_h, 1), (inter_h, 2), (quant_b, 0), (quant_h, 2)], 9: [(inter_h, 3), (quant_h, 3)],
-                 10: [(quant_b, 2)]}
-        first = {11: [(quant_b, 1)]}
+        vector += [(inter_a, 2, 0, 4, "v"), (quant_a, 1, 0, 4)] + by_vector(runs[1]) + [(quant, units[1]), (inter_a, 3, 0, 2, "v")]
+        vector += [(quant_a, 2, 0, 4), (quant_a, 3, 0, 4)]
+        extra = {8: [(inter_h, 0), (inter_h, 1), (quant_h, 0)], 9: [(quant_h, 1), (inter_h, 2), (quant_b, 0), (quant_h, 2)],
+                 10: [(inter_h, 3), (quant_h, 3)]}
+        first = {11: [(quant_b, 2)], 12: []}
         held = []
-        stream = by_vector(units[sum(RUNS[:2]) :])
-        vector += stream[:AHEAD]
-        stream = stream[AHEAD:]
         for n in range(1, len(runs)):
-            count = len(by_vector(runs[n + 1])) if n + 1 < len(runs) else 0
-            nxt, stream = stream[:count], stream[count:]
+            nxt = by_vector(runs[n + 1]) if n + 1 < len(runs) else []
             rest = results(n, (finish, add, add_part))
-            more = extra.get(n, [])
             if RUNS[n] == 1:
-                vector += nxt[:4] + [(quant, runs[n][0])] + nxt[4:] + more
+                vector += nxt[:4] + [(quant, runs[n][0])] + nxt[4:]
             else:
+                if n + 1 == len(runs):
+                    nxt, rest = [None] * LEAD1 + rest[:1], rest[1:]
+                    vector += first[n] + held + [(quant, runs[n][0])] + nxt[LEAD1:] + [(quant, runs[n][1])] + rest
+                    continue
                 vector += held + first.get(n, []) + nxt[:LEAD1] + [(quant, runs[n][0])] + nxt[LEAD1:LEAD2] + [(quant, runs[n][1])]
-                keep = len(rest) - (HELD if n + 1 < len(runs) else 0)
-                mixed = more + rest[:keep]
-                vector += weave([[step] for step in mixed[:3]] or [[]], nxt[LEAD2:]) + mixed[3:]
+                keep = len(rest) - (HELD if n + 2 < len(runs) else 3)
+                vector += nxt[LEAD2:] + extra.get(n, []) + rest[:keep]
+                if n + 2 == len(runs):
+                    vector.insert(len(vector) - 2, (quant_b, 1))
                 held = rest[keep:]
 
         scalar = by_scalar(runs[0]) + each(empty, runs[0][:1]) + [(inter_a, 1, 0, 4, "s")] + each(empty, runs[0][1:2])
-        scalar += by_scalar(runs[1]) + [(cast_lam,)]
+        scalar += by_scalar(runs[1]) + [(inter_a, 3, 2, 4, "s"), (cast_lam,)]
         late = []
-        fill = [(inter_b, s, part) for s in (0, 2, 1) for part in range(4)]
+        fill = [(cast_c,)] + by_scalar(units[3:]) + [(inter_b, s, part) for s in (0, 2, 1) for part in range(4)]
         for n in range(1, len(runs)):
-            nxt = by_scalar(runs[n + 2]) if n + 2 < len(runs) else []
             mine = results(n, (scale_h, park, scale_d))
             keep = len(mine) - (1 if RUNS[n] == 1 and len(mine) == 2 else 0)
-            count = FILL[n]
-            scalar += each(empty, runs[n]) + late + nxt + [step for k in range(max(keep, count)) for step in mine[k : min(k + 1, keep)] + fill[k : min(k + 1, count)]]
-            fill = fill[count:]
+            scalar += each(empty, runs[n]) + late + alternate(fill[: FILL[n]], mine[:keep])
+            fill = fill[FILL[n] :]
             late = mine[keep:]
-            if n == 2:
-                scalar += [(cast_c,)]
 
         bank_users = [step for step in tensor if step[0] in (turn, up, base_part) or step[-1] == 0]
         int_users = [step for step in vector if step[0] == quant_a]
@@ -467,7 +513,7 @@ def tile_fp8_base_lora_d2_kernel(tc, x_bytes, x_scale, w_bytes, w_scale, a, lam,
                 old = w_units[s - W_CODE_BUFS]
                 return halves(empty, args[0]) + ([(base, PAIRS - 1, int(old[0][1:]), old[1])] if s >= W_CODE_BUFS else [])
             if fn == quant_a:
-                return [s for s in vector + scalar if s[:2] == (inter_a, args[0]) and s[2] <= args[1] < s[3]]
+                return [s for s in vector + scalar if s[:2] == (inter_a, args[0]) and s[2] < args[2] and args[1] < s[3]]
             if fn == inter_b:
                 return int_users
             if fn == quant_b:
@@ -485,7 +531,7 @@ def tile_fp8_base_lora_d2_kernel(tc, x_bytes, x_scale, w_bytes, w_scale, a, lam,
                 return bank + [(quant_h, args[0] // 2), (quant_b, args[1])]
             if fn == scale_d:
                 m, s = args
-                return [(up,) + args, (cast_c,), (finish, m - m % 2, s - 2), (finish, m - m % 2 + 1, s - 2)]
+                return [(up,) + args, (cast_c,)]
             if fn == base:
                 return bank + [(quant, ("x%d" % args[0], args[2])), (quant, ("w%d" % args[1], args[2]))]
             if fn == base_part:

@@ -28,7 +28,7 @@ SPANS = N // SPAN
 PIECES = 4
 
 ORDER = "x0 x1 w0 x2 x3 w1 w2 w3 w4 w5"
-LOAD_ORDER = "xs x00 x01 a0 a1 a2 x10 a3 lam x11 ws w0 x2 x3 c w1 b0 w2 w3 b2 w4 b1 w5"
+LOAD_ORDER = "xs x00 x01 a0 a1 a2 x10 a3 lam c x11 ws w0 x2 x3 w1 b0 w2 w3 b2 w4 b1 w5"
 RUNS = (2, 1, 1, 1, 1, 1, 1, 2, 2, 2, 2, 2, 2)
 PLAIN_PASSES = 1
 W_STEPPED = 0
@@ -111,11 +111,14 @@ def tile_fp8_base_lora_d2_kernel(tc, x_bytes, x_scale, w_bytes, w_scale, a, lam,
             elif what[0] == "w":
                 idx = int(what[1:])
                 rows = w_bytes[WIDTH * idx : WIDTH * (idx + 1), :].rearrange("(p r) (j k) -> p r j k", r=2, k=P)
-                blocks = loads.tile([P, K_BLOCKS, 2, P], U8, name="%s_bytes" % what, align_bytes=64)
+                plain = 4 * PLAIN_PASSES
+                front = loads.tile([P, 2, plain, P], U8, name="%s_front" % what, align_bytes=64)
+                nc.sync.dma_start(out=front[:], in_=rows[:, :, :plain, :])
+                blocks = loads.tile([P, K_BLOCKS - plain, 2, P], U8, name="%s_bytes" % what, align_bytes=64)
                 for r in range(2):
-                    nc.sync.dma_start(out=blocks[:, :, r, :], in_=rows[:, r, :, :])
-                for h in range(2):
-                    raw[what, h] = blocks[:, K_BLOCKS // 2 * h : K_BLOCKS // 2 * (h + 1), :, :]
+                    nc.sync.dma_start(out=blocks[:, :, r, :], in_=rows[:, r, plain:, :])
+                for j in range(K_BLOCKS):
+                    raw[what, j] = front[:, :, j, :] if j < plain else blocks[:, j - plain, :, :]
             else:
                 idx = int(what[1])
                 rows = x_view[:, 2 * idx : 2 * idx + 2, :]
@@ -151,7 +154,7 @@ def tile_fp8_base_lora_d2_kernel(tc, x_bytes, x_scale, w_bytes, w_scale, a, lam,
                 if paired and (W_STEPPED or not plain):
                     if r == 0:
                         both = wide[unit][:, i : i + 2, :, :, :]
-                        src = raw[unit][:, j, :, :].bitcast(FP8)
+                        src = raw[what, K_BLOCKS // 2 * h + j].bitcast(FP8)
                         if plain:
                             dst = both.rearrange("p r u w e -> p r (u w e)")[:, :, P * q : P * (q + 1)]
                         else:
@@ -159,7 +162,7 @@ def tile_fp8_base_lora_d2_kernel(tc, x_bytes, x_scale, w_bytes, w_scale, a, lam,
                             src = src.rearrange("p r (m u) -> p r m u", u=2)
                         nc.vector.tensor_scalar(out=dst, in0=src, scalar1=scale, scalar2=None, op0=MULT)
                     continue
-                src = (raw[unit][:, r, P * j : P * (j + 1)] if not paired else raw[unit][:, j, r, :]).bitcast(FP8)
+                src = (raw[unit][:, r, P * j : P * (j + 1)] if not paired else raw[what, K_BLOCKS // 2 * h + j][:, r, :]).bitcast(FP8)
                 words = wide[unit][:, i, :, 32 * q : 32 * (q + 1), :]
                 if i < on_scalar[unit]:
                     flat = wide[unit][:, i, :, :, :].rearrange("p u w e -> p (u w e)")

@@ -23,22 +23,23 @@ PASSES = K // 512
 K_BLOCKS = K // P
 WIDTH = 256
 CHUNKS = N // WIDTH
-SPAN = 2 * WIDTH
-SPANS = N // SPAN
+PARKED = 2
 PIECES = 4
 
 ORDER = "x0 x1 w0 x2 x3 w1 w2 w3 w4 w5"
-LOAD_ORDER = "xs x00 x01 a0 a1 a2 x10 a3 lam c x11 ws w0 x2 x3 w1 b0 w2 w3 b2 w4 b1 w5"
+LOAD_ORDER = "xs x00 x01 a0 a1 a2 x10 a3 lam c x11 ws w0 x2 x3 b2 w1 b0 w2 b3 w3 b1 b4 w4 b5 w5"
 RUNS = (2, 1, 1, 1, 1, 1, 1, 2, 2, 2, 2, 2, 2)
 PLAIN_PASSES = 1
-W_STEPPED = 0
 ON_SCALAR = (2, 0, 2, 0, 0, 0, 1, 0, 2)
 BANKS = 8
-UPS = ((0, 0, 0, 0, 0), (0, 1, 1, 1, 1), (0, 1, 5, 3, 3), (3, 2, 2, 1, 0))
-LEAD1, LEAD2, HELD = 4, 6, 1
-H_ON_SCALAR = 0
-FILL = (0, 0, 1, 1, 1, 1, 1, 0, 2, 2, 4, 3, 0)
-WIDE_BUFS, GROUP_BUFS, INT_BUFS, W_CODE_BUFS, H_BUFS = 6, 3, 4, 6, 4
+WIDE_BUFS, GROUP_BUFS, A_BUFS, B_BUFS, W_CODE_BUFS, H_BUFS, Y_BUFS = 6, 3, 4, 3, 6, 2, 6
+UP_AHEAD = 2
+UNPARK_FROM = 0
+HELD = 0
+W_RUN = 7
+LATE_TO = 0
+AT = 2
+UNPARK = (0, 3, 3, 2)
 SCALE_PAD = 64
 SCALE_ROW = {"w": 4, "b": 4, "x": 8, "h": 8, "a": 12}
 
@@ -98,16 +99,16 @@ def tile_fp8_base_lora_d2_kernel(tc, x_bytes, x_scale, w_bytes, w_scale, a, lam,
                     nc.sync.dma_start(out=ws[P // 2 * h : P // 2 * (h + 1), :], in_=mine.partition_broadcast(P // 2))
             elif what[0] == "a":
                 g = int(what[1:])
-                a_raw[g] = loads.tile([P, 4, R], BF16, name="a_raw%d" % g, tag="shared%d" % g, align_bytes=64)
+                a_raw[g] = loads.tile([P, 4, R], BF16, name="a_raw%d" % g, align_bytes=64)
                 if g < PLAIN_PASSES:
                     nc.sync.dma_start(out=a_raw[g][:], in_=a_view[g])
                 else:
                     for u in range(2):
                         nc.sync.dma_start(out=a_raw[g][:, 2 * u : 2 * u + 2, :], in_=a_view[g][:, u::2, :])
             elif what[0] == "b":
-                s = int(what[1:])
-                b_raw[s] = loads.tile([P, 4, SPAN], BF16, name="b_raw%d" % s, align_bytes=64)
-                nc.sync.dma_start(out=b_raw[s][:], in_=b_view[:, :, SPAN * s : SPAN * (s + 1)])
+                ci = int(what[1:])
+                b_raw[ci] = loads.tile([P, 4, WIDTH], BF16, name="b_raw%d" % ci, align_bytes=64)
+                nc.sync.dma_start(out=b_raw[ci][:], in_=b_view[:, :, WIDTH * ci : WIDTH * (ci + 1)])
             elif what[0] == "w":
                 idx = int(what[1:])
                 rows = w_bytes[WIDTH * idx : WIDTH * (idx + 1), :].rearrange("(p r) (j k) -> p r j k", r=2, k=P)
@@ -151,15 +152,12 @@ def tile_fp8_base_lora_d2_kernel(tc, x_bytes, x_scale, w_bytes, w_scale, a, lam,
                 first_row = 2 * int(what[1:])
                 at = K_BLOCKS * (first_row + (0 if paired else r)) + K_BLOCKS // 2 * h + j
                 scale = (ws if paired else xs)[:, at : at + 1]
-                if paired and (W_STEPPED or not plain):
+                if paired and not plain:
                     if r == 0:
                         both = wide[unit][:, i : i + 2, :, :, :]
                         src = raw[what, K_BLOCKS // 2 * h + j].bitcast(FP8)
-                        if plain:
-                            dst = both.rearrange("p r u w e -> p r (u w e)")[:, :, P * q : P * (q + 1)]
-                        else:
-                            dst = both[:, :, :, 32 * q : 32 * (q + 1), :].rearrange("p r u w e -> p r (w e) u")
-                            src = src.rearrange("p r (m u) -> p r m u", u=2)
+                        dst = both[:, :, :, 32 * q : 32 * (q + 1), :].rearrange("p r u w e -> p r (w e) u")
+                        src = src.rearrange("p r (m u) -> p r m u", u=2)
                         nc.vector.tensor_scalar(out=dst, in0=src, scalar1=scale, scalar2=None, op0=MULT)
                     continue
                 src = (raw[unit][:, r, P * j : P * (j + 1)] if not paired else raw[what, K_BLOCKS // 2 * h + j][:, r, :]).bitcast(FP8)
@@ -190,7 +188,7 @@ def tile_fp8_base_lora_d2_kernel(tc, x_bytes, x_scale, w_bytes, w_scale, a, lam,
             for i in range(2):
                 piece = wide[unit][:, 2 * half + i, :, :, :]
                 for u in range(2):
-                    if 2 * half + i < on_scalar[unit] or (W_STEPPED and unit[0][0] == "w" and 2 * unit[1] + half < PLAIN_PASSES):
+                    if 2 * half + i < on_scalar[unit]:
                         words = piece.rearrange("p u w e -> p (u w e)").bitcast(F32)[:, u::2]
                     else:
                         words = piece[:, u, :, :].rearrange("p w e -> p (w e)").bitcast(F32)
@@ -222,7 +220,7 @@ def tile_fp8_base_lora_d2_kernel(tc, x_bytes, x_scale, w_bytes, w_scale, a, lam,
 
         def inter_a(g, t0, t1, on):
             if g not in a_int:
-                a_int[g] = ring(work, "ab_int", INT_BUFS, [P, 4, P, 4], BF16)
+                a_int[g] = ring(work, "a_int", A_BUFS, [P, 4, P, 4], BF16)
             (nc.scalar.copy if on == "s" else nc.vector.tensor_copy)(
                 out=a_int[g][:, t0:t1, :, :].rearrange("p t (q m) j -> p q t m j", m=2),
                 in_=a_raw[g][:].rearrange("p j (q m t) -> p q t m j", m=2, t=4)[:, :, t0:t1, :, :],
@@ -237,19 +235,16 @@ def tile_fp8_base_lora_d2_kernel(tc, x_bytes, x_scale, w_bytes, w_scale, a, lam,
                 in_=a_int[g][:, t0:t1, :, :].rearrange("p t m j -> p (t m j)"),
             )
 
-        def inter_b(s, part):
-            if part == 0:
-                b_int[s] = ring(work, "ab_int", INT_BUFS, [P, SPAN, 4], BF16)
-            cols = slice(P * part, P * (part + 1))
+        def inter_b(ci):
+            b_int[ci] = ring(work, "b_int", B_BUFS, [P, WIDTH, 4], BF16)
             nc.scalar.copy(
-                out=b_int[s][:, cols, :].rearrange("p (n i) j -> p n j i", i=4),
-                in_=b_raw[s][:, :, cols].rearrange("p j (n i) -> p n j i", i=4),
+                out=b_int[ci][:].rearrange("p (n i) j -> p n j i", i=4), in_=b_raw[ci][:].rearrange("p j (n i) -> p n j i", i=4)
             )
 
-        def quant_b(s):
-            b_codes[s], b_scales[s] = mx_operand("b", s, SPAN)
+        def quant_b(ci):
+            b_codes[ci], b_scales[ci] = mx_operand("b", ci, WIDTH)
             nc.vector.quantize_mx(
-                out=b_codes[s][:].bitcast(FP8X4), scales=b_scales[s], in_=b_int[s][:].rearrange("p n j -> p (n j)")
+                out=b_codes[ci][:].bitcast(FP8X4), scales=b_scales[ci], in_=b_int[ci][:].rearrange("p n j -> p (n j)")
             )
 
         h_banks, h_rows, h_int, h_codes, h_scales = {}, {}, {}, {}, {}
@@ -280,7 +275,7 @@ def tile_fp8_base_lora_d2_kernel(tc, x_bytes, x_scale, w_bytes, w_scale, a, lam,
 
         def inter_h(j):
             h_int[j] = ring(work, "h_int", H_BUFS, [P, 2 * P, 4], BF16)
-            (nc.scalar.copy if j < H_ON_SCALAR else nc.vector.tensor_copy)(
+            nc.vector.tensor_copy(
                 out=h_int[j][:].rearrange("p (n i) t -> p n t i", i=4), in_=h_rows[j][:].rearrange("p t (n i) -> p n t i", i=4)
             )
 
@@ -292,26 +287,18 @@ def tile_fp8_base_lora_d2_kernel(tc, x_bytes, x_scale, w_bytes, w_scale, a, lam,
 
         y, base_parts, d_banks = {}, {}, {}
 
-        def result(j, s):
-            if (j, s) not in y:
-                if s == SPANS - 1:
-                    y[j, s] = loads.tile([P, 2, SPAN], F32, name="y%d_%d" % (j, s), tag="shared%d" % j, align_bytes=64)
-                else:
-                    y[j, s] = work.tile([P, 2, SPAN], F32, name="y%d_%d" % (j, s), align_bytes=64)
-            return y[j, s]
-
-        def up(m, s):
-            d_banks[m, s] = ring(psum, "bank", BANKS, [P, SPAN], F32)
-            j, i = divmod(m, 2)
-            nc.tensor.matmul_mx(
-                out=d_banks[m, s][:],
-                lhsT=h_codes[j][:, P * i : P * (i + 1)].bitcast(FP8X4),
-                lhsT_scale=h_scales[j][:, P * i : P * (i + 1)],
-                rhs=b_codes[s][:].bitcast(FP8X4),
-                rhs_scale=b_scales[s],
-                start=True,
-                stop=True,
-            )
+        def up(j, ci):
+            d_banks[j, ci] = ring(psum, "bank", BANKS, [P, 2, WIDTH], F32)
+            for i in range(2):
+                nc.tensor.matmul_mx(
+                    out=d_banks[j, ci][:, i, :],
+                    lhsT=h_codes[j][:, P * i : P * (i + 1)].bitcast(FP8X4),
+                    lhsT_scale=h_scales[j][:, P * i : P * (i + 1)],
+                    rhs=b_codes[ci][:].bitcast(FP8X4),
+                    rhs_scale=b_scales[ci],
+                    start=True,
+                    stop=True,
+                )
 
         def base(j, ci, h):
             if h == 0:
@@ -347,34 +334,39 @@ def tile_fp8_base_lora_d2_kernel(tc, x_bytes, x_scale, w_bytes, w_scale, a, lam,
                 )
 
         def park(j, ci):
-            n0 = WIDTH * (ci % 2)
+            y[j, ci] = const.tile([P, 2, WIDTH], F32, name="parked%d_%d" % (j, ci), align_bytes=64)
             nc.scalar.copy(
-                out=result(j, ci // 2)[:, :, n0 : n0 + WIDTH].rearrange("p i (c r) -> p i c r", r=2),
+                out=y[j, ci][:].rearrange("p i (c r) -> p i c r", r=2),
                 in_=base_parts[j, ci][:].rearrange("p i (r c) -> p i c r", r=2),
             )
 
-        def finish(m, s):
-            j, i = divmod(m, 2)
-            mine = y[j, s][:, i, :]
-            nc.vector.scalar_tensor_tensor(out=mine, in0=d_banks[m, s][:], scalar=c_f[:, m : m + 1], in1=mine, op0=MULT, op1=ADD)
-            nc.sync.dma_start(out=out_view[:, m, SPAN * s : SPAN * (s + 1)], in_=mine)
+        def store(j, ci):
+            nc.sync.dma_start(out=out_view[:, 2 * j : 2 * j + 2, WIDTH * ci : WIDTH * (ci + 1)], in_=y[j, ci][:])
 
-        def scale_d(m, s):
-            j, i = divmod(m, 2)
-            nc.scalar.activation(out=result(j, s)[:, i, :], in_=d_banks[m, s][:], func=COPY, scale=c_f[:, m : m + 1])
+        def finish_parked(j, ci):
+            for i in range(2):
+                mine, m = y[j, ci][:, i, :], 2 * j + i
+                nc.vector.scalar_tensor_tensor(
+                    out=mine, in0=d_banks[j, ci][:, i, :], scalar=c_f[:, m : m + 1], in1=mine, op0=MULT, op1=ADD
+                )
+            store(j, ci)
+
+        def scale_d(j, ci):
+            y[j, ci] = ring(work, "y", Y_BUFS, [P, 2, WIDTH], F32)
+            for i in range(2):
+                m = 2 * j + i
+                nc.scalar.activation(out=y[j, ci][:, i, :], in_=d_banks[j, ci][:, i, :], func=COPY, scale=c_f[:, m : m + 1])
 
         def add(j, ci):
-            n0 = WIDTH * (ci % 2)
-            mine = y[j, ci // 2][:, :, n0 : n0 + WIDTH]
-            pairs = mine.rearrange("p i (c r) -> p i c r", r=2)
+            pairs = y[j, ci][:].rearrange("p i (c r) -> p i c r", r=2)
             nc.vector.tensor_tensor(out=pairs, in0=base_parts[j, ci][:].rearrange("p i (r c) -> p i c r", r=2), in1=pairs, op=ADD)
-            nc.sync.dma_start(out=out_view[:, 2 * j : 2 * j + 2, WIDTH * ci : WIDTH * (ci + 1)], in_=mine)
+            store(j, ci)
 
         def add_part(j, i, n0, n1):
-            mine = y[j, SPANS - 1][:, i, WIDTH + n0 : WIDTH + n1]
+            mine = y[j, CHUNKS - 1][:, i, :]
             pairs = mine.rearrange("p (c r) -> p c r", r=2)
             nc.vector.tensor_tensor(out=pairs, in0=base_parts[j, i, n0][:].rearrange("p (r c) -> p c r", r=2), in1=pairs, op=ADD)
-            nc.sync.dma_start(out=out_view[:, 2 * j + i, N - WIDTH + n0 : N - WIDTH + n1], in_=mine)
+            nc.sync.dma_start(out=out_view[:, 2 * j + i, N - WIDTH :], in_=mine)
 
         def cast_lam():
             nc.scalar.activation(out=lam_f[:], in_=lam_b[:], func=COPY)
@@ -405,9 +397,6 @@ def tile_fp8_base_lora_d2_kernel(tc, x_bytes, x_scale, w_bytes, w_scale, a, lam,
         def downs(j):
             return [(down, j, side, h) for h in range(2) for side in range(2)]
 
-        def ups(s, m0, m1):
-            return [(up, m, s) for m in range(m0, m1)]
-
         ending = [(j, i, 0, WIDTH) for j in range(PAIRS - 2, PAIRS) for i in range(2)]
 
         def bases(ci, h, j0, j1):
@@ -427,18 +416,26 @@ def tile_fp8_base_lora_d2_kernel(tc, x_bytes, x_scale, w_bytes, w_scale, a, lam,
             downs(2)[2:] + bases(0, 1, 2, 3) + downs(3)[:2],
             downs(3)[2:] + whole(0, 3, 4) + whole(1, 0, 2),
         ]
-        todo = ups(0, 0, 5) + ups(2, 0, 2) + ups(0, 5, 6) + ups(2, 2, 4) + ups(0, 6, 7) + ups(2, 4, 6) + ups(0, 7, TILES) + ups(1, 0, 3) + ups(2, 6, TILES) + ups(1, 3, TILES)
-        for ci in range(2, CHUNKS):
-            steps = todo[: UPS[ci - 2][0]]
-            todo = todo[UPS[ci - 2][0] :]
-            for j, chunk in ((2, ci - 1), (3, ci - 1), (0, ci), (1, ci)):
-                count = UPS[ci - 2][1 + (j + 2) % 4]
-                steps += whole(chunk, j, j + 1) + todo[:count]
-                todo = todo[count:]
+        products = [(j, ci) for ci in range(CHUNKS) for j in range(PAIRS)]
+        parked = products[: PARKED * PAIRS]
+        unparked = {}
+        for ci in range(PARKED, CHUNKS):
+            done = sum(UNPARK[: ci - PARKED])
+            unparked[ci] = parked[done : done + UNPARK[ci - PARKED]]
+            steps = []
+            last = PAIRS * ci + 2 if ci + 1 < CHUNKS else len(products)
+            for n in range(PAIRS * ci - 2, last):
+                j, chunk = products[n]
+                if chunk == CHUNKS - 1 and j >= PAIRS - 2:
+                    steps += [(base_part,) + part for part in ending if part[0] == j]
+                else:
+                    steps += whole(chunk, j, j + 1)
+                if n + UP_AHEAD < len(products) and products[n + UP_AHEAD] not in parked:
+                    steps += [(up,) + products[n + UP_AHEAD]]
+                slot = n - (PAIRS * ci - 2) - UNPARK_FROM
+                if slot >= 0:
+                    steps += [(up,) + product for product in unparked[ci][slot : slot + 1]]
             after.append(steps)
-        for part in ending:
-            after[-1] += [(base_part,) + part] + todo[:1]
-            todo = todo[1:]
 
         tensor = []
         for n, run in enumerate(runs):
@@ -447,9 +444,9 @@ def tile_fp8_base_lora_d2_kernel(tc, x_bytes, x_scale, w_bytes, w_scale, a, lam,
         def reader(step):
             fn, args = step[0], step[1:]
             if fn == up:
-                return (scale_d if args[1] == SPANS - 1 else finish,) + args
+                return (finish_parked if args in parked else scale_d,) + args
             if fn == base:
-                return (add if args[1] // 2 == SPANS - 1 else park,) + args[:2]
+                return (park if args[:2] in parked else add,) + args[:2]
             if fn == down:
                 return (scale_h,) + args[:2]
             return ({turn: empty, base_part: add_part}[fn],) + args
@@ -461,43 +458,56 @@ def tile_fp8_base_lora_d2_kernel(tc, x_bytes, x_scale, w_bytes, w_scale, a, lam,
         def alternate(first, second):
             return [step for k in range(max(len(first), len(second))) for step in first[k : k + 1] + second[k : k + 1]]
 
+        held = []
         vector = by_vector(runs[0]) + [(inter_a, 0, 0, 4, "v"), (quant, units[0]), (quant_a, 0, 0, 4)]
         vector += [(inter_a, 2, 0, 4, "v"), (quant_a, 1, 0, 4)] + by_vector(runs[1]) + [(quant, units[1]), (inter_a, 3, 0, 2, "v")]
         vector += [(quant_a, 2, 0, 4), (quant_a, 3, 0, 4)]
-        extra = {8: [(inter_h, 0), (inter_h, 1), (quant_h, 0)], 9: [(quant_h, 1), (inter_h, 2), (quant_b, 0), (quant_h, 2)],
-                 10: [(inter_h, 3), (quant_h, 3)]}
-        first = {11: [(quant_b, 2)], 12: []}
-        held = []
         for n in range(1, len(runs)):
             nxt = by_vector(runs[n + 1]) if n + 1 < len(runs) else []
-            rest = results(n, (finish, add, add_part))
+            first, second = [(quant, unit) for unit in runs[n]][:1], [(quant, unit) for unit in runs[n]][1:]
+            ci = n - W_RUN
             if RUNS[n] == 1:
-                vector += nxt[:4] + [(quant, runs[n][0])] + nxt[4:]
+                vector += nxt[:4] + first + nxt[4:]
+            elif ci < 1:
+                vector += nxt[:4] + first + nxt[4:6] + second + nxt[6:]
+            elif ci == 1:
+                vector += nxt[:4] + first + nxt[4:6] + second + [(inter_h, 0), (inter_h, 1), (quant_h, 0), (quant_b, 2), (quant_h, 1)] + nxt[6:]
+            elif ci == 2:
+                vector += nxt[:4] + first + [(inter_h, 2)] + second + [(quant_h, 2), (inter_h, 3)] + nxt[4:6] + [(quant_h, 3), (add, 0, ci)] + nxt[6:] + [(quant_b, 3), (quant_b, 0)]
             else:
-                if n + 1 == len(runs):
-                    nxt, rest = [None] * LEAD1 + rest[:1], rest[1:]
-                    vector += first[n] + held + [(quant, runs[n][0])] + nxt[LEAD1:] + [(quant, runs[n][1])] + rest
-                    continue
-                vector += held + first.get(n, []) + nxt[:LEAD1] + [(quant, runs[n][0])] + nxt[LEAD1:LEAD2] + [(quant, runs[n][1])]
-                keep = len(rest) - (HELD if n + 2 < len(runs) else 3)
-                vector += nxt[LEAD2:] + extra.get(n, []) + rest[:keep]
-                if n + 2 == len(runs):
-                    vector.insert(len(vector) - 2, (quant_b, 1))
-                held = rest[keep:]
+                rest = results(n, (finish_parked, add, add_part))
+                late_b = [(quant_b, 1)] if ci == 3 else []
+                vector += [(add, 1, ci - 1)] + held + nxt[:4] + first + rest[:1] + nxt[4:6] + second + late_b
+                rest = rest[1:]
+                if ci + 1 < CHUNKS:
+                    rest.remove((add, 1, ci))
+                    vector += rest[:1] + nxt[6:] + rest[1:2] + [(quant_b, ci + 1)] + rest[2 : len(rest) - HELD]
+                    held = rest[len(rest) - HELD :]
+                else:
+                    vector += rest
 
         scalar = by_scalar(runs[0]) + each(empty, runs[0][:1]) + [(inter_a, 1, 0, 4, "s")] + each(empty, runs[0][1:2])
         scalar += by_scalar(runs[1]) + [(inter_a, 3, 2, 4, "s"), (cast_lam,)]
         late = []
-        fill = [(cast_c,)] + by_scalar(units[3:]) + [(inter_b, s, part) for s in (0, 2, 1) for part in range(4)]
+        side = {2: [(cast_c,)], 3: by_scalar(units[6:7]), 4: by_scalar(units[8:9])[:1], 5: by_scalar(units[8:9])[1:], 6: [(inter_b, 2)]}
         for n in range(1, len(runs)):
             mine = results(n, (scale_h, park, scale_d))
-            keep = len(mine) - (1 if RUNS[n] == 1 and len(mine) == 2 else 0)
-            scalar += each(empty, runs[n]) + late + alternate(fill[: FILL[n]], mine[:keep])
-            fill = fill[FILL[n] :]
-            late = mine[keep:]
+            ci = n - W_RUN
+            if ci < 1:
+                keep = len(mine) - (1 if RUNS[n] == 1 and len(mine) == 2 else 0)
+                scalar += each(empty, runs[n]) + late + side.get(n, []) + mine[:keep]
+                late = mine[keep:]
+            else:
+                early = [(inter_b, 1)] if ci == 3 else []
+                nxt = [(inter_b, ci + 1 if ci > 1 else 0)] if ci + 1 < CHUNKS else []
+                keep = len(mine) - (1 if PARKED <= ci < LATE_TO else 0)
+                at = 1 if ci == 1 else len(mine) - AT
+                scalar += each(empty, runs[n]) + late + early + mine[:at] + nxt + mine[at:keep]
+                late = mine[keep:]
 
         bank_users = [step for step in tensor if step[0] in (turn, up, base_part) or step[-1] == 0]
-        int_users = [step for step in vector if step[0] == quant_a]
+        y_users = [step for step in scalar if step[0] == scale_d]
+        b_users = [step for step in scalar if step[0] == inter_b]
 
         def needs(step):
             fn, args = step[0], step[1:]
@@ -518,9 +528,10 @@ def tile_fp8_base_lora_d2_kernel(tc, x_bytes, x_scale, w_bytes, w_scale, a, lam,
             if fn == quant_a:
                 return [s for s in vector + scalar if s[:2] == (inter_a, args[0]) and s[2] < args[2] and args[1] < s[3]]
             if fn == inter_b:
-                return int_users
+                n = b_users.index(step)
+                return [(quant_b, b_users[n - B_BUFS][1])] if n >= B_BUFS else []
             if fn == quant_b:
-                return [(inter_b, args[0], part) for part in range(4)]
+                return [(inter_b,) + args]
             if fn == down:
                 j, side, h = args
                 return bank + [(quant, ("x%d" % j, h))] + [s for s in vector if s[0] == quant_a and s[1] // 2 == h and s[2] <= 2 * side < s[3]]
@@ -531,23 +542,22 @@ def tile_fp8_base_lora_d2_kernel(tc, x_bytes, x_scale, w_bytes, w_scale, a, lam,
             if fn == quant_h:
                 return [(inter_h,) + args]
             if fn == up:
-                return bank + [(quant_h, args[0] // 2), (quant_b, args[1])]
+                return bank + [(quant_h, args[0]), (quant_b, args[1])]
             if fn == scale_d:
-                m, s = args
-                return [(up,) + args, (cast_c,)]
+                n = y_users.index(step)
+                return [(up,) + args, (cast_c,)] + ([(add,) + y_users[n - Y_BUFS][1:]] if n >= Y_BUFS else [])
             if fn == base:
                 return bank + [(quant, ("x%d" % args[0], args[2])), (quant, ("w%d" % args[1], args[2]))]
             if fn == base_part:
                 return bank + [(quant, ("w%d" % (CHUNKS - 1), 1))]
             if fn == park:
                 return [(base,) + args + (1,)]
-            if fn == finish:
-                m, s = args
-                return [(up,) + args, (park, m // 2, 2 * s), (park, m // 2, 2 * s + 1), (cast_c,)]
+            if fn == finish_parked:
+                return [(up,) + args, (park,) + args, (cast_c,)]
             if fn == add:
-                return [(base,) + args + (1,), (scale_d, 2 * args[0], SPANS - 1), (scale_d, 2 * args[0] + 1, SPANS - 1)]
+                return [(base,) + args + (1,), (scale_d,) + args]
             if fn == add_part:
-                return [(base_part,) + args, (scale_d, 2 * args[0] + args[1], SPANS - 1)]
+                return [(base_part,) + args, (scale_d, args[0], CHUNKS - 1)]
             return []
 
         written = set()

@@ -40,7 +40,8 @@ W_RUN = 7
 LATE_TO = 0
 AT = 2
 UNPARK = (0, 3, 3, 2)
-SCALE_PAD = 64
+CODE_AT = {"w": 0, "b": 0, "x": 64, "h": 64, "a": 128}
+SCALE_AT = {"w": 128, "b": 128, "x": 192, "h": 192, "a": 0}
 SCALE_ROW = {"w": 4, "b": 4, "x": 8, "h": 8, "a": 12}
 
 
@@ -61,10 +62,15 @@ def tile_fp8_base_lora_d2_kernel(tc, x_bytes, x_scale, w_bytes, w_scale, a, lam,
                 return pool.tile(shape, dtype, name="%s%d" % (what, n % depth))
             return pool.tile(shape, dtype, name="%s%d" % (what, n % depth), align_bytes=64)
 
+        stores = {}
+        for what, (count, width) in {"x": (2 * PAIRS, 512), "w": (W_CODE_BUFS, 512), "a": (PASSES, R), "b": (CHUNKS, WIDTH), "h": (PAIRS, 2 * P)}.items():
+            words = codes.tile([P, CODE_AT[what] // 4 + count * width], U32, name="%s_codes" % what, align_bytes=256)
+            plane = codes.tile([P, SCALE_AT[what] + count * width], U8, name="%s_scales" % what, align_bytes=256)
+            stores[what] = (words[:, CODE_AT[what] // 4 :], plane[SCALE_ROW[what] :, SCALE_AT[what] :])
+
         def mx_operand(what, index, width):
-            words = codes.tile([P, width], U32, name="%s_codes%d" % (what, index), align_bytes=64)
-            plane = codes.tile([P, SCALE_PAD + width], U8, name="%s_scales%d" % (what, index), align_bytes=64)
-            return words, plane[SCALE_ROW[what] :, SCALE_PAD:]
+            words, plane = stores[what]
+            return words[:, width * index : width * (index + 1)], plane[:, width * index : width * (index + 1)]
 
         ctx.enter_context(tc.manual_schedule())
 
@@ -207,10 +213,10 @@ def tile_fp8_base_lora_d2_kernel(tc, x_bytes, x_scale, w_bytes, w_scale, a, lam,
 
         def quant(unit):
             kind = unit[0][0]
-            index = w_units.index(unit) % W_CODE_BUFS if kind == "w" else units.index(unit)
+            index = w_units.index(unit) % W_CODE_BUFS if kind == "w" else 2 * int(unit[0][1:]) + unit[1]
             unit_codes[unit], unit_scales[unit] = mx_operand(kind, index, PIECES * P)
             nc.vector.quantize_mx(
-                out=unit_codes[unit][:].bitcast(FP8X4),
+                out=unit_codes[unit].bitcast(FP8X4),
                 scales=unit_scales[unit],
                 in_=grouped[unit][:].rearrange("p i w t -> p (i w t)"),
             )
@@ -244,7 +250,7 @@ def tile_fp8_base_lora_d2_kernel(tc, x_bytes, x_scale, w_bytes, w_scale, a, lam,
         def quant_b(ci):
             b_codes[ci], b_scales[ci] = mx_operand("b", ci, WIDTH)
             nc.vector.quantize_mx(
-                out=b_codes[ci][:].bitcast(FP8X4), scales=b_scales[ci], in_=b_int[ci][:].rearrange("p n j -> p (n j)")
+                out=b_codes[ci].bitcast(FP8X4), scales=b_scales[ci], in_=b_int[ci][:].rearrange("p n j -> p (n j)")
             )
 
         h_banks, h_rows, h_int, h_codes, h_scales = {}, {}, {}, {}, {}
@@ -282,7 +288,7 @@ def tile_fp8_base_lora_d2_kernel(tc, x_bytes, x_scale, w_bytes, w_scale, a, lam,
         def quant_h(j):
             h_codes[j], h_scales[j] = mx_operand("h", j, 2 * P)
             nc.vector.quantize_mx(
-                out=h_codes[j][:].bitcast(FP8X4), scales=h_scales[j], in_=h_int[j][:].rearrange("p w t -> p (w t)")
+                out=h_codes[j].bitcast(FP8X4), scales=h_scales[j], in_=h_int[j][:].rearrange("p w t -> p (w t)")
             )
 
         y, base_parts, d_banks = {}, {}, {}
@@ -294,7 +300,7 @@ def tile_fp8_base_lora_d2_kernel(tc, x_bytes, x_scale, w_bytes, w_scale, a, lam,
                     out=d_banks[j, ci][:, i, :],
                     lhsT=h_codes[j][:, P * i : P * (i + 1)].bitcast(FP8X4),
                     lhsT_scale=h_scales[j][:, P * i : P * (i + 1)],
-                    rhs=b_codes[ci][:].bitcast(FP8X4),
+                    rhs=b_codes[ci].bitcast(FP8X4),
                     rhs_scale=b_scales[ci],
                     start=True,
                     stop=True,

@@ -30,7 +30,7 @@ ORDER = "x0 x1 w0 x2 x3 w1 w2 w3 w4 w5"
 LOAD_ORDER = "xs x00 x01 a0 a1 a2 x10 a3 lam c x11 ws w0 x2 x3 b2 w1 b0 w2 b3 w3 b1 b4 w4 b5 w5"
 RUNS = (2, 1, 1, 1, 1, 1, 1, 2, 2, 2, 2, 2, 2)
 PLAIN_PASSES = 1
-ON_SCALAR = (2, 0, 2, 0, 0, 0, 1, 0, 2)
+ON_SCALAR = (2, 0, 2, 0, 0, 0, 1, 0, 1)
 BANKS = 8
 WIDE_BUFS, GROUP_BUFS, A_BUFS, B_BUFS, W_CODE_BUFS, H_BUFS, Y_BUFS = 6, 3, 4, 3, 6, 2, 6
 UP_AHEAD = 2
@@ -495,7 +495,7 @@ def tile_fp8_base_lora_d2_kernel(tc, x_bytes, x_scale, w_bytes, w_scale, a, lam,
         scalar = by_scalar(runs[0]) + each(empty, runs[0][:1]) + [(inter_a, 1, 0, 4, "s")] + each(empty, runs[0][1:2])
         scalar += by_scalar(runs[1]) + [(inter_a, 3, 2, 4, "s"), (cast_lam,)]
         late = []
-        side = {2: [(cast_c,)], 3: by_scalar(units[6:7]), 4: by_scalar(units[8:9])[:1], 5: by_scalar(units[8:9])[1:], 6: [(inter_b, 2)]}
+        side = {2: [(cast_c,)] + by_scalar(units[6:7]), 5: by_scalar(units[8:9]), 6: [(inter_b, 2)]}
         for n in range(1, len(runs)):
             mine = results(n, (scale_h, park, scale_d))
             ci = n - W_RUN

@@ -23,26 +23,23 @@ PASSES = K // 512
 K_BLOCKS = K // P
 WIDTH = 256
 CHUNKS = N // WIDTH
-PARKED = 2
+LAST = CHUNKS - 1
 PIECES = 4
+BANKS = 8
 
 ORDER = "x0 x1 w0 x2 x3 w1 w2 w3 w4 w5"
 LOAD_ORDER = "xs x00 x01 a0 a1 a2 x10 a3 lam c x11 ws w0 x2 x3 b2 w1 b0 w2 b3 w3 b1 b4 w4 b5 w5"
-RUNS = (2, 1, 1, 1, 1, 1, 1, 2, 2, 2, 2, 2, 2)
-PLAIN_PASSES = 1
-ON_SCALAR = (2, 0, 2, 0, 0, 0, 1, 0, 1)
-BANKS = 8
-WIDE_BUFS, GROUP_BUFS, A_BUFS, B_BUFS, W_CODE_BUFS, H_BUFS, Y_BUFS = 6, 3, 4, 3, 6, 2, 6
+SINGLES = 6
+ON_SCALAR = (2, 2, 1, 1)
+PARKED = 2
+UNPARK = {2: 0, 3: 2, 4: 3, 5: 3}
+B1_CHUNK = 4
 UP_AHEAD = 2
-UNPARK_FROM = 0
-HELD = 0
-W_RUN = 7
-LATE_TO = 0
-AT = 2
-UNPARK = (0, 3, 3, 2)
+WIDE_BUFS, GROUP_BUFS, B_BUFS, W_CODE_BUFS, H_BUFS, Y_BUFS = 6, 3, 3, 6, 2, 6
 CODE_AT = {"w": 0, "b": 0, "x": 64, "h": 64, "a": 128}
 SCALE_AT = {"w": 128, "b": 128, "x": 192, "h": 192, "a": 0}
 SCALE_ROW = {"w": 4, "b": 4, "x": 8, "h": 8, "a": 12}
+ENDING = ((PAIRS - 2, 0, 0, WIDTH), (PAIRS - 2, 1, 0, WIDTH), (PAIRS - 1, 0, 0, WIDTH), (PAIRS - 1, 1, 0, P), (PAIRS - 1, 1, P, WIDTH))
 
 
 def tile_fp8_base_lora_d2_kernel(tc, x_bytes, x_scale, w_bytes, w_scale, a, lam, b, c, out):
@@ -62,14 +59,16 @@ def tile_fp8_base_lora_d2_kernel(tc, x_bytes, x_scale, w_bytes, w_scale, a, lam,
                 return pool.tile(shape, dtype, name="%s%d" % (what, n % depth))
             return pool.tile(shape, dtype, name="%s%d" % (what, n % depth), align_bytes=64)
 
-        stores = {}
-        for what, (count, width) in {"x": (2 * PAIRS, 512), "w": (W_CODE_BUFS, 512), "a": (PASSES, R), "b": (CHUNKS, WIDTH), "h": (PAIRS, 2 * P)}.items():
+        slots = {"x": (2 * PAIRS, 512), "w": (W_CODE_BUFS, 512), "a": (PASSES, R), "b": (CHUNKS, WIDTH), "h": (PAIRS, 2 * P)}
+        operands = {}
+        for what, (count, width) in slots.items():
             words = codes.tile([P, CODE_AT[what] // 4 + count * width], U32, name="%s_codes" % what, align_bytes=256)
             plane = codes.tile([P, SCALE_AT[what] + count * width], U8, name="%s_scales" % what, align_bytes=256)
-            stores[what] = (words[:, CODE_AT[what] // 4 :], plane[SCALE_ROW[what] :, SCALE_AT[what] :])
+            operands[what] = (words[:, CODE_AT[what] // 4 :], plane[SCALE_ROW[what] :, SCALE_AT[what] :])
 
-        def mx_operand(what, index, width):
-            words, plane = stores[what]
+        def mx_slot(what, index):
+            words, plane = operands[what]
+            width = slots[what][1]
             return words[:, width * index : width * (index + 1)], plane[:, width * index : width * (index + 1)]
 
         ctx.enter_context(tc.manual_schedule())
@@ -78,7 +77,8 @@ def tile_fp8_base_lora_d2_kernel(tc, x_bytes, x_scale, w_bytes, w_scale, a, lam,
         a_view = a.rearrange("(g p j) r -> g p j r", p=P, j=4)
         b_view = b.rearrange("(p j) n -> p j n", j=4)
         out_view = out.rearrange("(p m) n -> p m n", m=TILES)
-        raw, a_raw, b_raw = {}, {}, {}
+        rows_of, blocks_of, a_raw, b_raw = {}, {}, {}, {}
+        last_chunk = "w%d" % LAST
 
         ident = const.tile([P, P], F32, name="ident")
         make_identity(nc, ident[:])
@@ -91,7 +91,15 @@ def tile_fp8_base_lora_d2_kernel(tc, x_bytes, x_scale, w_bytes, w_scale, a, lam,
         xs = const.tile([P, TILES * K_BLOCKS], F32, name="xs")
         lam_b = const.tile([P, 4], BF16, name="lam_b")
         c_b = const.tile([P, TILES], BF16, name="c_b")
-        ws = const.tile([P, (2 * CHUNKS - 1) * K_BLOCKS], F32, name="ws")
+        ws = const.tile([P, (2 * LAST - 1) * K_BLOCKS], F32, name="ws")
+        ws_last = const.tile([P, 2 * K_BLOCKS], F32, name="ws_last")
+
+        def load_rows(what, rows):
+            both = loads.tile([P, 2, K], U8, name="%s_bytes" % what, align_bytes=64)
+            nc.sync.dma_start(out=both[:], in_=rows)
+            for h in range(2):
+                rows_of[what, h] = both[:, :, K // 2 * h : K // 2 * (h + 1)]
+
         for what in LOAD_ORDER.split(" "):
             if what == "xs":
                 nc.sync.dma_start(out=xs[:], in_=x_scale.rearrange("(p m) j -> p (m j)", m=TILES))
@@ -101,12 +109,15 @@ def tile_fp8_base_lora_d2_kernel(tc, x_bytes, x_scale, w_bytes, w_scale, a, lam,
                 nc.sync.dma_start(out=c_b[:], in_=c.rearrange("(p m) -> p m", m=TILES))
             elif what == "ws":
                 for h in range(2):
-                    mine = w_scale[h : h + 2 * CHUNKS - 1, :].rearrange("i j -> (i j)")
+                    mine = w_scale[h : h + 2 * LAST - 1, :].rearrange("i j -> (i j)")
                     nc.sync.dma_start(out=ws[P // 2 * h : P // 2 * (h + 1), :], in_=mine.partition_broadcast(P // 2))
+            elif what == last_chunk:
+                nc.sync.dma_start(out=ws_last[:], in_=w_scale[2 * LAST :, :].rearrange("i j -> (i j)").partition_broadcast(P))
+                load_rows(what, w_bytes[N - WIDTH :, :].rearrange("(r p) k -> p r k", r=2))
             elif what[0] == "a":
                 g = int(what[1:])
                 a_raw[g] = loads.tile([P, 4, R], BF16, name="a_raw%d" % g, align_bytes=64)
-                if g < PLAIN_PASSES:
+                if g == 0:
                     nc.sync.dma_start(out=a_raw[g][:], in_=a_view[g])
                 else:
                     for u in range(2):
@@ -116,34 +127,31 @@ def tile_fp8_base_lora_d2_kernel(tc, x_bytes, x_scale, w_bytes, w_scale, a, lam,
                 b_raw[ci] = loads.tile([P, 4, WIDTH], BF16, name="b_raw%d" % ci, align_bytes=64)
                 nc.sync.dma_start(out=b_raw[ci][:], in_=b_view[:, :, WIDTH * ci : WIDTH * (ci + 1)])
             elif what[0] == "w":
-                idx = int(what[1:])
-                rows = w_bytes[WIDTH * idx : WIDTH * (idx + 1), :].rearrange("(p r) (j k) -> p r j k", r=2, k=P)
-                plain = 4 * PLAIN_PASSES
-                front = loads.tile([P, 2, plain, P], U8, name="%s_front" % what, align_bytes=64)
-                nc.sync.dma_start(out=front[:], in_=rows[:, :, :plain, :])
-                blocks = loads.tile([P, K_BLOCKS - plain, 2, P], U8, name="%s_bytes" % what, align_bytes=64)
+                ci = int(what[1:])
+                rows = w_bytes[WIDTH * ci : WIDTH * (ci + 1), :].rearrange("(p r) (j k) -> p r j k", r=2, k=P)
+                front = loads.tile([P, 2, 4, P], U8, name="%s_front" % what, align_bytes=64)
+                nc.sync.dma_start(out=front[:], in_=rows[:, :, :4, :])
+                rest = loads.tile([P, K_BLOCKS - 4, 2, P], U8, name="%s_bytes" % what, align_bytes=64)
                 for r in range(2):
-                    nc.sync.dma_start(out=blocks[:, :, r, :], in_=rows[:, r, plain:, :])
+                    nc.sync.dma_start(out=rest[:, :, r, :], in_=rows[:, r, 4:, :])
                 for j in range(K_BLOCKS):
-                    raw[what, j] = front[:, :, j, :] if j < plain else blocks[:, j - plain, :, :]
+                    blocks_of[what, j] = front[:, :, j, :] if j < 4 else rest[:, j - 4, :, :]
+            elif len(what) == 3:
+                j, h = int(what[1]), int(what[2])
+                rows_of[what[:2], h] = loads.tile([P, 2, K // 2], U8, name="%s_bytes" % what, align_bytes=64)
+                nc.sync.dma_start(out=rows_of[what[:2], h][:], in_=x_view[:, 2 * j : 2 * j + 2, K // 2 * h : K // 2 * (h + 1)])
             else:
-                idx = int(what[1])
-                rows = x_view[:, 2 * idx : 2 * idx + 2, :]
-                if len(what) == 3:
-                    h = int(what[2])
-                    raw[what[:2], h] = loads.tile([P, 2, K // 2], U8, name="%s_bytes" % what, align_bytes=64)
-                    nc.sync.dma_start(out=raw[what[:2], h][:], in_=rows[:, :, K // 2 * h : K // 2 * (h + 1)])
-                else:
-                    both = loads.tile([P, 2, K], U8, name="%s_bytes" % what, align_bytes=64)
-                    nc.sync.dma_start(out=both[:], in_=rows)
-                    for h in range(2):
-                        raw[what, h] = both[:, :, K // 2 * h : K // 2 * (h + 1)]
+                j = int(what[1])
+                load_rows(what, x_view[:, 2 * j : 2 * j + 2, :])
 
         lam_f = const.tile([P, 4], F32, name="lam_f")
         c_f = const.tile([P, TILES], F32, name="c_f")
 
         units = [(what, h) for what in ORDER.split(" ") for h in range(2)]
-        on_scalar = {unit: (ON_SCALAR[s] if s < len(ON_SCALAR) else 0) for s, unit in enumerate(units)}
+        w_units = [unit for unit in units if unit[0][0] == "w"]
+        on_scalar = {unit: 0 for unit in units}
+        for j in range(PAIRS):
+            on_scalar["x%d" % j, 0] = ON_SCALAR[j]
         wide, turned, grouped, unit_codes, unit_scales = {}, {}, {}, {}, {}
 
         def widen(unit, i):
@@ -151,42 +159,35 @@ def tile_fp8_base_lora_d2_kernel(tc, x_bytes, x_scale, w_bytes, w_scale, a, lam,
                 wide[unit] = work.tile([P, PIECES, 2, P, 2], BF16, name="wide%d" % (units.index(unit) % WIDE_BUFS), align_bytes=64)
             what, h = unit
             g, r = divmod(i, 2)
-            plain = 2 * h + g < PLAIN_PASSES
+            index = int(what[1:])
+            plain = h == 0 and g == 0
+            paired = what[0] == "w" and what != last_chunk
+            if paired and not plain and r == 1:
+                return
             for q in range(4):
-                j = 4 * g + q
-                paired = what[0] == "w"
-                first_row = 2 * int(what[1:])
-                at = K_BLOCKS * (first_row + (0 if paired else r)) + K_BLOCKS // 2 * h + j
-                scale = (ws if paired else xs)[:, at : at + 1]
+                j = K_BLOCKS // 2 * h + 4 * g + q
+                if paired:
+                    src, scales, at = blocks_of[what, j], ws, K_BLOCKS * 2 * index + j
+                else:
+                    src = rows_of[unit][:, :, P * (4 * g + q) : P * (4 * g + q + 1)]
+                    scales, at = (ws_last, K_BLOCKS * r + j) if what == last_chunk else (xs, K_BLOCKS * (2 * index + r) + j)
+                scale = scales[:, at : at + 1]
                 if paired and not plain:
-                    if r == 0:
-                        both = wide[unit][:, i : i + 2, :, :, :]
-                        src = raw[what, K_BLOCKS // 2 * h + j].bitcast(FP8)
-                        dst = both[:, :, :, 32 * q : 32 * (q + 1), :].rearrange("p r u w e -> p r (w e) u")
-                        src = src.rearrange("p r (m u) -> p r m u", u=2)
-                        nc.vector.tensor_scalar(out=dst, in0=src, scalar1=scale, scalar2=None, op0=MULT)
+                    dst = wide[unit][:, i : i + 2, :, 32 * q : 32 * (q + 1), :].rearrange("p r u w e -> p r (w e) u")
+                    src = src.bitcast(FP8).rearrange("p r (m u) -> p r m u", u=2)
+                    nc.vector.tensor_scalar(out=dst, in0=src, scalar1=scale, scalar2=None, op0=MULT)
                     continue
-                src = (raw[unit][:, r, P * j : P * (j + 1)] if not paired else raw[what, K_BLOCKS // 2 * h + j][:, r, :]).bitcast(FP8)
+                src = src[:, r, :].bitcast(FP8)
                 words = wide[unit][:, i, :, 32 * q : 32 * (q + 1), :]
                 if i < on_scalar[unit]:
                     flat = wide[unit][:, i, :, :, :].rearrange("p u w e -> p (u w e)")
                     nc.scalar.activation(out=flat[:, P * q : P * (q + 1)], in_=src, func=COPY, scale=scale)
                 elif plain:
-                    nc.vector.tensor_scalar(
-                        out=words.rearrange("p u w e -> p w u e"),
-                        in0=src.rearrange("p (w u e) -> p w u e", u=2, e=2),
-                        scalar1=scale,
-                        scalar2=None,
-                        op0=MULT,
-                    )
+                    dst, src = words.rearrange("p u w e -> p w u e"), src.rearrange("p (w u e) -> p w u e", u=2, e=2)
+                    nc.vector.tensor_scalar(out=dst, in0=src, scalar1=scale, scalar2=None, op0=MULT)
                 else:
-                    nc.vector.tensor_scalar(
-                        out=words.rearrange("p u w e -> p (w e) u"),
-                        in0=src.rearrange("p (m u) -> p m u", u=2),
-                        scalar1=scale,
-                        scalar2=None,
-                        op0=MULT,
-                    )
+                    dst, src = words.rearrange("p u w e -> p (w e) u"), src.rearrange("p (m u) -> p m u", u=2)
+                    nc.vector.tensor_scalar(out=dst, in0=src, scalar1=scale, scalar2=None, op0=MULT)
 
         def turn(unit, half):
             bank = ring(psum, "bank", BANKS, [P, 4, P], F32)
@@ -209,37 +210,28 @@ def tile_fp8_base_lora_d2_kernel(tc, x_bytes, x_scale, w_bytes, w_scale, a, lam,
                 in_=turned[unit, half][:].rearrange("p (i u) w -> p i w u", u=2),
             )
 
-        w_units = [unit for unit in units if unit[0][0] == "w"]
-
         def quant(unit):
-            kind = unit[0][0]
-            index = w_units.index(unit) % W_CODE_BUFS if kind == "w" else 2 * int(unit[0][1:]) + unit[1]
-            unit_codes[unit], unit_scales[unit] = mx_operand(kind, index, PIECES * P)
+            what, h = unit
+            index = w_units.index(unit) % W_CODE_BUFS if what[0] == "w" else 2 * int(what[1:]) + h
+            unit_codes[unit], unit_scales[unit] = mx_slot(what[0], index)
             nc.vector.quantize_mx(
-                out=unit_codes[unit].bitcast(FP8X4),
-                scales=unit_scales[unit],
-                in_=grouped[unit][:].rearrange("p i w t -> p (i w t)"),
+                out=unit_codes[unit].bitcast(FP8X4), scales=unit_scales[unit], in_=grouped[unit][:].rearrange("p i w t -> p (i w t)")
             )
 
         a_int, a_codes, a_scales = {}, {}, {}
         b_int, b_codes, b_scales = {}, {}, {}
 
-        def inter_a(g, t0, t1, on):
+        def inter_a(g, t0, t1, engine):
             if g not in a_int:
-                a_int[g] = ring(work, "a_int", A_BUFS, [P, 4, P, 4], BF16)
-            (nc.scalar.copy if on == "s" else nc.vector.tensor_copy)(
+                a_int[g] = ring(work, "a_int", PASSES, [P, 4, P, 4], BF16)
+            (nc.scalar.copy if engine == "scalar" else nc.vector.tensor_copy)(
                 out=a_int[g][:, t0:t1, :, :].rearrange("p t (q m) j -> p q t m j", m=2),
                 in_=a_raw[g][:].rearrange("p j (q m t) -> p q t m j", m=2, t=4)[:, :, t0:t1, :, :],
             )
 
-        def quant_a(g, t0, t1):
-            if t0 == 0:
-                a_codes[g], a_scales[g] = mx_operand("a", g, R)
-            nc.vector.quantize_mx(
-                out=a_codes[g][:, P * t0 : P * t1].bitcast(FP8X4),
-                scales=a_scales[g][:, P * t0 : P * t1],
-                in_=a_int[g][:, t0:t1, :, :].rearrange("p t m j -> p (t m j)"),
-            )
+        def quant_a(g):
+            a_codes[g], a_scales[g] = mx_slot("a", g)
+            nc.vector.quantize_mx(out=a_codes[g].bitcast(FP8X4), scales=a_scales[g], in_=a_int[g][:].rearrange("p t m j -> p (t m j)"))
 
         def inter_b(ci):
             b_int[ci] = ring(work, "b_int", B_BUFS, [P, WIDTH, 4], BF16)
@@ -248,10 +240,8 @@ def tile_fp8_base_lora_d2_kernel(tc, x_bytes, x_scale, w_bytes, w_scale, a, lam,
             )
 
         def quant_b(ci):
-            b_codes[ci], b_scales[ci] = mx_operand("b", ci, WIDTH)
-            nc.vector.quantize_mx(
-                out=b_codes[ci].bitcast(FP8X4), scales=b_scales[ci], in_=b_int[ci][:].rearrange("p n j -> p (n j)")
-            )
+            b_codes[ci], b_scales[ci] = mx_slot("b", ci)
+            nc.vector.quantize_mx(out=b_codes[ci].bitcast(FP8X4), scales=b_scales[ci], in_=b_int[ci][:].rearrange("p n j -> p (n j)"))
 
         h_banks, h_rows, h_int, h_codes, h_scales = {}, {}, {}, {}, {}
 
@@ -286,12 +276,10 @@ def tile_fp8_base_lora_d2_kernel(tc, x_bytes, x_scale, w_bytes, w_scale, a, lam,
             )
 
         def quant_h(j):
-            h_codes[j], h_scales[j] = mx_operand("h", j, 2 * P)
-            nc.vector.quantize_mx(
-                out=h_codes[j].bitcast(FP8X4), scales=h_scales[j], in_=h_int[j][:].rearrange("p w t -> p (w t)")
-            )
+            h_codes[j], h_scales[j] = mx_slot("h", j)
+            nc.vector.quantize_mx(out=h_codes[j].bitcast(FP8X4), scales=h_scales[j], in_=h_int[j][:].rearrange("p w t -> p (w t)"))
 
-        y, base_parts, d_banks = {}, {}, {}
+        y, base_banks, d_banks = {}, {}, {}
 
         def up(j, ci):
             d_banks[j, ci] = ring(psum, "bank", BANKS, [P, 2, WIDTH], F32)
@@ -308,13 +296,13 @@ def tile_fp8_base_lora_d2_kernel(tc, x_bytes, x_scale, w_bytes, w_scale, a, lam,
 
         def base(j, ci, h):
             if h == 0:
-                base_parts[j, ci] = ring(psum, "bank", BANKS, [P, 2, WIDTH], F32)
+                base_banks[j, ci] = ring(psum, "bank", BANKS, [P, 2, WIDTH], F32)
             tokens, rows = ("x%d" % j, h), ("w%d" % ci, h)
             for g in range(2):
                 for i in range(2):
                     at = 2 * P * g + P * i
                     nc.tensor.matmul_mx(
-                        out=base_parts[j, ci][:, i, :],
+                        out=base_banks[j, ci][:, i, :],
                         lhsT=unit_codes[tokens][:, at : at + P].bitcast(FP8X4),
                         lhsT_scale=unit_scales[tokens][:, at : at + P],
                         rhs=unit_codes[rows][:, WIDTH * g : WIDTH * (g + 1)].bitcast(FP8X4),
@@ -325,9 +313,9 @@ def tile_fp8_base_lora_d2_kernel(tc, x_bytes, x_scale, w_bytes, w_scale, a, lam,
 
         def base_part(j, i, n0, n1):
             bank = ring(psum, "bank", BANKS, [P, WIDTH], F32)
-            base_parts[j, i, n0] = bank
+            base_banks[j, i, n0] = bank
             for g in range(PASSES):
-                tokens, rows = ("x%d" % j, g // 2), ("w%d" % (CHUNKS - 1), g // 2)
+                tokens, rows = ("x%d" % j, g // 2), (last_chunk, g // 2)
                 at, c0 = 2 * P * (g % 2) + P * i, WIDTH * (g % 2)
                 nc.tensor.matmul_mx(
                     out=bank[:, n0:n1],
@@ -339,15 +327,16 @@ def tile_fp8_base_lora_d2_kernel(tc, x_bytes, x_scale, w_bytes, w_scale, a, lam,
                     stop=(g == PASSES - 1),
                 )
 
-        def park(j, ci):
-            y[j, ci] = const.tile([P, 2, WIDTH], F32, name="parked%d_%d" % (j, ci), align_bytes=64)
-            nc.scalar.copy(
-                out=y[j, ci][:].rearrange("p i (c r) -> p i c r", r=2),
-                in_=base_parts[j, ci][:].rearrange("p i (r c) -> p i c r", r=2),
-            )
+        def in_order(j, ci):
+            order = "p i (c r) -> p i c r" if ci == LAST else "p i (r c) -> p i c r"
+            return base_banks[j, ci][:].rearrange(order, r=2)
 
         def store(j, ci):
             nc.sync.dma_start(out=out_view[:, 2 * j : 2 * j + 2, WIDTH * ci : WIDTH * (ci + 1)], in_=y[j, ci][:])
+
+        def park(j, ci):
+            y[j, ci] = const.tile([P, 2, WIDTH], F32, name="parked%d_%d" % (j, ci), align_bytes=64)
+            nc.scalar.copy(out=y[j, ci][:].rearrange("p i (c r) -> p i c r", r=2), in_=in_order(j, ci))
 
         def finish_parked(j, ci):
             for i in range(2):
@@ -365,14 +354,13 @@ def tile_fp8_base_lora_d2_kernel(tc, x_bytes, x_scale, w_bytes, w_scale, a, lam,
 
         def add(j, ci):
             pairs = y[j, ci][:].rearrange("p i (c r) -> p i c r", r=2)
-            nc.vector.tensor_tensor(out=pairs, in0=base_parts[j, ci][:].rearrange("p i (r c) -> p i c r", r=2), in1=pairs, op=ADD)
+            nc.vector.tensor_tensor(out=pairs, in0=in_order(j, ci), in1=pairs, op=ADD)
             store(j, ci)
 
         def add_part(j, i, n0, n1):
-            mine = y[j, CHUNKS - 1][:, i, :]
-            pairs = mine.rearrange("p (c r) -> p c r", r=2)
-            nc.vector.tensor_tensor(out=pairs, in0=base_parts[j, i, n0][:].rearrange("p (r c) -> p c r", r=2), in1=pairs, op=ADD)
-            nc.sync.dma_start(out=out_view[:, 2 * j + i, N - WIDTH :], in_=mine)
+            mine = y[j, LAST][:, i, n0:n1]
+            nc.vector.tensor_tensor(out=mine, in0=base_banks[j, i, n0][:, n0:n1], in1=mine, op=ADD)
+            nc.sync.dma_start(out=out_view[:, 2 * j + i, N - WIDTH + n0 : N - WIDTH + n1], in_=mine)
 
         def cast_lam():
             nc.scalar.activation(out=lam_f[:], in_=lam_b[:], func=COPY)
@@ -392,57 +380,32 @@ def tile_fp8_base_lora_d2_kernel(tc, x_bytes, x_scale, w_bytes, w_scale, a, lam,
         def by_scalar(some_units):
             return [(widen, unit, i) for unit in some_units for i in range(on_scalar[unit])]
 
-        def weave(results, pieces):
-            steps = []
-            for n, result_steps in enumerate(results):
-                steps += result_steps + pieces[n * len(pieces) // len(results) : (n + 1) * len(pieces) // len(results)]
-            return steps
+        def downs(j, h):
+            return [(down, j, side, h) for side in range(2)]
 
-        runs = [units[sum(RUNS[:n]) : sum(RUNS[: n + 1])] for n in range(len(RUNS))]
+        def bases(pairs, ci, h):
+            return [(base, j, ci, h) for j in pairs]
 
-        def downs(j):
-            return [(down, j, side, h) for h in range(2) for side in range(2)]
-
-        ending = [(j, i, 0, WIDTH) for j in range(PAIRS - 2, PAIRS) for i in range(2)]
-
-        def bases(ci, h, j0, j1):
-            return [(base, j, ci, h) for j in range(j0, j1)]
-
-        def whole(ci, j0, j1):
-            return [step for j in range(j0, j1) for step in halves(base, j, ci)]
-
-        after = [
-            downs(0)[:2],
-            downs(0)[2:],
-            downs(1)[:2],
-            downs(1)[2:],
-            bases(0, 0, 0, 2),
-            bases(0, 1, 0, 2),
-            downs(2)[:2] + bases(0, 0, 2, 3),
-            downs(2)[2:] + bases(0, 1, 2, 3) + downs(3)[:2],
-            downs(3)[2:] + whole(0, 3, 4) + whole(1, 0, 2),
-        ]
+        runs = [units[:2]] + [[unit] for unit in units[2 : 2 + SINGLES]]
+        runs += [units[s : s + 2] for s in range(2 + SINGLES, len(units), 2)]
+        run_of = {ci: runs.index([("w%d" % ci, 0), ("w%d" % ci, 1)]) for ci in range(1, CHUNKS)}
+        after = [downs(0, 0), downs(0, 1), downs(1, 0), downs(1, 1), bases((0, 1), 0, 0), bases((0, 1), 0, 1)]
+        after += [downs(2, 0) + bases((2,), 0, 0), downs(2, 1) + bases((2,), 0, 1) + downs(3, 0)]
+        after += [downs(3, 1) + halves(base, 3, 0) + halves(base, 0, 1) + halves(base, 1, 1)]
         products = [(j, ci) for ci in range(CHUNKS) for j in range(PAIRS)]
         parked = products[: PARKED * PAIRS]
-        unparked = {}
+        waiting = list(parked)
         for ci in range(PARKED, CHUNKS):
-            done = sum(UNPARK[: ci - PARKED])
-            unparked[ci] = parked[done : done + UNPARK[ci - PARKED]]
+            first = PAIRS * ci - 2
             steps = []
-            last = PAIRS * ci + 2 if ci + 1 < CHUNKS else len(products)
-            for n in range(PAIRS * ci - 2, last):
-                j, chunk = products[n]
-                if chunk == CHUNKS - 1 and j >= PAIRS - 2:
-                    steps += [(base_part,) + part for part in ending if part[0] == j]
-                else:
-                    steps += whole(chunk, j, j + 1)
-                if n + UP_AHEAD < len(products) and products[n + UP_AHEAD] not in parked:
+            for n in range(first, first + PAIRS if ci < LAST else len(products)):
+                parts = [(base_part,) + part for part in ENDING if (part[0], LAST) == products[n]]
+                steps += parts if parts else halves(base, *products[n])
+                if n + UP_AHEAD < len(products):
                     steps += [(up,) + products[n + UP_AHEAD]]
-                slot = n - (PAIRS * ci - 2) - UNPARK_FROM
-                if slot >= 0:
-                    steps += [(up,) + product for product in unparked[ci][slot : slot + 1]]
+                if n - first < UNPARK[ci]:
+                    steps += [(up,) + waiting.pop(0)]
             after.append(steps)
-
         tensor = []
         for n, run in enumerate(runs):
             tensor += each(turn, run) + after[n]
@@ -461,101 +424,95 @@ def tile_fp8_base_lora_d2_kernel(tc, x_bytes, x_scale, w_bytes, w_scale, a, lam,
             done = [step for step in after[n] if step[0] in (up, base_part) or step[-1] == 1]
             return [reader(step) for step in done if reader(step)[0] in fns]
 
-        def alternate(first, second):
-            return [step for k in range(max(len(first), len(second))) for step in first[k : k + 1] + second[k : k + 1]]
-
-        held = []
-        vector = by_vector(runs[0]) + [(inter_a, 0, 0, 4, "v"), (quant, units[0]), (quant_a, 0, 0, 4)]
-        vector += [(inter_a, 2, 0, 4, "v"), (quant_a, 1, 0, 4)] + by_vector(runs[1]) + [(quant, units[1]), (inter_a, 3, 0, 2, "v")]
-        vector += [(quant_a, 2, 0, 4), (quant_a, 3, 0, 4)]
+        vector = by_vector(runs[0]) + [(inter_a, 0, 0, 4, "vector"), (quant, units[0]), (quant_a, 0)]
+        vector += [(inter_a, 2, 0, 4, "vector"), (quant_a, 1)] + by_vector(runs[1]) + [(quant, units[1])]
+        vector += [(inter_a, 3, 0, 2, "vector"), (quant_a, 2), (quant_a, 3)]
         for n in range(1, len(runs)):
-            nxt = by_vector(runs[n + 1]) if n + 1 < len(runs) else []
-            first, second = [(quant, unit) for unit in runs[n]][:1], [(quant, unit) for unit in runs[n]][1:]
-            ci = n - W_RUN
-            if RUNS[n] == 1:
-                vector += nxt[:4] + first + nxt[4:]
-            elif ci < 1:
-                vector += nxt[:4] + first + nxt[4:6] + second + nxt[6:]
-            elif ci == 1:
-                vector += nxt[:4] + first + nxt[4:6] + second + [(inter_h, 0), (inter_h, 1), (quant_h, 0), (quant_b, 2), (quant_h, 1)] + nxt[6:]
-            elif ci == 2:
-                vector += nxt[:4] + first + [(inter_h, 2)] + second + [(quant_h, 2), (inter_h, 3)] + nxt[4:6] + [(quant_h, 3), (add, 0, ci)] + nxt[6:] + [(quant_b, 3), (quant_b, 0)]
+            ahead = by_vector(runs[n + 1]) if n + 1 < len(runs) else []
+            lead, more, rest = ahead[:PIECES], ahead[PIECES : PIECES + 2], ahead[PIECES + 2 :]
+            one, two = [(quant, runs[n][0])], [(quant, unit) for unit in runs[n][1:]]
+            if n < run_of[1]:
+                vector += lead + one + more + two + rest
+            elif n == run_of[1]:
+                vector += lead + one + more + two + [(inter_h, 0), (inter_h, 1), (quant_h, 0), (quant_b, 2), (quant_h, 1)] + rest
+            elif n == run_of[2]:
+                vector += lead + one + [(inter_h, 2)] + two + [(quant_h, 2), (inter_h, 3)] + more + [(quant_h, 3), (add, 0, 2)]
+                vector += rest + [(quant_b, 3), (quant_b, 0)]
             else:
-                rest = results(n, (finish_parked, add, add_part))
-                late_b = [(quant_b, 1)] if ci == 3 else []
-                vector += [(add, 1, ci - 1)] + held + nxt[:4] + first + rest[:1] + nxt[4:6] + second + late_b
-                rest = rest[1:]
-                if ci + 1 < CHUNKS:
-                    rest.remove((add, 1, ci))
-                    vector += rest[:1] + nxt[6:] + rest[1:2] + [(quant_b, ci + 1)] + rest[2 : len(rest) - HELD]
-                    held = rest[len(rest) - HELD :]
+                ci = n - run_of[1] + 1
+                sums = results(n, (finish_parked, add, add_part))
+                vector += [(add, 1, ci - 1)] + lead + one + sums[:1] + more + two
+                if ci == B1_CHUNK:
+                    vector += [(quant_b, 1)]
+                if ci < LAST:
+                    vector += sums[1:2] + rest + sums[2:3] + [(quant_b, ci + 1)] + sums[3:-1]
                 else:
-                    vector += rest
+                    vector += sums[1:]
 
-        scalar = by_scalar(runs[0]) + each(empty, runs[0][:1]) + [(inter_a, 1, 0, 4, "s")] + each(empty, runs[0][1:2])
-        scalar += by_scalar(runs[1]) + [(inter_a, 3, 2, 4, "s"), (cast_lam,)]
+        scalar = by_scalar(runs[0]) + halves(empty, units[0]) + [(inter_a, 1, 0, 4, "scalar")] + halves(empty, units[1])
+        scalar += by_scalar(runs[1]) + [(inter_a, 3, 2, 4, "scalar"), (cast_lam,)]
+        extra = {2: [(cast_c,)] + by_scalar([("x2", 0)]), 5: by_scalar([("x3", 0)]), SINGLES: [(inter_b, 2)]}
         late = []
-        side = {2: [(cast_c,)] + by_scalar(units[6:7]), 5: by_scalar(units[8:9]), 6: [(inter_b, 2)]}
-        for n in range(1, len(runs)):
-            mine = results(n, (scale_h, park, scale_d))
-            ci = n - W_RUN
-            if ci < 1:
-                keep = len(mine) - (1 if RUNS[n] == 1 and len(mine) == 2 else 0)
-                scalar += each(empty, runs[n]) + late + side.get(n, []) + mine[:keep]
-                late = mine[keep:]
+        for n in range(1, run_of[1]):
+            mine = results(n, (scale_h, park))
+            keep = 1 if n <= SINGLES else len(mine)
+            scalar += each(empty, runs[n]) + late + extra.get(n, []) + mine[:keep]
+            late = mine[keep:]
+        for ci in range(1, CHUNKS):
+            mine = results(run_of[ci], (scale_h, park, scale_d))
+            scalar += each(empty, runs[run_of[ci]])
+            if ci == B1_CHUNK:
+                scalar += [(inter_b, 1)]
+            if ci == 1:
+                scalar += mine[:1] + [(inter_b, 0)] + mine[1:]
+            elif ci < LAST:
+                scalar += mine[:-2] + [(inter_b, ci + 1)] + mine[-2:]
             else:
-                early = [(inter_b, 1)] if ci == 3 else []
-                nxt = [(inter_b, ci + 1 if ci > 1 else 0)] if ci + 1 < CHUNKS else []
-                keep = len(mine) - (1 if PARKED <= ci < LATE_TO else 0)
-                at = 1 if ci == 1 else len(mine) - AT
-                scalar += each(empty, runs[n]) + late + early + mine[:at] + nxt + mine[at:keep]
-                late = mine[keep:]
+                scalar += mine
 
         bank_users = [step for step in tensor if step[0] in (turn, up, base_part) or step[-1] == 0]
         y_users = [step for step in scalar if step[0] == scale_d]
         b_users = [step for step in scalar if step[0] == inter_b]
 
+        def before(users, step, depth):
+            n = users.index(step) if step in users else 0
+            return users[n - depth : n - depth + 1] if n >= depth else []
+
         def needs(step):
             fn, args = step[0], step[1:]
-            n = bank_users.index(step) if step in bank_users else 0
-            bank = [reader(bank_users[n - BANKS])] if n >= BANKS else []
+            bank = [reader(old) for old in before(bank_users, step, BANKS)]
             if fn == widen:
-                s = units.index(args[0])
-                return halves(turn, units[s - WIDE_BUFS]) if s >= WIDE_BUFS else []
+                return each(turn, before(units, args[0], WIDE_BUFS))
             if fn == turn:
                 return [(widen, args[0], 2 * args[1]), (widen, args[0], 2 * args[1] + 1)] + bank
             if fn == empty:
-                s = units.index(args[0])
-                return [(turn,) + args] + ([(quant, units[s - GROUP_BUFS])] if s >= GROUP_BUFS else [])
+                return [(turn,) + args] + [(quant, old) for old in before(units, args[0], GROUP_BUFS)]
             if fn == quant:
-                s = w_units.index(args[0]) if args[0] in w_units else 0
-                old = w_units[s - W_CODE_BUFS]
-                return halves(empty, args[0]) + ([(base, PAIRS - 1, int(old[0][1:]), old[1])] if s >= W_CODE_BUFS else [])
+                freed = [(base, PAIRS - 1, int(old[0][1:]), old[1]) for old in before(w_units, args[0], W_CODE_BUFS)]
+                return halves(empty, args[0]) + freed
             if fn == quant_a:
-                return [s for s in vector + scalar if s[:2] == (inter_a, args[0]) and s[2] < args[2] and args[1] < s[3]]
+                return [other for other in vector + scalar if other[:2] == (inter_a, args[0])]
             if fn == inter_b:
-                n = b_users.index(step)
-                return [(quant_b, b_users[n - B_BUFS][1])] if n >= B_BUFS else []
+                return [(quant_b, old[1]) for old in before(b_users, step, B_BUFS)]
             if fn == quant_b:
                 return [(inter_b,) + args]
             if fn == down:
                 j, side, h = args
-                return bank + [(quant, ("x%d" % j, h))] + [s for s in vector if s[0] == quant_a and s[1] // 2 == h and s[2] <= 2 * side < s[3]]
+                return bank + [(quant, ("x%d" % j, h)), (quant_a, 2 * h), (quant_a, 2 * h + 1)]
             if fn == scale_h:
                 return [(down,) + args + (1,), (cast_lam,)]
             if fn == inter_h:
-                return halves(scale_h, args[0]) + ([(quant_h, args[0] - H_BUFS)] if args[0] >= H_BUFS else [])
+                return halves(scale_h, args[0]) + [(quant_h, old) for old in before(list(range(PAIRS)), args[0], H_BUFS)]
             if fn == quant_h:
                 return [(inter_h,) + args]
             if fn == up:
                 return bank + [(quant_h, args[0]), (quant_b, args[1])]
             if fn == scale_d:
-                n = y_users.index(step)
-                return [(up,) + args, (cast_c,)] + ([(add,) + y_users[n - Y_BUFS][1:]] if n >= Y_BUFS else [])
+                return [(up,) + args, (cast_c,)] + [(add,) + old[1:] for old in before(y_users, step, Y_BUFS)]
             if fn == base:
                 return bank + [(quant, ("x%d" % args[0], args[2])), (quant, ("w%d" % args[1], args[2]))]
             if fn == base_part:
-                return bank + [(quant, ("w%d" % (CHUNKS - 1), 1))]
+                return bank + [(quant, (last_chunk, 1))]
             if fn == park:
                 return [(base,) + args + (1,)]
             if fn == finish_parked:
@@ -563,7 +520,7 @@ def tile_fp8_base_lora_d2_kernel(tc, x_bytes, x_scale, w_bytes, w_scale, a, lam,
             if fn == add:
                 return [(base,) + args + (1,), (scale_d,) + args]
             if fn == add_part:
-                return [(base_part,) + args, (scale_d, args[0], CHUNKS - 1)]
+                return [(base_part,) + args, (scale_d, args[0], LAST)]
             return []
 
         written = set()

@@ -18,28 +18,17 @@ ADD = mybir.AluOpType.add
 COPY = mybir.ActivationFunctionType.Copy
 
 TILES = T // P
-PAIRS = TILES // 2
 PASSES = K // 512
 K_BLOCKS = K // P
-WIDTH = 256
+WIDTH = 512
 CHUNKS = N // WIDTH
-LAST = CHUNKS - 1
-PIECES = 4
-BANKS = 8
-
-ORDER = "x0 x1 w0 x2 x3 w1 w2 w3 w4 w5"
-LOAD_ORDER = "xs x00 x01 a0 a1 a2 x10 a3 lam c x11 ws w0 x2 x3 b2 w1 b0 w2 b3 w3 b1 b4 w4 b5 w5"
-SINGLES = 6
-ON_SCALAR = (2, 2, 1, 1)
-PARKED = 2
-UNPARK = {2: 0, 3: 2, 4: 3, 5: 3}
-B1_CHUNK = 4
-UP_AHEAD = 2
-WIDE_BUFS, GROUP_BUFS, B_BUFS, W_CODE_BUFS, H_BUFS, Y_BUFS = 6, 3, 3, 6, 2, 6
 CODE_AT = {"w": 0, "b": 0, "x": 64, "h": 64, "a": 128}
 SCALE_AT = {"w": 128, "b": 128, "x": 192, "h": 192, "a": 0}
 SCALE_ROW = {"w": 4, "b": 4, "x": 8, "h": 8, "a": 12}
-ENDING = ((PAIRS - 2, 0, 0, WIDTH), (PAIRS - 2, 1, 0, WIDTH), (PAIRS - 1, 0, 0, WIDTH), (PAIRS - 1, 1, 0, P), (PAIRS - 1, 1, P, WIDTH))
+LOAD_ORDER = "xs x001 ws w001 x012 w012 x024 w024 t4 t6 a0 a1 a2 a3 lam c w102 w124 b0 b1 w202 w224 b2"
+PLAIN = 4
+WIDE_BUFS, GROUP_BUFS, INTER_BUFS = 5, 3, 4
+BANKS = 8
 
 
 def tile_fp8_base_lora_d2_kernel(tc, x_bytes, x_scale, w_bytes, w_scale, a, lam, b, c, out):
@@ -50,35 +39,31 @@ def tile_fp8_base_lora_d2_kernel(tc, x_bytes, x_scale, w_bytes, w_scale, a, lam,
         loads = ctx.enter_context(tc.tile_pool(name="loads", bufs=1))
         work = ctx.enter_context(tc.tile_pool(name="work", bufs=1))
         psum = ctx.enter_context(tc.psum_pool(name="psum", bufs=1))
-        taken = {}
 
-        def ring(pool, what, depth, shape, dtype):
-            n = taken.get(what, 0)
-            taken[what] = n + 1
-            if pool == psum:
-                return pool.tile(shape, dtype, name="%s%d" % (what, n % depth))
-            return pool.tile(shape, dtype, name="%s%d" % (what, n % depth), align_bytes=64)
-
-        slots = {"x": (2 * PAIRS, 512), "w": (W_CODE_BUFS, 512), "a": (PASSES, R), "b": (CHUNKS, WIDTH), "h": (PAIRS, 2 * P)}
+        slots = {"x": 2 * PASSES, "w": CHUNKS * PASSES, "a": PASSES, "b": CHUNKS, "h": 2}
         operands = {}
-        for what, (count, width) in slots.items():
-            words = codes.tile([P, CODE_AT[what] // 4 + count * width], U32, name="%s_codes" % what, align_bytes=256)
-            plane = codes.tile([P, SCALE_AT[what] + count * width], U8, name="%s_scales" % what, align_bytes=256)
+        for what, count in slots.items():
+            words = codes.tile([P, CODE_AT[what] // 4 + count * 512], U32, name="%s_codes" % what, align_bytes=256)
+            plane = codes.tile([P, SCALE_AT[what] + count * 512], U8, name="%s_scales" % what, align_bytes=256)
             operands[what] = (words[:, CODE_AT[what] // 4 :], plane[SCALE_ROW[what] :, SCALE_AT[what] :])
 
-        def mx_slot(what, index):
+        def mx(what, slot, n0=0, n1=512):
             words, plane = operands[what]
-            width = slots[what][1]
-            return words[:, width * index : width * (index + 1)], plane[:, width * index : width * (index + 1)]
+            return words[:, 512 * slot + n0 : 512 * slot + n1].bitcast(FP8X4), plane[:, 512 * slot + n0 : 512 * slot + n1]
+
+        def product(dst, fixed, moving, start, stop):
+            nc.tensor.matmul_mx(out=dst, lhsT=fixed[0], lhsT_scale=fixed[1], rhs=moving[0], rhs_scale=moving[1], start=start, stop=stop)
+
+        def quantize(dst, src):
+            nc.vector.quantize_mx(out=dst[0], scales=dst[1], in_=src)
 
         ctx.enter_context(tc.manual_schedule())
 
         x_view = x_bytes.rearrange("(p m) k -> p m k", m=TILES)
+        w_view = w_bytes.rearrange("(c p r) k -> c p r k", p=P, r=4)
         a_view = a.rearrange("(g p j) r -> g p j r", p=P, j=4)
         b_view = b.rearrange("(p j) n -> p j n", j=4)
         out_view = out.rearrange("(p m) n -> p m n", m=TILES)
-        rows_of, blocks_of, a_raw, b_raw = {}, {}, {}, {}
-        last_chunk = "w%d" % LAST
 
         ident = const.tile([P, P], F32, name="ident")
         make_identity(nc, ident[:])
@@ -89,278 +74,204 @@ def tile_fp8_base_lora_d2_kernel(tc, x_bytes, x_scale, w_bytes, w_scale, a, lam,
         nc.scalar.activation(out=unread[:], in_=seed[:], func=COPY)
 
         xs = const.tile([P, TILES * K_BLOCKS], F32, name="xs")
+        ws_all = const.tile([P, 4 * CHUNKS * K_BLOCKS], F32, name="ws_all")
+        ws = const.tile([P, CHUNKS, K_BLOCKS], F32, name="ws")
         lam_b = const.tile([P, 4], BF16, name="lam_b")
         c_b = const.tile([P, TILES], BF16, name="c_b")
-        ws = const.tile([P, (2 * LAST - 1) * K_BLOCKS], F32, name="ws")
-        ws_last = const.tile([P, 2 * K_BLOCKS], F32, name="ws_last")
-
-        def load_rows(what, rows):
-            both = loads.tile([P, 2, K], U8, name="%s_bytes" % what, align_bytes=64)
-            nc.sync.dma_start(out=both[:], in_=rows)
-            for h in range(2):
-                rows_of[what, h] = both[:, :, K // 2 * h : K // 2 * (h + 1)]
+        lam_f = const.tile([P, 4], F32, name="lam_f")
+        c_f = const.tile([P, TILES], F32, name="c_f")
+        rows, a_raw, b_raw = {}, {}, {}
 
         for what in LOAD_ORDER.split(" "):
             if what == "xs":
                 nc.sync.dma_start(out=xs[:], in_=x_scale.rearrange("(p m) j -> p (m j)", m=TILES))
+            elif what == "ws":
+                nc.sync.dma_start(out=ws_all[:], in_=w_scale.rearrange("i j -> (i j)").partition_broadcast(P))
             elif what == "lam":
                 nc.sync.dma_start(out=lam_b[:], in_=lam.rearrange("(p t) -> p t", t=4))
             elif what == "c":
                 nc.sync.dma_start(out=c_b[:], in_=c.rearrange("(p m) -> p m", m=TILES))
-            elif what == "ws":
-                for h in range(2):
-                    mine = w_scale[h : h + 2 * LAST - 1, :].rearrange("i j -> (i j)")
-                    nc.sync.dma_start(out=ws[P // 2 * h : P // 2 * (h + 1), :], in_=mine.partition_broadcast(P // 2))
-            elif what == last_chunk:
-                nc.sync.dma_start(out=ws_last[:], in_=w_scale[2 * LAST :, :].rearrange("i j -> (i j)").partition_broadcast(P))
-                load_rows(what, w_bytes[N - WIDTH :, :].rearrange("(r p) k -> p r k", r=2))
             elif what[0] == "a":
-                g = int(what[1:])
+                g = int(what[1])
                 a_raw[g] = loads.tile([P, 4, R], BF16, name="a_raw%d" % g, align_bytes=64)
-                if g == 0:
+                if g < PLAIN:
                     nc.sync.dma_start(out=a_raw[g][:], in_=a_view[g])
                 else:
                     for u in range(2):
                         nc.sync.dma_start(out=a_raw[g][:, 2 * u : 2 * u + 2, :], in_=a_view[g][:, u::2, :])
             elif what[0] == "b":
-                ci = int(what[1:])
+                ci = int(what[1])
                 b_raw[ci] = loads.tile([P, 4, WIDTH], BF16, name="b_raw%d" % ci, align_bytes=64)
                 nc.sync.dma_start(out=b_raw[ci][:], in_=b_view[:, :, WIDTH * ci : WIDTH * (ci + 1)])
-            elif what[0] == "w":
-                ci = int(what[1:])
-                rows = w_bytes[WIDTH * ci : WIDTH * (ci + 1), :].rearrange("(p r) (j k) -> p r j k", r=2, k=P)
-                front = loads.tile([P, 2, 4, P], U8, name="%s_front" % what, align_bytes=64)
-                nc.sync.dma_start(out=front[:], in_=rows[:, :, :4, :])
-                rest = loads.tile([P, K_BLOCKS - 4, 2, P], U8, name="%s_bytes" % what, align_bytes=64)
-                for r in range(2):
-                    nc.sync.dma_start(out=rest[:, :, r, :], in_=rows[:, r, 4:, :])
-                for j in range(K_BLOCKS):
-                    blocks_of[what, j] = front[:, :, j, :] if j < 4 else rest[:, j - 4, :, :]
-            elif len(what) == 3:
-                j, h = int(what[1]), int(what[2])
-                rows_of[what[:2], h] = loads.tile([P, 2, K // 2], U8, name="%s_bytes" % what, align_bytes=64)
-                nc.sync.dma_start(out=rows_of[what[:2], h][:], in_=x_view[:, 2 * j : 2 * j + 2, K // 2 * h : K // 2 * (h + 1)])
+            elif what[0] == "t":
+                m = int(what[1])
+                both = loads.tile([P, 2, K], U8, name="%s_bytes" % what, align_bytes=64)
+                nc.sync.dma_start(out=both[:], in_=x_view[:, m : m + 2, :])
+                for i in range(2):
+                    rows["t", m + i] = both[:, i, :].rearrange("p (g k) -> p g k", g=PASSES)
             else:
-                j = int(what[1])
-                load_rows(what, x_view[:, 2 * j : 2 * j + 2, :])
+                index, g0, g1 = int(what[1]), int(what[2]), int(what[3])
+                four = x_view[:, :4, :] if what[0] == "x" else w_view[index]
+                part = loads.tile([P, 4, 512 * (g1 - g0)], U8, name="%s_bytes" % what, align_bytes=64)
+                step = 2 if what == "x001" else 4
+                for r in range(0, 4, step):
+                    nc.sync.dma_start(out=part[:, r : r + step, :], in_=four[:, r : r + step, 512 * g0 : 512 * g1])
+                for g in range(g0, g1):
+                    rows[what[0], PASSES * index + g] = part[:, :, 512 * (g - g0) : 512 * (g - g0 + 1)]
 
-        lam_f = const.tile([P, 4], F32, name="lam_f")
-        c_f = const.tile([P, TILES], F32, name="c_f")
+        wide, grouped, inter, h_rows, y, banks = {}, {}, {}, {}, {}, {}
 
-        units = [(what, h) for what in ORDER.split(" ") for h in range(2)]
-        w_units = [unit for unit in units if unit[0][0] == "w"]
-        on_scalar = {unit: 0 for unit in units}
-        for j in range(PAIRS):
-            on_scalar["x%d" % j, 0] = ON_SCALAR[j]
-        wide, turned, grouped, unit_codes, unit_scales = {}, {}, {}, {}, {}
+        def bank(step, shape):
+            banks[step] = psum.tile(shape, F32, name="bank%d" % bank_of[step])
+            return banks[step]
+
+        def pick_scales():
+            for q in range(4):
+                mine = ws_all[32 * q : 32 * (q + 1), :].rearrange("p (c q j) -> p c q j", q=4, j=K_BLOCKS)
+                nc.scalar.copy(out=ws[32 * q : 32 * (q + 1), :, :], in_=mine[:, :, q, :])
 
         def widen(unit, i):
             if unit not in wide:
-                wide[unit] = work.tile([P, PIECES, 2, P, 2], BF16, name="wide%d" % (units.index(unit) % WIDE_BUFS), align_bytes=64)
-            what, h = unit
-            g, r = divmod(i, 2)
-            index = int(what[1:])
-            plain = h == 0 and g == 0
-            paired = what[0] == "w" and what != last_chunk
-            if paired and not plain and r == 1:
-                return
-            for q in range(4):
-                j = K_BLOCKS // 2 * h + 4 * g + q
-                if paired:
-                    src, scales, at = blocks_of[what, j], ws, K_BLOCKS * 2 * index + j
+                wide[unit] = work.tile([P, 4, 2, P, 2], BF16, name="wide%d" % (units.index(unit) % WIDE_BUFS), align_bytes=64)
+            kind, index = unit
+            if kind == "w":
+                ci, g = divmod(index, PASSES)
+                scale = ws[:, ci, 4 * g + i : 4 * g + i + 1]
+                src = rows[unit][:, :, P * i : P * (i + 1)].bitcast(FP8)
+                dst = wide[unit][:, :, :, 32 * i : 32 * (i + 1), :]
+                if g < PLAIN:
+                    for u in range(2):
+                        nc.vector.tensor_scalar(
+                            out=dst[:, :, u, :, :],
+                            in0=src.rearrange("p r (w u e) -> p r u w e", u=2, e=2)[:, :, u, :, :],
+                            scalar1=scale,
+                            scalar2=None,
+                            op0=MULT,
+                        )
                 else:
-                    src = rows_of[unit][:, :, P * (4 * g + q) : P * (4 * g + q + 1)]
-                    scales, at = (ws_last, K_BLOCKS * r + j) if what == last_chunk else (xs, K_BLOCKS * (2 * index + r) + j)
-                scale = scales[:, at : at + 1]
-                if paired and not plain:
-                    dst = wide[unit][:, i : i + 2, :, 32 * q : 32 * (q + 1), :].rearrange("p r u w e -> p r (w e) u")
-                    src = src.bitcast(FP8).rearrange("p r (m u) -> p r m u", u=2)
-                    nc.vector.tensor_scalar(out=dst, in0=src, scalar1=scale, scalar2=None, op0=MULT)
-                    continue
-                src = src[:, r, :].bitcast(FP8)
-                words = wide[unit][:, i, :, 32 * q : 32 * (q + 1), :]
-                if i < on_scalar[unit]:
+                    nc.vector.tensor_scalar(
+                        out=dst.rearrange("p r u w e -> p r u (w e)"),
+                        in0=src.rearrange("p r (m u) -> p r u m", u=2),
+                        scalar1=scale,
+                        scalar2=None,
+                        op0=MULT,
+                    )
+                return
+            m, g = (i, index) if kind == "x" else (index, i)
+            for q in range(4):
+                scale = xs[:, K_BLOCKS * m + 4 * g + q : K_BLOCKS * m + 4 * g + q + 1]
+                src = rows[unit][:, i, P * q : P * (q + 1)].bitcast(FP8)
+                dst = wide[unit][:, i, :, 32 * q : 32 * (q + 1), :]
+                if (unit, i) in on_scalar:
                     flat = wide[unit][:, i, :, :, :].rearrange("p u w e -> p (u w e)")
                     nc.scalar.activation(out=flat[:, P * q : P * (q + 1)], in_=src, func=COPY, scale=scale)
-                elif plain:
-                    dst, src = words.rearrange("p u w e -> p w u e"), src.rearrange("p (w u e) -> p w u e", u=2, e=2)
+                elif g < PLAIN:
+                    src = src.rearrange("p (w u e) -> p u w e", u=2, e=2)
                     nc.vector.tensor_scalar(out=dst, in0=src, scalar1=scale, scalar2=None, op0=MULT)
                 else:
-                    dst, src = words.rearrange("p u w e -> p (w e) u"), src.rearrange("p (m u) -> p m u", u=2)
+                    dst, src = dst.rearrange("p u w e -> p u (w e)"), src.rearrange("p (m u) -> p u m", u=2)
                     nc.vector.tensor_scalar(out=dst, in0=src, scalar1=scale, scalar2=None, op0=MULT)
 
         def turn(unit, half):
-            bank = ring(psum, "bank", BANKS, [P, 4, P], F32)
-            turned[unit, half] = bank
+            mine = bank((turn, unit, half), [P, 4, P])
             for i in range(2):
                 piece = wide[unit][:, 2 * half + i, :, :, :]
                 for u in range(2):
-                    if 2 * half + i < on_scalar[unit]:
+                    if (unit, 2 * half + i) in on_scalar:
                         words = piece.rearrange("p u w e -> p (u w e)").bitcast(F32)[:, u::2]
                     else:
                         words = piece[:, u, :, :].rearrange("p w e -> p (w e)").bitcast(F32)
-                    nc.tensor.transpose(bank[:, 2 * i + u, :], words, ident[:])
+                    nc.tensor.transpose(mine[:, 2 * i + u, :], words, ident[:])
 
-        def empty(unit, half):
-            if half == 0:
-                grouped[unit] = ring(work, "grouped", GROUP_BUFS, [P, PIECES, P, 4], BF16)
-            words = grouped[unit][:, 2 * half : 2 * half + 2, :, :].rearrange("p i w t -> p (i w t)").bitcast(F32)
-            nc.scalar.copy(
-                out=words.rearrange("p (i w u) -> p i w u", i=2, u=2),
-                in_=turned[unit, half][:].rearrange("p (i u) w -> p i w u", u=2),
-            )
+        def copier(engine):
+            return nc.scalar.copy if engine == "scalar" else nc.vector.tensor_copy
+
+        def empty(unit, half, engine):
+            if unit not in grouped:
+                grouped[unit] = work.tile([P, 2048], BF16, name="grouped%d" % (units.index(unit) % GROUP_BUFS), align_bytes=64)
+            words, src = grouped[unit][:].bitcast(F32), banks[turn, unit, half][:]
+            if unit[0] == "w":
+                dst = words.rearrange("p (w z) -> p w z", z=8)[:, :, 4 * half : 4 * half + 4]
+                copier(engine)(out=dst, in_=src.rearrange("p z w -> p w z"))
+            else:
+                dst = words.rearrange("p (i w u) -> p i w u", i=4, u=2)[:, 2 * half : 2 * half + 2, :, :]
+                copier(engine)(out=dst, in_=src.rearrange("p (i u) w -> p i w u", u=2))
 
         def quant(unit):
-            what, h = unit
-            index = w_units.index(unit) % W_CODE_BUFS if what[0] == "w" else 2 * int(what[1:]) + h
-            unit_codes[unit], unit_scales[unit] = mx_slot(what[0], index)
-            nc.vector.quantize_mx(
-                out=unit_codes[unit].bitcast(FP8X4), scales=unit_scales[unit], in_=grouped[unit][:].rearrange("p i w t -> p (i w t)")
-            )
+            kind, index = unit
+            if kind == "t":
+                at = P * (index - 4)
+                for g in range(PASSES):
+                    quantize(mx("x", PASSES + g, at, at + P), grouped[unit][:, 512 * g : 512 * (g + 1)])
+            else:
+                quantize(mx(kind, index), grouped[unit][:])
 
-        a_int, a_codes, a_scales = {}, {}, {}
-        b_int, b_codes, b_scales = {}, {}, {}
+        def staged(what):
+            if what not in inter:
+                inter[what] = work.tile([P, 2048], BF16, name="inter%d" % (stages.index(what) % INTER_BUFS), align_bytes=64)
+            return inter[what]
 
-        def inter_a(g, t0, t1, engine):
-            if g not in a_int:
-                a_int[g] = ring(work, "a_int", PASSES, [P, 4, P, 4], BF16)
-            (nc.scalar.copy if engine == "scalar" else nc.vector.tensor_copy)(
-                out=a_int[g][:, t0:t1, :, :].rearrange("p t (q m) j -> p q t m j", m=2),
-                in_=a_raw[g][:].rearrange("p j (q m t) -> p q t m j", m=2, t=4)[:, :, t0:t1, :, :],
-            )
+        def weave(what, half, engine):
+            kind, index = what
+            if kind == "a":
+                dst = staged(what)[:].rearrange("p (t q m j) -> p q t m j", t=4, m=2, j=4)
+                src = a_raw[index][:].rearrange("p j (q m t) -> p q t m j", m=2, t=4)
+                copier(engine)(out=dst[:, :, 2 * half : 2 * half + 2, :, :], in_=src[:, :, 2 * half : 2 * half + 2, :, :])
+            else:
+                dst = staged(what)[:].rearrange("p (n i j) -> p n j i", i=4, j=4)
+                src = (b_raw if kind == "b" else h_rows)[index][:].rearrange("p j (n i) -> p n j i", i=4)
+                copier(engine)(out=dst[:, 64 * half : 64 * (half + 1), :, :], in_=src[:, 64 * half : 64 * (half + 1), :, :])
 
-        def quant_a(g):
-            a_codes[g], a_scales[g] = mx_slot("a", g)
-            nc.vector.quantize_mx(out=a_codes[g].bitcast(FP8X4), scales=a_scales[g], in_=a_int[g][:].rearrange("p t m j -> p (t m j)"))
+        def pack(what):
+            quantize(mx(what[0], what[1]), inter[what][:])
 
-        def inter_b(ci):
-            b_int[ci] = ring(work, "b_int", B_BUFS, [P, WIDTH, 4], BF16)
-            nc.scalar.copy(
-                out=b_int[ci][:].rearrange("p (n i) j -> p n j i", i=4), in_=b_raw[ci][:].rearrange("p j (n i) -> p n j i", i=4)
-            )
+        def down(h, t, g):
+            dst = bank((down, h, t, 0), [P, 512]) if g == 0 else banks[down, h, t, 0]
+            product(dst[:], mx("a", g, P * t, P * (t + 1)), mx("x", PASSES * h + g), g == 0, g == PASSES - 1)
 
-        def quant_b(ci):
-            b_codes[ci], b_scales[ci] = mx_slot("b", ci)
-            nc.vector.quantize_mx(out=b_codes[ci].bitcast(FP8X4), scales=b_scales[ci], in_=b_int[ci][:].rearrange("p n j -> p (n j)"))
+        def scale_h(h, t, engine):
+            if h not in h_rows:
+                h_rows[h] = const.tile([P, 4, 512], BF16, name="h_rows%d" % h, align_bytes=64)
+            scaled(h_rows[h][:, t, :], banks[down, h, t, 0][:], lam_f[:, t : t + 1], engine)
 
-        h_banks, h_rows, h_int, h_codes, h_scales = {}, {}, {}, {}, {}
+        def scaled(dst, src, scale, engine):
+            if engine == "scalar":
+                nc.scalar.activation(out=dst, in_=src, func=COPY, scale=scale)
+            else:
+                nc.vector.tensor_scalar(out=dst, in0=src, scalar1=scale, scalar2=None, op0=MULT)
 
-        def down(j, side, h):
-            if h == 0:
-                h_banks[j, side] = ring(psum, "bank", BANKS, [P, 2, 2 * P], F32)
-            unit = ("x%d" % j, h)
-            for g in range(2):
-                for i in range(2):
-                    t = 2 * side + i
-                    nc.tensor.matmul_mx(
-                        out=h_banks[j, side][:, i, :],
-                        lhsT=a_codes[2 * h + g][:, P * t : P * (t + 1)].bitcast(FP8X4),
-                        lhsT_scale=a_scales[2 * h + g][:, P * t : P * (t + 1)],
-                        rhs=unit_codes[unit][:, 2 * P * g : 2 * P * (g + 1)].bitcast(FP8X4),
-                        rhs_scale=unit_scales[unit][:, 2 * P * g : 2 * P * (g + 1)],
-                        start=(h == 0 and g == 0 and i == 0),
-                        stop=(h == 1 and g == 1 and i == 1),
-                    )
+        def tokens(what, m, g):
+            return mx(what, (PASSES * (m // 4) + g) if what == "x" else m // 4, P * (m % 4), P * (m % 4 + 1))
 
-        def scale_h(j, side):
-            if side == 0:
-                h_rows[j] = const.tile([P, 4, 2 * P], BF16, name="h_rows%d" % j, align_bytes=64)
-            for i in range(2):
-                t = 2 * side + i
-                nc.scalar.activation(out=h_rows[j][:, t, :], in_=h_banks[j, side][:, i, :], func=COPY, scale=lam_f[:, t : t + 1])
+        def base(m, ci, g, n0=0, n1=WIDTH):
+            first = (base, m, ci, 0) + ((n0, n1) if n1 - n0 < WIDTH else ())
+            dst = bank(first, [P, WIDTH]) if g == 0 else banks[first]
+            product(dst[:, n0:n1], tokens("x", m, g), mx("w", PASSES * ci + g, n0, n1), g == 0, g == PASSES - 1)
 
-        def inter_h(j):
-            h_int[j] = ring(work, "h_int", H_BUFS, [P, 2 * P, 4], BF16)
-            nc.vector.tensor_copy(
-                out=h_int[j][:].rearrange("p (n i) t -> p n t i", i=4), in_=h_rows[j][:].rearrange("p t (n i) -> p n t i", i=4)
-            )
+        def up(m, ci):
+            product(bank((up, m, ci), [P, WIDTH])[:], tokens("h", m, 0), mx("b", ci), True, True)
 
-        def quant_h(j):
-            h_codes[j], h_scales[j] = mx_slot("h", j)
-            nc.vector.quantize_mx(out=h_codes[j].bitcast(FP8X4), scales=h_scales[j], in_=h_int[j][:].rearrange("p w t -> p (w t)"))
+        def store(m, ci, n0=0, n1=WIDTH):
+            nc.sync.dma_start(out=out_view[:, m, WIDTH * ci + n0 : WIDTH * ci + n1], in_=y[m, ci][:, n0:n1])
 
-        y, base_banks, d_banks = {}, {}, {}
+        def park(m, ci, engine):
+            y[m, ci] = const.tile([P, WIDTH], F32, name="parked%d_%d" % (m, ci), align_bytes=64)
+            copier(engine)(out=y[m, ci][:], in_=banks[base, m, ci, 0][:])
 
-        def up(j, ci):
-            d_banks[j, ci] = ring(psum, "bank", BANKS, [P, 2, WIDTH], F32)
-            for i in range(2):
-                nc.tensor.matmul_mx(
-                    out=d_banks[j, ci][:, i, :],
-                    lhsT=h_codes[j][:, P * i : P * (i + 1)].bitcast(FP8X4),
-                    lhsT_scale=h_scales[j][:, P * i : P * (i + 1)],
-                    rhs=b_codes[ci].bitcast(FP8X4),
-                    rhs_scale=b_scales[ci],
-                    start=True,
-                    stop=True,
-                )
+        def fuse(m, ci):
+            mine = y[m, ci][:]
+            nc.vector.scalar_tensor_tensor(out=mine, in0=banks[up, m, ci][:], scalar=c_f[:, m : m + 1], in1=mine, op0=MULT, op1=ADD)
+            store(m, ci)
 
-        def base(j, ci, h):
-            if h == 0:
-                base_banks[j, ci] = ring(psum, "bank", BANKS, [P, 2, WIDTH], F32)
-            tokens, rows = ("x%d" % j, h), ("w%d" % ci, h)
-            for g in range(2):
-                for i in range(2):
-                    at = 2 * P * g + P * i
-                    nc.tensor.matmul_mx(
-                        out=base_banks[j, ci][:, i, :],
-                        lhsT=unit_codes[tokens][:, at : at + P].bitcast(FP8X4),
-                        lhsT_scale=unit_scales[tokens][:, at : at + P],
-                        rhs=unit_codes[rows][:, WIDTH * g : WIDTH * (g + 1)].bitcast(FP8X4),
-                        rhs_scale=unit_scales[rows][:, WIDTH * g : WIDTH * (g + 1)],
-                        start=(h == 0 and g == 0 and i == 0),
-                        stop=(h == 1 and g == 1 and i == 1),
-                    )
+        def scale_d(m, ci):
+            y[m, ci] = const.tile([P, WIDTH], F32, name="parked%d_0" % m, align_bytes=64)
+            scaled(y[m, ci][:], banks[up, m, ci][:], c_f[:, m : m + 1], "scalar")
 
-        def base_part(j, i, n0, n1):
-            bank = ring(psum, "bank", BANKS, [P, WIDTH], F32)
-            base_banks[j, i, n0] = bank
-            for g in range(PASSES):
-                tokens, rows = ("x%d" % j, g // 2), (last_chunk, g // 2)
-                at, c0 = 2 * P * (g % 2) + P * i, WIDTH * (g % 2)
-                nc.tensor.matmul_mx(
-                    out=bank[:, n0:n1],
-                    lhsT=unit_codes[tokens][:, at : at + P].bitcast(FP8X4),
-                    lhsT_scale=unit_scales[tokens][:, at : at + P],
-                    rhs=unit_codes[rows][:, c0 + n0 : c0 + n1].bitcast(FP8X4),
-                    rhs_scale=unit_scales[rows][:, c0 + n0 : c0 + n1],
-                    start=(g == 0),
-                    stop=(g == PASSES - 1),
-                )
-
-        def in_order(j, ci):
-            order = "p i (c r) -> p i c r" if ci == LAST else "p i (r c) -> p i c r"
-            return base_banks[j, ci][:].rearrange(order, r=2)
-
-        def store(j, ci):
-            nc.sync.dma_start(out=out_view[:, 2 * j : 2 * j + 2, WIDTH * ci : WIDTH * (ci + 1)], in_=y[j, ci][:])
-
-        def park(j, ci):
-            y[j, ci] = const.tile([P, 2, WIDTH], F32, name="parked%d_%d" % (j, ci), align_bytes=64)
-            nc.scalar.copy(out=y[j, ci][:].rearrange("p i (c r) -> p i c r", r=2), in_=in_order(j, ci))
-
-        def finish_parked(j, ci):
-            for i in range(2):
-                mine, m = y[j, ci][:, i, :], 2 * j + i
-                nc.vector.scalar_tensor_tensor(
-                    out=mine, in0=d_banks[j, ci][:, i, :], scalar=c_f[:, m : m + 1], in1=mine, op0=MULT, op1=ADD
-                )
-            store(j, ci)
-
-        def scale_d(j, ci):
-            y[j, ci] = ring(work, "y", Y_BUFS, [P, 2, WIDTH], F32)
-            for i in range(2):
-                m = 2 * j + i
-                nc.scalar.activation(out=y[j, ci][:, i, :], in_=d_banks[j, ci][:, i, :], func=COPY, scale=c_f[:, m : m + 1])
-
-        def add(j, ci):
-            pairs = y[j, ci][:].rearrange("p i (c r) -> p i c r", r=2)
-            nc.vector.tensor_tensor(out=pairs, in0=in_order(j, ci), in1=pairs, op=ADD)
-            store(j, ci)
-
-        def add_part(j, i, n0, n1):
-            mine = y[j, LAST][:, i, n0:n1]
-            nc.vector.tensor_tensor(out=mine, in0=base_banks[j, i, n0][:, n0:n1], in1=mine, op=ADD)
-            nc.sync.dma_start(out=out_view[:, 2 * j + i, N - WIDTH + n0 : N - WIDTH + n1], in_=mine)
+        def add(m, ci, n0=0, n1=WIDTH):
+            first = (base, m, ci, 0) + ((n0, n1) if n1 - n0 < WIDTH else ())
+            mine = y[m, ci][:, n0:n1]
+            nc.vector.tensor_tensor(out=mine, in0=banks[first][:, n0:n1], in1=mine, op=ADD)
+            store(m, ci, n0, n1)
 
         def cast_lam():
             nc.scalar.activation(out=lam_f[:], in_=lam_b[:], func=COPY)
@@ -368,166 +279,155 @@ def tile_fp8_base_lora_d2_kernel(tc, x_bytes, x_scale, w_bytes, w_scale, a, lam,
         def cast_c():
             nc.scalar.activation(out=c_f[:], in_=c_b[:], func=COPY)
 
-        def halves(fn, *args):
-            return [(fn,) + args + (half,) for half in range(2)]
+        S, V = "scalar", "vector"
+        units = [unit for g in range(PASSES) for unit in (("x", g), ("w", g))] + [("t", m) for m in range(4, TILES)]
+        units += [("w", n) for n in range(PASSES, CHUNKS * PASSES)]
+        stages = [("a", g) for g in range(PASSES)] + [("b", 0), ("h", 0), ("b", 1), ("h", 1), ("b", 2)]
+        on_scalar = [(("x", 0), 1), (("x", 1), 0), (("x", 1), 1), (("x", 2), 0), (("x", 3), 0), (("x", 3), 1), (("t", 4), 0), (("t", 5), 0)]
+        parked = [(m, ci) for ci in range(2) for m in range(TILES)]
 
-        def each(fn, some_units):
-            return [step for unit in some_units for step in halves(fn, unit)]
+        def turns(unit):
+            return [(turn, unit, half) for half in range(2)]
 
-        def by_vector(some_units):
-            return [(widen, unit, i) for unit in some_units for i in range(on_scalar[unit], PIECES)]
+        def empties(unit, engine=S):
+            return [(empty, unit, half, engine) for half in range(2)]
 
-        def by_scalar(some_units):
-            return [(widen, unit, i) for unit in some_units for i in range(on_scalar[unit])]
+        def widens(unit, mine=False):
+            return [(widen, unit, i) for i in range(4) if ((unit, i) in on_scalar) == mine]
 
-        def downs(j, h):
-            return [(down, j, side, h) for side in range(2)]
+        def across(ci, g):
+            return [(base, m, ci, g) for m in range(4)]
 
-        def bases(pairs, ci, h):
-            return [(base, j, ci, h) for j in pairs]
+        def along(m, ci):
+            return [(base, m, ci, g) for g in range(PASSES)]
 
-        runs = [units[:2]] + [[unit] for unit in units[2 : 2 + SINGLES]]
-        runs += [units[s : s + 2] for s in range(2 + SINGLES, len(units), 2)]
-        run_of = {ci: runs.index([("w%d" % ci, 0), ("w%d" % ci, 1)]) for ci in range(1, CHUNKS)}
-        after = [downs(0, 0), downs(0, 1), downs(1, 0), downs(1, 1), bases((0, 1), 0, 0), bases((0, 1), 0, 1)]
-        after += [downs(2, 0) + bases((2,), 0, 0), downs(2, 1) + bases((2,), 0, 1) + downs(3, 0)]
-        after += [downs(3, 1) + halves(base, 3, 0) + halves(base, 0, 1) + halves(base, 1, 1)]
-        products = [(j, ci) for ci in range(CHUNKS) for j in range(PAIRS)]
-        parked = products[: PARKED * PAIRS]
-        waiting = list(parked)
-        for ci in range(PARKED, CHUNKS):
-            first = PAIRS * ci - 2
-            steps = []
-            for n in range(first, first + PAIRS if ci < LAST else len(products)):
-                parts = [(base_part,) + part for part in ENDING if (part[0], LAST) == products[n]]
-                steps += parts if parts else halves(base, *products[n])
-                if n + UP_AHEAD < len(products):
-                    steps += [(up,) + products[n + UP_AHEAD]]
-                if n - first < UNPARK[ci]:
-                    steps += [(up,) + waiting.pop(0)]
-            after.append(steps)
-        tensor = []
-        for n, run in enumerate(runs):
-            tensor += each(turn, run) + after[n]
+        def downs(h, g):
+            return [(down, h, t, g) for t in range(4)]
+
+        def weaves(what, engine):
+            return [(weave, what, half, engine) for half in range(2)]
+
+        w = {n: ("w", n) for n in range(CHUNKS * PASSES)}
+        tensor = turns(units[0]) + turns(units[1])
+        for g in range(PASSES):
+            tensor += turns(units[2 * g + 2]) + turns(units[2 * g + 3]) + across(0, g)
+        tensor += turns(("t", 6)) + turns(("t", 7)) + along(4, 0) + along(5, 0) + along(6, 0) + downs(0, 0) + along(7, 0)
+        tensor += downs(1, 0) + downs(0, 1) + downs(0, 2) + downs(0, 3) + downs(1, 1)
+        tensor += turns(w[4]) + downs(1, 2) + turns(w[5]) + downs(1, 3) + turns(w[6]) + turns(w[7])
+        for g in range(PASSES):
+            tensor += across(1, g)
+        tensor += along(4, 1) + [(up, 0, 0), (up, 1, 0)] + along(5, 1) + [(up, 2, 0), (up, 3, 0)] + turns(w[8])
+        tensor += along(6, 1) + [(up, 0, 1), (up, 1, 1)] + along(7, 1) + [(up, 2, 1), (up, 3, 1)] + turns(w[9])
+        tensor += [(up, 4, 0), (up, 5, 0)] + across(2, 0) + [(up, 6, 0), (up, 7, 0)] + turns(w[10]) + across(2, 1) + [(up, 4, 1), (up, 0, 2)] + turns(w[11])
+        tensor += [(up, 5, 1), (up, 1, 2)] + across(2, 2) + [(up, 6, 1), (up, 2, 2), (up, 7, 1), (up, 3, 2)] + across(2, 3)
+        tensor += [(up, 4, 2), (up, 5, 2)] + along(4, 2) + [(up, 6, 2)] + along(5, 2) + [(up, 7, 2)] + along(6, 2)
+        ending = ((0, 256), (256, 384), (384, 512))
+        for part in ending:
+            tensor += [(base, TILES - 1, 2, g) + part for g in range(PASSES)]
+
+        vector = widens(units[0]) + widens(units[1])
+        for n in range(8):
+            vector += widens(units[n + 2]) + [(quant, units[n])]
+        vector += widens(("t", 6)) + widens(("t", 7)) + [(quant, ("t", 4)), (quant, ("t", 5))]
+        vector += weaves(("a", 0), V) + [(quant, ("t", 6)), (pack, ("a", 0)), (weave, ("a", 1), 0, V), (quant, ("t", 7)), (weave, ("a", 1), 1, V)]
+        vector += [(weave, ("a", 3), 0, V), (pack, ("a", 1))] + widens(w[4])[:2] + [(pack, ("a", 2))] + widens(w[4])[2:] + [(pack, ("a", 3))]
+        vector += widens(w[5]) + widens(w[6]) + widens(w[7]) + weaves(("h", 0), V) + [(quant, w[4])]
+        vector += [(scale_h, 1, 1, V), (scale_h, 1, 3, V), (quant, w[5]), (pack, ("h", 0)), (quant, w[6])] + widens(w[8])[:2] + [(quant, w[7])]
+        vector += widens(w[8])[2:] + [(pack, ("b", 0))] + widens(w[9]) + [(pack, ("b", 1)), (fuse, 0, 0), (fuse, 1, 0)] + widens(w[10]) + [(fuse, 2, 0), (fuse, 3, 0)]
+        vector += [(pack, ("h", 1)), (fuse, 0, 1), (fuse, 1, 1), (quant, w[8]), (fuse, 2, 1), (fuse, 3, 1)] + widens(w[11])[:2]
+        vector += [(fuse, 4, 0), (fuse, 5, 0), (quant, w[9])] + widens(w[11])[2:] + [(pack, ("b", 2)), (fuse, 6, 0), (fuse, 7, 0), (quant, w[10]), (fuse, 4, 1), (fuse, 5, 1), (quant, w[11])]
+        vector += [(fuse, 6, 1), (fuse, 7, 1)] + [(add, m, 2) for m in range(TILES - 1)]
+        vector += [(add, TILES - 1, 2) + part for part in ending]
+
+        scalar = widens(units[0], True) + [(pick_scales,)] + empties(units[0]) + widens(units[2], True) + empties(units[1])
+        scalar += widens(units[4], True) + empties(units[2]) + empties(units[3]) + widens(units[6], True) + empties(units[4]) + empties(units[5])
+        scalar += widens(("t", 4), True) + empties(units[6]) + widens(("t", 5), True) + empties(units[7]) + widens(("t", 6), True) + widens(("t", 7), True)
+        scalar += empties(("t", 4)) + empties(("t", 5)) + [(park, 0, 0, S), (park, 1, 0, S)]
+        scalar += empties(("t", 6)) + [(park, 2, 0, S), (park, 3, 0, S)] + empties(("t", 7)) + [(cast_lam,), (park, 4, 0, S)]
+        scalar += [(park, 5, 0, S), (weave, ("a", 2), 0, S), (park, 6, 0, S), (weave, ("a", 2), 1, S), (park, 7, 0, S), (weave, ("a", 3), 1, S), (cast_c,)]
+        scalar += weaves(("b", 0), S) + [(scale_h, 0, t, S) for t in range(4)] + empties(w[4]) + empties(w[5])
+        scalar += [(scale_h, 1, 0, S), (scale_h, 1, 2, S)] + empties(w[6]) + empties(w[7]) + weaves(("b", 1), S)
+        scalar += [(park, 0, 1, S), (park, 1, 1, S), (park, 2, 1, S), (park, 3, 1, S), (weave, ("h", 1), 0, S), (park, 4, 1, S), (weave, ("h", 1), 1, S), (park, 5, 1, S)] + empties(w[8])
+        scalar += [(park, 6, 1, S), (weave, ("b", 2), 0, S), (park, 7, 1, S)] + empties(w[9]) + [(weave, ("b", 2), 1, S)] + empties(w[10]) + [(scale_d, 0, 2)] + empties(w[11])
+        scalar += [(scale_d, m, 2) for m in range(1, TILES)]
+
+        bank_of, idle, held = {}, list(range(BANKS)), {}
+        for step in tensor:
+            whole = step[0] in (turn, up)
+            if whole or step[3] == 0:
+                bank_of[step] = idle.pop(0)
+                held[step[:3] + step[4:]] = bank_of[step]
+            if whole or step[3] == PASSES - 1:
+                idle.append(held[step[:3] + step[4:]])
 
         def reader(step):
             fn, args = step[0], step[1:]
             if fn == up:
-                return (finish_parked if args in parked else scale_d,) + args
+                return (fuse if args in parked else scale_d,) + args
             if fn == base:
-                return (park if args[:2] in parked else add,) + args[:2]
+                return ((park if args[:2] in parked else add,) + args[:2] + args[3:])
             if fn == down:
                 return (scale_h,) + args[:2]
-            return ({turn: empty, base_part: add_part}[fn],) + args
+            return (empty,) + args
 
-        def results(n, fns):
-            done = [step for step in after[n] if step[0] in (up, base_part) or step[-1] == 1]
-            return [reader(step) for step in done if reader(step)[0] in fns]
+        def key(step):
+            return step[:-1] if step[-1] in ("scalar", "vector") else step
 
-        vector = by_vector(runs[0]) + [(inter_a, 0, 0, 4, "vector"), (quant, units[0]), (quant_a, 0)]
-        vector += [(inter_a, 2, 0, 4, "vector"), (quant_a, 1)] + by_vector(runs[1]) + [(quant, units[1])]
-        vector += [(inter_a, 3, 0, 2, "vector"), (quant_a, 2), (quant_a, 3)]
-        for n in range(1, len(runs)):
-            ahead = by_vector(runs[n + 1]) if n + 1 < len(runs) else []
-            lead, more, rest = ahead[:PIECES], ahead[PIECES : PIECES + 2], ahead[PIECES + 2 :]
-            one, two = [(quant, runs[n][0])], [(quant, unit) for unit in runs[n][1:]]
-            if n < run_of[1]:
-                vector += lead + one + more + two + rest
-            elif n == run_of[1]:
-                vector += lead + one + more + two + [(inter_h, 0), (inter_h, 1), (quant_h, 0), (quant_b, 2), (quant_h, 1)] + rest
-            elif n == run_of[2]:
-                vector += lead + one + [(inter_h, 2)] + two + [(quant_h, 2), (inter_h, 3)] + more + [(quant_h, 3), (add, 0, 2)]
-                vector += rest + [(quant_b, 3), (quant_b, 0)]
-            else:
-                ci = n - run_of[1] + 1
-                sums = results(n, (finish_parked, add, add_part))
-                vector += [(add, 1, ci - 1)] + lead + one + sums[:1] + more + two
-                if ci == B1_CHUNK:
-                    vector += [(quant_b, 1)]
-                if ci < LAST:
-                    vector += sums[1:2] + rest + sums[2:3] + [(quant_b, ci + 1)] + sums[3:-1]
-                else:
-                    vector += sums[1:]
-
-        scalar = by_scalar(runs[0]) + halves(empty, units[0]) + [(inter_a, 1, 0, 4, "scalar")] + halves(empty, units[1])
-        scalar += by_scalar(runs[1]) + [(inter_a, 3, 2, 4, "scalar"), (cast_lam,)]
-        extra = {2: [(cast_c,)] + by_scalar([("x2", 0)]), 5: by_scalar([("x3", 0)]), SINGLES: [(inter_b, 2)]}
-        late = []
-        for n in range(1, run_of[1]):
-            mine = results(n, (scale_h, park))
-            keep = 1 if n <= SINGLES else len(mine)
-            scalar += each(empty, runs[n]) + late + extra.get(n, []) + mine[:keep]
-            late = mine[keep:]
-        for ci in range(1, CHUNKS):
-            mine = results(run_of[ci], (scale_h, park, scale_d))
-            scalar += each(empty, runs[run_of[ci]])
-            if ci == B1_CHUNK:
-                scalar += [(inter_b, 1)]
-            if ci == 1:
-                scalar += mine[:1] + [(inter_b, 0)] + mine[1:]
-            elif ci < LAST:
-                scalar += mine[:-2] + [(inter_b, ci + 1)] + mine[-2:]
-            else:
-                scalar += mine
-
-        bank_users = [step for step in tensor if step[0] in (turn, up, base_part) or step[-1] == 0]
-        y_users = [step for step in scalar if step[0] == scale_d]
-        b_users = [step for step in scalar if step[0] == inter_b]
-
-        def before(users, step, depth):
-            n = users.index(step) if step in users else 0
+        def before(users, one, depth):
+            n = users.index(one)
             return users[n - depth : n - depth + 1] if n >= depth else []
+
+        holder = {}
+        freed = {}
+        for step in tensor:
+            if step in bank_of:
+                freed[step] = [reader(holder[bank_of[step]])] if bank_of[step] in holder else []
+                holder[bank_of[step]] = step
+
+        def token_unit(m, g):
+            return ("x", g) if m < 4 else ("t", m)
 
         def needs(step):
             fn, args = step[0], step[1:]
-            bank = [reader(old) for old in before(bank_users, step, BANKS)]
+            free = freed.get(step, [])
             if fn == widen:
-                return each(turn, before(units, args[0], WIDE_BUFS))
+                return [(turn, old, half) for old in before(units, args[0], WIDE_BUFS) for half in range(2)] + ([(pick_scales,)] if args[0][0] == "w" else [])
             if fn == turn:
-                return [(widen, args[0], 2 * args[1]), (widen, args[0], 2 * args[1] + 1)] + bank
+                pieces = range(4) if args[0][0] == "w" else (2 * args[1], 2 * args[1] + 1)
+                return [(widen, args[0], i) for i in pieces] + free
             if fn == empty:
                 return [(turn,) + args] + [(quant, old) for old in before(units, args[0], GROUP_BUFS)]
             if fn == quant:
-                freed = [(base, PAIRS - 1, int(old[0][1:]), old[1]) for old in before(w_units, args[0], W_CODE_BUFS)]
-                return halves(empty, args[0]) + freed
-            if fn == quant_a:
-                return [other for other in vector + scalar if other[:2] == (inter_a, args[0])]
-            if fn == inter_b:
-                return [(quant_b, old[1]) for old in before(b_users, step, B_BUFS)]
-            if fn == quant_b:
-                return [(inter_b,) + args]
+                return [(empty, args[0], half) for half in range(2)]
+            if fn == weave:
+                made = [(scale_h, args[0][1], t) for t in range(4)] if args[0][0] == "h" else []
+                return made + [(pack, old) for old in before(stages, args[0], INTER_BUFS)]
+            if fn == pack:
+                return [(weave, args[0], half) for half in range(2)]
             if fn == down:
-                j, side, h = args
-                return bank + [(quant, ("x%d" % j, h)), (quant_a, 2 * h), (quant_a, 2 * h + 1)]
+                h, t, g = args
+                return free + [(pack, ("a", g))] + [(quant, token_unit(m, g)) for m in range(4 * h, 4 * h + 4)]
             if fn == scale_h:
-                return [(down,) + args + (1,), (cast_lam,)]
-            if fn == inter_h:
-                return halves(scale_h, args[0]) + [(quant_h, old) for old in before(list(range(PAIRS)), args[0], H_BUFS)]
-            if fn == quant_h:
-                return [(inter_h,) + args]
+                return [(down,) + args + (PASSES - 1,), (cast_lam,)]
             if fn == up:
-                return bank + [(quant_h, args[0]), (quant_b, args[1])]
-            if fn == scale_d:
-                return [(up,) + args, (cast_c,)] + [(add,) + old[1:] for old in before(y_users, step, Y_BUFS)]
+                return free + [(pack, ("h", args[0] // 4)), (pack, ("b", args[1]))]
             if fn == base:
-                return bank + [(quant, ("x%d" % args[0], args[2])), (quant, ("w%d" % args[1], args[2]))]
-            if fn == base_part:
-                return bank + [(quant, (last_chunk, 1))]
+                return free + [(quant, token_unit(args[0], args[2])), (quant, ("w", PASSES * args[1] + args[2]))]
+            if fn == scale_d:
+                return [(up,) + args, (cast_c,), (fuse, args[0], 0)]
             if fn == park:
-                return [(base,) + args + (1,)]
-            if fn == finish_parked:
+                return [(base,) + args + (PASSES - 1,)]
+            if fn == fuse:
                 return [(up,) + args, (park,) + args, (cast_c,)]
             if fn == add:
-                return [(base,) + args + (1,), (scale_d,) + args]
-            if fn == add_part:
-                return [(base_part,) + args, (scale_d, args[0], LAST)]
+                return [(base,) + args[:2] + (PASSES - 1,) + args[2:], (scale_d,) + args[:2]]
             return []
 
         written = set()
         lists = [tensor, vector, scalar]
         while any(lists):
-            ready = [steps for steps in lists if steps and all(need in written for need in needs(steps[0]))]
+            ready = [steps for steps in lists if steps and all(need in written for need in needs(key(steps[0])))]
             step = ready[0][0]
             step[0](*step[1:])
-            written.add(step)
+            written.add(key(step))
             lists = [steps[1:] if steps and steps[0] == step else steps for steps in lists]

@@ -25,7 +25,7 @@ CHUNKS = N // WIDTH
 CODE_AT = {"w": 0, "b": 0, "x": 64, "h": 64, "a": 128}
 SCALE_AT = {"w": 128, "b": 128, "x": 192, "h": 192, "a": 0}
 SCALE_ROW = {"w": 4, "b": 4, "x": 8, "h": 8, "a": 12}
-LOAD_ORDER = "xs x001 ws w001 x012 w012 x024 w024 t4 t6 a0 a1 a2 a3 lam c w102 w124 b0 b1 w202 w224 b2"
+LOAD_ORDER = "xs x001 w001 ws0 x012 w012 x024 w024 t4 t6 ws a0 a1 a2 a3 lam c w102 w124 b0 b1 w202 w224 b2"
 PLAIN = 4
 WIDE_BUFS, GROUP_BUFS, INTER_BUFS = 5, 3, 4
 BANKS = 8
@@ -74,8 +74,8 @@ def tile_fp8_base_lora_d2_kernel(tc, x_bytes, x_scale, w_bytes, w_scale, a, lam,
         nc.scalar.activation(out=unread[:], in_=seed[:], func=COPY)
 
         xs = const.tile([P, TILES * K_BLOCKS], F32, name="xs")
-        ws_all = const.tile([P, 4 * CHUNKS * K_BLOCKS], F32, name="ws_all")
-        ws = const.tile([P, CHUNKS, K_BLOCKS], F32, name="ws")
+        ws_first = const.tile([P, K_BLOCKS], F32, name="ws_first")
+        ws_rest = const.tile([P, 5 * K_BLOCKS], F32, name="ws_rest")
         lam_b = const.tile([P, 4], BF16, name="lam_b")
         c_b = const.tile([P, TILES], BF16, name="c_b")
         lam_f = const.tile([P, 4], F32, name="lam_f")
@@ -85,8 +85,13 @@ def tile_fp8_base_lora_d2_kernel(tc, x_bytes, x_scale, w_bytes, w_scale, a, lam,
         for what in LOAD_ORDER.split(" "):
             if what == "xs":
                 nc.sync.dma_start(out=xs[:], in_=x_scale.rearrange("(p m) j -> p (m j)", m=TILES))
+            elif what == "ws0":
+                for q in range(4):
+                    nc.sync.dma_start(out=ws_first[32 * q : 32 * (q + 1), :], in_=w_scale[q].partition_broadcast(32))
             elif what == "ws":
-                nc.sync.dma_start(out=ws_all[:], in_=w_scale.rearrange("i j -> (i j)").partition_broadcast(P))
+                for q in range(4):
+                    mine = w_scale[4 + q : 9 + q, :].rearrange("i j -> (i j)")
+                    nc.sync.dma_start(out=ws_rest[32 * q : 32 * (q + 1), :], in_=mine.partition_broadcast(32))
             elif what == "lam":
                 nc.sync.dma_start(out=lam_b[:], in_=lam.rearrange("(p t) -> p t", t=4))
             elif what == "c":
@@ -125,18 +130,14 @@ def tile_fp8_base_lora_d2_kernel(tc, x_bytes, x_scale, w_bytes, w_scale, a, lam,
             banks[step] = psum.tile(shape, F32, name="bank%d" % bank_of[step])
             return banks[step]
 
-        def pick_scales():
-            for q in range(4):
-                mine = ws_all[32 * q : 32 * (q + 1), :].rearrange("p (c q j) -> p c q j", q=4, j=K_BLOCKS)
-                nc.scalar.copy(out=ws[32 * q : 32 * (q + 1), :, :], in_=mine[:, :, q, :])
-
         def widen(unit, i):
             if unit not in wide:
                 wide[unit] = work.tile([P, 4, 2, P, 2], BF16, name="wide%d" % (units.index(unit) % WIDE_BUFS), align_bytes=64)
             kind, index = unit
             if kind == "w":
                 ci, g = divmod(index, PASSES)
-                scale = ws[:, ci, 4 * g + i : 4 * g + i + 1]
+                scales, at = (ws_first, 4 * g + i) if ci == 0 else (ws_rest, 4 * K_BLOCKS * (ci - 1) + 4 * g + i)
+                scale = scales[:, at : at + 1]
                 src = rows[unit][:, :, P * i : P * (i + 1)].bitcast(FP8)
                 dst = wide[unit][:, :, :, 32 * i : 32 * (i + 1), :]
                 if g < PLAIN:
@@ -339,7 +340,7 @@ def tile_fp8_base_lora_d2_kernel(tc, x_bytes, x_scale, w_bytes, w_scale, a, lam,
         vector += [(fuse, 6, 1), (fuse, 7, 1)] + [(add, m, 2) for m in range(TILES - 1)]
         vector += [(add, TILES - 1, 2) + part for part in ending]
 
-        scalar = widens(units[0], True) + [(pick_scales,)] + empties(units[0]) + widens(units[2], True) + empties(units[1])
+        scalar = widens(units[0], True) + empties(units[0]) + widens(units[2], True) + empties(units[1])
         scalar += widens(units[4], True) + empties(units[2]) + empties(units[3]) + widens(units[6], True) + empties(units[4]) + empties(units[5])
         scalar += widens(("t", 4), True) + empties(units[6]) + widens(("t", 5), True) + empties(units[7]) + widens(("t", 6), True) + widens(("t", 7), True)
         scalar += empties(("t", 4)) + empties(("t", 5)) + [(park, 0, 0, S), (park, 1, 0, S)]
@@ -391,7 +392,7 @@ def tile_fp8_base_lora_d2_kernel(tc, x_bytes, x_scale, w_bytes, w_scale, a, lam,
             fn, args = step[0], step[1:]
             free = freed.get(step, [])
             if fn == widen:
-                return [(turn, old, half) for old in before(units, args[0], WIDE_BUFS) for half in range(2)] + ([(pick_scales,)] if args[0][0] == "w" else [])
+                return [(turn, old, half) for old in before(units, args[0], WIDE_BUFS) for half in range(2)]
             if fn == turn:
                 pieces = range(4) if args[0][0] == "w" else (2 * args[1], 2 * args[1] + 1)
                 return [(widen, args[0], i) for i in pieces] + free

@@ -130,6 +130,14 @@ def tile_fp8_base_lora_d2_kernel(tc, x_bytes, x_scale, w_bytes, w_scale, a, lam,
             banks[step] = psum.tile(shape, F32, name="bank%d" % bank_of[step])
             return banks[step]
 
+        zeros = const.tile([P, 512], BF16, name="zeros", align_bytes=64)
+        nc.vector.memset(zeros[:], 0.0)
+        spare = psum.tile([P, 512], F32, name="bank%d" % (BANKS - 1))
+
+        def warm(round_, count):
+            for n in range(count):
+                nc.tensor.matmul(out=spare[:], lhsT=zeros[:, :P], rhs=zeros[:], start=True, stop=True)
+
         def widen(unit, i):
             if unit not in wide:
                 wide[unit] = work.tile([P, 4, 2, P, 2], BF16, name="wide%d" % (units.index(unit) % WIDE_BUFS), align_bytes=64)
@@ -309,9 +317,9 @@ def tile_fp8_base_lora_d2_kernel(tc, x_bytes, x_scale, w_bytes, w_scale, a, lam,
             return [(weave, what, half, engine) for half in range(2)]
 
         w = {n: ("w", n) for n in range(CHUNKS * PASSES)}
-        tensor = turns(units[0]) + turns(units[1])
+        tensor = [(warm, 0, 4)] + turns(units[0]) + [(warm, 1, 2)] + turns(units[1])
         for g in range(PASSES):
-            tensor += turns(units[2 * g + 2]) + turns(units[2 * g + 3]) + across(0, g)
+            tensor += turns(units[2 * g + 2]) + ([(warm, 2, 2)] if g == 0 else []) + turns(units[2 * g + 3]) + across(0, g)
         tensor += turns(("t", 6)) + turns(("t", 7)) + along(4, 0) + along(5, 0) + along(6, 0) + downs(0, 0) + along(7, 0)
         tensor += downs(1, 0) + downs(0, 1) + downs(0, 2) + downs(0, 3) + downs(1, 1)
         tensor += turns(w[4]) + downs(1, 2) + turns(w[5]) + downs(1, 3) + turns(w[6]) + turns(w[7])
@@ -353,7 +361,7 @@ def tile_fp8_base_lora_d2_kernel(tc, x_bytes, x_scale, w_bytes, w_scale, a, lam,
         scalar += [(scale_d, m, 2) for m in range(1, TILES)]
 
         bank_of, idle, held = {}, list(range(BANKS)), {}
-        for step in tensor:
+        for step in [step for step in tensor if step[0] != warm]:
             whole = step[0] in (turn, up)
             if whole or step[3] == 0:
                 bank_of[step] = idle.pop(0)

@@ -273,7 +273,7 @@ def tile_fp8_base_lora_d2_kernel(tc, x_bytes, x_scale, w_bytes, w_scale, a, lam,
             store(m, ci)
 
         def scale_d(m, ci):
-            y[m, ci] = const.tile([P, WIDTH], F32, name="parked%d_0" % m, align_bytes=64)
+            y[m, ci] = const.tile([P, WIDTH], F32, name="sum%d" % m, align_bytes=64)
             scaled(y[m, ci][:], banks[up, m, ci][:], c_f[:, m : m + 1], "scalar")
 
         def add(m, ci, n0=0, n1=WIDTH):
@@ -291,9 +291,9 @@ def tile_fp8_base_lora_d2_kernel(tc, x_bytes, x_scale, w_bytes, w_scale, a, lam,
         S, V = "scalar", "vector"
         units = [unit for g in range(PASSES) for unit in (("x", g), ("w", g))] + [("t", m) for m in range(4, TILES)]
         units += [("w", n) for n in range(PASSES, CHUNKS * PASSES)]
-        stages = [("a", g) for g in range(PASSES)] + [("b", 0), ("h", 0), ("b", 1), ("h", 1), ("b", 2)]
+        stages = [("a", g) for g in range(PASSES)] + [("b", 1), ("h", 0), ("h", 1), ("b", 0), ("b", 2)]
         on_scalar = [(("x", 0), 1), (("x", 1), 0), (("x", 1), 1), (("x", 2), 0), (("x", 3), 0), (("x", 3), 1), (("t", 4), 0), (("t", 5), 0)]
-        parked = [(m, ci) for ci in range(2) for m in range(TILES)]
+        parked = [(m, 0) for m in range(TILES)]
 
         def turns(unit):
             return [(turn, unit, half) for half in range(2)]
@@ -321,15 +321,14 @@ def tile_fp8_base_lora_d2_kernel(tc, x_bytes, x_scale, w_bytes, w_scale, a, lam,
         for g in range(PASSES):
             tensor += turns(units[2 * g + 2]) + ([(warm, 2, 2)] if g == 0 else []) + turns(units[2 * g + 3]) + across(0, g)
         tensor += turns(("t", 6)) + turns(("t", 7)) + along(4, 0) + along(5, 0) + along(6, 0) + downs(0, 0) + along(7, 0)
-        tensor += downs(1, 0) + downs(0, 1) + downs(0, 2) + downs(0, 3) + downs(1, 1)
-        tensor += turns(w[4]) + downs(1, 2) + turns(w[5]) + downs(1, 3) + turns(w[6]) + turns(w[7])
-        for g in range(PASSES):
-            tensor += across(1, g)
-        tensor += along(4, 1) + [(up, 0, 0), (up, 1, 0)] + along(5, 1) + [(up, 2, 0), (up, 3, 0)] + turns(w[8])
-        tensor += along(6, 1) + [(up, 0, 1), (up, 1, 1)] + along(7, 1) + [(up, 2, 1), (up, 3, 1)] + turns(w[9])
-        tensor += [(up, 4, 0), (up, 5, 0)] + across(2, 0) + [(up, 6, 0), (up, 7, 0)] + turns(w[10]) + across(2, 1) + [(up, 4, 1), (up, 0, 2)] + turns(w[11])
-        tensor += [(up, 5, 1), (up, 1, 2)] + across(2, 2) + [(up, 6, 1), (up, 2, 2), (up, 7, 1), (up, 3, 2)] + across(2, 3)
-        tensor += [(up, 4, 2), (up, 5, 2)] + along(4, 2) + [(up, 6, 2)] + along(5, 2) + [(up, 7, 2)] + along(6, 2)
+        tensor += downs(1, 0) + downs(0, 1) + downs(0, 2) + downs(1, 1) + downs(0, 3)
+        tensor += downs(1, 2) + turns(w[4]) + turns(w[5]) + downs(1, 3) + turns(w[6]) + turns(w[7])
+        tensor += across(1, 0) + across(1, 1) + across(1, 2) + [(up, m, 1) for m in range(4)] + across(1, 3)
+        tensor += [(up, 4, 1)] + along(4, 1) + [(up, 5, 1)] + along(5, 1) + turns(w[8]) + turns(w[9])
+        tensor += [(up, 6, 1)] + along(6, 1) + [(up, 7, 1), (up, 0, 0)] + along(7, 1) + [(up, 1, 0)] + turns(w[10]) + turns(w[11])
+        tensor += across(2, 0) + across(2, 1) + [(up, 2, 0), (up, 3, 0), (up, 0, 2), (up, 1, 2)] + across(2, 2)
+        tensor += [(up, 4, 0), (up, 2, 2), (up, 5, 0), (up, 3, 2)] + across(2, 3)
+        tensor += [(up, 4, 2), (up, 5, 2)] + along(4, 2) + [(up, 6, 2), (up, 6, 0)] + along(5, 2) + [(up, 7, 2), (up, 7, 0)] + along(6, 2)
         ending = ((0, 256), (256, 384), (384, 512))
         for part in ending:
             tensor += [(base, TILES - 1, 2, g) + part for g in range(PASSES)]
@@ -338,14 +337,14 @@ def tile_fp8_base_lora_d2_kernel(tc, x_bytes, x_scale, w_bytes, w_scale, a, lam,
         for n in range(8):
             vector += widens(units[n + 2]) + [(quant, units[n])]
         vector += widens(("t", 6)) + widens(("t", 7)) + [(quant, ("t", 4)), (quant, ("t", 5))]
-        vector += weaves(("a", 0), V) + [(quant, ("t", 6)), (pack, ("a", 0)), (weave, ("a", 1), 0, V), (quant, ("t", 7)), (weave, ("a", 1), 1, V)]
-        vector += [(weave, ("a", 3), 0, V), (pack, ("a", 1))] + widens(w[4])[:2] + [(pack, ("a", 2))] + widens(w[4])[2:] + [(pack, ("a", 3))]
-        vector += widens(w[5]) + widens(w[6]) + widens(w[7]) + weaves(("h", 0), V) + [(quant, w[4])]
-        vector += [(scale_h, 1, 1, V), (scale_h, 1, 3, V), (quant, w[5]), (pack, ("h", 0)), (quant, w[6])] + widens(w[8])[:2] + [(quant, w[7])]
-        vector += widens(w[8])[2:] + [(pack, ("b", 0))] + widens(w[9]) + [(pack, ("b", 1)), (fuse, 0, 0), (fuse, 1, 0)] + widens(w[10]) + [(fuse, 2, 0), (fuse, 3, 0)]
-        vector += [(pack, ("h", 1)), (fuse, 0, 1), (fuse, 1, 1), (quant, w[8]), (fuse, 2, 1), (fuse, 3, 1)] + widens(w[11])[:2]
-        vector += [(fuse, 4, 0), (fuse, 5, 0), (quant, w[9])] + widens(w[11])[2:] + [(pack, ("b", 2)), (fuse, 6, 0), (fuse, 7, 0), (quant, w[10]), (fuse, 4, 1), (fuse, 5, 1), (quant, w[11])]
-        vector += [(fuse, 6, 1), (fuse, 7, 1)] + [(add, m, 2) for m in range(TILES - 1)]
+        vector += weaves(("a", 0), V) + [(quant, ("t", 6)), (pack, ("a", 0)), (weave, ("a", 1), 0, V), (quant, ("t", 7))]
+        vector += [(weave, ("a", 2), 0, V), (pack, ("a", 1)), (weave, ("a", 2), 1, V)] + widens(w[4])[:2] + [(pack, ("a", 2))] + widens(w[4])[2:]
+        vector += widens(w[5])[:2] + [(pack, ("a", 3))] + widens(w[5])[2:] + widens(w[6]) + widens(w[7]) + [(weave, ("b", 1), 1, V)] + weaves(("h", 0), V) + [(quant, w[4])]
+        vector += [(scale_h, 1, 1, V), (scale_h, 1, 3, V), (quant, w[5]), (pack, ("h", 0)), (quant, w[6]), (pack, ("b", 1))]
+        vector += widens(w[8])[:2] + [(quant, w[7])] + widens(w[8])[2:] + widens(w[9])[:2] + [(pack, ("h", 1))] + widens(w[9])[2:] + [(add, m, 1) for m in range(4)]
+        vector += widens(w[10]) + [(add, 4, 1), (pack, ("b", 0)), (add, 5, 1)] + widens(w[11]) + [(quant, w[8]), (add, 6, 1), (fuse, 0, 0), (quant, w[9]), (add, 7, 1), (fuse, 1, 0)]
+        vector += [(pack, ("b", 2)), (quant, w[10]), (fuse, 2, 0), (fuse, 3, 0), (quant, w[11]), (fuse, 4, 0), (fuse, 5, 0)]
+        vector += [(add, m, 2) for m in range(5)] + [(fuse, 6, 0), (add, 5, 2), (fuse, 7, 0), (add, 6, 2)]
         vector += [(add, TILES - 1, 2) + part for part in ending]
 
         scalar = widens(units[0], True) + empties(units[0]) + widens(units[2], True) + empties(units[1])
@@ -353,12 +352,12 @@ def tile_fp8_base_lora_d2_kernel(tc, x_bytes, x_scale, w_bytes, w_scale, a, lam,
         scalar += widens(("t", 4), True) + empties(units[6]) + widens(("t", 5), True) + empties(units[7]) + widens(("t", 6), True) + widens(("t", 7), True)
         scalar += empties(("t", 4)) + empties(("t", 5)) + [(park, 0, 0, S), (park, 1, 0, S)]
         scalar += empties(("t", 6)) + [(park, 2, 0, S), (park, 3, 0, S)] + empties(("t", 7)) + [(cast_lam,), (park, 4, 0, S)]
-        scalar += [(park, 5, 0, S), (weave, ("a", 2), 0, S), (park, 6, 0, S), (weave, ("a", 2), 1, S), (park, 7, 0, S), (weave, ("a", 3), 1, S), (cast_c,)]
-        scalar += weaves(("b", 0), S) + [(scale_h, 0, t, S) for t in range(4)] + empties(w[4]) + empties(w[5])
-        scalar += [(scale_h, 1, 0, S), (scale_h, 1, 2, S)] + empties(w[6]) + empties(w[7]) + weaves(("b", 1), S)
-        scalar += [(park, 0, 1, S), (park, 1, 1, S), (park, 2, 1, S), (park, 3, 1, S), (weave, ("h", 1), 0, S), (park, 4, 1, S), (weave, ("h", 1), 1, S), (park, 5, 1, S)] + empties(w[8])
-        scalar += [(park, 6, 1, S), (weave, ("b", 2), 0, S), (park, 7, 1, S)] + empties(w[9]) + [(weave, ("b", 2), 1, S)] + empties(w[10]) + [(scale_d, 0, 2)] + empties(w[11])
-        scalar += [(scale_d, m, 2) for m in range(1, TILES)]
+        scalar += [(weave, ("a", 1), 1, S), (park, 5, 0, S), (park, 6, 0, S), (park, 7, 0, S)] + weaves(("a", 3), S) + [(cast_c,)]
+        scalar += [(weave, ("b", 1), 0, S)] + [(scale_h, 0, t, S) for t in range(4)] + empties(w[4]) + empties(w[5])
+        scalar += [(scale_h, 1, 0, S), (scale_h, 1, 2, S)] + empties(w[6]) + empties(w[7]) + weaves(("h", 1), S)
+        scalar += [(scale_d, m, 1) for m in range(4)] + [(weave, ("b", 0), 0, S), (scale_d, 4, 1), (weave, ("b", 0), 1, S), (scale_d, 5, 1)] + empties(w[8])
+        scalar += [(scale_d, 6, 1)] + empties(w[9]) + [(scale_d, 7, 1)] + weaves(("b", 2), S) + empties(w[10]) + empties(w[11])
+        scalar += [(scale_d, m, 2) for m in range(TILES)]
 
         bank_of, idle, held = {}, list(range(BANKS)), {}
         for step in [step for step in tensor if step[0] != warm]:
@@ -423,7 +422,7 @@ def tile_fp8_base_lora_d2_kernel(tc, x_bytes, x_scale, w_bytes, w_scale, a, lam,
             if fn == base:
                 return free + [(quant, token_unit(args[0], args[2])), (quant, ("w", PASSES * args[1] + args[2]))]
             if fn == scale_d:
-                return [(up,) + args, (cast_c,), (fuse, args[0], 0)]
+                return [(up,) + args, (cast_c,)] + ([(add, args[0], 1)] if args[1] == 2 else [])
             if fn == park:
                 return [(base,) + args + (PASSES - 1,)]
             if fn == fuse:

@@ -318,9 +318,10 @@ def tile_fp8_base_lora_d2_kernel(tc, x_bytes, x_scale, w_bytes, w_scale, a, lam,
 
         w = {n: ("w", n) for n in range(CHUNKS * PASSES)}
         tensor = [(warm, 0, 4)] + turns(units[0]) + [(warm, 1, 2)] + turns(units[1])
+        tensor += turns(units[2]) + [(warm, 2, 2)] + turns(units[3])
         for g in range(PASSES):
-            tensor += turns(units[2 * g + 2]) + ([(warm, 2, 2)] if g == 0 else []) + turns(units[2 * g + 3]) + across(0, g)
-        tensor += turns(("t", 6)) + turns(("t", 7)) + along(4, 0) + along(5, 0) + along(6, 0) + downs(0, 0) + along(7, 0)
+            tensor += across(0, g)[:2] + turns(units[2 * g + 4]) + across(0, g)[2:] + turns(units[2 * g + 5])
+        tensor += along(4, 0) + along(5, 0) + along(6, 0) + downs(0, 0) + along(7, 0)
         tensor += downs(1, 0) + downs(0, 1) + downs(0, 2) + downs(1, 1) + downs(0, 3)
         tensor += downs(1, 2) + turns(w[4]) + turns(w[5]) + downs(1, 3) + turns(w[6]) + turns(w[7])
         tensor += across(1, 0) + across(1, 1) + across(1, 2) + [(up, m, 1) for m in range(4)] + across(1, 3)
@@ -328,10 +329,10 @@ def tile_fp8_base_lora_d2_kernel(tc, x_bytes, x_scale, w_bytes, w_scale, a, lam,
         tensor += [(up, 6, 1)] + along(6, 1) + [(up, 7, 1), (up, 0, 0)] + along(7, 1) + [(up, 1, 0)] + turns(w[10]) + turns(w[11])
         tensor += across(2, 0) + across(2, 1) + [(up, 2, 0), (up, 3, 0), (up, 0, 2), (up, 1, 2)] + across(2, 2)
         tensor += [(up, 4, 0), (up, 2, 2), (up, 5, 0), (up, 3, 2)] + across(2, 3)
-        tensor += [(up, 4, 2), (up, 5, 2)] + along(4, 2) + [(up, 6, 2), (up, 6, 0)] + along(5, 2) + [(up, 7, 2), (up, 7, 0)] + along(6, 2)
-        ending = ((0, 256), (256, 384), (384, 512))
-        for part in ending:
-            tensor += [(base, TILES - 1, 2, g) + part for g in range(PASSES)]
+        tensor += [(up, 4, 2), (up, 5, 2)] + along(4, 2) + [(up, 6, 2), (up, 6, 0)] + along(5, 2) + [(up, 7, 2), (up, 7, 0)]
+        ending = ((6, 0, 256), (6, 256, 512), (7, 0, 256), (7, 256, 384), (7, 384, 512))
+        for m, n0, n1 in ending:
+            tensor += [(base, m, 2, g, n0, n1) for g in range(PASSES)]
 
         vector = widens(units[0]) + widens(units[1])
         for n in range(8):
@@ -339,23 +340,23 @@ def tile_fp8_base_lora_d2_kernel(tc, x_bytes, x_scale, w_bytes, w_scale, a, lam,
         vector += widens(("t", 6)) + widens(("t", 7)) + [(quant, ("t", 4)), (quant, ("t", 5))]
         vector += weaves(("a", 0), V) + [(quant, ("t", 6)), (pack, ("a", 0)), (weave, ("a", 1), 0, V), (quant, ("t", 7))]
         vector += [(weave, ("a", 2), 0, V), (pack, ("a", 1)), (weave, ("a", 2), 1, V)] + widens(w[4])[:2] + [(pack, ("a", 2))] + widens(w[4])[2:]
-        vector += widens(w[5])[:2] + [(pack, ("a", 3))] + widens(w[5])[2:] + widens(w[6]) + widens(w[7]) + [(weave, ("b", 1), 1, V)] + weaves(("h", 0), V) + [(quant, w[4])]
-        vector += [(scale_h, 1, 1, V), (scale_h, 1, 3, V), (quant, w[5]), (pack, ("h", 0)), (quant, w[6]), (pack, ("b", 1))]
+        vector += widens(w[5])[:2] + [(pack, ("a", 3))] + widens(w[5])[2:] + widens(w[6]) + widens(w[7]) + [(pack, ("b", 1))] + weaves(("h", 0), V) + [(quant, w[4])]
+        vector += [(scale_h, 1, 1, V), (scale_h, 1, 3, V), (quant, w[5]), (pack, ("h", 0)), (weave, ("h", 1), 0, V), (quant, w[6])]
         vector += widens(w[8])[:2] + [(quant, w[7])] + widens(w[8])[2:] + widens(w[9])[:2] + [(pack, ("h", 1))] + widens(w[9])[2:] + [(add, m, 1) for m in range(4)]
         vector += widens(w[10]) + [(add, 4, 1), (pack, ("b", 0)), (add, 5, 1)] + widens(w[11]) + [(quant, w[8]), (add, 6, 1), (fuse, 0, 0), (quant, w[9]), (add, 7, 1), (fuse, 1, 0)]
         vector += [(pack, ("b", 2)), (quant, w[10]), (fuse, 2, 0), (fuse, 3, 0), (quant, w[11]), (fuse, 4, 0), (fuse, 5, 0)]
-        vector += [(add, m, 2) for m in range(5)] + [(fuse, 6, 0), (add, 5, 2), (fuse, 7, 0), (add, 6, 2)]
-        vector += [(add, TILES - 1, 2) + part for part in ending]
+        vector += [(add, m, 2) for m in range(5)] + [(fuse, 6, 0), (add, 5, 2), (fuse, 7, 0)]
+        vector += [(add, m, 2, n0, n1) for m, n0, n1 in ending]
 
         scalar = widens(units[0], True) + empties(units[0]) + widens(units[2], True) + empties(units[1])
         scalar += widens(units[4], True) + empties(units[2]) + empties(units[3]) + widens(units[6], True) + empties(units[4]) + empties(units[5])
         scalar += widens(("t", 4), True) + empties(units[6]) + widens(("t", 5), True) + empties(units[7]) + widens(("t", 6), True) + widens(("t", 7), True)
         scalar += empties(("t", 4)) + empties(("t", 5)) + [(park, 0, 0, S), (park, 1, 0, S)]
         scalar += empties(("t", 6)) + [(park, 2, 0, S), (park, 3, 0, S)] + empties(("t", 7)) + [(cast_lam,), (park, 4, 0, S)]
-        scalar += [(weave, ("a", 1), 1, S), (park, 5, 0, S), (park, 6, 0, S), (park, 7, 0, S)] + weaves(("a", 3), S) + [(cast_c,)]
-        scalar += [(weave, ("b", 1), 0, S)] + [(scale_h, 0, t, S) for t in range(4)] + empties(w[4]) + empties(w[5])
-        scalar += [(scale_h, 1, 0, S), (scale_h, 1, 2, S)] + empties(w[6]) + empties(w[7]) + weaves(("h", 1), S)
-        scalar += [(scale_d, m, 1) for m in range(4)] + [(weave, ("b", 0), 0, S), (scale_d, 4, 1), (weave, ("b", 0), 1, S), (scale_d, 5, 1)] + empties(w[8])
+        scalar += [(weave, ("a", 1), 1, S), (park, 5, 0, S), (park, 6, 0, S), (weave, ("a", 3), 0, S), (park, 7, 0, S), (weave, ("a", 3), 1, S), (cast_c,)]
+        scalar += weaves(("b", 1), S) + [(scale_h, 0, t, S) for t in range(4)] + empties(w[4]) + empties(w[5])
+        scalar += [(scale_h, 1, 0, S), (scale_h, 1, 2, S)] + empties(w[6]) + empties(w[7]) + [(weave, ("h", 1), 1, S), (weave, ("b", 0), 0, S)]
+        scalar += [(scale_d, m, 1) for m in range(5)] + [(weave, ("b", 0), 1, S), (scale_d, 5, 1)] + empties(w[8])
         scalar += [(scale_d, 6, 1)] + empties(w[9]) + [(scale_d, 7, 1)] + weaves(("b", 2), S) + empties(w[10]) + empties(w[11])
         scalar += [(scale_d, m, 2) for m in range(TILES)]
 

@@ -25,8 +25,9 @@ CHUNKS = N // WIDTH
 CODE_AT = {"w": 0, "b": 0, "x": 64, "h": 64, "a": 128}
 SCALE_AT = {"w": 128, "b": 128, "x": 192, "h": 192, "a": 0}
 SCALE_ROW = {"w": 4, "b": 4, "x": 8, "h": 8, "a": 12}
-LOAD_ORDER = "xs x001 w001 ws0 x012 w012 x024 w024 t4 t6 ws a0 a1 a2 a3 lam c w102 w124 b0 b1 w202 w224 b2"
+LOAD_ORDER = "xs x001 w001 ws0 x012 w012 x024 w024 t4 t6 ws a0 a1 a2 a3 lam c w104 b1 b0 w204 b2"
 PLAIN = 4
+NEIGHBOURS = 1
 WIDE_BUFS, GROUP_BUFS, INTER_BUFS = 5, 3, 4
 BANKS = 8
 
@@ -61,6 +62,7 @@ def tile_fp8_base_lora_d2_kernel(tc, x_bytes, x_scale, w_bytes, w_scale, a, lam,
 
         x_view = x_bytes.rearrange("(p m) k -> p m k", m=TILES)
         w_view = w_bytes.rearrange("(c p r) k -> c p r k", p=P, r=4)
+        w_runs = w_bytes.rearrange("(c a r j) k -> c r a j k", a=16, r=4, j=8)
         a_view = a.rearrange("(g p j) r -> g p j r", p=P, j=4)
         b_view = b.rearrange("(p j) n -> p j n", j=4)
         out_view = out.rearrange("(p m) n -> p m n", m=TILES)
@@ -118,9 +120,13 @@ def tile_fp8_base_lora_d2_kernel(tc, x_bytes, x_scale, w_bytes, w_scale, a, lam,
                 index, g0, g1 = int(what[1]), int(what[2]), int(what[3])
                 four = x_view[:, :4, :] if what[0] == "x" else w_view[index]
                 part = loads.tile([P, 4, 512 * (g1 - g0)], U8, name="%s_bytes" % what, align_bytes=64)
-                step = 2 if what == "x001" else 4
-                for r in range(0, 4, step):
-                    nc.sync.dma_start(out=part[:, r : r + step, :], in_=four[:, r : r + step, 512 * g0 : 512 * g1])
+                if what[0] == "w" and PASSES * index + g0 >= NEIGHBOURS:
+                    for r in range(4):
+                        nc.sync.dma_start(out=part[:, r, :], in_=w_runs[index, r][:, :, 512 * g0 : 512 * g1])
+                else:
+                    step = 2 if what == "x001" else 4
+                    for r in range(0, 4, step):
+                        nc.sync.dma_start(out=part[:, r : r + step, :], in_=four[:, r : r + step, 512 * g0 : 512 * g1])
                 for g in range(g0, g1):
                     rows[what[0], PASSES * index + g] = part[:, :, 512 * (g - g0) : 512 * (g - g0 + 1)]
 
@@ -199,7 +205,10 @@ def tile_fp8_base_lora_d2_kernel(tc, x_bytes, x_scale, w_bytes, w_scale, a, lam,
             if unit not in grouped:
                 grouped[unit] = work.tile([P, 2048], BF16, name="grouped%d" % (units.index(unit) % GROUP_BUFS), align_bytes=64)
             words, src = grouped[unit][:].bitcast(F32), banks[turn, unit, half][:]
-            if unit[0] == "w":
+            if unit[0] == "w" and unit[1] >= NEIGHBOURS:
+                dst = words.rearrange("p (a r j u) -> p r a j u", r=4, j=8, u=2)[:, 2 * half : 2 * half + 2, :, :, :]
+                copier(engine)(out=dst, in_=src.rearrange("p (i u) (a j) -> p i a j u", u=2, j=8))
+            elif unit[0] == "w":
                 dst = words.rearrange("p (w z) -> p w z", z=8)[:, :, 4 * half : 4 * half + 4]
                 copier(engine)(out=dst, in_=src.rearrange("p z w -> p w z"))
             else:
@@ -292,7 +301,7 @@ def tile_fp8_base_lora_d2_kernel(tc, x_bytes, x_scale, w_bytes, w_scale, a, lam,
         units = [unit for g in range(PASSES) for unit in (("x", g), ("w", g))] + [("t", m) for m in range(4, TILES)]
         units += [("w", n) for n in range(PASSES, CHUNKS * PASSES)]
         stages = [("a", g) for g in range(PASSES)] + [("b", 1), ("h", 0), ("h", 1), ("b", 0), ("b", 2)]
-        on_scalar = [(("x", 0), 1), (("x", 1), 0), (("x", 1), 1), (("x", 2), 0), (("x", 3), 0), (("x", 3), 1), (("t", 4), 0), (("t", 5), 0)]
+        on_scalar = [(("x", 0), 1), (("x", 1), 0), (("x", 1), 1), (("x", 2), 0), (("x", 3), 0), (("x", 3), 1), (("t", 4), 0), (("t", 5), 0), (("t", 6), 0)]
         parked = [(m, 0) for m in range(TILES)]
 
         def turns(unit):
@@ -341,8 +350,8 @@ def tile_fp8_base_lora_d2_kernel(tc, x_bytes, x_scale, w_bytes, w_scale, a, lam,
         vector += weaves(("a", 0), V) + [(quant, ("t", 6)), (pack, ("a", 0)), (weave, ("a", 1), 0, V), (quant, ("t", 7))]
         vector += [(weave, ("a", 2), 0, V), (pack, ("a", 1)), (weave, ("a", 2), 1, V)] + widens(w[4])[:2] + [(pack, ("a", 2))] + widens(w[4])[2:]
         vector += widens(w[5])[:2] + [(pack, ("a", 3))] + widens(w[5])[2:] + widens(w[6]) + widens(w[7]) + [(pack, ("b", 1))] + weaves(("h", 0), V) + [(quant, w[4])]
-        vector += [(scale_h, 1, 1, V), (scale_h, 1, 3, V), (quant, w[5]), (pack, ("h", 0)), (weave, ("h", 1), 0, V), (quant, w[6])]
-        vector += widens(w[8])[:2] + [(quant, w[7])] + widens(w[8])[2:] + widens(w[9])[:2] + [(pack, ("h", 1))] + widens(w[9])[2:] + [(add, m, 1) for m in range(4)]
+        vector += [(scale_h, 1, 1, V), (scale_h, 1, 3, V), (quant, w[5]), (pack, ("h", 0))] + widens(w[8])[:1] + [(quant, w[6]), (weave, ("h", 1), 0, V)]
+        vector += widens(w[8])[1:2] + [(quant, w[7])] + widens(w[8])[2:] + widens(w[9])[:2] + [(pack, ("h", 1))] + widens(w[9])[2:] + [(add, m, 1) for m in range(4)]
         vector += widens(w[10]) + [(add, 4, 1), (pack, ("b", 0)), (add, 5, 1)] + widens(w[11]) + [(quant, w[8]), (add, 6, 1), (fuse, 0, 0), (quant, w[9]), (add, 7, 1), (fuse, 1, 0)]
         vector += [(pack, ("b", 2)), (quant, w[10]), (fuse, 2, 0), (fuse, 3, 0), (quant, w[11]), (fuse, 4, 0), (fuse, 5, 0)]
         vector += [(add, m, 2) for m in range(5)] + [(fuse, 6, 0), (add, 5, 2), (fuse, 7, 0)]

@@ -301,7 +301,7 @@ def tile_fp8_base_lora_d2_kernel(tc, x_bytes, x_scale, w_bytes, w_scale, a, lam,
         units = [unit for g in range(PASSES) for unit in (("x", g), ("w", g))] + [("t", m) for m in range(4, TILES)]
         units += [("w", n) for n in range(PASSES, CHUNKS * PASSES)]
         stages = [("a", g) for g in range(PASSES)] + [("b", 1), ("h", 0), ("h", 1), ("b", 0), ("b", 2)]
-        on_scalar = [(("x", 0), 1), (("x", 1), 0), (("x", 1), 1), (("x", 2), 0), (("x", 3), 0), (("x", 3), 1), (("t", 4), 0), (("t", 5), 0), (("t", 6), 0)]
+        on_scalar = [(("x", 0), 1), (("x", 1), 0), (("x", 1), 1), (("x", 2), 0), (("x", 3), 0), (("t", 4), 0), (("t", 5), 0), (("t", 6), 0)]
         parked = [(m, 0) for m in range(TILES)]
 
         def turns(unit):
@@ -328,9 +328,10 @@ def tile_fp8_base_lora_d2_kernel(tc, x_bytes, x_scale, w_bytes, w_scale, a, lam,
         w = {n: ("w", n) for n in range(CHUNKS * PASSES)}
         tensor = [(warm, 0, 4)] + turns(units[0]) + [(warm, 1, 2)] + turns(units[1])
         tensor += turns(units[2]) + [(warm, 2, 2)] + turns(units[3])
-        for g in range(PASSES):
+        for g in range(3):
             tensor += across(0, g)[:2] + turns(units[2 * g + 4]) + across(0, g)[2:] + turns(units[2 * g + 5])
-        tensor += along(4, 0) + along(5, 0) + along(6, 0) + downs(0, 0) + along(7, 0)
+        tensor += across(0, 3) + turns(units[10]) + turns(units[11])
+        tensor += along(4, 0) + along(5, 0) + along(6, 0) + along(7, 0) + downs(0, 0)
         tensor += downs(1, 0) + downs(0, 1) + downs(0, 2) + downs(1, 1) + downs(0, 3)
         tensor += downs(1, 2) + turns(w[4]) + turns(w[5]) + downs(1, 3) + turns(w[6]) + turns(w[7])
         tensor += across(1, 0) + across(1, 1) + across(1, 2) + [(up, m, 1) for m in range(4)] + across(1, 3)
@@ -347,7 +348,7 @@ def tile_fp8_base_lora_d2_kernel(tc, x_bytes, x_scale, w_bytes, w_scale, a, lam,
         for n in range(8):
             vector += widens(units[n + 2]) + [(quant, units[n])]
         vector += widens(("t", 6)) + widens(("t", 7)) + [(quant, ("t", 4)), (quant, ("t", 5))]
-        vector += weaves(("a", 0), V) + [(quant, ("t", 6)), (pack, ("a", 0)), (weave, ("a", 1), 0, V), (quant, ("t", 7))]
+        vector += [(weave, ("a", 0), 0, V), (quant, ("t", 6)), (weave, ("a", 0), 1, V), (quant, ("t", 7)), (pack, ("a", 0)), (weave, ("a", 1), 0, V)]
         vector += [(weave, ("a", 2), 0, V), (pack, ("a", 1)), (weave, ("a", 2), 1, V)] + widens(w[4])[:2] + [(pack, ("a", 2))] + widens(w[4])[2:]
         vector += widens(w[5])[:2] + [(pack, ("a", 3))] + widens(w[5])[2:] + widens(w[6]) + widens(w[7]) + [(pack, ("b", 1))] + weaves(("h", 0), V) + [(quant, w[4])]
         vector += [(scale_h, 1, 1, V), (scale_h, 1, 3, V), (quant, w[5]), (pack, ("h", 0))] + widens(w[8])[:1] + [(quant, w[6]), (weave, ("h", 1), 0, V)]
@@ -361,8 +362,8 @@ def tile_fp8_base_lora_d2_kernel(tc, x_bytes, x_scale, w_bytes, w_scale, a, lam,
         scalar += widens(units[4], True) + empties(units[2]) + empties(units[3]) + widens(units[6], True) + empties(units[4]) + empties(units[5])
         scalar += widens(("t", 4), True) + empties(units[6]) + widens(("t", 5), True) + empties(units[7]) + widens(("t", 6), True) + widens(("t", 7), True)
         scalar += empties(("t", 4)) + empties(("t", 5)) + [(park, 0, 0, S), (park, 1, 0, S)]
-        scalar += empties(("t", 6)) + [(park, 2, 0, S), (park, 3, 0, S)] + empties(("t", 7)) + [(cast_lam,), (park, 4, 0, S)]
-        scalar += [(weave, ("a", 1), 1, S), (park, 5, 0, S), (park, 6, 0, S), (weave, ("a", 3), 0, S), (park, 7, 0, S), (weave, ("a", 3), 1, S), (cast_c,)]
+        scalar += empties(("t", 6)) + [(park, 2, 0, S)] + empties(("t", 7)) + [(park, 3, 0, S), (cast_lam,), (park, 4, 0, S)]
+        scalar += [(weave, ("a", 1), 1, S), (park, 5, 0, S), (park, 6, 0, S), (park, 7, 0, S), (weave, ("a", 3), 0, S), (weave, ("a", 3), 1, S), (cast_c,)]
         scalar += weaves(("b", 1), S) + [(scale_h, 0, t, S) for t in range(4)] + empties(w[4]) + empties(w[5])
         scalar += [(scale_h, 1, 0, S), (scale_h, 1, 2, S)] + empties(w[6]) + empties(w[7]) + [(weave, ("h", 1), 1, S), (weave, ("b", 0), 0, S)]
         scalar += [(scale_d, m, 1) for m in range(5)] + [(weave, ("b", 0), 1, S), (scale_d, 5, 1)] + empties(w[8])

@@ -18,18 +18,21 @@ ADD = mybir.AluOpType.add
 COPY = mybir.ActivationFunctionType.Copy
 
 TILES = T // P
-PASSES = K // 512
+QUAD = 4
+SPAN = 512
+PASSES = K // SPAN
 K_BLOCKS = K // P
-WIDTH = 512
-CHUNKS = N // WIDTH
+CHUNKS = N // SPAN
+BANKS = 8
 CODE_AT = {"w": 0, "b": 0, "x": 64, "h": 64, "a": 128}
 SCALE_AT = {"w": 128, "b": 128, "x": 192, "h": 192, "a": 0}
 SCALE_ROW = {"w": 4, "b": 4, "x": 8, "h": 8, "a": 12}
-LOAD_ORDER = "xs x001 w001 ws0 x012 w012 x024 w024 t4 t6 ws a0 a1 a2 a3 lam c w104 b1 b0 w204 b2"
-PLAIN = 4
-NEIGHBOURS = 1
-WIDE_BUFS, GROUP_BUFS, INTER_BUFS = 5, 3, 4
-BANKS = 8
+LOAD_ORDER = "xs x002 ws0 w001 w012 x024 w024 t4 t6 ws a0 a1 a2 a3 lam c w104 b1 b0 w204 b2"
+FIRST_LOAD, FIRST_PARTS = "x002", ((0, 1), (1, 2), (2, 4))
+ON_SCALAR = {("x", 1): (0, 1, 3), ("x", 2): (0, 1), ("x", 3): (0,), ("t", 4): (0,), ("t", 5): (0,), ("t", 6): (0,)}
+WIDE_BUFS, GROUP_BUFS, WOVEN_BUFS = 5, 3, 4
+ENDING = ((6, 0, 256), (6, 256, 512), (7, 0, 256), (7, 256, 384), (7, 384, 512))
+SCALAR, VECTOR = "scalar", "vector"
 
 
 def tile_fp8_base_lora_d2_kernel(tc, x_bytes, x_scale, w_bytes, w_scale, a, lam, b, c, out):
@@ -44,13 +47,13 @@ def tile_fp8_base_lora_d2_kernel(tc, x_bytes, x_scale, w_bytes, w_scale, a, lam,
         slots = {"x": 2 * PASSES, "w": CHUNKS * PASSES, "a": PASSES, "b": CHUNKS, "h": 2}
         operands = {}
         for what, count in slots.items():
-            words = codes.tile([P, CODE_AT[what] // 4 + count * 512], U32, name="%s_codes" % what, align_bytes=256)
-            plane = codes.tile([P, SCALE_AT[what] + count * 512], U8, name="%s_scales" % what, align_bytes=256)
+            words = codes.tile([P, CODE_AT[what] // 4 + count * SPAN], U32, name="%s_codes" % what, align_bytes=256)
+            plane = codes.tile([P, SCALE_AT[what] + count * SPAN], U8, name="%s_scales" % what, align_bytes=256)
             operands[what] = (words[:, CODE_AT[what] // 4 :], plane[SCALE_ROW[what] :, SCALE_AT[what] :])
 
-        def mx(what, slot, n0=0, n1=512):
+        def mx(what, slot, n0=0, n1=SPAN):
             words, plane = operands[what]
-            return words[:, 512 * slot + n0 : 512 * slot + n1].bitcast(FP8X4), plane[:, 512 * slot + n0 : 512 * slot + n1]
+            return words[:, SPAN * slot + n0 : SPAN * slot + n1].bitcast(FP8X4), plane[:, SPAN * slot + n0 : SPAN * slot + n1]
 
         def product(dst, fixed, moving, start, stop):
             nc.tensor.matmul_mx(out=dst, lhsT=fixed[0], lhsT_scale=fixed[1], rhs=moving[0], rhs_scale=moving[1], start=start, stop=stop)
@@ -61,11 +64,12 @@ def tile_fp8_base_lora_d2_kernel(tc, x_bytes, x_scale, w_bytes, w_scale, a, lam,
         ctx.enter_context(tc.manual_schedule())
 
         x_view = x_bytes.rearrange("(p m) k -> p m k", m=TILES)
-        w_view = w_bytes.rearrange("(c p r) k -> c p r k", p=P, r=4)
-        w_runs = w_bytes.rearrange("(c a r j) k -> c r a j k", a=16, r=4, j=8)
-        a_view = a.rearrange("(g p j) r -> g p j r", p=P, j=4)
-        b_view = b.rearrange("(p j) n -> p j n", j=4)
+        w_neighbours = w_bytes.rearrange("(c p r) k -> c p r k", p=P, r=QUAD)
+        w_runs = w_bytes.rearrange("(c a r j) k -> c r a j k", a=16, r=QUAD, j=8)
+        a_view = a.rearrange("(g p j) r -> g p j r", p=P, j=QUAD)
+        b_view = b.rearrange("(p j) n -> p j n", j=QUAD)
         out_view = out.rearrange("(p m) n -> p m n", m=TILES)
+        first_w = ("w", 0)
 
         ident = const.tile([P, P], F32, name="ident")
         make_identity(nc, ident[:])
@@ -77,10 +81,10 @@ def tile_fp8_base_lora_d2_kernel(tc, x_bytes, x_scale, w_bytes, w_scale, a, lam,
 
         xs = const.tile([P, TILES * K_BLOCKS], F32, name="xs")
         ws_first = const.tile([P, K_BLOCKS], F32, name="ws_first")
-        ws_rest = const.tile([P, 5 * K_BLOCKS], F32, name="ws_rest")
-        lam_b = const.tile([P, 4], BF16, name="lam_b")
+        ws_rest = const.tile([P, (QUAD + 1) * K_BLOCKS], F32, name="ws_rest")
+        lam_b = const.tile([P, QUAD], BF16, name="lam_b")
         c_b = const.tile([P, TILES], BF16, name="c_b")
-        lam_f = const.tile([P, 4], F32, name="lam_f")
+        lam_f = const.tile([P, QUAD], F32, name="lam_f")
         c_f = const.tile([P, TILES], F32, name="c_f")
         rows, a_raw, b_raw = {}, {}, {}
 
@@ -88,28 +92,24 @@ def tile_fp8_base_lora_d2_kernel(tc, x_bytes, x_scale, w_bytes, w_scale, a, lam,
             if what == "xs":
                 nc.sync.dma_start(out=xs[:], in_=x_scale.rearrange("(p m) j -> p (m j)", m=TILES))
             elif what == "ws0":
-                for q in range(4):
+                for q in range(QUAD):
                     nc.sync.dma_start(out=ws_first[32 * q : 32 * (q + 1), :], in_=w_scale[q].partition_broadcast(32))
             elif what == "ws":
-                for q in range(4):
-                    mine = w_scale[4 + q : 9 + q, :].rearrange("i j -> (i j)")
-                    nc.sync.dma_start(out=ws_rest[32 * q : 32 * (q + 1), :], in_=mine.partition_broadcast(32))
+                for q in range(QUAD):
+                    run = w_scale[QUAD + q : 2 * QUAD + q + 1, :].rearrange("i j -> (i j)")
+                    nc.sync.dma_start(out=ws_rest[32 * q : 32 * (q + 1), :], in_=run.partition_broadcast(32))
             elif what == "lam":
-                nc.sync.dma_start(out=lam_b[:], in_=lam.rearrange("(p t) -> p t", t=4))
+                nc.sync.dma_start(out=lam_b[:], in_=lam.rearrange("(p t) -> p t", t=QUAD))
             elif what == "c":
                 nc.sync.dma_start(out=c_b[:], in_=c.rearrange("(p m) -> p m", m=TILES))
             elif what[0] == "a":
                 g = int(what[1])
-                a_raw[g] = loads.tile([P, 4, R], BF16, name="a_raw%d" % g, align_bytes=64)
-                if g < PLAIN:
-                    nc.sync.dma_start(out=a_raw[g][:], in_=a_view[g])
-                else:
-                    for u in range(2):
-                        nc.sync.dma_start(out=a_raw[g][:, 2 * u : 2 * u + 2, :], in_=a_view[g][:, u::2, :])
+                a_raw[g] = loads.tile([P, QUAD, R], BF16, name="a_raw%d" % g, align_bytes=64)
+                nc.sync.dma_start(out=a_raw[g][:], in_=a_view[g])
             elif what[0] == "b":
                 ci = int(what[1])
-                b_raw[ci] = loads.tile([P, 4, WIDTH], BF16, name="b_raw%d" % ci, align_bytes=64)
-                nc.sync.dma_start(out=b_raw[ci][:], in_=b_view[:, :, WIDTH * ci : WIDTH * (ci + 1)])
+                b_raw[ci] = loads.tile([P, QUAD, SPAN], BF16, name="b_raw%d" % ci, align_bytes=64)
+                nc.sync.dma_start(out=b_raw[ci][:], in_=b_view[:, :, SPAN * ci : SPAN * (ci + 1)])
             elif what[0] == "t":
                 m = int(what[1])
                 both = loads.tile([P, 2, K], U8, name="%s_bytes" % what, align_bytes=64)
@@ -117,178 +117,156 @@ def tile_fp8_base_lora_d2_kernel(tc, x_bytes, x_scale, w_bytes, w_scale, a, lam,
                 for i in range(2):
                     rows["t", m + i] = both[:, i, :].rearrange("p (g k) -> p g k", g=PASSES)
             else:
-                index, g0, g1 = int(what[1]), int(what[2]), int(what[3])
-                four = x_view[:, :4, :] if what[0] == "x" else w_view[index]
-                part = loads.tile([P, 4, 512 * (g1 - g0)], U8, name="%s_bytes" % what, align_bytes=64)
-                if what[0] == "w" and PASSES * index + g0 >= NEIGHBOURS:
-                    for r in range(4):
-                        nc.sync.dma_start(out=part[:, r, :], in_=w_runs[index, r][:, :, 512 * g0 : 512 * g1])
+                kind, index, g0, g1 = what[0], int(what[1]), int(what[2]), int(what[3])
+                k_range = slice(SPAN * g0, SPAN * g1)
+                part = loads.tile([P, QUAD, SPAN * (g1 - g0)], U8, name="%s_bytes" % what, align_bytes=64)
+                if kind == "x":
+                    for m0, m1 in FIRST_PARTS if what == FIRST_LOAD else ((0, QUAD),):
+                        nc.sync.dma_start(out=part[:, m0:m1, :], in_=x_view[:, m0:m1, k_range])
+                elif (kind, PASSES * index + g0) == first_w:
+                    nc.sync.dma_start(out=part[:], in_=w_neighbours[index][:, :, k_range])
                 else:
-                    step = 2 if what == "x001" else 4
-                    for r in range(0, 4, step):
-                        nc.sync.dma_start(out=part[:, r : r + step, :], in_=four[:, r : r + step, 512 * g0 : 512 * g1])
+                    for r in range(QUAD):
+                        nc.sync.dma_start(out=part[:, r, :], in_=w_runs[index, r][:, :, k_range])
                 for g in range(g0, g1):
-                    rows[what[0], PASSES * index + g] = part[:, :, 512 * (g - g0) : 512 * (g - g0 + 1)]
+                    rows[kind, PASSES * index + g] = part[:, :, SPAN * (g - g0) : SPAN * (g - g0 + 1)]
 
-        wide, grouped, inter, h_rows, y, banks = {}, {}, {}, {}, {}, {}
+        w = [("w", n) for n in range(CHUNKS * PASSES)]
+        units = [("x", 0), ("x", 1), w[0], w[1], ("x", 2), w[2], ("x", 3), w[3]] + [("t", m) for m in range(QUAD, TILES)] + w[PASSES:]
+        stages = [("a", g) for g in range(PASSES)] + [("b", 1), ("h", 0), ("h", 1), ("b", 0), ("b", 2)]
+        wide, grouped, woven, h_rows, y, banks, bank_of = {}, {}, {}, {}, {}, {}, {}
 
         def bank(step, shape):
             banks[step] = psum.tile(shape, F32, name="bank%d" % bank_of[step])
             return banks[step]
 
-        zeros = const.tile([P, 512], BF16, name="zeros", align_bytes=64)
+        zeros = const.tile([P, SPAN], BF16, name="zeros", align_bytes=64)
         nc.vector.memset(zeros[:], 0.0)
-        spare = psum.tile([P, 512], F32, name="bank%d" % (BANKS - 1))
+        spare = psum.tile([P, SPAN], F32, name="bank%d" % (BANKS - 1))
 
-        def warm(round_, count):
+        def warm(gap, count):
             for n in range(count):
                 nc.tensor.matmul(out=spare[:], lhsT=zeros[:, :P], rhs=zeros[:], start=True, stop=True)
 
         def widen(unit, i):
             if unit not in wide:
-                wide[unit] = work.tile([P, 4, 2, P, 2], BF16, name="wide%d" % (units.index(unit) % WIDE_BUFS), align_bytes=64)
+                wide[unit] = work.tile([P, QUAD, 2, P, 2], BF16, name="wide%d" % (units.index(unit) % WIDE_BUFS), align_bytes=64)
             kind, index = unit
             if kind == "w":
                 ci, g = divmod(index, PASSES)
-                scales, at = (ws_first, 4 * g + i) if ci == 0 else (ws_rest, 4 * K_BLOCKS * (ci - 1) + 4 * g + i)
-                scale = scales[:, at : at + 1]
-                src = rows[unit][:, :, P * i : P * (i + 1)].bitcast(FP8)
+                scales, at = (ws_first, 0) if ci == 0 else (ws_rest, QUAD * K_BLOCKS * (ci - 1))
+                scale = scales[:, at + 4 * g + i : at + 4 * g + i + 1]
+                src = rows[unit][:, :, P * i : P * (i + 1)].bitcast(FP8).rearrange("p r (v u e) -> p r u v e", u=2, e=2)
                 dst = wide[unit][:, :, :, 32 * i : 32 * (i + 1), :]
-                if g < PLAIN:
-                    for u in range(2):
-                        nc.vector.tensor_scalar(
-                            out=dst[:, :, u, :, :],
-                            in0=src.rearrange("p r (w u e) -> p r u w e", u=2, e=2)[:, :, u, :, :],
-                            scalar1=scale,
-                            scalar2=None,
-                            op0=MULT,
-                        )
-                else:
-                    nc.vector.tensor_scalar(
-                        out=dst.rearrange("p r u w e -> p r u (w e)"),
-                        in0=src.rearrange("p r (m u) -> p r u m", u=2),
-                        scalar1=scale,
-                        scalar2=None,
-                        op0=MULT,
-                    )
+                for u in range(2):
+                    nc.vector.tensor_scalar(out=dst[:, :, u, :, :], in0=src[:, :, u, :, :], scalar1=scale, scalar2=None, op0=MULT)
                 return
             m, g = (i, index) if kind == "x" else (index, i)
             for q in range(4):
                 scale = xs[:, K_BLOCKS * m + 4 * g + q : K_BLOCKS * m + 4 * g + q + 1]
                 src = rows[unit][:, i, P * q : P * (q + 1)].bitcast(FP8)
-                dst = wide[unit][:, i, :, 32 * q : 32 * (q + 1), :]
-                if (unit, i) in on_scalar:
-                    flat = wide[unit][:, i, :, :, :].rearrange("p u w e -> p (u w e)")
+                if i in ON_SCALAR.get(unit, ()):
+                    flat = wide[unit][:, i, :, :, :].rearrange("p u v e -> p (u v e)")
                     nc.scalar.activation(out=flat[:, P * q : P * (q + 1)], in_=src, func=COPY, scale=scale)
-                elif g < PLAIN:
-                    src = src.rearrange("p (w u e) -> p u w e", u=2, e=2)
-                    nc.vector.tensor_scalar(out=dst, in0=src, scalar1=scale, scalar2=None, op0=MULT)
                 else:
-                    dst, src = dst.rearrange("p u w e -> p u (w e)"), src.rearrange("p (m u) -> p u m", u=2)
+                    dst, src = wide[unit][:, i, :, 32 * q : 32 * (q + 1), :], src.rearrange("p (v u e) -> p u v e", u=2, e=2)
                     nc.vector.tensor_scalar(out=dst, in0=src, scalar1=scale, scalar2=None, op0=MULT)
 
         def turn(unit, half):
             mine = bank((turn, unit, half), [P, 4, P])
             for i in range(2):
-                piece = wide[unit][:, 2 * half + i, :, :, :]
+                row = wide[unit][:, 2 * half + i, :, :, :]
                 for u in range(2):
-                    if (unit, 2 * half + i) in on_scalar:
-                        words = piece.rearrange("p u w e -> p (u w e)").bitcast(F32)[:, u::2]
+                    if 2 * half + i in ON_SCALAR.get(unit, ()):
+                        words = row.rearrange("p u v e -> p (u v e)").bitcast(F32)[:, u::2]
                     else:
-                        words = piece[:, u, :, :].rearrange("p w e -> p (w e)").bitcast(F32)
+                        words = row[:, u, :, :].rearrange("p v e -> p (v e)").bitcast(F32)
                     nc.tensor.transpose(mine[:, 2 * i + u, :], words, ident[:])
 
-        def copier(engine):
-            return nc.scalar.copy if engine == "scalar" else nc.vector.tensor_copy
-
-        def empty(unit, half, engine):
+        def empty(unit, half):
             if unit not in grouped:
-                grouped[unit] = work.tile([P, 2048], BF16, name="grouped%d" % (units.index(unit) % GROUP_BUFS), align_bytes=64)
+                grouped[unit] = work.tile([P, QUAD * SPAN], BF16, name="grouped%d" % (units.index(unit) % GROUP_BUFS), align_bytes=64)
             words, src = grouped[unit][:].bitcast(F32), banks[turn, unit, half][:]
-            if unit[0] == "w" and unit[1] >= NEIGHBOURS:
-                dst = words.rearrange("p (a r j u) -> p r a j u", r=4, j=8, u=2)[:, 2 * half : 2 * half + 2, :, :, :]
-                copier(engine)(out=dst, in_=src.rearrange("p (i u) (a j) -> p i a j u", u=2, j=8))
+            if unit == first_w:
+                dst = words.rearrange("p (n z) -> p n z", z=8)[:, :, 4 * half : 4 * half + 4]
+                nc.scalar.copy(out=dst, in_=src.rearrange("p z n -> p n z"))
             elif unit[0] == "w":
-                dst = words.rearrange("p (w z) -> p w z", z=8)[:, :, 4 * half : 4 * half + 4]
-                copier(engine)(out=dst, in_=src.rearrange("p z w -> p w z"))
+                dst = words.rearrange("p (a r j u) -> p r a j u", r=QUAD, j=8, u=2)[:, 2 * half : 2 * half + 2, :, :, :]
+                nc.scalar.copy(out=dst, in_=src.rearrange("p (i u) (a j) -> p i a j u", u=2, j=8))
             else:
-                dst = words.rearrange("p (i w u) -> p i w u", i=4, u=2)[:, 2 * half : 2 * half + 2, :, :]
-                copier(engine)(out=dst, in_=src.rearrange("p (i u) w -> p i w u", u=2))
+                dst = words.rearrange("p (i n u) -> p i n u", i=QUAD, u=2)[:, 2 * half : 2 * half + 2, :, :]
+                nc.scalar.copy(out=dst, in_=src.rearrange("p (i u) n -> p i n u", u=2))
 
         def quant(unit):
             kind, index = unit
             if kind == "t":
-                at = P * (index - 4)
+                at = P * (index - QUAD)
                 for g in range(PASSES):
-                    quantize(mx("x", PASSES + g, at, at + P), grouped[unit][:, 512 * g : 512 * (g + 1)])
+                    quantize(mx("x", PASSES + g, at, at + P), grouped[unit][:, SPAN * g : SPAN * (g + 1)])
             else:
                 quantize(mx(kind, index), grouped[unit][:])
 
-        def staged(what):
-            if what not in inter:
-                inter[what] = work.tile([P, 2048], BF16, name="inter%d" % (stages.index(what) % INTER_BUFS), align_bytes=64)
-            return inter[what]
-
         def weave(what, half, engine):
+            if what not in woven:
+                woven[what] = work.tile([P, QUAD * SPAN], BF16, name="inter%d" % (stages.index(what) % WOVEN_BUFS), align_bytes=64)
             kind, index = what
+            copy = nc.scalar.copy if engine == SCALAR else nc.vector.tensor_copy
             if kind == "a":
-                dst = staged(what)[:].rearrange("p (t q m j) -> p q t m j", t=4, m=2, j=4)
+                dst = woven[what][:].rearrange("p (t q m j) -> p q t m j", t=4, m=2, j=QUAD)
                 src = a_raw[index][:].rearrange("p j (q m t) -> p q t m j", m=2, t=4)
-                copier(engine)(out=dst[:, :, 2 * half : 2 * half + 2, :, :], in_=src[:, :, 2 * half : 2 * half + 2, :, :])
+                copy(out=dst[:, :, 2 * half : 2 * half + 2, :, :], in_=src[:, :, 2 * half : 2 * half + 2, :, :])
             else:
-                dst = staged(what)[:].rearrange("p (n i j) -> p n j i", i=4, j=4)
+                dst = woven[what][:].rearrange("p (n i j) -> p n j i", i=4, j=QUAD)
                 src = (b_raw if kind == "b" else h_rows)[index][:].rearrange("p j (n i) -> p n j i", i=4)
-                copier(engine)(out=dst[:, 64 * half : 64 * (half + 1), :, :], in_=src[:, 64 * half : 64 * (half + 1), :, :])
+                copy(out=dst[:, 64 * half : 64 * (half + 1), :, :], in_=src[:, 64 * half : 64 * (half + 1), :, :])
 
         def pack(what):
-            quantize(mx(what[0], what[1]), inter[what][:])
+            quantize(mx(what[0], what[1]), woven[what][:])
 
-        def down(h, t, g):
-            dst = bank((down, h, t, 0), [P, 512]) if g == 0 else banks[down, h, t, 0]
-            product(dst[:], mx("a", g, P * t, P * (t + 1)), mx("x", PASSES * h + g), g == 0, g == PASSES - 1)
+        def down(quad, t, g):
+            dst = bank((down, quad, t, 0), [P, SPAN]) if g == 0 else banks[down, quad, t, 0]
+            product(dst[:], mx("a", g, P * t, P * (t + 1)), mx("x", PASSES * quad + g), g == 0, g == PASSES - 1)
 
-        def scale_h(h, t, engine):
-            if h not in h_rows:
-                h_rows[h] = const.tile([P, 4, 512], BF16, name="h_rows%d" % h, align_bytes=64)
-            scaled(h_rows[h][:, t, :], banks[down, h, t, 0][:], lam_f[:, t : t + 1], engine)
-
-        def scaled(dst, src, scale, engine):
-            if engine == "scalar":
+        def scale_h(quad, t, engine):
+            if quad not in h_rows:
+                h_rows[quad] = const.tile([P, QUAD, SPAN], BF16, name="h_rows%d" % quad, align_bytes=64)
+            dst, src, scale = h_rows[quad][:, t, :], banks[down, quad, t, 0][:], lam_f[:, t : t + 1]
+            if engine == SCALAR:
                 nc.scalar.activation(out=dst, in_=src, func=COPY, scale=scale)
             else:
                 nc.vector.tensor_scalar(out=dst, in0=src, scalar1=scale, scalar2=None, op0=MULT)
 
-        def tokens(what, m, g):
-            return mx(what, (PASSES * (m // 4) + g) if what == "x" else m // 4, P * (m % 4), P * (m % 4 + 1))
-
-        def base(m, ci, g, n0=0, n1=WIDTH):
-            first = (base, m, ci, 0) + ((n0, n1) if n1 - n0 < WIDTH else ())
-            dst = bank(first, [P, WIDTH]) if g == 0 else banks[first]
-            product(dst[:, n0:n1], tokens("x", m, g), mx("w", PASSES * ci + g, n0, n1), g == 0, g == PASSES - 1)
+        def base(m, ci, g, *part):
+            n0, n1 = part if part else (0, SPAN)
+            dst = bank((base, m, ci, 0) + part, [P, SPAN]) if g == 0 else banks[(base, m, ci, 0) + part]
+            quad, i = divmod(m, QUAD)
+            tokens = mx("x", PASSES * quad + g, P * i, P * (i + 1))
+            product(dst[:, n0:n1], tokens, mx("w", PASSES * ci + g, n0, n1), g == 0, g == PASSES - 1)
 
         def up(m, ci):
-            product(bank((up, m, ci), [P, WIDTH])[:], tokens("h", m, 0), mx("b", ci), True, True)
+            quad, i = divmod(m, QUAD)
+            product(bank((up, m, ci), [P, SPAN])[:], mx("h", quad, P * i, P * (i + 1)), mx("b", ci), True, True)
 
-        def store(m, ci, n0=0, n1=WIDTH):
-            nc.sync.dma_start(out=out_view[:, m, WIDTH * ci + n0 : WIDTH * ci + n1], in_=y[m, ci][:, n0:n1])
+        def store(m, ci, n0=0, n1=SPAN):
+            nc.sync.dma_start(out=out_view[:, m, SPAN * ci + n0 : SPAN * ci + n1], in_=y[m, ci][:, n0:n1])
 
-        def park(m, ci, engine):
-            y[m, ci] = const.tile([P, WIDTH], F32, name="parked%d_%d" % (m, ci), align_bytes=64)
-            copier(engine)(out=y[m, ci][:], in_=banks[base, m, ci, 0][:])
+        def park(m):
+            y[m, 0] = const.tile([P, SPAN], F32, name="parked%d_0" % m, align_bytes=64)
+            nc.scalar.copy(out=y[m, 0][:], in_=banks[base, m, 0, 0][:])
 
-        def fuse(m, ci):
-            mine = y[m, ci][:]
-            nc.vector.scalar_tensor_tensor(out=mine, in0=banks[up, m, ci][:], scalar=c_f[:, m : m + 1], in1=mine, op0=MULT, op1=ADD)
-            store(m, ci)
+        def fuse(m):
+            mine = y[m, 0][:]
+            nc.vector.scalar_tensor_tensor(out=mine, in0=banks[up, m, 0][:], scalar=c_f[:, m : m + 1], in1=mine, op0=MULT, op1=ADD)
+            store(m, 0)
 
         def scale_d(m, ci):
-            y[m, ci] = const.tile([P, WIDTH], F32, name="sum%d" % m, align_bytes=64)
-            scaled(y[m, ci][:], banks[up, m, ci][:], c_f[:, m : m + 1], "scalar")
+            y[m, ci] = const.tile([P, SPAN], F32, name="sum%d" % m, align_bytes=64)
+            nc.scalar.activation(out=y[m, ci][:], in_=banks[up, m, ci][:], func=COPY, scale=c_f[:, m : m + 1])
 
-        def add(m, ci, n0=0, n1=WIDTH):
-            first = (base, m, ci, 0) + ((n0, n1) if n1 - n0 < WIDTH else ())
+        def add(m, ci, *part):
+            n0, n1 = part if part else (0, SPAN)
             mine = y[m, ci][:, n0:n1]
-            nc.vector.tensor_tensor(out=mine, in0=banks[first][:, n0:n1], in1=mine, op=ADD)
+            nc.vector.tensor_tensor(out=mine, in0=banks[(base, m, ci, 0) + part][:, n0:n1], in1=mine, op=ADD)
             store(m, ci, n0, n1)
 
         def cast_lam():
@@ -297,150 +275,150 @@ def tile_fp8_base_lora_d2_kernel(tc, x_bytes, x_scale, w_bytes, w_scale, a, lam,
         def cast_c():
             nc.scalar.activation(out=c_f[:], in_=c_b[:], func=COPY)
 
-        S, V = "scalar", "vector"
-        units = [unit for g in range(PASSES) for unit in (("x", g), ("w", g))] + [("t", m) for m in range(4, TILES)]
-        units += [("w", n) for n in range(PASSES, CHUNKS * PASSES)]
-        stages = [("a", g) for g in range(PASSES)] + [("b", 1), ("h", 0), ("h", 1), ("b", 0), ("b", 2)]
-        on_scalar = [(("x", 0), 1), (("x", 1), 0), (("x", 1), 1), (("x", 2), 0), (("x", 3), 0), (("t", 4), 0), (("t", 5), 0), (("t", 6), 0)]
-        parked = [(m, 0) for m in range(TILES)]
+        def turns(*some):
+            return [(turn, unit, half) for unit in some for half in range(2)]
 
-        def turns(unit):
-            return [(turn, unit, half) for half in range(2)]
+        def empties(*some):
+            return [(empty, unit, half) for unit in some for half in range(2)]
 
-        def empties(unit, engine=S):
-            return [(empty, unit, half, engine) for half in range(2)]
+        def by_vector(*some):
+            return [(widen, unit, i) for unit in some for i in range(QUAD) if i not in ON_SCALAR.get(unit, ())]
 
-        def widens(unit, mine=False):
-            return [(widen, unit, i) for i in range(4) if ((unit, i) in on_scalar) == mine]
+        def by_scalar(unit):
+            return [(widen, unit, i) for i in ON_SCALAR[unit]]
 
-        def across(ci, g):
-            return [(base, m, ci, g) for m in range(4)]
-
-        def along(m, ci):
-            return [(base, m, ci, g) for g in range(PASSES)]
-
-        def downs(h, g):
-            return [(down, h, t, g) for t in range(4)]
+        def quants(*some):
+            return [(quant, unit) for unit in some]
 
         def weaves(what, engine):
             return [(weave, what, half, engine) for half in range(2)]
 
-        w = {n: ("w", n) for n in range(CHUNKS * PASSES)}
-        tensor = [(warm, 0, 4)] + turns(units[0]) + [(warm, 1, 2)] + turns(units[1])
-        tensor += turns(units[2]) + [(warm, 2, 2)] + turns(units[3])
-        for g in range(3):
+        def across(ci, g):
+            return [(base, m, ci, g) for m in range(QUAD)]
+
+        def along(m, ci):
+            return [(base, m, ci, g) for g in range(PASSES)]
+
+        def downs(*steps):
+            return [(down, quad, t, g) for quad, g in steps for t in range(4)]
+
+        def ups(*products):
+            return [(up, m, ci) for m, ci in products]
+
+        tile_unit = {m: ("t", m) for m in range(QUAD, TILES)}
+
+        tensor = [(warm, 0, 4)] + turns(*units[:2]) + [(warm, 1, 2)] + turns(w[0]) + [(warm, 2, 2)] + turns(w[1])
+        for g in range(PASSES - 1):
             tensor += across(0, g)[:2] + turns(units[2 * g + 4]) + across(0, g)[2:] + turns(units[2 * g + 5])
-        tensor += across(0, 3) + turns(units[10]) + turns(units[11])
-        tensor += along(4, 0) + along(5, 0) + along(6, 0) + along(7, 0) + downs(0, 0)
-        tensor += downs(1, 0) + downs(0, 1) + downs(0, 2) + downs(1, 1) + downs(0, 3)
-        tensor += downs(1, 2) + turns(w[4]) + turns(w[5]) + downs(1, 3) + turns(w[6]) + turns(w[7])
-        tensor += across(1, 0) + across(1, 1) + across(1, 2) + [(up, m, 1) for m in range(4)] + across(1, 3)
-        tensor += [(up, 4, 1)] + along(4, 1) + [(up, 5, 1)] + along(5, 1) + turns(w[8]) + turns(w[9])
-        tensor += [(up, 6, 1)] + along(6, 1) + [(up, 7, 1), (up, 0, 0)] + along(7, 1) + [(up, 1, 0)] + turns(w[10]) + turns(w[11])
-        tensor += across(2, 0) + across(2, 1) + [(up, 2, 0), (up, 3, 0), (up, 0, 2), (up, 1, 2)] + across(2, 2)
-        tensor += [(up, 4, 0), (up, 2, 2), (up, 5, 0), (up, 3, 2)] + across(2, 3)
-        tensor += [(up, 4, 2), (up, 5, 2)] + along(4, 2) + [(up, 6, 2), (up, 6, 0)] + along(5, 2) + [(up, 7, 2), (up, 7, 0)]
-        ending = ((6, 0, 256), (6, 256, 512), (7, 0, 256), (7, 256, 384), (7, 384, 512))
-        for m, n0, n1 in ending:
+        tensor += across(0, PASSES - 1) + turns(tile_unit[6], tile_unit[7])
+        for m in tile_unit:
+            tensor += along(m, 0)
+        tensor += downs((0, 0), (1, 0), (0, 1), (0, 2), (1, 1), (0, 3), (1, 2)) + turns(w[4], w[5]) + downs((1, 3)) + turns(w[6], w[7])
+        tensor += across(1, 0) + across(1, 1) + across(1, 2) + ups(*[(m, 1) for m in range(QUAD)]) + across(1, 3)
+        tensor += ups((4, 1)) + along(4, 1) + ups((5, 1)) + along(5, 1) + turns(w[8], w[9])
+        tensor += ups((6, 1)) + along(6, 1) + ups((7, 1), (0, 0)) + along(7, 1) + turns(w[10], w[11])
+        tensor += across(2, 0) + across(2, 1) + ups((1, 0), (2, 0), (0, 2), (1, 2)) + across(2, 2)
+        tensor += ups((3, 0), (2, 2), (4, 0), (3, 2)) + across(2, 3)
+        tensor += ups((4, 2), (5, 2), (5, 0)) + along(4, 2) + ups((6, 2), (6, 0)) + along(5, 2) + ups((7, 2), (7, 0))
+        for m, n0, n1 in ENDING:
             tensor += [(base, m, 2, g, n0, n1) for g in range(PASSES)]
 
-        vector = widens(units[0]) + widens(units[1])
-        for n in range(8):
-            vector += widens(units[n + 2]) + [(quant, units[n])]
-        vector += widens(("t", 6)) + widens(("t", 7)) + [(quant, ("t", 4)), (quant, ("t", 5))]
-        vector += [(weave, ("a", 0), 0, V), (quant, ("t", 6)), (weave, ("a", 0), 1, V), (quant, ("t", 7)), (pack, ("a", 0)), (weave, ("a", 1), 0, V)]
-        vector += [(weave, ("a", 2), 0, V), (pack, ("a", 1)), (weave, ("a", 2), 1, V)] + widens(w[4])[:2] + [(pack, ("a", 2))] + widens(w[4])[2:]
-        vector += widens(w[5])[:2] + [(pack, ("a", 3))] + widens(w[5])[2:] + widens(w[6]) + widens(w[7]) + [(pack, ("b", 1))] + weaves(("h", 0), V) + [(quant, w[4])]
-        vector += [(scale_h, 1, 1, V), (scale_h, 1, 3, V), (quant, w[5]), (pack, ("h", 0))] + widens(w[8])[:1] + [(quant, w[6]), (weave, ("h", 1), 0, V)]
-        vector += widens(w[8])[1:2] + [(quant, w[7])] + widens(w[8])[2:] + widens(w[9])[:2] + [(pack, ("h", 1))] + widens(w[9])[2:] + [(add, m, 1) for m in range(4)]
-        vector += widens(w[10]) + [(add, 4, 1), (pack, ("b", 0)), (add, 5, 1)] + widens(w[11]) + [(quant, w[8]), (add, 6, 1), (fuse, 0, 0), (quant, w[9]), (add, 7, 1), (fuse, 1, 0)]
-        vector += [(pack, ("b", 2)), (quant, w[10]), (fuse, 2, 0), (fuse, 3, 0), (quant, w[11]), (fuse, 4, 0), (fuse, 5, 0)]
-        vector += [(add, m, 2) for m in range(5)] + [(fuse, 6, 0), (add, 5, 2), (fuse, 7, 0)]
-        vector += [(add, m, 2, n0, n1) for m, n0, n1 in ending]
+        vector = by_vector(*units[:4]) + quants(units[0]) + by_vector(units[4]) + quants(w[0], units[1])
+        for n in range(3, 2 * PASSES):
+            vector += by_vector(units[n + 2]) + quants(units[n])
+        vector += by_vector(tile_unit[6], tile_unit[7]) + quants(tile_unit[4], tile_unit[5])
+        a0, a2 = weaves(("a", 0), VECTOR), weaves(("a", 2), VECTOR)
+        vector += a0[:1] + quants(tile_unit[6]) + a0[1:] + quants(tile_unit[7]) + [(pack, ("a", 0)), (weave, ("a", 1), 0, VECTOR)]
+        vector += a2[:1] + [(pack, ("a", 1))] + a2[1:] + by_vector(w[4])[:2] + [(pack, ("a", 2))] + by_vector(w[4])[2:]
+        vector += by_vector(w[5])[:2] + [(pack, ("a", 3))] + by_vector(w[5])[2:] + by_vector(w[6], w[7]) + [(pack, ("b", 1))]
+        vector += weaves(("h", 0), VECTOR) + quants(w[4]) + [(scale_h, 1, 1, VECTOR), (scale_h, 1, 3, VECTOR)] + quants(w[5])
+        vector += [(pack, ("h", 0))] + by_vector(w[8])[:1] + quants(w[6]) + [(weave, ("h", 1), 0, VECTOR)] + by_vector(w[8])[1:2]
+        vector += quants(w[7]) + by_vector(w[8])[2:] + by_vector(w[9])[:2] + [(pack, ("h", 1))] + by_vector(w[9])[2:]
+        vector += [(add, m, 1) for m in range(QUAD)] + by_vector(w[10]) + [(add, 4, 1), (pack, ("b", 0)), (add, 5, 1)] + by_vector(w[11])
+        vector += quants(w[8]) + [(add, 6, 1), (fuse, 0)] + quants(w[9]) + [(add, 7, 1), (pack, ("b", 2))]
+        vector += quants(w[10]) + [(fuse, 1), (fuse, 2)] + quants(w[11]) + [(fuse, 3), (fuse, 4)]
+        vector += [(add, m, 2) for m in range(QUAD)] + [(fuse, 5), (add, 4, 2), (fuse, 6), (add, 5, 2), (fuse, 7)]
+        vector += [(add, m, 2, n0, n1) for m, n0, n1 in ENDING]
 
-        scalar = widens(units[0], True) + empties(units[0]) + widens(units[2], True) + empties(units[1])
-        scalar += widens(units[4], True) + empties(units[2]) + empties(units[3]) + widens(units[6], True) + empties(units[4]) + empties(units[5])
-        scalar += widens(("t", 4), True) + empties(units[6]) + widens(("t", 5), True) + empties(units[7]) + widens(("t", 6), True) + widens(("t", 7), True)
-        scalar += empties(("t", 4)) + empties(("t", 5)) + [(park, 0, 0, S), (park, 1, 0, S)]
-        scalar += empties(("t", 6)) + [(park, 2, 0, S)] + empties(("t", 7)) + [(park, 3, 0, S), (cast_lam,), (park, 4, 0, S)]
-        scalar += [(weave, ("a", 1), 1, S), (park, 5, 0, S), (park, 6, 0, S), (park, 7, 0, S), (weave, ("a", 3), 0, S), (weave, ("a", 3), 1, S), (cast_c,)]
-        scalar += weaves(("b", 1), S) + [(scale_h, 0, t, S) for t in range(4)] + empties(w[4]) + empties(w[5])
-        scalar += [(scale_h, 1, 0, S), (scale_h, 1, 2, S)] + empties(w[6]) + empties(w[7]) + [(weave, ("h", 1), 1, S), (weave, ("b", 0), 0, S)]
-        scalar += [(scale_d, m, 1) for m in range(5)] + [(weave, ("b", 0), 1, S), (scale_d, 5, 1)] + empties(w[8])
-        scalar += [(scale_d, 6, 1)] + empties(w[9]) + [(scale_d, 7, 1)] + weaves(("b", 2), S) + empties(w[10]) + empties(w[11])
+        scalar = by_scalar(("x", 1)) + empties(*units[:3]) + by_scalar(("x", 2)) + empties(w[1]) + by_scalar(("x", 3))
+        scalar += empties(("x", 2), w[2]) + by_scalar(tile_unit[4]) + empties(("x", 3)) + by_scalar(tile_unit[5]) + empties(w[3])
+        scalar += by_scalar(tile_unit[6]) + empties(tile_unit[4], tile_unit[5])
+        scalar += [(park, 0), (park, 1)] + empties(tile_unit[6]) + [(park, 2)] + empties(tile_unit[7]) + [(park, 3), (cast_lam,), (park, 4)]
+        scalar += [(weave, ("a", 1), 1, SCALAR), (park, 5), (park, 6), (park, 7)] + weaves(("a", 3), SCALAR) + [(cast_c,)]
+        scalar += weaves(("b", 1), SCALAR) + [(scale_h, 0, t, SCALAR) for t in range(4)] + empties(w[4], w[5])
+        scalar += [(scale_h, 1, 0, SCALAR), (scale_h, 1, 2, SCALAR)] + empties(w[6], w[7]) + [(weave, ("h", 1), 1, SCALAR)]
+        b0 = weaves(("b", 0), SCALAR)
+        scalar += b0[:1] + [(scale_d, m, 1) for m in range(QUAD + 1)] + b0[1:] + [(scale_d, 5, 1)] + empties(w[8])
+        scalar += [(scale_d, 6, 1)] + empties(w[9]) + [(scale_d, 7, 1)] + weaves(("b", 2), SCALAR) + empties(w[10], w[11])
         scalar += [(scale_d, m, 2) for m in range(TILES)]
-
-        bank_of, idle, held = {}, list(range(BANKS)), {}
-        for step in [step for step in tensor if step[0] != warm]:
-            whole = step[0] in (turn, up)
-            if whole or step[3] == 0:
-                bank_of[step] = idle.pop(0)
-                held[step[:3] + step[4:]] = bank_of[step]
-            if whole or step[3] == PASSES - 1:
-                idle.append(held[step[:3] + step[4:]])
 
         def reader(step):
             fn, args = step[0], step[1:]
             if fn == up:
-                return (fuse if args in parked else scale_d,) + args
+                return (fuse, args[0]) if args[1] == 0 else (scale_d,) + args
             if fn == base:
-                return ((park if args[:2] in parked else add,) + args[:2] + args[3:])
+                return (park, args[0]) if args[1] == 0 else (add,) + args[:2] + args[3:]
             if fn == down:
                 return (scale_h,) + args[:2]
             return (empty,) + args
 
-        def key(step):
-            return step[:-1] if step[-1] in ("scalar", "vector") else step
+        idle, held, opener, freed = list(range(BANKS)), {}, {}, {}
+        for step in tensor:
+            if step[0] == warm:
+                continue
+            whole, group = step[0] in (turn, up), step[:3] + step[4:]
+            if whole or step[3] == 0:
+                held[group] = bank_of[step] = idle.pop(0)
+                freed[step] = [reader(opener[held[group]])] if held[group] in opener else []
+                opener[held[group]] = step
+            if whole or step[3] == PASSES - 1:
+                idle.append(held[group])
 
         def before(users, one, depth):
             n = users.index(one)
             return users[n - depth : n - depth + 1] if n >= depth else []
 
-        holder = {}
-        freed = {}
-        for step in tensor:
-            if step in bank_of:
-                freed[step] = [reader(holder[bank_of[step]])] if bank_of[step] in holder else []
-                holder[bank_of[step]] = step
-
         def token_unit(m, g):
-            return ("x", g) if m < 4 else ("t", m)
+            return ("x", g) if m < QUAD else tile_unit[m]
 
         def needs(step):
             fn, args = step[0], step[1:]
             free = freed.get(step, [])
             if fn == widen:
-                return [(turn, old, half) for old in before(units, args[0], WIDE_BUFS) for half in range(2)]
+                return turns(*before(units, args[0], WIDE_BUFS))
             if fn == turn:
-                pieces = range(4) if args[0][0] == "w" else (2 * args[1], 2 * args[1] + 1)
+                pieces = range(QUAD) if args[0][0] == "w" else (2 * args[1], 2 * args[1] + 1)
                 return [(widen, args[0], i) for i in pieces] + free
             if fn == empty:
-                return [(turn,) + args] + [(quant, old) for old in before(units, args[0], GROUP_BUFS)]
+                return [(turn,) + args] + quants(*before(units, args[0], GROUP_BUFS))
             if fn == quant:
-                return [(empty, args[0], half) for half in range(2)]
+                return empties(args[0])
             if fn == weave:
                 made = [(scale_h, args[0][1], t) for t in range(4)] if args[0][0] == "h" else []
-                return made + [(pack, old) for old in before(stages, args[0], INTER_BUFS)]
+                return made + [(pack, old) for old in before(stages, args[0], WOVEN_BUFS)]
             if fn == pack:
                 return [(weave, args[0], half) for half in range(2)]
             if fn == down:
-                h, t, g = args
-                return free + [(pack, ("a", g))] + [(quant, token_unit(m, g)) for m in range(4 * h, 4 * h + 4)]
+                quad, g = args[0], args[2]
+                return free + [(pack, ("a", g))] + quants(*[token_unit(m, g) for m in range(QUAD * quad, QUAD * (quad + 1))])
             if fn == scale_h:
                 return [(down,) + args + (PASSES - 1,), (cast_lam,)]
             if fn == up:
-                return free + [(pack, ("h", args[0] // 4)), (pack, ("b", args[1]))]
+                return free + [(pack, ("h", args[0] // QUAD)), (pack, ("b", args[1]))]
             if fn == base:
-                return free + [(quant, token_unit(args[0], args[2])), (quant, ("w", PASSES * args[1] + args[2]))]
+                return free + quants(token_unit(args[0], args[2]), w[PASSES * args[1] + args[2]])
             if fn == scale_d:
                 return [(up,) + args, (cast_c,)] + ([(add, args[0], 1)] if args[1] == 2 else [])
             if fn == park:
-                return [(base,) + args + (PASSES - 1,)]
+                return [(base, args[0], 0, PASSES - 1)]
             if fn == fuse:
-                return [(up,) + args, (park,) + args, (cast_c,)]
+                return [(up, args[0], 0), (park,) + args, (cast_c,)]
             if fn == add:
                 return [(base,) + args[:2] + (PASSES - 1,) + args[2:], (scale_d,) + args[:2]]
             return []
+
+        def key(step):
+            return step[:-1] if step[-1] in (SCALAR, VECTOR) else step
 
         written = set()
         lists = [tensor, vector, scalar]

from contextlib import ExitStack

import concourse.mybir as mybir
from concourse.masks import make_identity

T, K, N, R = 1024, 2048, 1536, 512
P = 128
FLOPS = 2 * T * K * N + 2 * T * K * R + 2 * T * R * N

F32 = mybir.dt.float32
BF16 = mybir.dt.bfloat16
U32 = mybir.dt.uint32
U8 = mybir.dt.uint8
FP8 = mybir.dt.float8_e4m3fn
FP8X4 = mybir.dt.float8_e4m3fn_x4
MULT = mybir.AluOpType.mult
ADD = mybir.AluOpType.add
COPY = mybir.ActivationFunctionType.Copy

TILES = T // P
QUAD = 4
SPAN = 512
PASSES = K // SPAN
K_BLOCKS = K // P
CHUNKS = N // SPAN
BANKS = 8
CODE_AT = {"w": 0, "b": 0, "x": 64, "h": 64, "a": 128}
SCALE_AT = {"w": 128, "b": 128, "x": 192, "h": 192, "a": 0}
SCALE_ROW = {"w": 4, "b": 4, "x": 8, "h": 8, "a": 12}
LOAD_ORDER = "xs x002 ws0 w001 w012 x024 w024 t4 t6 ws a0 a1 a2 a3 lam c w104 b1 b0 w204 b2"
FIRST_LOAD, FIRST_PARTS = "x002", ((0, 1), (1, 2), (2, 4))
ON_SCALAR = {("x", 1): (0, 1, 3), ("x", 2): (0, 1), ("x", 3): (0,), ("t", 4): (0,), ("t", 5): (0,), ("t", 6): (0,)}
WIDE_BUFS, GROUP_BUFS, WOVEN_BUFS = 5, 3, 4
ENDING = ((6, 0, 256), (6, 256, 512), (7, 0, 256), (7, 256, 384), (7, 384, 512))
SCALAR, VECTOR = "scalar", "vector"


def tile_fp8_base_lora_d2_kernel(tc, x_bytes, x_scale, w_bytes, w_scale, a, lam, b, c, out):
    nc = tc.nc
    with ExitStack() as ctx:
        const = ctx.enter_context(tc.tile_pool(name="const", bufs=1))
        codes = ctx.enter_context(tc.tile_pool(name="codes", bufs=1))
        loads = ctx.enter_context(tc.tile_pool(name="loads", bufs=1))
        work = ctx.enter_context(tc.tile_pool(name="work", bufs=1))
        psum = ctx.enter_context(tc.psum_pool(name="psum", bufs=1))

        slots = {"x": 2 * PASSES, "w": CHUNKS * PASSES, "a": PASSES, "b": CHUNKS, "h": 2}
        operands = {}
        for what, count in slots.items():
            words = codes.tile([P, CODE_AT[what] // 4 + count * SPAN], U32, name="%s_codes" % what, align_bytes=256)
            plane = codes.tile([P, SCALE_AT[what] + count * SPAN], U8, name="%s_scales" % what, align_bytes=256)
            operands[what] = (words[:, CODE_AT[what] // 4 :], plane[SCALE_ROW[what] :, SCALE_AT[what] :])

        def mx(what, slot, n0=0, n1=SPAN):
            words, plane = operands[what]
            return words[:, SPAN * slot + n0 : SPAN * slot + n1].bitcast(FP8X4), plane[:, SPAN * slot + n0 : SPAN * slot + n1]

        def product(dst, fixed, moving, start, stop):
            nc.tensor.matmul_mx(out=dst, lhsT=fixed[0], lhsT_scale=fixed[1], rhs=moving[0], rhs_scale=moving[1], start=start, stop=stop)

        def quantize(dst, src):
            nc.vector.quantize_mx(out=dst[0], scales=dst[1], in_=src)

        ctx.enter_context(tc.manual_schedule())

        x_view = x_bytes.rearrange("(p m) k -> p m k", m=TILES)
        w_neighbours = w_bytes.rearrange("(c p r) k -> c p r k", p=P, r=QUAD)
        w_runs = w_bytes.rearrange("(c a r j) k -> c r a j k", a=16, r=QUAD, j=8)
        a_view = a.rearrange("(g p j) r -> g p j r", p=P, j=QUAD)
        b_view = b.rearrange("(p j) n -> p j n", j=QUAD)
        out_view = out.rearrange("(p m) n -> p m n", m=TILES)
        first_w = ("w", 0)

        ident = const.tile([P, P], F32, name="ident")
        make_identity(nc, ident[:])

        seed = const.tile([P, 8], F32, name="seed")
        nc.vector.memset(seed[:], 0.0)
        unread = const.tile([P, 8], F32, name="unread")
        nc.scalar.activation(out=unread[:], in_=seed[:], func=COPY)

        xs = const.tile([P, TILES * K_BLOCKS], F32, name="xs")
        ws_first = const.tile([P, K_BLOCKS], F32, name="ws_first")
        ws_rest = const.tile([P, (QUAD + 1) * K_BLOCKS], F32, name="ws_rest")
        lam_b = const.tile([P, QUAD], BF16, name="lam_b")
        c_b = const.tile([P, TILES], BF16, name="c_b")
        lam_f = const.tile([P, QUAD], F32, name="lam_f")
        c_f = const.tile([P, TILES], F32, name="c_f")
        rows, a_raw, b_raw = {}, {}, {}

        for what in LOAD_ORDER.split(" "):
            if what == "xs":
                nc.sync.dma_start(out=xs[:], in_=x_scale.rearrange("(p m) j -> p (m j)", m=TILES))
            elif what == "ws0":
                for q in range(QUAD):
                    nc.sync.dma_start(out=ws_first[32 * q : 32 * (q + 1), :], in_=w_scale[q].partition_broadcast(32))
            elif what == "ws":
                for q in range(QUAD):
                    run = w_scale[QUAD + q : 2 * QUAD + q + 1, :].rearrange("i j -> (i j)")
                    nc.sync.dma_start(out=ws_rest[32 * q : 32 * (q + 1), :], in_=run.partition_broadcast(32))
            elif what == "lam":
                nc.sync.dma_start(out=lam_b[:], in_=lam.rearrange("(p t) -> p t", t=QUAD))
            elif what == "c":
                nc.sync.dma_start(out=c_b[:], in_=c.rearrange("(p m) -> p m", m=TILES))
            elif what[0] == "a":
                g = int(what[1])
                a_raw[g] = loads.tile([P, QUAD, R], BF16, name="a_raw%d" % g, align_bytes=64)
                nc.sync.dma_start(out=a_raw[g][:], in_=a_view[g])
            elif what[0] == "b":
                ci = int(what[1])
                b_raw[ci] = loads.tile([P, QUAD, SPAN], BF16, name="b_raw%d" % ci, align_bytes=64)
                nc.sync.dma_start(out=b_raw[ci][:], in_=b_view[:, :, SPAN * ci : SPAN * (ci + 1)])
            elif what[0] == "t":
                m = int(what[1])
                both = loads.tile([P, 2, K], U8, name="%s_bytes" % what, align_bytes=64)
                nc.sync.dma_start(out=both[:], in_=x_view[:, m : m + 2, :])
                for i in range(2):
                    rows["t", m + i] = both[:, i, :].rearrange("p (g k) -> p g k", g=PASSES)
            else:
                kind, index, g0, g1 = what[0], int(what[1]), int(what[2]), int(what[3])
                k_range = slice(SPAN * g0, SPAN * g1)
                part = loads.tile([P, QUAD, SPAN * (g1 - g0)], U8, name="%s_bytes" % what, align_bytes=64)
                if kind == "x":
                    for m0, m1 in FIRST_PARTS if what == FIRST_LOAD else ((0, QUAD),):
                        nc.sync.dma_start(out=part[:, m0:m1, :], in_=x_view[:, m0:m1, k_range])
                elif (kind, PASSES * index + g0) == first_w:
                    nc.sync.dma_start(out=part[:], in_=w_neighbours[index][:, :, k_range])
                else:
                    for r in range(QUAD):
                        nc.sync.dma_start(out=part[:, r, :], in_=w_runs[index, r][:, :, k_range])
                for g in range(g0, g1):
                    rows[kind, PASSES * index + g] = part[:, :, SPAN * (g - g0) : SPAN * (g - g0 + 1)]

        w = [("w", n) for n in range(CHUNKS * PASSES)]
        units = [("x", 0), ("x", 1), w[0], w[1], ("x", 2), w[2], ("x", 3), w[3]] + [("t", m) for m in range(QUAD, TILES)] + w[PASSES:]
        stages = [("a", g) for g in range(PASSES)] + [("b", 1), ("h", 0), ("h", 1), ("b", 0), ("b", 2)]
        wide, grouped, woven, h_rows, y, banks, bank_of = {}, {}, {}, {}, {}, {}, {}

        def bank(step, shape):
            banks[step] = psum.tile(shape, F32, name="bank%d" % bank_of[step])
            return banks[step]

        zeros = const.tile([P, SPAN], BF16, name="zeros", align_bytes=64)
        nc.vector.memset(zeros[:], 0.0)
        spare = psum.tile([P, SPAN], F32, name="bank%d" % (BANKS - 1))

        def warm(gap, count):
            for n in range(count):
                nc.tensor.matmul(out=spare[:], lhsT=zeros[:, :P], rhs=zeros[:], start=True, stop=True)

        def widen(unit, i):
            if unit not in wide:
                wide[unit] = work.tile([P, QUAD, 2, P, 2], BF16, name="wide%d" % (units.index(unit) % WIDE_BUFS), align_bytes=64)
            kind, index = unit
            if kind == "w":
                ci, g = divmod(index, PASSES)
                scales, at = (ws_first, 0) if ci == 0 else (ws_rest, QUAD * K_BLOCKS * (ci - 1))
                scale = scales[:, at + 4 * g + i : at + 4 * g + i + 1]
                src = rows[unit][:, :, P * i : P * (i + 1)].bitcast(FP8).rearrange("p r (v u e) -> p r u v e", u=2, e=2)
                dst = wide[unit][:, :, :, 32 * i : 32 * (i + 1), :]
                for u in range(2):
                    nc.vector.tensor_scalar(out=dst[:, :, u, :, :], in0=src[:, :, u, :, :], scalar1=scale, scalar2=None, op0=MULT)
                return
            m, g = (i, index) if kind == "x" else (index, i)
            for q in range(4):
                scale = xs[:, K_BLOCKS * m + 4 * g + q : K_BLOCKS * m + 4 * g + q + 1]
                src = rows[unit][:, i, P * q : P * (q + 1)].bitcast(FP8)
                if i in ON_SCALAR.get(unit, ()):
                    flat = wide[unit][:, i, :, :, :].rearrange("p u v e -> p (u v e)")
                    nc.scalar.activation(out=flat[:, P * q : P * (q + 1)], in_=src, func=COPY, scale=scale)
                else:
                    dst, src = wide[unit][:, i, :, 32 * q : 32 * (q + 1), :], src.rearrange("p (v u e) -> p u v e", u=2, e=2)
                    nc.vector.tensor_scalar(out=dst, in0=src, scalar1=scale, scalar2=None, op0=MULT)

        def turn(unit, half):
            mine = bank((turn, unit, half), [P, 4, P])
            for i in range(2):
                row = wide[unit][:, 2 * half + i, :, :, :]
                for u in range(2):
                    if 2 * half + i in ON_SCALAR.get(unit, ()):
                        words = row.rearrange("p u v e -> p (u v e)").bitcast(F32)[:, u::2]
                    else:
                        words = row[:, u, :, :].rearrange("p v e -> p (v e)").bitcast(F32)
                    nc.tensor.transpose(mine[:, 2 * i + u, :], words, ident[:])

        def empty(unit, half):
            if unit not in grouped:
                grouped[unit] = work.tile([P, QUAD * SPAN], BF16, name="grouped%d" % (units.index(unit) % GROUP_BUFS), align_bytes=64)
            words, src = grouped[unit][:].bitcast(F32), banks[turn, unit, half][:]
            if unit == first_w:
                dst = words.rearrange("p (n z) -> p n z", z=8)[:, :, 4 * half : 4 * half + 4]
                nc.scalar.copy(out=dst, in_=src.rearrange("p z n -> p n z"))
            elif unit[0] == "w":
                dst = words.rearrange("p (a r j u) -> p r a j u", r=QUAD, j=8, u=2)[:, 2 * half : 2 * half + 2, :, :, :]
                nc.scalar.copy(out=dst, in_=src.rearrange("p (i u) (a j) -> p i a j u", u=2, j=8))
            else:
                dst = words.rearrange("p (i n u) -> p i n u", i=QUAD, u=2)[:, 2 * half : 2 * half + 2, :, :]
                nc.scalar.copy(out=dst, in_=src.rearrange("p (i u) n -> p i n u", u=2))

        def quant(unit):
            kind, index = unit
            if kind == "t":
                at = P * (index - QUAD)
                for g in range(PASSES):
                    quantize(mx("x", PASSES + g, at, at + P), grouped[unit][:, SPAN * g : SPAN * (g + 1)])
            else:
                quantize(mx(kind, index), grouped[unit][:])

        def weave(what, half, engine):
            if what not in woven:
                woven[what] = work.tile([P, QUAD * SPAN], BF16, name="inter%d" % (stages.index(what) % WOVEN_BUFS), align_bytes=64)
            kind, index = what
            copy = nc.scalar.copy if engine == SCALAR else nc.vector.tensor_copy
            if kind == "a":
                dst = woven[what][:].rearrange("p (t q m j) -> p q t m j", t=4, m=2, j=QUAD)
                src = a_raw[index][:].rearrange("p j (q m t) -> p q t m j", m=2, t=4)
                copy(out=dst[:, :, 2 * half : 2 * half + 2, :, :], in_=src[:, :, 2 * half : 2 * half + 2, :, :])
            else:
                dst = woven[what][:].rearrange("p (n i j) -> p n j i", i=4, j=QUAD)
                src = (b_raw if kind == "b" else h_rows)[index][:].rearrange("p j (n i) -> p n j i", i=4)
                copy(out=dst[:, 64 * half : 64 * (half + 1), :, :], in_=src[:, 64 * half : 64 * (half + 1), :, :])

        def pack(what):
            quantize(mx(what[0], what[1]), woven[what][:])

        def down(quad, t, g):
            dst = bank((down, quad, t, 0), [P, SPAN]) if g == 0 else banks[down, quad, t, 0]
            product(dst[:], mx("a", g, P * t, P * (t + 1)), mx("x", PASSES * quad + g), g == 0, g == PASSES - 1)

        def scale_h(quad, t, engine):
            if quad not in h_rows:
                h_rows[quad] = const.tile([P, QUAD, SPAN], BF16, name="h_rows%d" % quad, align_bytes=64)
            dst, src, scale = h_rows[quad][:, t, :], banks[down, quad, t, 0][:], lam_f[:, t : t + 1]
            if engine == SCALAR:
                nc.scalar.activation(out=dst, in_=src, func=COPY, scale=scale)
            else:
                nc.vector.tensor_scalar(out=dst, in0=src, scalar1=scale, scalar2=None, op0=MULT)

        def base(m, ci, g, *part):
            n0, n1 = part if part else (0, SPAN)
            dst = bank((base, m, ci, 0) + part, [P, SPAN]) if g == 0 else banks[(base, m, ci, 0) + part]
            quad, i = divmod(m, QUAD)
            tokens = mx("x", PASSES * quad + g, P * i, P * (i + 1))
            product(dst[:, n0:n1], tokens, mx("w", PASSES * ci + g, n0, n1), g == 0, g == PASSES - 1)

        def up(m, ci):
            quad, i = divmod(m, QUAD)
            product(bank((up, m, ci), [P, SPAN])[:], mx("h", quad, P * i, P * (i + 1)), mx("b", ci), True, True)

        def store(m, ci, n0=0, n1=SPAN):
            nc.sync.dma_start(out=out_view[:, m, SPAN * ci + n0 : SPAN * ci + n1], in_=y[m, ci][:, n0:n1])

        def park(m):
            y[m, 0] = const.tile([P, SPAN], F32, name="parked%d_0" % m, align_bytes=64)
            nc.scalar.copy(out=y[m, 0][:], in_=banks[base, m, 0, 0][:])

        def fuse(m):
            mine = y[m, 0][:]
            nc.vector.scalar_tensor_tensor(out=mine, in0=banks[up, m, 0][:], scalar=c_f[:, m : m + 1], in1=mine, op0=MULT, op1=ADD)
            store(m, 0)

        def scale_d(m, ci):
            y[m, ci] = const.tile([P, SPAN], F32, name="sum%d" % m, align_bytes=64)
            nc.scalar.activation(out=y[m, ci][:], in_=banks[up, m, ci][:], func=COPY, scale=c_f[:, m : m + 1])

        def add(m, ci, *part):
            n0, n1 = part if part else (0, SPAN)
            mine = y[m, ci][:, n0:n1]
            nc.vector.tensor_tensor(out=mine, in0=banks[(base, m, ci, 0) + part][:, n0:n1], in1=mine, op=ADD)
            store(m, ci, n0, n1)

        def cast_lam():
            nc.scalar.activation(out=lam_f[:], in_=lam_b[:], func=COPY)

        def cast_c():
            nc.scalar.activation(out=c_f[:], in_=c_b[:], func=COPY)

        def turns(*some):
            return [(turn, unit, half) for unit in some for half in range(2)]

        def empties(*some):
            return [(empty, unit, half) for unit in some for half in range(2)]

        def by_vector(*some):
            return [(widen, unit, i) for unit in some for i in range(QUAD) if i not in ON_SCALAR.get(unit, ())]

        def by_scalar(unit):
            return [(widen, unit, i) for i in ON_SCALAR[unit]]

        def quants(*some):
            return [(quant, unit) for unit in some]

        def weaves(what, engine):
            return [(weave, what, half, engine) for half in range(2)]

        def across(ci, g):
            return [(base, m, ci, g) for m in range(QUAD)]

        def along(m, ci):
            return [(base, m, ci, g) for g in range(PASSES)]

        def downs(*steps):
            return [(down, quad, t, g) for quad, g in steps for t in range(4)]

        def ups(*products):
            return [(up, m, ci) for m, ci in products]

        tile_unit = {m: ("t", m) for m in range(QUAD, TILES)}

        tensor = [(warm, 0, 4)] + turns(*units[:2]) + [(warm, 1, 2)] + turns(w[0]) + [(warm, 2, 2)] + turns(w[1])
        for g in range(PASSES - 1):
            tensor += across(0, g)[:2] + turns(units[2 * g + 4]) + across(0, g)[2:] + turns(units[2 * g + 5])
        tensor += across(0, PASSES - 1) + turns(tile_unit[6], tile_unit[7])
        for m in tile_unit:
            tensor += along(m, 0)
        tensor += downs((0, 0), (1, 0), (0, 1), (0, 2), (1, 1), (0, 3), (1, 2)) + turns(w[4], w[5]) + downs((1, 3)) + turns(w[6], w[7])
        tensor += across(1, 0) + across(1, 1) + across(1, 2) + ups(*[(m, 1) for m in range(QUAD)]) + across(1, 3)
        tensor += ups((4, 1)) + along(4, 1) + ups((5, 1)) + along(5, 1) + turns(w[8], w[9])
        tensor += ups((6, 1)) + along(6, 1) + ups((7, 1), (0, 0)) + along(7, 1) + turns(w[10], w[11])
        tensor += across(2, 0) + across(2, 1) + ups((1, 0), (2, 0), (0, 2), (1, 2)) + across(2, 2)
        tensor += ups((3, 0), (2, 2), (4, 0), (3, 2)) + across(2, 3)
        tensor += ups((4, 2), (5, 2), (5, 0)) + along(4, 2) + ups((6, 2), (6, 0)) + along(5, 2) + ups((7, 2), (7, 0))
        for m, n0, n1 in ENDING:
            tensor += [(base, m, 2, g, n0, n1) for g in range(PASSES)]

        vector = by_vector(*units[:4]) + quants(units[0]) + by_vector(units[4]) + quants(w[0], units[1])
        for n in range(3, 2 * PASSES):
            vector += by_vector(units[n + 2]) + quants(units[n])
        vector += by_vector(tile_unit[6], tile_unit[7]) + quants(tile_unit[4], tile_unit[5])
        a0, a2 = weaves(("a", 0), VECTOR), weaves(("a", 2), VECTOR)
        vector += a0[:1] + quants(tile_unit[6]) + a0[1:] + quants(tile_unit[7]) + [(pack, ("a", 0)), (weave, ("a", 1), 0, VECTOR)]
        vector += a2[:1] + [(pack, ("a", 1))] + a2[1:] + by_vector(w[4])[:2] + [(pack, ("a", 2))] + by_vector(w[4])[2:]
        vector += by_vector(w[5])[:2] + [(pack, ("a", 3))] + by_vector(w[5])[2:] + by_vector(w[6], w[7]) + [(pack, ("b", 1))]
        vector += weaves(("h", 0), VECTOR) + quants(w[4]) + [(scale_h, 1, 1, VECTOR), (scale_h, 1, 3, VECTOR)] + quants(w[5])
        vector += [(pack, ("h", 0))] + by_vector(w[8])[:1] + quants(w[6]) + [(weave, ("h", 1), 0, VECTOR)] + by_vector(w[8])[1:2]
        vector += quants(w[7]) + by_vector(w[8])[2:] + by_vector(w[9])[:2] + [(pack, ("h", 1))] + by_vector(w[9])[2:]
        vector += [(add, m, 1) for m in range(QUAD)] + by_vector(w[10]) + [(add, 4, 1), (pack, ("b", 0)), (add, 5, 1)] + by_vector(w[11])
        vector += quants(w[8]) + [(add, 6, 1), (fuse, 0)] + quants(w[9]) + [(add, 7, 1), (pack, ("b", 2))]
        vector += quants(w[10]) + [(fuse, 1), (fuse, 2)] + quants(w[11]) + [(fuse, 3), (fuse, 4)]
        vector += [(add, m, 2) for m in range(QUAD)] + [(fuse, 5), (add, 4, 2), (fuse, 6), (add, 5, 2), (fuse, 7)]
        vector += [(add, m, 2, n0, n1) for m, n0, n1 in ENDING]

        scalar = by_scalar(("x", 1)) + empties(*units[:3]) + by_scalar(("x", 2)) + empties(w[1]) + by_scalar(("x", 3))
        scalar += empties(("x", 2), w[2]) + by_scalar(tile_unit[4]) + empties(("x", 3)) + by_scalar(tile_unit[5]) + empties(w[3])
        scalar += by_scalar(tile_unit[6]) + empties(tile_unit[4], tile_unit[5])
        scalar += [(park, 0), (park, 1)] + empties(tile_unit[6]) + [(park, 2)] + empties(tile_unit[7]) + [(park, 3), (cast_lam,), (park, 4)]
        scalar += [(weave, ("a", 1), 1, SCALAR), (park, 5), (park, 6), (park, 7)] + weaves(("a", 3), SCALAR) + [(cast_c,)]
        scalar += weaves(("b", 1), SCALAR) + [(scale_h, 0, t, SCALAR) for t in range(4)] + empties(w[4], w[5])
        scalar += [(scale_h, 1, 0, SCALAR), (scale_h, 1, 2, SCALAR)] + empties(w[6], w[7]) + [(weave, ("h", 1), 1, SCALAR)]
        b0 = weaves(("b", 0), SCALAR)
        scalar += b0[:1] + [(scale_d, m, 1) for m in range(QUAD + 1)] + b0[1:] + [(scale_d, 5, 1)] + empties(w[8])
        scalar += [(scale_d, 6, 1)] + empties(w[9]) + [(scale_d, 7, 1)] + weaves(("b", 2), SCALAR) + empties(w[10], w[11])
        scalar += [(scale_d, m, 2) for m in range(TILES)]

        def reader(step):
            fn, args = step[0], step[1:]
            if fn == up:
                return (fuse, args[0]) if args[1] == 0 else (scale_d,) + args
            if fn == base:
                return (park, args[0]) if args[1] == 0 else (add,) + args[:2] + args[3:]
            if fn == down:
                return (scale_h,) + args[:2]
            return (empty,) + args

        idle, held, opener, freed = list(range(BANKS)), {}, {}, {}
        for step in tensor:
            if step[0] == warm:
                continue
            whole, group = step[0] in (turn, up), step[:3] + step[4:]
            if whole or step[3] == 0:
                held[group] = bank_of[step] = idle.pop(0)
                freed[step] = [reader(opener[held[group]])] if held[group] in opener else []
                opener[held[group]] = step
            if whole or step[3] == PASSES - 1:
                idle.append(held[group])

        def before(users, one, depth):
            n = users.index(one)
            return users[n - depth : n - depth + 1] if n >= depth else []

        def token_unit(m, g):
            return ("x", g) if m < QUAD else tile_unit[m]

        def needs(step):
            fn, args = step[0], step[1:]
            free = freed.get(step, [])
            if fn == widen:
                return turns(*before(units, args[0], WIDE_BUFS))
            if fn == turn:
                pieces = range(QUAD) if args[0][0] == "w" else (2 * args[1], 2 * args[1] + 1)
                return [(widen, args[0], i) for i in pieces] + free
            if fn == empty:
                return [(turn,) + args] + quants(*before(units, args[0], GROUP_BUFS))
            if fn == quant:
                return empties(args[0])
            if fn == weave:
                made = [(scale_h, args[0][1], t) for t in range(4)] if args[0][0] == "h" else []
                return made + [(pack, old) for old in before(stages, args[0], WOVEN_BUFS)]
            if fn == pack:
                return [(weave, args[0], half) for half in range(2)]
            if fn == down:
                quad, g = args[0], args[2]
                return free + [(pack, ("a", g))] + quants(*[token_unit(m, g) for m in range(QUAD * quad, QUAD * (quad + 1))])
            if fn == scale_h:
                return [(down,) + args + (PASSES - 1,), (cast_lam,)]
            if fn == up:
                return free + [(pack, ("h", args[0] // QUAD)), (pack, ("b", args[1]))]
            if fn == base:
                return free + quants(token_unit(args[0], args[2]), w[PASSES * args[1] + args[2]])
            if fn == scale_d:
                return [(up,) + args, (cast_c,)] + ([(add, args[0], 1)] if args[1] == 2 else [])
            if fn == park:
                return [(base, args[0], 0, PASSES - 1)]
            if fn == fuse:
                return [(up, args[0], 0), (park,) + args, (cast_c,)]
            if fn == add:
                return [(base,) + args[:2] + (PASSES - 1,) + args[2:], (scale_d,) + args[:2]]
            return []

        def key(step):
            return step[:-1] if step[-1] in (SCALAR, VECTOR) else step

        written = set()
        lists = [tensor, vector, scalar]
        while any(lists):
            ready = [steps for steps in lists if steps and all(need in written for need in needs(key(steps[0])))]
            step = ready[0][0]
            step[0](*step[1:])
            written.add(key(step))
            lists = [steps[1:] if steps and steps[0] == step else steps for steps in lists]
